import numpy as np
import ml_dtypes


def mxq(x, axis, fmt="e4m3"):
    dtype, down = {"e4m3": (ml_dtypes.float8_e4m3fn, 7), "e5m2": (ml_dtypes.float8_e5m2, 14)}[fmt]
    v = np.moveaxis(np.asarray(x, np.float32).astype(ml_dtypes.bfloat16).astype(np.float64), axis, -1)
    blocks = v.reshape(v.shape[:-1] + (-1, 32))
    amax = np.abs(blocks).max(-1, keepdims=True)
    byte = np.maximum(np.where(amax > 0, np.frexp(amax)[1] - 1 + 127, 0) - down, 1)
    scale = np.exp2(byte - 127.0)
    codes = (blocks / scale).astype(np.float32).astype(dtype).astype(np.float64)
    return np.moveaxis((codes * scale).reshape(v.shape), -1, axis)


WIDE = False


def mx_kscale(k):
    if not WIDE:
        return np.ones(k)
    levels = np.array([10, -10, 5, -5, 0])
    if k % 512:
        return np.exp2(np.random.permutation(np.resize(levels, k // 32))).repeat(32)
    a = np.empty((k // 512, 16))
    for p in range(k // 512):
        a[p, :8] = np.random.permutation(np.resize(levels, 8))
        for g in range(8):
            far = levels[np.abs(levels - a[p, g]) >= 10]
            a[p, g + 8] = far[np.random.randint(len(far))]
    return np.exp2(a.ravel()).repeat(32)


BF16 = ml_dtypes.bfloat16


def bf(x):
    return np.asarray(x, np.float32).astype(BF16)


def f64(x):
    return np.asarray(x).astype(np.float64)


M, K, J, F, D, C = 1024, 1024, 3, 1024, 512, 1024


def draw0():
    s, u = mx_kscale(K), mx_kscale(D)
    t = mx_kscale(F)
    amp = F ** -0.25
    tj = np.tile(t, J)
    return {"x": bf(np.random.standard_normal((M, K)) * s),
            "w": bf(np.random.standard_normal((K, J * F)) * amp / np.sqrt(K) / s[:, None] * tj),
            "b": bf(0.3 * np.random.standard_normal(J * F) * amp * tj),
            "e": bf(np.random.standard_normal((C, D)) * u),
            "g": bf(np.random.standard_normal((D, F)) * amp / np.sqrt(D) / u[:, None] / t),
            "a": bf(0.3 * np.random.standard_normal(F) * amp / t),
            "r": bf(1 + 0.1 * np.random.standard_normal(C)),
            "d": bf(0.3 * np.random.standard_normal(C))}


def core(x, w, b, e, g, a, r, d):
    z = (mxq(f64(x), 1, "e4m3") @ mxq(f64(w), 0, "e4m3")) + f64(b)
    h = np.max(z.reshape(M, J, F), axis=1)
    v = (mxq(f64(e), 1, "e4m3") @ mxq(f64(g), 0, "e4m3")) + f64(a)
    y = mxq(h, 1, "e4m3") @ mxq(v, 1, "e4m3").T
    return y * f64(r) + f64(d)


def e4m3fn_bytes(y):
    return np.clip(np.asarray(y, np.float64), -448.0, 448.0).astype(np.float32).astype(ml_dtypes.float8_e4m3fn).view(np.uint8)


def e4m3fn_values(b):
    return np.asarray(b, np.uint8).view(ml_dtypes.float8_e4m3fn).astype(np.float64)


def setup_inputs():
    d = draw0()
    x0 = np.asarray(d['x']).astype(np.float64)
    s = (np.max(np.abs(x0), axis=(0,), keepdims=True) / 448.0).astype(np.float32)
    out = {}
    for k, v in d.items():
        if k == 'x':
            out['x_bytes'] = e4m3fn_bytes(x0 / s.astype(np.float64))
            out['x_scale'] = s
        else:
            out[k] = v
    return out


def reference(x_bytes, x_scale, w, b, e, g, a, r, d):
    return core(e4m3fn_values(x_bytes) * x_scale.astype(np.float64), w, b, e, g, a, r, d)

@@ -1,0 +1,487 @@
+from contextlib import ExitStack
+
+import concourse.mybir as mybir
+from concourse.masks import make_identity
+
+M, K, J, F, D, C = 1024, 1024, 3, 1024, 512, 1024
+FLOPS = 2 * M * K * J * F + 2 * C * D * F + 2 * M * F * C
+
+P = 128
+F32 = mybir.dt.float32
+BF16 = mybir.dt.bfloat16
+U8 = mybir.dt.uint8
+U32 = mybir.dt.uint32
+FP8 = mybir.dt.float8_e4m3fn
+FP8X4 = mybir.dt.float8_e4m3fn_x4
+ADD = mybir.AluOpType.add
+MULT = mybir.AluOpType.mult
+MAX = mybir.AluOpType.max
+IDENTITY = mybir.ActivationFunctionType.Identity
+
+W_VEC = [[1, 3], [1, 2], [1, 2], [4, 2], [2, 0], [2, 0]]
+G_VEC = [3, 3]
+V_VEC = [True, True, True, True]
+V_OUT_VEC = [1]
+E_AT = 13
+X_AT = 20
+G_AT = 8
+V_AT = [20, 24, 23, 27]
+Y_AT = [36, 36, 35, 41]
+YT_AT = [38, 42, 41, 49]
+H_LAG = [1, 3]
+X_LAG = [4, 4]
+W_AT = [0, 1, 3, 5, 14]
+W_LAG = 2
+X1_AT = [1, 3, 9, 12]
+Z_ORDER = [[0, 0], [1, 0], [2, 0], [3, 0], [4, 0], [5, 0], [0, 1], [1, 1], [2, 1], [3, 1], [4, 1], [5, 1]]
+ADD_GP = [[0, 1, 1, 1], [1, 0, 1, 1]]
+
+
+def tile_maxout_generated_head_f5_kernel(tc, x_bytes, x_scale, w, b, e, g, a, r, d, out):
+    nc = tc.nc
+    with ExitStack() as ctx:
+        keep = ctx.enter_context(tc.tile_pool(name="keep", bufs=1))
+        work = ctx.enter_context(tc.tile_pool(name="work", bufs=2))
+        psum = ctx.enter_context(tc.psum_pool(name="psum", bufs=8))
+
+        def kept(name, shape, dtype):
+            return keep.tile(shape, dtype, name=name, align_bytes=64)
+
+        def new_bank():
+            bank = psum.tile([P, 512], F32, name="bank")
+            return bank
+
+        xs = kept("xs", [P, K], F32)
+        x_raw = [kept(f"x_raw{h}", [P, 4, K], U8) for h in range(2)]
+        x_bf = {}
+        x_grp = {}
+        x_codes = [kept(f"x_codes{h}", [P, 2, 512], U32) for h in range(2)]
+        x_scales = [kept(f"x_scales{h}", [P, 2, 512], U8) for h in range(2)]
+        w_codes = [[kept(f"w_codes{c}_{q}", [P, 512], U32) for q in range(2)] for c in range(6)]
+        w_scales = [[kept(f"w_scales{c}_{q}", [P, 512], U8) for q in range(2)] for c in range(6)]
+        e_raw = kept("e_raw", [P, 8, D], BF16)
+        e_grp = {}
+        e_codes = kept("e_codes", [P, C], U32)
+        e_scales = kept("e_scales", [P, C], U8)
+        g_raw = kept("g_raw", [P, 4, F], BF16)
+        g_codes = [kept(f"g_codes{q}", [P, 512], U32) for q in range(2)]
+        g_scales = [kept(f"g_scales{q}", [P, 512], U8) for q in range(2)]
+        v_codes = [[kept(f"v_codes{q}_{n}", [P, 512], U32) for n in range(2)] for q in range(2)]
+        v_scales = [[kept(f"v_scales{q}_{n}", [P, 512], U8) for n in range(2)] for q in range(2)]
+        h_codes = [[kept(f"h_codes{q}_{h}", [P, 512], U32) for h in range(2)] for q in range(2)]
+        h_scales = [[kept(f"h_scales{q}_{h}", [P, 512], U8) for h in range(2)] for q in range(2)]
+        r_all = kept("r_all", [P, C], BF16)
+        d_all = kept("d_all", [P, C], BF16)
+        bias_rows = kept("bias_rows", [P, P], BF16)
+        bias = kept("bias", [P, 48], F32)
+        ident = kept("ident", [P, P], F32)
+        ident_bf = kept("ident_bf", [P, P], BF16)
+        warm = kept("warm", [P, 2], F32)
+
+        w_raw = {}
+
+        def load_w(c, q):
+            group, piece = c // 3, c % 3
+            t = work.tile([P, 4, 512], BF16, name="w_raw", bufs=5, align_bytes=64)
+            col = piece * F + group * 512
+            nc.sync.dma_start(
+                out=t[:],
+                in_=w[q * 512 : (q + 1) * 512, col : col + 512].rearrange("(p s) n -> p s n", s=4),
+            )
+            w_raw[c, q] = t
+
+        x_rows = x_bytes.rearrange("(p i) k -> p i k", i=8)
+
+        def load_x(h, i0, i1):
+            nc.sync.dma_start(out=x_raw[h][:, i0:i1, :], in_=x_rows[:, 4 * h + i0 : 4 * h + i1, :])
+
+        nc.scalar.dma_start(out=xs[:], in_=x_scale.rearrange("o k -> (o k)").partition_broadcast(P))
+        load_x(0, 0, 1)
+        load_x(0, 1, 4)
+        load_w(0, 0)
+        load_w(0, 1)
+        nc.vector.memset(warm[:], 0.0)
+        nc.scalar.activation(out=warm[:, 0:1], in_=warm[:, 1:2], func=IDENTITY)
+        nc.gpsimd.memset(bias_rows[:], 0.0)
+        make_identity(nc, ident[:])
+        make_identity(nc, ident_bf[:])
+        for c in range(8):
+            row = b[c * 512 : (c + 1) * 512] if c < 6 else a[(c - 6) * 512 : (c - 5) * 512]
+            nc.scalar.dma_start(
+                out=bias_rows[4 * c : 4 * c + 4, :].rearrange("t (B i) -> t B i", i=8),
+                in_=row.rearrange("(B t i) -> t B i", t=4, i=8),
+            )
+
+        for row, vec in ((32, r), (40, d)):
+            nc.scalar.dma_start(out=bias_rows[row : row + 8, :], in_=vec.rearrange("(n p) -> n p", p=P))
+
+        def copy(engine, out, in_):
+            if engine == "v":
+                nc.vector.tensor_copy(out=out, in_=in_)
+            else:
+                nc.scalar.copy(out=out, in_=in_)
+
+        def x_product(h, i):
+            t = work.tile([P, K], BF16, name="x_bf", bufs=3, align_bytes=64)
+            x_bf[h, i] = t
+            nc.vector.tensor_tensor(out=t[:], in0=x_raw[h][:, i, :].bitcast(FP8), in1=xs[:], op=MULT)
+
+        held = {}
+
+        def x_turn(h, i):
+            bank = new_bank()
+            words = x_bf[h, i][:].bitcast(F32)
+            for q in range(2):
+                for u in range(2):
+                    s = 2 * q + u
+                    nc.tensor.transpose(bank[:, s * P : (s + 1) * P], words[:, 256 * q + u : 256 * (q + 1) : 2], ident[:])
+            held["x", h, i] = bank
+
+        def x_out(h, i, engine):
+            bank = held.pop(("x", h, i))
+            if i == 0:
+                t = work.tile([P, 2, 2048], BF16, name="x_grp", bufs=1, align_bytes=64)
+                x_grp[h] = t
+            copy(
+                engine,
+                x_grp[h][:].bitcast(F32).rearrange("p q (i r u) -> p i q r u", i=4, u=2)[:, i],
+                bank[:].rearrange("p (q u r) -> p q r u", q=2, u=2),
+            )
+
+        def x_quant(h, q):
+            nc.vector.quantize_mx(out=x_codes[h][:, q, :].bitcast(FP8X4), scales=x_scales[h][:, q, :], in_=x_grp[h][:, q, :])
+
+        w_grp = {}
+
+        def w_ilv(c, q, engine):
+            if (c, q) not in w_grp:
+                t = work.tile([P, 2048], BF16, name="grp", bufs=8, align_bytes=64)
+                w_grp[c, q] = t
+            n = W_VEC[c][q]
+            t0, t1 = (4 - n, 4) if engine == "v" else (0, 4 - n)
+            if t0 < t1:
+                copy(
+                    engine,
+                    w_grp[c, q][:].rearrange("p (t B i s) -> p t B s i", t=4, i=8, s=4)[:, t0:t1],
+                    w_raw[c, q][:].rearrange("p s (B t i) -> p t B s i", t=4, i=8)[:, t0:t1],
+                )
+
+        def w_quant(c, q):
+            nc.vector.quantize_mx(out=w_codes[c][q][:].bitcast(FP8X4), scales=w_scales[c][q][:], in_=w_grp[c, q][:])
+
+        def z_mm(c, h, t):
+            bank = new_bank()
+            cols = slice(t * P, (t + 1) * P)
+            for q in range(2):
+                nc.tensor.matmul_mx(
+                    out=bank[:],
+                    lhsT=w_codes[c][q][:, cols].bitcast(FP8X4),
+                    lhsT_scale=w_scales[c][q][:, cols],
+                    rhs=x_codes[h][:, q, :].bitcast(FP8X4),
+                    rhs_scale=x_scales[h][:, q, :],
+                    start=(q == 0),
+                    stop=(q == 1),
+                )
+            held["z", t] = bank
+
+        top = {}
+
+        def z_out(c, h, t):
+            group, piece = c // 3, c % 3
+            bank = held.pop(("z", t))
+            col = bias[:, 4 * c_bias(group, piece) + t : 4 * c_bias(group, piece) + t + 1]
+            if t == 0:
+                z_piece = work.tile([P, 4, 512], BF16, name=f"z_piece{piece}", align_bytes=64)
+                top[h, piece] = z_piece
+            if piece == 1:
+                nc.vector.scalar_tensor_tensor(out=top[h, 1][:, t, :], in0=bank[:], scalar=col, in1=top[h, 0][:, t, :], op0=ADD, op1=MAX)
+            else:
+                nc.scalar.activation(out=top[h, piece][:, t, :], in_=bank[:], func=IDENTITY, bias=col)
+
+        def c_bias(group, piece):
+            return 2 * piece + group
+
+        h_grp = {}
+
+        def h_max(tiles, group, h, half):
+            if half == 0:
+                t = work.tile([P, 2048], BF16, name="grp", bufs=8, align_bytes=64)
+                h_grp[group, h] = t
+            cols = slice(256 * half, 256 * (half + 1))
+            nc.vector.tensor_tensor(
+                out=h_grp[group, h][:, 1024 * half : 1024 * (half + 1)].rearrange("p (c i t) -> p c t i", i=4, t=4),
+                in0=tiles[h, 1][:, :, cols].rearrange("p t (c i) -> p c t i", i=4),
+                in1=tiles[h, 2][:, :, cols].rearrange("p t (c i) -> p c t i", i=4),
+                op=MAX,
+            )
+
+        def h_quant(group, h, half):
+            cols = slice(256 * half, 256 * (half + 1))
+            nc.vector.quantize_mx(
+                out=h_codes[group][h][:, cols].bitcast(FP8X4),
+                scales=h_scales[group][h][:, cols],
+                in_=h_grp[group, h][:, 1024 * half : 1024 * (half + 1)],
+            )
+
+        def e_turn(n):
+            bank = new_bank()
+            for i in range(2):
+                words = e_raw[:, 2 * n + i, :].bitcast(F32)
+                for u in range(2):
+                    s = 2 * i + u
+                    nc.tensor.transpose(bank[:, s * P : (s + 1) * P], words[:, u : 256 : 2], ident[:])
+            held["e", n] = bank
+
+        def e_out(n, engine):
+            bank = held.pop(("e", n))
+            if n % 2 == 0:
+                t = work.tile([P, 2048], BF16, name="grp", bufs=8, align_bytes=64)
+                e_grp[n // 2] = t
+            copy(
+                engine,
+                e_grp[n // 2][:].bitcast(F32)[:, 512 * (n % 2) : 512 * (n % 2 + 1)].rearrange("p (i r u) -> p i r u", i=2, u=2),
+                bank[:].rearrange("p (i u r) -> p i r u", i=2, u=2),
+            )
+
+        def e_quant(n):
+            nc.vector.quantize_mx(
+                out=e_codes[:, 512 * n : 512 * (n + 1)].bitcast(FP8X4),
+                scales=e_scales[:, 512 * n : 512 * (n + 1)],
+                in_=e_grp[n][:],
+            )
+
+        g_grp = {}
+
+        def g_ilv(q, engine):
+            if q not in g_grp:
+                t = work.tile([P, 2048], BF16, name="grp", bufs=8, align_bytes=64)
+                g_grp[q] = t
+            n = G_VEC[q]
+            t0, t1 = (4 - n, 4) if engine == "v" else (0, 4 - n)
+            if t0 < t1:
+                copy(
+                    engine,
+                    g_grp[q][:].rearrange("p (t B i s) -> p t B s i", t=4, i=8, s=4)[:, t0:t1],
+                    g_raw[:, :, 512 * q : 512 * (q + 1)].rearrange("p s (B t i) -> p t B s i", t=4, i=8)[:, t0:t1],
+                )
+
+        def g_quant(q):
+            nc.vector.quantize_mx(out=g_codes[q][:].bitcast(FP8X4), scales=g_scales[q][:], in_=g_grp[q][:])
+
+        v_raw = {}
+
+        def v_mm(q, n, t):
+            bank = new_bank()
+            cols = slice(t * P, (t + 1) * P)
+            rows = slice(512 * n, 512 * (n + 1))
+            nc.tensor.matmul_mx(
+                out=bank[:],
+                lhsT=g_codes[q][:, cols].bitcast(FP8X4),
+                lhsT_scale=g_scales[q][:, cols],
+                rhs=e_codes[:, rows].bitcast(FP8X4),
+                rhs_scale=e_scales[:, rows],
+                start=True,
+                stop=True,
+            )
+            held["v", q, n, t] = bank
+
+        def v_out(q, n, t):
+            bank = held.pop(("v", q, n, t))
+            if t == 0:
+                tile = work.tile([P, 4, 512], BF16, name="v_raw", align_bytes=64)
+                v_raw[q, n] = tile
+            col = bias[:, 24 + 4 * q + t : 25 + 4 * q + t]
+            if t in V_OUT_VEC:
+                nc.vector.tensor_scalar(out=v_raw[q, n][:, t, :], in0=bank[:], scalar1=col, scalar2=None, op0=ADD)
+            else:
+                nc.scalar.activation(out=v_raw[q, n][:, t, :], in_=bank[:], func=IDENTITY, bias=col)
+
+        v_grp = {}
+
+        def v_ilv(q, n):
+            t = work.tile([P, 2048], BF16, name="grp", bufs=8, align_bytes=64)
+            v_grp[q, n] = t
+            copy(
+                "v" if V_VEC[2 * q + n] else "s",
+                t[:].rearrange("p (c i t) -> p c t i", i=8, t=4),
+                v_raw[q, n][:].rearrange("p t (c i) -> p c t i", i=8),
+            )
+
+        def v_quant(q, n):
+            nc.vector.quantize_mx(out=v_codes[q][n][:].bitcast(FP8X4), scales=v_scales[q][n][:], in_=v_grp[q, n][:])
+
+        def y_mm(h, i, n):
+            bank = new_bank()
+            cols = slice(i * P, (i + 1) * P)
+            for q in range(2):
+                nc.tensor.matmul_mx(
+                    out=bank[:],
+                    lhsT=h_codes[q][h][:, cols].bitcast(FP8X4),
+                    lhsT_scale=h_scales[q][h][:, cols],
+                    rhs=v_codes[q][n][:].bitcast(FP8X4),
+                    rhs_scale=v_scales[q][n][:],
+                    start=(q == 0),
+                    stop=(q == 1),
+                )
+            held["y", h, i, n] = bank
+
+        out_rows = out.rearrange("(p i) c -> p i c", i=8)
+
+        y_sb = {}
+
+        def y_scale(h, i, n):
+            bank = held.pop(("y", h, i, n))
+            t = work.tile([P, 512], F32, name="y_sb", bufs=6, align_bytes=64)
+            y_sb[h, i, n] = t
+            nc.vector.tensor_tensor(out=t[:], in0=bank[:], in1=r_all[:, 512 * n : 512 * (n + 1)], op=MULT)
+
+        def y_store(h, i, n):
+            t = y_sb.pop((h, i, n))
+            cols = slice(512 * n, 512 * (n + 1))
+            engine = nc.gpsimd if ADD_GP[h][i] else nc.vector
+            engine.tensor_tensor(out=t[:], in0=t[:], in1=d_all[:, cols], op=ADD)
+            nc.sync.dma_start(out=out_rows[:, 4 * h + i, cols], in_=t[:])
+
+        def yt_mm(h, n):
+            bank = new_bank()
+            cols = slice(n * P, (n + 1) * P)
+            for q in range(2):
+                nc.tensor.matmul_mx(
+                    out=bank[:],
+                    lhsT=v_codes[q][1][:, cols].bitcast(FP8X4),
+                    lhsT_scale=v_scales[q][1][:, cols],
+                    rhs=h_codes[q][h][:].bitcast(FP8X4),
+                    rhs_scale=h_scales[q][h][:],
+                    start=(q == 0),
+                    stop=(q == 1),
+                )
+            held["yt", h, n] = bank
+
+        def yt_scale(h, n):
+            bank = held.pop(("yt", h, n))
+            t = work.tile([P, 512], F32, name="yt_sb", bufs=2, align_bytes=64)
+            y_sb["t", h, n] = t
+            nc.scalar.activation(out=t[:], in_=bank[:], func=IDENTITY, scale=bias[:, 36 + n : 37 + n], bias=bias[:, 44 + n : 45 + n])
+
+        def yt_turn(h, n):
+            t = y_sb.pop(("t", h, n))
+            bank = new_bank()
+            for i in range(4):
+                nc.tensor.transpose(bank[:, i * P : (i + 1) * P], t[:, i * P : (i + 1) * P], ident[:])
+            held["yr", h, n] = bank
+
+        def yt_store(h, n):
+            bank = held.pop(("yr", h, n))
+            t = work.tile([P, 512], F32, name="y_turned", bufs=4, align_bytes=64)
+            nc.scalar.copy(out=t[:], in_=bank[:])
+            nc.sync.dma_start(
+                out=out_rows[:, 4 * h : 4 * h + 4, 512 + n * P : 512 + (n + 1) * P],
+                in_=t[:].rearrange("p (i c) -> p i c", i=4),
+            )
+
+        load_w(1, 0)
+        load_w(1, 1)
+        x_product(0, 0)
+        x_product(0, 1)
+        w_ilv(0, 0, "s")
+        x_turn(0, 0)
+        x_out(0, 0, "s")
+        x_product(0, 2)
+        x_turn(0, 1)
+        x_out(0, 1, "s")
+        x_product(0, 3)
+        w_ilv(0, 0, "v")
+        x_turn(0, 2)
+        x_out(0, 2, "s")
+        w_ilv(0, 1, "v")
+        x_turn(0, 3)
+        x_out(0, 3, "s")
+        w_ilv(0, 1, "s")
+        w_quant(0, 0)
+        x_quant(0, 0)
+        x_quant(0, 1)
+        w_quant(0, 1)
+        bias_bank = new_bank()
+        nc.tensor.matmul(bias_bank[:, 0:48], lhsT=bias_rows[:], rhs=ident_bf[:, 0:48], start=True, stop=True)
+        nc.vector.tensor_copy(out=bias[:], in_=bias_bank[:, 0:48])
+        load_w(2, 0)
+        load_w(2, 1)
+        load_x(1, 0, 4)
+        load_w(3, 0)
+        load_w(3, 1)
+        nc.sync.dma_start(out=e_raw[:], in_=e.rearrange("(i p) k -> p i k", p=P))
+        load_w(4, 0)
+        load_w(4, 1)
+        nc.sync.dma_start(out=g_raw[:], in_=g.rearrange("(p s) f -> p s f", s=4))
+        load_w(5, 0)
+        load_w(5, 1)
+        nc.sync.dma_start(out=r_all[:], in_=r.partition_broadcast(P))
+        nc.sync.dma_start(out=d_all[:], in_=d.partition_broadcast(P))
+
+        fill = [[] for s in range(54)]
+
+        def put(s, fn, *args):
+            fill[s].append((fn, args))
+
+        for c in range(1, 6):
+            s = W_AT[c - 1]
+            for q in range(2):
+                put(s + q, w_ilv, c, q, "s")
+                put(s + q, w_ilv, c, q, "v")
+                put(s + q + W_LAG, w_quant, c, q)
+        for i in range(4):
+            s = X1_AT[i]
+            put(s, x_product, 1, i)
+            put(s + X_LAG[0], x_turn, 1, i)
+            put(s + X_LAG[1], x_out, 1, i, "s")
+        for n in range(4):
+            put(E_AT + n, e_turn, n)
+            put(E_AT + n + 1, e_out, n, "s")
+        for q in range(2):
+            put(E_AT + 4 + 2 * q, e_quant, q)
+            put(X_AT + q, x_quant, 1, q)
+            put(G_AT + 2 * q, g_ilv, q, "s")
+            put(G_AT + 2 * q, g_ilv, q, "v")
+            put(G_AT + 2 * q + 2, g_quant, q)
+        for at, (q, n) in enumerate(((0, 0), (1, 0), (0, 1), (1, 1))):
+            s = V_AT[at]
+            for t in range(4):
+                put(s + t // 2, v_mm, q, n, t)
+                put(s + t // 2, v_out, q, n, t)
+            put(s + 3, v_ilv, q, n)
+            put(s + 4, v_quant, q, n)
+        for n in range(4):
+            put(Y_AT[n], y_mm, 0, n, 0)
+            put(Y_AT[n], y_scale, 0, n, 0)
+            put(Y_AT[n] + 1, y_store, 0, n, 0)
+            put(YT_AT[n], yt_mm, 0, n)
+            put(YT_AT[n], yt_scale, 0, n)
+            put(YT_AT[n] + 1, yt_turn, 0, n)
+            put(YT_AT[n] + 1, yt_store, 0, n)
+
+        for s in range(54):
+            t = s % 4
+            if s < 48:
+                c, h = Z_ORDER[s // 4]
+                z_mm(c, h, t)
+            for fn, args in fill[s]:
+                fn(*args)
+            if s < 48:
+                z_out(c, h, t)
+                if c % 3 == 2 and t == 3:
+                    tiles = dict(top)
+                    for half in range(2):
+                        fill[s + H_LAG[half]].insert(0, (h_max, (tiles, c // 3, h, half)))
+                        fill[s + H_LAG[half] + 1].insert(0, (h_quant, (c // 3, h, half)))
+
+        for n in range(6):
+            if n < 4:
+                y_mm(1, n, 0)
+                y_scale(1, n, 0)
+            if 0 < n < 5:
+                yt_mm(1, n - 1)
+                y_store(1, n - 1, 0)
+                yt_scale(1, n - 1)
+            if n > 1:
+                yt_turn(1, n - 2)
+                yt_store(1, n - 2)

@@ -18,470 +18,519 @@ MULT = mybir.AluOpType.mult
 MAX = mybir.AluOpType.max
 IDENTITY = mybir.ActivationFunctionType.Identity
 
-W_VEC = [[1, 3], [1, 2], [1, 2], [4, 2], [2, 0], [2, 0]]
-G_VEC = [3, 3]
-V_VEC = [True, True, True, True]
-V_OUT_VEC = [1]
-E_AT = 13
-X_AT = 20
-G_AT = 8
-V_AT = [20, 24, 23, 27]
-Y_AT = [36, 36, 35, 41]
-YT_AT = [38, 42, 41, 49]
-H_LAG = [1, 3]
-X_LAG = [4, 4]
-W_AT = [0, 1, 3, 5, 14]
-W_LAG = 2
-X1_AT = [1, 3, 9, 12]
-Z_ORDER = [[0, 0], [1, 0], [2, 0], [3, 0], [4, 0], [5, 0], [0, 1], [1, 1], [2, 1], [3, 1], [4, 1], [5, 1]]
-ADD_GP = [[0, 1, 1, 1], [1, 0, 1, 1]]
+RUN = 8
+AHEAD = 2
+ADD_GP = 4
+GP_TICKS = 6
+REACH = 5
+WARM = 4
+MANUAL = True
 
 
 def tile_maxout_generated_head_f5_kernel(tc, x_bytes, x_scale, w, b, e, g, a, r, d, out):
     nc = tc.nc
     with ExitStack() as ctx:
         keep = ctx.enter_context(tc.tile_pool(name="keep", bufs=1))
-        work = ctx.enter_context(tc.tile_pool(name="work", bufs=2))
-        psum = ctx.enter_context(tc.psum_pool(name="psum", bufs=8))
+        psum = ctx.enter_context(tc.psum_pool(name="psum", bufs=1))
+        if MANUAL:
+            ctx.enter_context(tc.manual_schedule())
 
         def kept(name, shape, dtype):
             return keep.tile(shape, dtype, name=name, align_bytes=64)
 
-        def new_bank():
-            bank = psum.tile([P, 512], F32, name="bank")
-            return bank
+        banks = [psum.tile([P, 512], F32, name=f"bank{n}") for n in range(8)]
+        grouped = [kept(f"grouped{n}", [P, 2048], BF16) for n in range(7)]
+        wide = [kept(f"x_wide{n}", [P, K], BF16) for n in range(3)]
+        results = [kept(f"result{n}", [P, 512], F32) for n in range(10)]
+        by_class = [kept(f"by_class{n}", [P, 512], F32) for n in range(4)]
+        raws = [kept(f"raw{n}", [P, 4, 512], BF16) for n in range(8)]
+        planes = [kept(f"plane{n}", [P, 4, 512], BF16) for n in range(7)]
+        held = {}
 
-        xs = kept("xs", [P, K], F32)
-        x_raw = [kept(f"x_raw{h}", [P, 4, K], U8) for h in range(2)]
-        x_bf = {}
-        x_grp = {}
-        x_codes = [kept(f"x_codes{h}", [P, 2, 512], U32) for h in range(2)]
-        x_scales = [kept(f"x_scales{h}", [P, 2, 512], U8) for h in range(2)]
-        w_codes = [[kept(f"w_codes{c}_{q}", [P, 512], U32) for q in range(2)] for c in range(6)]
-        w_scales = [[kept(f"w_scales{c}_{q}", [P, 512], U8) for q in range(2)] for c in range(6)]
-        e_raw = kept("e_raw", [P, 8, D], BF16)
-        e_grp = {}
-        e_codes = kept("e_codes", [P, C], U32)
-        e_scales = kept("e_scales", [P, C], U8)
-        g_raw = kept("g_raw", [P, 4, F], BF16)
-        g_codes = [kept(f"g_codes{q}", [P, 512], U32) for q in range(2)]
-        g_scales = [kept(f"g_scales{q}", [P, 512], U8) for q in range(2)]
-        v_codes = [[kept(f"v_codes{q}_{n}", [P, 512], U32) for n in range(2)] for q in range(2)]
-        v_scales = [[kept(f"v_scales{q}_{n}", [P, 512], U8) for n in range(2)] for q in range(2)]
-        h_codes = [[kept(f"h_codes{q}_{h}", [P, 512], U32) for h in range(2)] for q in range(2)]
-        h_scales = [[kept(f"h_scales{q}_{h}", [P, 512], U8) for h in range(2)] for q in range(2)]
-        r_all = kept("r_all", [P, C], BF16)
-        d_all = kept("d_all", [P, C], BF16)
-        bias_rows = kept("bias_rows", [P, P], BF16)
-        bias = kept("bias", [P, 48], F32)
+        def take(free, key):
+            held[key] = free.pop(0)
+            return held[key]
+
+        def give(free, key):
+            free.append(held[key])
+            return held.pop(key)
+
+        def operand(name):
+            return kept(name + "_codes", [P, 512], U32), kept(name + "_scales", [P, 512], U8)
+
+        x_raw = [[kept(f"x_raw{h}_{j}", [P, 2, K], U8) for j in range(2)] for h in range(2)]
+        e_raw = [kept(f"e_raw{n}", [P, 4, D], BF16) for n in range(2)]
+        x_mx = [[operand(f"x{h}_{q}") for q in range(2)] for h in range(2)]
+        w_mx = [[operand(f"w{c}_{q}") for q in range(2)] for c in range(6)]
+        e_mx = [operand(f"e{n}") for n in range(2)]
+        g_mx = [operand(f"g{q}") for q in range(2)]
+        v_mx = [[operand(f"v{q}_{n}") for n in range(2)] for q in range(2)]
+        h_mx = [[operand(f"h{q}_{h}") for h in range(2)] for q in range(2)]
+        xs = kept("xs", [P, 2, 4], F32)
+        r_all = kept("r_all", [P, 512], BF16)
+        d_all = kept("d_all", [P, 512], BF16)
+        rows_raw = kept("rows_raw", [8, 512], BF16)
+        rows = kept("rows", [P, 512], BF16)
+        columns = kept("columns", [P, 10, 4], F32)
         ident = kept("ident", [P, P], F32)
         ident_bf = kept("ident_bf", [P, P], BF16)
-        warm = kept("warm", [P, 2], F32)
-
-        w_raw = {}
-
-        def load_w(c, q):
-            group, piece = c // 3, c % 3
-            t = work.tile([P, 4, 512], BF16, name="w_raw", bufs=5, align_bytes=64)
-            col = piece * F + group * 512
-            nc.sync.dma_start(
-                out=t[:],
-                in_=w[q * 512 : (q + 1) * 512, col : col + 512].rearrange("(p s) n -> p s n", s=4),
-            )
-            w_raw[c, q] = t
 
         x_rows = x_bytes.rearrange("(p i) k -> p i k", i=8)
+        out_rows = out.rearrange("(p i) c -> p i c", i=8)
 
-        def load_x(h, i0, i1):
-            nc.sync.dma_start(out=x_raw[h][:, i0:i1, :], in_=x_rows[:, 4 * h + i0 : 4 * h + i1, :])
+        def load_x(h, j):
+            nc.sync.dma_start(out=x_raw[h][j][:], in_=x_rows[:, 4 * h + 2 * j : 4 * h + 2 * j + 2, :])
 
-        nc.scalar.dma_start(out=xs[:], in_=x_scale.rearrange("o k -> (o k)").partition_broadcast(P))
-        load_x(0, 0, 1)
-        load_x(0, 1, 4)
-        load_w(0, 0)
-        load_w(0, 1)
-        nc.vector.memset(warm[:], 0.0)
-        nc.scalar.activation(out=warm[:, 0:1], in_=warm[:, 1:2], func=IDENTITY)
-        nc.gpsimd.memset(bias_rows[:], 0.0)
-        make_identity(nc, ident[:])
-        make_identity(nc, ident_bf[:])
-        for c in range(8):
-            row = b[c * 512 : (c + 1) * 512] if c < 6 else a[(c - 6) * 512 : (c - 5) * 512]
-            nc.scalar.dma_start(
-                out=bias_rows[4 * c : 4 * c + 4, :].rearrange("t (B i) -> t B i", i=8),
-                in_=row.rearrange("(B t i) -> t B i", t=4, i=8),
+        def load_w(c, q):
+            col = (c % 3) * F + (c // 3) * 512
+            rows_q = w[q * 512 : (q + 1) * 512, col : col + 512]
+            nc.sync.dma_start(out=take(raws, ("raw", "w", c, q))[:], in_=rows_q.rearrange("(p s) n -> p s n", s=4))
+
+        def load_g(q):
+            nc.sync.dma_start(out=take(raws, ("raw", "g", q))[:], in_=g[:, 512 * q : 512 * (q + 1)].rearrange("(p s) f -> p s f", s=4))
+
+        def load_e(n):
+            nc.sync.dma_start(out=e_raw[n][:], in_=e[512 * n : 512 * (n + 1), :].rearrange("(i p) k -> p i k", p=P))
+
+        def load(tile, source):
+            nc.sync.dma_start(out=tile, in_=source)
+
+        def quantize(mx, grouped, cols=slice(0, 512)):
+            codes, scales = mx
+            nc.vector.quantize_mx(
+                out=codes[:, cols].bitcast(FP8X4), scales=scales[:, cols], in_=grouped[:, 4 * cols.start : 4 * cols.stop]
             )
 
-        for row, vec in ((32, r), (40, d)):
-            nc.scalar.dma_start(out=bias_rows[row : row + 8, :], in_=vec.rearrange("(n p) -> n p", p=P))
+        def product(bank, lhs, lhs_cols, rhs, rhs_cols, start, stop):
+            nc.tensor.matmul_mx(
+                out=bank,
+                lhsT=lhs[0][:, lhs_cols].bitcast(FP8X4),
+                lhsT_scale=lhs[1][:, lhs_cols],
+                rhs=rhs[0][:, rhs_cols].bitcast(FP8X4),
+                rhs_scale=rhs[1][:, rhs_cols],
+                start=start,
+                stop=stop,
+            )
 
-        def copy(engine, out, in_):
-            if engine == "v":
+        def block(n):
+            return slice(n * P, (n + 1) * P)
+
+        def copy(on_vector, out, in_):
+            if on_vector:
                 nc.vector.tensor_copy(out=out, in_=in_)
             else:
                 nc.scalar.copy(out=out, in_=in_)
 
-        def x_product(h, i):
-            t = work.tile([P, K], BF16, name="x_bf", bufs=3, align_bytes=64)
-            x_bf[h, i] = t
-            nc.vector.tensor_tensor(out=t[:], in0=x_raw[h][:, i, :].bitcast(FP8), in1=xs[:], op=MULT)
+        whole = slice(0, 512)
 
-        held = {}
+        def x_widen(h, i, q):
+            if q == 0:
+                take(wide, ("wide", h, i))
+            cols = slice(512 * q, 512 * (q + 1))
+            nc.scalar.copy(out=held["wide", h, i][:, cols], in_=x_raw[h][i // 2][:, i % 2, cols].bitcast(FP8))
+
+        def x_widen_vector(h, i):
+            nc.vector.tensor_copy(out=take(wide, ("wide", h, i))[:], in_=x_raw[h][i // 2][:, i % 2, :].bitcast(FP8))
 
         def x_turn(h, i):
-            bank = new_bank()
-            words = x_bf[h, i][:].bitcast(F32)
+            bank = take(banks, ("xbank", h, i))
+            words = give(wide, ("wide", h, i))[:].bitcast(F32)
             for q in range(2):
                 for u in range(2):
-                    s = 2 * q + u
-                    nc.tensor.transpose(bank[:, s * P : (s + 1) * P], words[:, 256 * q + u : 256 * (q + 1) : 2], ident[:])
-            held["x", h, i] = bank
+                    nc.tensor.transpose(bank[:, block(2 * q + u)], words[:, 256 * q + u : 256 * (q + 1) : 2], ident[:])
 
-        def x_out(h, i, engine):
-            bank = held.pop(("x", h, i))
+        def x_out(h, i, q):
+            pairs = held["xbank", h, i][:].bitcast(BF16)
+            if q == 1:
+                give(banks, ("xbank", h, i))
             if i == 0:
-                t = work.tile([P, 2, 2048], BF16, name="x_grp", bufs=1, align_bytes=64)
-                x_grp[h] = t
-            copy(
-                engine,
-                x_grp[h][:].bitcast(F32).rearrange("p q (i r u) -> p i q r u", i=4, u=2)[:, i],
-                bank[:].rearrange("p (q u r) -> p q r u", q=2, u=2),
-            )
-
-        def x_quant(h, q):
-            nc.vector.quantize_mx(out=x_codes[h][:, q, :].bitcast(FP8X4), scales=x_scales[h][:, q, :], in_=x_grp[h][:, q, :])
-
-        w_grp = {}
-
-        def w_ilv(c, q, engine):
-            if (c, q) not in w_grp:
-                t = work.tile([P, 2048], BF16, name="grp", bufs=8, align_bytes=64)
-                w_grp[c, q] = t
-            n = W_VEC[c][q]
-            t0, t1 = (4 - n, 4) if engine == "v" else (0, 4 - n)
-            if t0 < t1:
-                copy(
-                    engine,
-                    w_grp[c, q][:].rearrange("p (t B i s) -> p t B s i", t=4, i=8, s=4)[:, t0:t1],
-                    w_raw[c, q][:].rearrange("p s (B t i) -> p t B s i", t=4, i=8)[:, t0:t1],
-                )
-
-        def w_quant(c, q):
-            nc.vector.quantize_mx(out=w_codes[c][q][:].bitcast(FP8X4), scales=w_scales[c][q][:], in_=w_grp[c, q][:])
-
-        def z_mm(c, h, t):
-            bank = new_bank()
-            cols = slice(t * P, (t + 1) * P)
-            for q in range(2):
-                nc.tensor.matmul_mx(
-                    out=bank[:],
-                    lhsT=w_codes[c][q][:, cols].bitcast(FP8X4),
-                    lhsT_scale=w_scales[c][q][:, cols],
-                    rhs=x_codes[h][:, q, :].bitcast(FP8X4),
-                    rhs_scale=x_scales[h][:, q, :],
-                    start=(q == 0),
-                    stop=(q == 1),
-                )
-            held["z", t] = bank
-
-        top = {}
-
-        def z_out(c, h, t):
-            group, piece = c // 3, c % 3
-            bank = held.pop(("z", t))
-            col = bias[:, 4 * c_bias(group, piece) + t : 4 * c_bias(group, piece) + t + 1]
-            if t == 0:
-                z_piece = work.tile([P, 4, 512], BF16, name=f"z_piece{piece}", align_bytes=64)
-                top[h, piece] = z_piece
-            if piece == 1:
-                nc.vector.scalar_tensor_tensor(out=top[h, 1][:, t, :], in0=bank[:], scalar=col, in1=top[h, 0][:, t, :], op0=ADD, op1=MAX)
-            else:
-                nc.scalar.activation(out=top[h, piece][:, t, :], in_=bank[:], func=IDENTITY, bias=col)
-
-        def c_bias(group, piece):
-            return 2 * piece + group
-
-        h_grp = {}
-
-        def h_max(tiles, group, h, half):
-            if half == 0:
-                t = work.tile([P, 2048], BF16, name="grp", bufs=8, align_bytes=64)
-                h_grp[group, h] = t
-            cols = slice(256 * half, 256 * (half + 1))
+                take(grouped, ("x", h, q))
             nc.vector.tensor_tensor(
-                out=h_grp[group, h][:, 1024 * half : 1024 * (half + 1)].rearrange("p (c i t) -> p c t i", i=4, t=4),
-                in0=tiles[h, 1][:, :, cols].rearrange("p t (c i) -> p c t i", i=4),
-                in1=tiles[h, 2][:, :, cols].rearrange("p t (c i) -> p c t i", i=4),
-                op=MAX,
+                out=held["x", h, q][:, 512 * i : 512 * (i + 1)].rearrange("p (r u e) -> p r u e", u=2, e=2),
+                in0=pairs[:, 512 * q : 512 * (q + 1)].rearrange("p (u r e) -> p r u e", u=2, e=2),
+                in1=xs[:, q, :].rearrange("p (o u e) -> p o u e", o=1, u=2).to_broadcast([P, P, 2, 2]),
+                op=MULT,
             )
 
-        def h_quant(group, h, half):
-            cols = slice(256 * half, 256 * (half + 1))
-            nc.vector.quantize_mx(
-                out=h_codes[group][h][:, cols].bitcast(FP8X4),
-                scales=h_scales[group][h][:, cols],
-                in_=h_grp[group, h][:, 1024 * half : 1024 * (half + 1)],
-            )
-
-        def e_turn(n):
-            bank = new_bank()
-            for i in range(2):
-                words = e_raw[:, 2 * n + i, :].bitcast(F32)
-                for u in range(2):
-                    s = 2 * i + u
-                    nc.tensor.transpose(bank[:, s * P : (s + 1) * P], words[:, u : 256 : 2], ident[:])
-            held["e", n] = bank
-
-        def e_out(n, engine):
-            bank = held.pop(("e", n))
-            if n % 2 == 0:
-                t = work.tile([P, 2048], BF16, name="grp", bufs=8, align_bytes=64)
-                e_grp[n // 2] = t
-            copy(
-                engine,
-                e_grp[n // 2][:].bitcast(F32)[:, 512 * (n % 2) : 512 * (n % 2 + 1)].rearrange("p (i r u) -> p i r u", i=2, u=2),
-                bank[:].rearrange("p (i u r) -> p i r u", i=2, u=2),
-            )
-
-        def e_quant(n):
-            nc.vector.quantize_mx(
-                out=e_codes[:, 512 * n : 512 * (n + 1)].bitcast(FP8X4),
-                scales=e_scales[:, 512 * n : 512 * (n + 1)],
-                in_=e_grp[n][:],
-            )
-
-        g_grp = {}
-
-        def g_ilv(q, engine):
-            if q not in g_grp:
-                t = work.tile([P, 2048], BF16, name="grp", bufs=8, align_bytes=64)
-                g_grp[q] = t
-            n = G_VEC[q]
-            t0, t1 = (4 - n, 4) if engine == "v" else (0, 4 - n)
-            if t0 < t1:
-                copy(
-                    engine,
-                    g_grp[q][:].rearrange("p (t B i s) -> p t B s i", t=4, i=8, s=4)[:, t0:t1],
-                    g_raw[:, :, 512 * q : 512 * (q + 1)].rearrange("p s (B t i) -> p t B s i", t=4, i=8)[:, t0:t1],
-                )
-
-        def g_quant(q):
-            nc.vector.quantize_mx(out=g_codes[q][:].bitcast(FP8X4), scales=g_scales[q][:], in_=g_grp[q][:])
-
-        v_raw = {}
-
-        def v_mm(q, n, t):
-            bank = new_bank()
-            cols = slice(t * P, (t + 1) * P)
-            rows = slice(512 * n, 512 * (n + 1))
-            nc.tensor.matmul_mx(
-                out=bank[:],
-                lhsT=g_codes[q][:, cols].bitcast(FP8X4),
-                lhsT_scale=g_scales[q][:, cols],
-                rhs=e_codes[:, rows].bitcast(FP8X4),
-                rhs_scale=e_scales[:, rows],
-                start=True,
-                stop=True,
-            )
-            held["v", q, n, t] = bank
-
-        def v_out(q, n, t):
-            bank = held.pop(("v", q, n, t))
-            if t == 0:
-                tile = work.tile([P, 4, 512], BF16, name="v_raw", align_bytes=64)
-                v_raw[q, n] = tile
-            col = bias[:, 24 + 4 * q + t : 25 + 4 * q + t]
-            if t in V_OUT_VEC:
-                nc.vector.tensor_scalar(out=v_raw[q, n][:, t, :], in0=bank[:], scalar1=col, scalar2=None, op0=ADD)
+        def finish(mx, key, heir):
+            if heir is None:
+                quantize(mx, give(grouped, key))
             else:
-                nc.scalar.activation(out=v_raw[q, n][:, t, :], in_=bank[:], func=IDENTITY, bias=col)
+                held[heir] = held.pop(key)
+                quantize(mx, held[heir])
 
-        v_grp = {}
-
-        def v_ilv(q, n):
-            t = work.tile([P, 2048], BF16, name="grp", bufs=8, align_bytes=64)
-            v_grp[q, n] = t
+        def interleave(key, first, count, on_vector):
+            if first == 0:
+                take(grouped, key)
+            raw = give(raws, ("raw",) + key) if first + count == 4 else held[("raw",) + key]
+            blocks = slice(32 // RUN * first, 32 // RUN * (first + count))
             copy(
-                "v" if V_VEC[2 * q + n] else "s",
-                t[:].rearrange("p (c i t) -> p c t i", i=8, t=4),
-                v_raw[q, n][:].rearrange("p t (c i) -> p c t i", i=8),
+                on_vector,
+                held[key][:].rearrange("p (t B i s) -> p t B s i", t=4, i=RUN, s=4)[:, :, blocks],
+                raw[:].rearrange("p s (B t i) -> p t B s i", t=4, i=RUN)[:, :, blocks],
             )
 
-        def v_quant(q, n):
-            nc.vector.quantize_mx(out=v_codes[q][n][:].bitcast(FP8X4), scales=v_scales[q][n][:], in_=v_grp[q, n][:])
-
-        def y_mm(h, i, n):
-            bank = new_bank()
-            cols = slice(i * P, (i + 1) * P)
-            for q in range(2):
-                nc.tensor.matmul_mx(
-                    out=bank[:],
-                    lhsT=h_codes[q][h][:, cols].bitcast(FP8X4),
-                    lhsT_scale=h_scales[q][h][:, cols],
-                    rhs=v_codes[q][n][:].bitcast(FP8X4),
-                    rhs_scale=v_scales[q][n][:],
-                    start=(q == 0),
-                    stop=(q == 1),
-                )
-            held["y", h, i, n] = bank
-
-        out_rows = out.rearrange("(p i) c -> p i c", i=8)
-
-        y_sb = {}
-
-        def y_scale(h, i, n):
-            bank = held.pop(("y", h, i, n))
-            t = work.tile([P, 512], F32, name="y_sb", bufs=6, align_bytes=64)
-            y_sb[h, i, n] = t
-            nc.vector.tensor_tensor(out=t[:], in0=bank[:], in1=r_all[:, 512 * n : 512 * (n + 1)], op=MULT)
-
-        def y_store(h, i, n):
-            t = y_sb.pop((h, i, n))
-            cols = slice(512 * n, 512 * (n + 1))
-            engine = nc.gpsimd if ADD_GP[h][i] else nc.vector
-            engine.tensor_tensor(out=t[:], in0=t[:], in1=d_all[:, cols], op=ADD)
-            nc.sync.dma_start(out=out_rows[:, 4 * h + i, cols], in_=t[:])
-
-        def yt_mm(h, n):
-            bank = new_bank()
-            cols = slice(n * P, (n + 1) * P)
-            for q in range(2):
-                nc.tensor.matmul_mx(
-                    out=bank[:],
-                    lhsT=v_codes[q][1][:, cols].bitcast(FP8X4),
-                    lhsT_scale=v_scales[q][1][:, cols],
-                    rhs=h_codes[q][h][:].bitcast(FP8X4),
-                    rhs_scale=h_scales[q][h][:],
-                    start=(q == 0),
-                    stop=(q == 1),
-                )
-            held["yt", h, n] = bank
-
-        def yt_scale(h, n):
-            bank = held.pop(("yt", h, n))
-            t = work.tile([P, 512], F32, name="yt_sb", bufs=2, align_bytes=64)
-            y_sb["t", h, n] = t
-            nc.scalar.activation(out=t[:], in_=bank[:], func=IDENTITY, scale=bias[:, 36 + n : 37 + n], bias=bias[:, 44 + n : 45 + n])
-
-        def yt_turn(h, n):
-            t = y_sb.pop(("t", h, n))
-            bank = new_bank()
-            for i in range(4):
-                nc.tensor.transpose(bank[:, i * P : (i + 1) * P], t[:, i * P : (i + 1) * P], ident[:])
-            held["yr", h, n] = bank
-
-        def yt_store(h, n):
-            bank = held.pop(("yr", h, n))
-            t = work.tile([P, 512], F32, name="y_turned", bufs=4, align_bytes=64)
-            nc.scalar.copy(out=t[:], in_=bank[:])
-            nc.sync.dma_start(
-                out=out_rows[:, 4 * h : 4 * h + 4, 512 + n * P : 512 + (n + 1) * P],
-                in_=t[:].rearrange("p (i c) -> p i c", i=4),
+        def interleave_gpsimd(key, first):
+            if key not in held:
+                take(grouped, key)
+            raw = give(raws, ("raw",) + key)
+            blocks = slice(32 // RUN * first, 128 // RUN)
+            nc.gpsimd.tensor_scalar(
+                out=held[key][:].rearrange("p (t B i s) -> p B t i s", t=4, i=RUN, s=4)[:, blocks],
+                in0=raw[:].rearrange("p s (B t i) -> p B t i s", t=4, i=RUN)[:, blocks],
+                scalar1=1.0,
+                scalar2=0.0,
+                op0=MULT,
+                op1=ADD,
             )
 
-        load_w(1, 0)
-        load_w(1, 1)
-        x_product(0, 0)
-        x_product(0, 1)
-        w_ilv(0, 0, "s")
-        x_turn(0, 0)
-        x_out(0, 0, "s")
-        x_product(0, 2)
-        x_turn(0, 1)
-        x_out(0, 1, "s")
-        x_product(0, 3)
-        w_ilv(0, 0, "v")
-        x_turn(0, 2)
-        x_out(0, 2, "s")
-        w_ilv(0, 1, "v")
-        x_turn(0, 3)
-        x_out(0, 3, "s")
-        w_ilv(0, 1, "s")
-        w_quant(0, 0)
-        x_quant(0, 0)
-        x_quant(0, 1)
-        w_quant(0, 1)
-        bias_bank = new_bank()
-        nc.tensor.matmul(bias_bank[:, 0:48], lhsT=bias_rows[:], rhs=ident_bf[:, 0:48], start=True, stop=True)
-        nc.vector.tensor_copy(out=bias[:], in_=bias_bank[:, 0:48])
-        load_w(2, 0)
-        load_w(2, 1)
-        load_x(1, 0, 4)
-        load_w(3, 0)
-        load_w(3, 1)
-        nc.sync.dma_start(out=e_raw[:], in_=e.rearrange("(i p) k -> p i k", p=P))
-        load_w(4, 0)
-        load_w(4, 1)
-        nc.sync.dma_start(out=g_raw[:], in_=g.rearrange("(p s) f -> p s f", s=4))
-        load_w(5, 0)
-        load_w(5, 1)
-        nc.sync.dma_start(out=r_all[:], in_=r.partition_broadcast(P))
-        nc.sync.dma_start(out=d_all[:], in_=d.partition_broadcast(P))
+        def z_parts(s, split):
+            if split:
+                return [(2 * (s % 2) + n, slice(256 * (s // 2), 256 * (s // 2 + 1)), slice(256 * n, 256 * (n + 1))) for n in range(2)]
+            return [(s, whole, whole)]
 
-        fill = [[] for s in range(54)]
+        def z_product(c, h, s, split):
+            bank = take(banks, ("z", c, h, s))
+            for t, samples, place in z_parts(s, split):
+                for q in range(2):
+                    product(bank[:, place], w_mx[c][q], block(t), x_mx[h][q], samples, q == 0, q == 1)
 
-        def put(s, fn, *args):
-            fill[s].append((fn, args))
+        def z_out(c, h, s, split):
+            group, piece = divmod(c, 3)
+            bank = give(banks, ("z", c, h, s))
+            if s == 0:
+                take(planes, ("plane", c, h))
+            for t, samples, place in z_parts(s, split):
+                bias = columns[:, 2 * piece + group, t : t + 1]
+                now = held["plane", c, h][:, t, samples]
+                if piece == 0:
+                    nc.scalar.activation(out=now, in_=bank[:, place], func=IDENTITY, bias=bias)
+                else:
+                    nc.vector.scalar_tensor_tensor(out=now, in0=bank[:, place], scalar=bias, in1=held["plane", c - 1, h][:, t, samples], op0=ADD, op1=MAX)
+            if piece and s == 3:
+                give(planes, ("plane", c - 1, h))
 
-        for c in range(1, 6):
-            s = W_AT[c - 1]
-            for q in range(2):
-                put(s + q, w_ilv, c, q, "s")
-                put(s + q, w_ilv, c, q, "v")
-                put(s + q + W_LAG, w_quant, c, q)
-        for i in range(4):
-            s = X1_AT[i]
-            put(s, x_product, 1, i)
-            put(s + X_LAG[0], x_turn, 1, i)
-            put(s + X_LAG[1], x_out, 1, i, "s")
-        for n in range(4):
-            put(E_AT + n, e_turn, n)
-            put(E_AT + n + 1, e_out, n, "s")
-        for q in range(2):
-            put(E_AT + 4 + 2 * q, e_quant, q)
-            put(X_AT + q, x_quant, 1, q)
-            put(G_AT + 2 * q, g_ilv, q, "s")
-            put(G_AT + 2 * q, g_ilv, q, "v")
-            put(G_AT + 2 * q + 2, g_quant, q)
-        for at, (q, n) in enumerate(((0, 0), (1, 0), (0, 1), (1, 1))):
-            s = V_AT[at]
+        def z_aside(c, h, t):
+            group, piece = divmod(c, 3)
+            if t == 0:
+                take(planes, ("aside", c, h))
+            bias = columns[:, 2 * piece + group, t : t + 1]
+            nc.scalar.activation(out=held["aside", c, h][:, t, :], in_=give(banks, ("z", c, h, t))[:], func=IDENTITY, bias=bias)
+
+        def z_merge(c, h):
+            merged = take(planes, ("plane", c, h))
+            nc.vector.tensor_tensor(out=merged[:], in0=give(planes, ("aside", c, h))[:], in1=give(planes, ("plane", c - 1, h))[:], op=MAX)
+
+        def plane_interleave(key, source, first, count, on_vector):
+            if first == 0:
+                take(grouped, key)
+            copy(
+                on_vector,
+                held[key][:, 512 * first : 512 * (first + count)].rearrange("p (c i t) -> p c t i", i=4, t=4),
+                held[source][:, :, 128 * first : 128 * (first + count)].rearrange("p t (c i) -> p c t i", i=4),
+            )
+            if first + count == 4:
+                give(planes, source)
+
+        def h_quantize(group, h, part, last):
+            quantize(h_mx[group][h], held["h", group, h], slice(256 * part, 256 * (part + 1)))
+            if last:
+                give(grouped, ("h", group, h))
+
+        def e_turn(n, j):
+            bank = take(banks, ("ebank", n, j))
+            for i in range(2):
+                words = e_raw[n][:, 2 * j + i, :].bitcast(F32)
+                for u in range(2):
+                    nc.tensor.transpose(bank[:, block(2 * i + u)], words[:, u:256:2], ident[:])
+
+        def e_out(n, j):
+            if j == 0:
+                take(grouped, ("e", n))
+            nc.scalar.copy(
+                out=held["e", n][:].bitcast(F32)[:, 512 * j : 512 * (j + 1)].rearrange("p (i r u) -> p i r u", i=2, u=2),
+                in_=give(banks, ("ebank", n, j))[:].rearrange("p (i u r) -> p i r u", i=2, u=2),
+            )
+
+        def v_tile(q, n, j):
+            bank = take(banks, ("vbank", q, n, j))
             for t in range(4):
-                put(s + t // 2, v_mm, q, n, t)
-                put(s + t // 2, v_out, q, n, t)
-            put(s + 3, v_ilv, q, n)
-            put(s + 4, v_quant, q, n)
-        for n in range(4):
-            put(Y_AT[n], y_mm, 0, n, 0)
-            put(Y_AT[n], y_scale, 0, n, 0)
-            put(Y_AT[n] + 1, y_store, 0, n, 0)
-            put(YT_AT[n], yt_mm, 0, n)
-            put(YT_AT[n], yt_scale, 0, n)
-            put(YT_AT[n] + 1, yt_turn, 0, n)
-            put(YT_AT[n] + 1, yt_store, 0, n)
+                product(bank[:, block(t)], g_mx[q], block(t), e_mx[n], block(j), True, True)
 
-        for s in range(54):
-            t = s % 4
-            if s < 48:
-                c, h = Z_ORDER[s // 4]
-                z_mm(c, h, t)
-            for fn, args in fill[s]:
-                fn(*args)
-            if s < 48:
-                z_out(c, h, t)
-                if c % 3 == 2 and t == 3:
-                    tiles = dict(top)
-                    for half in range(2):
-                        fill[s + H_LAG[half]].insert(0, (h_max, (tiles, c // 3, h, half)))
-                        fill[s + H_LAG[half] + 1].insert(0, (h_quant, (c // 3, h, half)))
+        def v_out(q, n, j):
+            if j == 0:
+                take(grouped, ("v", q, n))
+            nc.vector.tensor_tensor(
+                out=held["v", q, n][:, 512 * j : 512 * (j + 1)].rearrange("p (c t) -> p c t", t=4),
+                in0=give(banks, ("vbank", q, n, j))[:].rearrange("p (t c) -> p c t", t=4),
+                in1=columns[:, 6 + q : 7 + q, :].to_broadcast([P, P, 4]),
+                op=ADD,
+            )
 
-        for n in range(6):
-            if n < 4:
-                y_mm(1, n, 0)
-                y_scale(1, n, 0)
-            if 0 < n < 5:
-                yt_mm(1, n - 1)
-                y_store(1, n - 1, 0)
-                yt_scale(1, n - 1)
-            if n > 1:
-                yt_turn(1, n - 2)
-                yt_store(1, n - 2)
+        def v_slot(q, n, t):
+            product(take(banks, ("vbank", q, n, t))[:], g_mx[q], block(t), e_mx[n], whole, True, True)
+
+        def v_slot_out(q, n, t):
+            if t == 0:
+                take(planes, ("vplane", q, n))
+            nc.scalar.activation(out=held["vplane", q, n][:, t, :], in_=give(banks, ("vbank", q, n, t))[:], func=IDENTITY, bias=columns[:, 6 + q, t : t + 1])
+
+        def y_product(i):
+            bank = take(banks, ("y", i))
+            for q in range(2):
+                product(bank[:], h_mx[q][i // 4], block(i % 4), v_mx[q][1], whole, q == 0, q == 1)
+
+        def y_scale(i):
+            nc.vector.tensor_tensor(out=take(results, ("y", "out", i))[:], in0=give(banks, ("y", i))[:], in1=r_all[:], op=MULT)
+
+        def y_add(i, engine):
+            t = held["y", "out", i]
+            engine.tensor_tensor(out=t[:], in0=t[:], in1=d_all[:], op=ADD)
+
+        def y_store(i):
+            nc.sync.dma_start(out=out_rows[:, i, 512:1024], in_=give(results, ("y", "out", i))[:])
+
+        def yt_product(j, m):
+            bank = take(banks, ("yt", j, m))
+            samples = slice(256 * (j % 2), 256 * (j % 2 + 1))
+            for n in range(2):
+                for q in range(2):
+                    product(bank[:, 256 * n : 256 * (n + 1)], v_mx[q][0], block(2 * m + n), h_mx[q][j // 2], samples, q == 0, q == 1)
+
+        def yt_scale(j, m):
+            bank = give(banks, ("yt", j, m))
+            t = take(by_class, ("cls", j, m))
+            for n in range(2):
+                cols = slice(256 * n, 256 * (n + 1))
+                k = 2 * m + n
+                nc.scalar.activation(out=t[:, cols], in_=bank[:, cols], func=IDENTITY, scale=columns[:, 8, k : k + 1], bias=columns[:, 9, k : k + 1])
+
+        def yt_turn_pair(j):
+            yt_turn(j, 0)
+            yt_turn(j, 1)
+
+        def yt_turn(j, m):
+            bank = take(banks, ("yr", j, m))
+            t = give(by_class, ("cls", j, m))
+            for i in range(2):
+                for n in range(2):
+                    nc.tensor.transpose(bank[:, block(2 * i + n)], t[:, block(2 * n + i)], ident[:])
+
+        def yt_out(j, m):
+            nc.scalar.copy(out=take(results, ("yt", "out", j, m))[:], in_=give(banks, ("yr", j, m))[:])
+
+        def yt_store(j, m):
+            t = give(results, ("yt", "out", j, m))
+            nc.sync.dma_start(
+                out=out_rows[:, 2 * j : 2 * j + 2, 256 * m : 256 * (m + 1)],
+                in_=t[:].rearrange("p (i c) -> p i c", i=2),
+            )
+
+        make_identity(nc, ident[:])
+        nc.vector.memset(rows[:], 0.0)
+        nc.scalar.activation(out=ident_bf[:], in_=ident[:], func=IDENTITY)
+
+        def run(stage):
+            stage[0](*stage[1:])
+
+        def permute_rows():
+            nc.vector.tensor_copy(
+                out=rows[0:8, :].rearrange("p (t B i) -> p t B i", t=4, i=RUN),
+                in_=rows_raw[:].rearrange("p (B t i) -> p t B i", t=4, i=RUN),
+            )
+
+        def columns_product():
+            bank = take(banks, "columns")
+            for n in range(WARM):
+                nc.tensor.matmul(bank[:], lhsT=ident_bf[:], rhs=rows[:], start=True, stop=True)
+            for t in range(4):
+                nc.tensor.matmul(bank[:, 16 * t : 16 * t + 10], lhsT=rows[:, block(t)], rhs=ident_bf[:, 0:10], start=True, stop=True)
+
+        def columns_out():
+            nc.scalar.copy(out=columns[:], in_=give(banks, "columns")[:, 0:64].rearrange("p (t j) -> p j t", t=4)[:, 0:10, :])
+
+        def unit(*stage, makes=(), needs=(), feed=None, feed_needs=()):
+            return (stage, makes, needs, feed, feed_needs)
+
+        def z_units(c, h, split=False):
+            units = []
+            for s in range(4):
+                slots = [t for t, samples, place in z_parts(s, split)]
+                needs = [("z", c - 1, h, t) for t in slots] if c % 3 else []
+                makes = [("z", c, h, s)]
+                feed_needs = [("w", c, q) for q in range(2)] + [("x", h, q) for q in range(2)]
+                units.append(unit(z_out, c, h, s, split, makes=makes, needs=needs + ["columns"], feed=(z_product, c, h, s, split), feed_needs=feed_needs))
+            return units
+
+        def z_aside_units(c, h):
+            feed_needs = [("w", c, q) for q in range(2)] + [("x", h, q) for q in range(2)]
+            return [unit(z_aside, c, h, t, makes=[("aside", c, h, t)], feed=(z_product, c, h, t, False), feed_needs=feed_needs) for t in range(4)]
+
+        def z_merge_unit(c, h):
+            return unit(z_merge, c, h, makes=[("z", c, h, t) for t in range(4)], needs=[("aside", c, h, t) for t in range(4)] + [("z", c - 1, h, t) for t in range(4)])
+
+        def parts(key, first, last, on_vector):
+            count = 2 if on_vector else 1
+            return [
+                unit(interleave, key, n, count, on_vector, makes=[key + (m,) for m in range(n, n + count)], needs=[("raw",) + key] + [key + (m,) for m in range(n) if m == 0 or n + count == 4])
+                for n in range(first, last, count)
+            ]
+
+        def quant(mx, key, heir=None):
+            return unit(finish, mx, key, heir, makes=[key, ("heir", heir)], needs=[key + (n,) for n in range(4)])
+
+        def on_gpsimd(key, inherits=True, first=0):
+            needs = [("raw",) + key] + ([("heir", key)] if inherits else []) + [key + (n,) for n in range(first)]
+            return [unit(interleave_gpsimd, key, first, needs=needs)] + [pause()] * (GP_TICKS - 2 - first) + [pause([key + (n,) for n in range(first, 4)])]
+
+        def w_quant(c, q, heir=None):
+            return quant(w_mx[c][q], ("w", c, q), heir)
+
+        def x_outs(h, tiles):
+            return [
+                unit(x_out, h, i, q, makes=[("x", h, q, i)], feed=None if q else (x_turn, h, i), feed_needs=[] if q else [("wide", h, i)]) for i in tiles for q in range(2)
+            ]
+
+        def x_quant(h, q, heir=None):
+            return quant(x_mx[h][q], ("x", h, q), heir)
+
+        def widen(h, tiles):
+            return [unit(x_widen, h, i, q, makes=[("wide", h, i)] if q else [], needs=[("xraw", h, i // 2)]) for i in tiles for q in range(2)]
+
+        def v_units(q, n):
+            return [unit(v_out, q, n, j, makes=[("v", q, n, j)], feed=(v_tile, q, n, j), feed_needs=[("g", q), ("e", n)]) for j in range(4)]
+
+        def v_scalar_units(q, n):
+            reads = [unit(v_slot_out, q, n, t, feed=(v_slot, q, n, t), feed_needs=[("g", q), ("e", n)]) for t in range(4)]
+            return reads + [unit(plane_interleave, ("v", q, n), ("vplane", q, n), j, 1, False, makes=[("v", q, n, j)]) for j in range(4)]
+
+        def v_quant(q, n, heir=None):
+            return quant(v_mx[q][n], ("v", q, n), heir)
+
+        def h_parts(group, h, first, last, on_vector, split=False):
+            count = 2 if on_vector else 1
+            return [
+                unit(
+                    plane_interleave, ("h", group, h), ("plane", 3 * group + 2, h), n, count, on_vector, makes=[("h", group, h, m) for m in range(n, n + count)],
+                    needs=[("z", 3 * group + 2, h, s) for s in range(4) if not split or s // 2 == n // 2] + [("h", group, h, m) for m in range(n) if m == 0 or n + count == 4],
+                )
+                for n in range(first, last, count)
+            ]
+
+        def h_quants(group, h, order=(0, 1)):
+            return [unit(h_quantize, group, h, part, part == order[1], makes=[("hq", group, h, part)], needs=[("h", group, h, 2 * part + n) for n in range(2)]) for part in order]
+
+        def w_s(c, q, first=0, last=4):
+            return parts(("w", c, q), first, last, False)
+
+        def w_v(c, q, first=0, last=4):
+            return parts(("w", c, q), first, last, True)
+
+        def mix(first, second):
+            marked = [((n + 0.5) / len(first), 0, n) for n in range(len(first))] + [((n + 0.5) / len(second), 1, n) for n in range(len(second))]
+            return [(first, second)[k][n] for at, k, n in sorted(marked)]
+
+        def y_needs(j, n):
+            return [("hq", q, j // 2, j % 2) for q in range(2)] + [("v", q, n) for q in range(2)]
+
+        def yt_scales(j):
+            return [unit(yt_scale, j, m, makes=[("yt", j, m)], feed=(yt_product, j, m), feed_needs=y_needs(j, 0)) for m in range(2)]
+
+        def yt_outs(j):
+            return [unit(yt_out, j, m, makes=[("yt", "out", j, m)], feed=None if m else (yt_turn_pair, j), feed_needs=[("yt", j, 0), ("yt", j, 1)]) for m in range(2)]
+
+        def pause(makes=()):
+            return unit(makes=makes)
+
+        e_units = [unit(e_out, n, j, makes=[("e", n, 2 * j), ("e", n, 2 * j + 1)], feed=(e_turn, n, j), feed_needs=[("eraw", n)]) for n in range(2) for j in range(2)]
+
+        def e_quant(n, heir=None):
+            return quant(e_mx[n], ("e", n), heir)
+
+        def g_quant(q, heir=None):
+            return quant(g_mx[q], ("g", q), heir)
+
+        last = z_units(5, 1, True)
+        ys = [unit(y_scale, i, makes=[("y", i)], needs=["r"], feed=(y_product, i), feed_needs=y_needs(i // 2, 1)) for i in range(8)]
+        adds = [unit(y_add, i, nc.vector, makes=[("y", "out", i)]) for i in range(ADD_GP, 8)]
+
+        def w_loads(c):
+            return [unit(load_w, c, q, makes=[("raw", "w", c, q)], needs=[("w", c - 3, q, 3)] if c > 2 else []) for q in range(2)]
+
+        def x_load(h, j):
+            return unit(load_x, h, j, makes=[("xraw", h, j)])
+
+        sync_lane = (
+            [x_load(0, 0), unit(load, xs[:], x_scale.rearrange("o (q p t) -> p (o q) t", q=2, t=4)), x_load(0, 1)] + w_loads(0) + [x_load(1, 0)]
+            + [unit(load, rows_raw[0:6, :], b.rearrange("(c n) -> c n", n=512)), unit(load, rows_raw[6:8, :], a.rearrange("(c n) -> c n", n=512))]
+            + w_loads(1)
+            + [unit(load, rows[8:9, :], r[0:512].rearrange("(o n) -> o n", o=1)), unit(load, rows[9:10, :], d[0:512].rearrange("(o n) -> o n", o=1))]
+            + [x_load(1, 1)] + w_loads(2)
+            + [unit(load_e, 0, makes=[("eraw", 0)]), unit(load_g, 0, makes=[("raw", "g", 0)]), unit(load_g, 1, makes=[("raw", "g", 1)])]
+            + w_loads(3) + [unit(load_e, 1, makes=[("eraw", 1)])] + w_loads(4) + w_loads(5)
+            + [unit(load, r_all[:], r[512:1024].partition_broadcast(P)), unit(load, d_all[:], d[512:1024].partition_broadcast(P), makes=["r"])]
+        )
+        for j, direct in ((0, (0,)), (1, (1, 2, 3)), (2, (4, 5)), (3, (6, 7))):
+            sync_lane += [unit(yt_store, j, m, needs=[("yt", "out", j, m)]) for m in range(2)]
+            sync_lane += [unit(y_store, n, needs=[("y", "out", n)]) for n in direct]
+        gpsimd_lane = on_gpsimd(("w", 0, 0), False) + on_gpsimd(("w", 0, 1), False, 2)
+        for key in (("w", 1, 1), ("w", 2, 0), ("g", 0)):
+            gpsimd_lane += on_gpsimd(key)
+        for c in (3, 4):
+            gpsimd_lane += on_gpsimd(("w", c, 0)) + on_gpsimd(("w", c, 1), False, 2)
+        gpsimd_lane += on_gpsimd(("w", 5, 0))
+        for i in range(ADD_GP):
+            gpsimd_lane += [unit(y_add, i, nc.gpsimd, needs=[("y", i)]), pause(), pause([("y", "out", i)])]
+        closing = z_units(5, 0, True)
+        vector_lane = (
+            [unit(x_widen_vector, 0, i, makes=[("wide", 0, i)], needs=[("xraw", 0, 0)]) for i in range(2)]
+            + x_outs(0, range(4))
+            + [unit(permute_rows, makes=["rows"]), x_quant(0, 0), w_quant(0, 0), x_quant(0, 1), w_quant(0, 1)]
+            + [unit(x_widen_vector, 1, 2, makes=[("wide", 1, 2)], needs=[("xraw", 1, 1)]), w_quant(1, 0, ("w", 1, 1))]
+            + x_outs(1, (0, 1, 2)) + [w_quant(1, 1, ("w", 2, 0))]
+            + x_outs(1, (3,)) + z_units(1, 0) + [x_quant(1, 0), x_quant(1, 1), w_quant(2, 0), w_quant(2, 1), e_quant(0, ("g", 0))]
+            + z_units(2, 0) + z_units(1, 1)[:2] + [g_quant(0), g_quant(1, ("w", 3, 0))]
+            + z_units(1, 1)[2:] + v_units(0, 0) + z_units(2, 1)[:2] + [w_quant(3, 0), w_quant(3, 1), e_quant(1), v_quant(0, 0, ("w", 4, 0))]
+            + z_units(2, 1)[2:] + v_units(0, 1) + v_units(1, 1)[:2] + [w_quant(4, 0), w_quant(4, 1), v_quant(1, 0)] + h_quants(0, 0) + [v_quant(0, 1, ("w", 5, 0))]
+            + v_units(1, 1)[2:] + z_units(4, 0) + [w_quant(5, 0), w_quant(5, 1), v_quant(1, 1)] + h_quants(0, 1)
+            + closing[:2] + h_parts(1, 0, 0, 2, True, True) + closing[2:3] + h_quants(1, 0)[:1] + closing[3:] + [z_merge_unit(4, 1)]
+            + last[:1] + h_quants(1, 0)[1:] + last[1:2] + ys[:1] + h_parts(1, 1, 0, 2, True, True) + last[2:3] + h_quants(1, 1)[:1] + last[3:] + ys[1:3]
+            + h_quants(1, 1)[1:] + ys[3:6] + adds[:1] + ys[6:7] + adds[1:2] + ys[7:] + adds[2:]
+        )
+        scalar_lane = (
+            widen(0, (2, 3)) + w_s(0, 1, 0, 2) + widen(1, (0,)) + w_s(1, 0) + widen(1, (1,))
+            + [unit(columns_out, makes=["columns"], feed=(columns_product,), feed_needs=["rows"])]
+            + z_units(0, 0)[:2] + widen(1, (3,)) + z_units(0, 0)[2:] + w_s(2, 1) + e_units[:2]
+            + parts(("g", 1), 0, 2, False) + mix(z_units(0, 1), parts(("g", 1), 2, 4, False)) + w_s(3, 1, 0, 2) + e_units[2:] + v_scalar_units(1, 0)
+            + w_s(4, 1, 0, 2) + z_units(3, 0) + h_parts(0, 0, 0, 4, False) + mix(w_s(5, 1), z_units(3, 1)) + h_parts(0, 1, 0, 4, False) + z_aside_units(4, 1)
+            + h_parts(1, 0, 2, 4, False, True)
+            + yt_scales(0) + yt_scales(1) + yt_outs(0) + h_parts(1, 1, 2, 4, False, True) + yt_outs(1) + yt_scales(2) + yt_scales(3) + yt_outs(2) + yt_outs(3)
+        )
+
+        lanes = [vector_lane, scalar_lane, gpsimd_lane, sync_lane]
+        made = set()
+        fed = [0] * 4
+        done = [0] * 4
+        while done != [len(lane) for lane in lanes]:
+            while done[3] < len(sync_lane) and all(n in made for n in sync_lane[done[3]][2]):
+                run(sync_lane[done[3]][0])
+                for n in sync_lane[done[3]][1]:
+                    made.add(n)
+                done[3] = done[3] + 1
+            ready = list(fed)
+            for k in range(3):
+                lane = lanes[k]
+                while fed[k] < min(len(lane), done[k] + REACH) and sum(1 for u in lane[done[k] : fed[k]] if u[3]) <= AHEAD and (lane[fed[k]][3] is None or (len(banks) > 1 and all(n in made for n in lane[fed[k]][4]))):
+                    if lane[fed[k]][3]:
+                        run(lane[fed[k]][3])
+                    fed[k] = fed[k] + 1
+            now = []
+            for k in range(3):
+                lane = lanes[k]
+                if done[k] < fed[k] and (done[k] < ready[k] or lane[done[k]][3] is None) and all(n in made for n in lane[done[k]][2]):
+                    if lane[done[k]][0]:
+                        run(lane[done[k]][0])
+                    now.extend(lane[done[k]][1])
+                    done[k] = done[k] + 1
+            for n in now:
+                made.add(n)

@@ -19,10 +19,8 @@ MAX = mybir.AluOpType.max
 IDENTITY = mybir.ActivationFunctionType.Identity
 
 RUN = 8
-AHEAD = 2
-ADD_GP = 4
+ADD_GP = 0
 GP_TICKS = 6
-REACH = 5
 WARM = 4
 MANUAL = True
 
@@ -40,7 +38,7 @@ def tile_maxout_generated_head_f5_kernel(tc, x_bytes, x_scale, w, b, e, g, a, r,
 
         banks = [psum.tile([P, 512], F32, name=f"bank{n}") for n in range(8)]
         grouped = [kept(f"grouped{n}", [P, 2048], BF16) for n in range(7)]
-        wide = [kept(f"x_wide{n}", [P, K], BF16) for n in range(3)]
+        wide = [kept(f"x_wide{n}", [P, K], BF16) for n in range(4)]
         results = [kept(f"result{n}", [P, 512], F32) for n in range(10)]
         by_class = [kept(f"by_class{n}", [P, 512], F32) for n in range(4)]
         raws = [kept(f"raw{n}", [P, 4, 512], BF16) for n in range(8)]
@@ -305,10 +303,6 @@ def tile_maxout_generated_head_f5_kernel(tc, x_bytes, x_scale, w, b, e, g, a, r,
                 k = 2 * m + n
                 nc.scalar.activation(out=t[:, cols], in_=bank[:, cols], func=IDENTITY, scale=columns[:, 8, k : k + 1], bias=columns[:, 9, k : k + 1])
 
-        def yt_turn_pair(j):
-            yt_turn(j, 0)
-            yt_turn(j, 1)
-
         def yt_turn(j, m):
             bank = take(banks, ("yr", j, m))
             t = give(by_class, ("cls", j, m))
@@ -350,7 +344,7 @@ def tile_maxout_generated_head_f5_kernel(tc, x_bytes, x_scale, w, b, e, g, a, r,
             nc.scalar.copy(out=columns[:], in_=give(banks, "columns")[:, 0:64].rearrange("p (t j) -> p j t", t=4)[:, 0:10, :])
 
         def unit(*stage, makes=(), needs=(), feed=None, feed_needs=()):
-            return (stage, makes, needs, feed, feed_needs)
+            return (stage, makes, list(needs) + ([feed] if feed else []), feed, feed_needs)
 
         def z_units(c, h, split=False):
             units = []
@@ -437,7 +431,10 @@ def tile_maxout_generated_head_f5_kernel(tc, x_bytes, x_scale, w, b, e, g, a, r,
             return [unit(yt_scale, j, m, makes=[("yt", j, m)], feed=(yt_product, j, m), feed_needs=y_needs(j, 0)) for m in range(2)]
 
         def yt_outs(j):
-            return [unit(yt_out, j, m, makes=[("yt", "out", j, m)], feed=None if m else (yt_turn_pair, j), feed_needs=[("yt", j, 0), ("yt", j, 1)]) for m in range(2)]
+            return [unit(yt_out, j, m, makes=[("yt", "out", j, m)], feed=(yt_turn, j, m), feed_needs=[("yt", j, m)]) for m in range(2)]
+
+        def feeds(units):
+            return [unit(*u[3], makes=[u[3]], needs=u[4]) for u in units if u[3]]
 
         def pause(makes=()):
             return unit(makes=makes)
@@ -466,71 +463,61 @@ def tile_maxout_generated_head_f5_kernel(tc, x_bytes, x_scale, w, b, e, g, a, r,
             + w_loads(1)
             + [unit(load, rows[8:9, :], r[0:512].rearrange("(o n) -> o n", o=1)), unit(load, rows[9:10, :], d[0:512].rearrange("(o n) -> o n", o=1))]
             + [x_load(1, 1)] + w_loads(2)
-            + [unit(load_e, 0, makes=[("eraw", 0)]), unit(load_g, 0, makes=[("raw", "g", 0)]), unit(load_g, 1, makes=[("raw", "g", 1)])]
-            + w_loads(3) + [unit(load_e, 1, makes=[("eraw", 1)])] + w_loads(4) + w_loads(5)
+            + [unit(load_g, 0, makes=[("raw", "g", 0)]), unit(load_e, 0, makes=[("eraw", 0)]), unit(load_e, 1, makes=[("eraw", 1)]), unit(load_g, 1, makes=[("raw", "g", 1)])]
+            + w_loads(3) + w_loads(4) + w_loads(5)
             + [unit(load, r_all[:], r[512:1024].partition_broadcast(P)), unit(load, d_all[:], d[512:1024].partition_broadcast(P), makes=["r"])]
         )
-        for j, direct in ((0, (0,)), (1, (1, 2, 3)), (2, (4, 5)), (3, (6, 7))):
-            sync_lane += [unit(yt_store, j, m, needs=[("yt", "out", j, m)]) for m in range(2)]
+        for j, direct in ((0, ()), (1, ()), (2, (0, 1)), (3, (2, 3)), (4, (4, 5, 6, 7))):
             sync_lane += [unit(y_store, n, needs=[("y", "out", n)]) for n in direct]
-        gpsimd_lane = on_gpsimd(("w", 0, 0), False) + on_gpsimd(("w", 0, 1), False, 2)
-        for key in (("w", 1, 1), ("w", 2, 0), ("g", 0)):
-            gpsimd_lane += on_gpsimd(key)
-        for c in (3, 4):
-            gpsimd_lane += on_gpsimd(("w", c, 0)) + on_gpsimd(("w", c, 1), False, 2)
-        gpsimd_lane += on_gpsimd(("w", 5, 0))
+            sync_lane += [unit(yt_store, j, m, needs=[("yt", "out", j, m)]) for m in range(2) if j < 4]
+        gpsimd_lane = on_gpsimd(("w", 0, 0), False) + on_gpsimd(("w", 0, 1), False, 2) + on_gpsimd(("w", 1, 1)) + on_gpsimd(("g", 0)) + on_gpsimd(("g", 1)) + on_gpsimd(("w", 3, 0)) + on_gpsimd(("w", 3, 1), False, 2) + on_gpsimd(("w", 4, 0)) + on_gpsimd(("w", 4, 1), False, 2) + on_gpsimd(("w", 5, 0))
         for i in range(ADD_GP):
             gpsimd_lane += [unit(y_add, i, nc.gpsimd, needs=[("y", i)]), pause(), pause([("y", "out", i)])]
         closing = z_units(5, 0, True)
+        scales = [u for j in range(4) for u in yt_scales(j)]
+        outs = [u for j in range(4) for u in yt_outs(j)]
+        column_unit = unit(columns_out, makes=["columns"], feed=(columns_product,), feed_needs=["rows"])
+        z = {(c, h): z_units(c, h) for c in range(5) for h in range(2)}
+        tensor_lane = feeds(
+            x_outs(0, range(4)) + x_outs(1, (0,)) + [column_unit] + z[0, 0][:1] + x_outs(1, (1,)) + z[0, 0][1:2] + x_outs(1, (2,)) + z[0, 0][2:] + x_outs(1, (3,))
+            + z[1, 0] + e_units + z[0, 1][:2] + mix(v_units(0, 0), z[0, 1][2:]) + z[1, 1]
+            + mix(z[2, 0], v_scalar_units(1, 0)[:4]) + z[2, 1] + mix(z[3, 0], v_units(0, 1)) + v_units(1, 1)[:2] + z[3, 1] + v_units(1, 1)[2:] + z[4, 0] + z_aside_units(4, 1)
+            + closing + last + scales[:3] + outs[:2] + scales[3:4] + ys[:2] + outs[2:4] + scales[4:6] + ys[2:3] + scales[6:7] + ys[3:4] + outs[4:6] + scales[7:] + ys[4:6] + outs[6:] + ys[6:]
+        )
         vector_lane = (
             [unit(x_widen_vector, 0, i, makes=[("wide", 0, i)], needs=[("xraw", 0, 0)]) for i in range(2)]
             + x_outs(0, range(4))
             + [unit(permute_rows, makes=["rows"]), x_quant(0, 0), w_quant(0, 0), x_quant(0, 1), w_quant(0, 1)]
-            + [unit(x_widen_vector, 1, 2, makes=[("wide", 1, 2)], needs=[("xraw", 1, 1)]), w_quant(1, 0, ("w", 1, 1))]
-            + x_outs(1, (0, 1, 2)) + [w_quant(1, 1, ("w", 2, 0))]
-            + x_outs(1, (3,)) + z_units(1, 0) + [x_quant(1, 0), x_quant(1, 1), w_quant(2, 0), w_quant(2, 1), e_quant(0, ("g", 0))]
-            + z_units(2, 0) + z_units(1, 1)[:2] + [g_quant(0), g_quant(1, ("w", 3, 0))]
-            + z_units(1, 1)[2:] + v_units(0, 0) + z_units(2, 1)[:2] + [w_quant(3, 0), w_quant(3, 1), e_quant(1), v_quant(0, 0, ("w", 4, 0))]
-            + z_units(2, 1)[2:] + v_units(0, 1) + v_units(1, 1)[:2] + [w_quant(4, 0), w_quant(4, 1), v_quant(1, 0)] + h_quants(0, 0) + [v_quant(0, 1, ("w", 5, 0))]
-            + v_units(1, 1)[2:] + z_units(4, 0) + [w_quant(5, 0), w_quant(5, 1), v_quant(1, 1)] + h_quants(0, 1)
-            + closing[:2] + h_parts(1, 0, 0, 2, True, True) + closing[2:3] + h_quants(1, 0)[:1] + closing[3:] + [z_merge_unit(4, 1)]
-            + last[:1] + h_quants(1, 0)[1:] + last[1:2] + ys[:1] + h_parts(1, 1, 0, 2, True, True) + last[2:3] + h_quants(1, 1)[:1] + last[3:] + ys[1:3]
-            + h_quants(1, 1)[1:] + ys[3:6] + adds[:1] + ys[6:7] + adds[1:2] + ys[7:] + adds[2:]
+            + [w_quant(1, 0, ("w", 1, 1))]
+            + x_outs(1, (0, 1, 2)) + [w_quant(1, 1, ("g", 0))]
+            + x_outs(1, (3,)) + z_units(1, 0) + [x_quant(1, 0), x_quant(1, 1), g_quant(0), e_quant(0), w_quant(2, 0, ("g", 1))]
+            + v_units(0, 0) + z_units(1, 1)[:2] + [w_quant(2, 1), g_quant(1), v_quant(0, 0, ("w", 3, 0))]
+            + z_units(1, 1)[2:] + z_units(2, 0) + z_units(2, 1)[:2] + [w_quant(3, 0), w_quant(3, 1), e_quant(1, ("w", 4, 0))]
+            + z_units(2, 1)[2:] + v_units(0, 1) + v_units(1, 1)[:2] + [w_quant(4, 0), w_quant(4, 1), v_quant(1, 0), v_quant(0, 1, ("w", 5, 0))]
+            + v_units(1, 1)[2:] + z_units(4, 0) + [w_quant(5, 0), w_quant(5, 1), v_quant(1, 1)] + h_quants(0, 0)
+            + closing + h_parts(1, 0, 2, 4, True, True) + h_quants(1, 0) + [z_merge_unit(4, 1)] + h_quants(0, 1)
+            + last[:3] + h_parts(1, 1, 0, 2, True, True) + last[3:] + h_quants(1, 1)[:1] + h_parts(1, 1, 2, 4, True, True) + ys[:1] + h_quants(1, 1)[1:] + mix(ys[1:], adds[:7]) + adds[7:]
         )
         scalar_lane = (
-            widen(0, (2, 3)) + w_s(0, 1, 0, 2) + widen(1, (0,)) + w_s(1, 0) + widen(1, (1,))
-            + [unit(columns_out, makes=["columns"], feed=(columns_product,), feed_needs=["rows"])]
-            + z_units(0, 0)[:2] + widen(1, (3,)) + z_units(0, 0)[2:] + w_s(2, 1) + e_units[:2]
-            + parts(("g", 1), 0, 2, False) + mix(z_units(0, 1), parts(("g", 1), 2, 4, False)) + w_s(3, 1, 0, 2) + e_units[2:] + v_scalar_units(1, 0)
-            + w_s(4, 1, 0, 2) + z_units(3, 0) + h_parts(0, 0, 0, 4, False) + mix(w_s(5, 1), z_units(3, 1)) + h_parts(0, 1, 0, 4, False) + z_aside_units(4, 1)
-            + h_parts(1, 0, 2, 4, False, True)
-            + yt_scales(0) + yt_scales(1) + yt_outs(0) + h_parts(1, 1, 2, 4, False, True) + yt_outs(1) + yt_scales(2) + yt_scales(3) + yt_outs(2) + yt_outs(3)
+            widen(0, (2, 3)) + w_s(0, 1, 0, 2) + widen(1, (0,)) + w_s(1, 0) + widen(1, (1, 2, 3))
+            + [column_unit] + z[0, 0] + w_s(2, 0) + e_units[:2] + w_s(2, 1, 0, 2) + z[0, 1] + w_s(2, 1, 2) + e_units[2:]
+            + w_s(3, 1, 0, 2) + v_scalar_units(1, 0)
+            + w_s(4, 1, 0, 2) + z[3, 0] + w_s(5, 1, 0, 2) + z[3, 1] + w_s(5, 1, 2) + h_parts(0, 0, 0, 4, False) + z_aside_units(4, 1)
+            + h_parts(0, 1, 0, 2, False) + h_parts(1, 0, 0, 2, False, True) + h_parts(0, 1, 2, 4, False)
+            + scales[:3] + outs[:2] + scales[3:4] + outs[2:4] + scales[4:7] + outs[4:6] + scales[7:] + outs[6:]
         )
 
-        lanes = [vector_lane, scalar_lane, gpsimd_lane, sync_lane]
+        lanes = [sync_lane, tensor_lane, vector_lane, scalar_lane, gpsimd_lane]
         made = set()
-        fed = [0] * 4
-        done = [0] * 4
+        done = [0] * len(lanes)
         while done != [len(lane) for lane in lanes]:
-            while done[3] < len(sync_lane) and all(n in made for n in sync_lane[done[3]][2]):
-                run(sync_lane[done[3]][0])
-                for n in sync_lane[done[3]][1]:
-                    made.add(n)
-                done[3] = done[3] + 1
-            ready = list(fed)
-            for k in range(3):
-                lane = lanes[k]
-                while fed[k] < min(len(lane), done[k] + REACH) and sum(1 for u in lane[done[k] : fed[k]] if u[3]) <= AHEAD and (lane[fed[k]][3] is None or (len(banks) > 1 and all(n in made for n in lane[fed[k]][4]))):
-                    if lane[fed[k]][3]:
-                        run(lane[fed[k]][3])
-                    fed[k] = fed[k] + 1
-            now = []
-            for k in range(3):
-                lane = lanes[k]
-                if done[k] < fed[k] and (done[k] < ready[k] or lane[done[k]][3] is None) and all(n in made for n in lane[done[k]][2]):
+            fresh = []
+            for k, lane in enumerate(lanes):
+                turn = len(lane) if k < 2 else done[k] + 1
+                while done[k] < min(turn, len(lane)) and all(n in made for n in lane[done[k]][2]) and (banks or lane is not tensor_lane):
                     if lane[done[k]][0]:
                         run(lane[done[k]][0])
-                    now.extend(lane[done[k]][1])
+                    fresh.extend(lane[done[k]][1])
                     done[k] = done[k] + 1
-            for n in now:
+            for n in fresh:
                 made.add(n)

@@ -19,9 +19,8 @@ MAX = mybir.AluOpType.max
 IDENTITY = mybir.ActivationFunctionType.Identity
 
 RUN = 8
-ADD_GP = 0
 GP_TICKS = 6
-WARM = 4
+WARM = 0
 MANUAL = True
 
 
@@ -37,7 +36,7 @@ def tile_maxout_generated_head_f5_kernel(tc, x_bytes, x_scale, w, b, e, g, a, r,
             return keep.tile(shape, dtype, name=name, align_bytes=64)
 
         banks = [psum.tile([P, 512], F32, name=f"bank{n}") for n in range(8)]
-        grouped = [kept(f"grouped{n}", [P, 2048], BF16) for n in range(7)]
+        grouped = [kept(f"grouped{n}", [P, 2048], BF16) for n in range(6)]
         wide = [kept(f"x_wide{n}", [P, K], BF16) for n in range(4)]
         results = [kept(f"result{n}", [P, 512], F32) for n in range(10)]
         by_class = [kept(f"by_class{n}", [P, 512], F32) for n in range(4)]
@@ -58,7 +57,9 @@ def tile_maxout_generated_head_f5_kernel(tc, x_bytes, x_scale, w, b, e, g, a, r,
 
         x_raw = [[kept(f"x_raw{h}_{j}", [P, 2, K], U8) for j in range(2)] for h in range(2)]
         e_raw = [kept(f"e_raw{n}", [P, 4, D], BF16) for n in range(2)]
-        x_mx = [[operand(f"x{h}_{q}") for q in range(2)] for h in range(2)]
+        x_grouped = kept("x_grouped", [P, 2, 2048], BF16)
+        x_both = [(kept(f"x{h}_codes", [P, 1024], U32), kept(f"x{h}_scales", [P, 1024], U8)) for h in range(2)]
+        x_mx = [[(codes[:, 512 * q : 512 * (q + 1)], scales[:, 512 * q : 512 * (q + 1)]) for q in range(2)] for codes, scales in x_both]
         w_mx = [[operand(f"w{c}_{q}") for q in range(2)] for c in range(6)]
         e_mx = [operand(f"e{n}") for n in range(2)]
         g_mx = [operand(f"g{q}") for q in range(2)]
@@ -121,34 +122,26 @@ def tile_maxout_generated_head_f5_kernel(tc, x_bytes, x_scale, w, b, e, g, a, r,
 
         whole = slice(0, 512)
 
-        def x_widen(h, i, q):
-            if q == 0:
-                take(wide, ("wide", h, i))
-            cols = slice(512 * q, 512 * (q + 1))
-            nc.scalar.copy(out=held["wide", h, i][:, cols], in_=x_raw[h][i // 2][:, i % 2, cols].bitcast(FP8))
-
-        def x_widen_vector(h, i):
-            nc.vector.tensor_copy(out=take(wide, ("wide", h, i))[:], in_=x_raw[h][i // 2][:, i % 2, :].bitcast(FP8))
+        def x_widen(h, i, on_vector):
+            copy(on_vector, take(wide, ("wide", h, i))[:], x_raw[h][i // 2][:, i % 2, :].bitcast(FP8))
 
         def x_turn(h, i):
             bank = take(banks, ("xbank", h, i))
             words = give(wide, ("wide", h, i))[:].bitcast(F32)
             for q in range(2):
                 for u in range(2):
-                    nc.tensor.transpose(bank[:, block(2 * q + u)], words[:, 256 * q + u : 256 * (q + 1) : 2], ident[:])
+                    nc.tensor.transpose(bank[:, block(2 * u + q)], words[:, 256 * q + u : 256 * (q + 1) : 2], ident[:])
 
-        def x_out(h, i, q):
-            pairs = held["xbank", h, i][:].bitcast(BF16)
-            if q == 1:
-                give(banks, ("xbank", h, i))
-            if i == 0:
-                take(grouped, ("x", h, q))
+        def x_out(h, i):
             nc.vector.tensor_tensor(
-                out=held["x", h, q][:, 512 * i : 512 * (i + 1)].rearrange("p (r u e) -> p r u e", u=2, e=2),
-                in0=pairs[:, 512 * q : 512 * (q + 1)].rearrange("p (u r e) -> p r u e", u=2, e=2),
-                in1=xs[:, q, :].rearrange("p (o u e) -> p o u e", o=1, u=2).to_broadcast([P, P, 2, 2]),
+                out=x_grouped[:, :, 512 * i : 512 * (i + 1)].rearrange("p q (r u e) -> p q r u e", u=2, e=2),
+                in0=give(banks, ("xbank", h, i))[:].bitcast(BF16).rearrange("p (u q r e) -> p q r u e", u=2, q=2, e=2),
+                in1=xs[:].rearrange("p q (o u e) -> p q o u e", o=1, u=2).to_broadcast([P, 2, P, 2, 2]),
                 op=MULT,
             )
+
+        def x_quantize(h, passes):
+            quantize(x_both[h], x_grouped[:].rearrange("p q n -> p (q n)"), slice(512 * passes[0], 512 * (passes[-1] + 1)))
 
         def finish(mx, key, heir):
             if heir is None:
@@ -161,21 +154,19 @@ def tile_maxout_generated_head_f5_kernel(tc, x_bytes, x_scale, w, b, e, g, a, r,
             if first == 0:
                 take(grouped, key)
             raw = give(raws, ("raw",) + key) if first + count == 4 else held[("raw",) + key]
-            blocks = slice(32 // RUN * first, 32 // RUN * (first + count))
             copy(
                 on_vector,
-                held[key][:].rearrange("p (t B i s) -> p t B s i", t=4, i=RUN, s=4)[:, :, blocks],
-                raw[:].rearrange("p s (B t i) -> p t B s i", t=4, i=RUN)[:, :, blocks],
+                held[key][:].rearrange("p (t B i s) -> p t B s i", t=4, i=RUN, s=4)[:, first : first + count],
+                raw[:].rearrange("p s (B t i) -> p t B s i", t=4, i=RUN)[:, first : first + count],
             )
 
         def interleave_gpsimd(key, first):
             if key not in held:
                 take(grouped, key)
             raw = give(raws, ("raw",) + key)
-            blocks = slice(32 // RUN * first, 128 // RUN)
             nc.gpsimd.tensor_scalar(
-                out=held[key][:].rearrange("p (t B i s) -> p B t i s", t=4, i=RUN, s=4)[:, blocks],
-                in0=raw[:].rearrange("p s (B t i) -> p B t i s", t=4, i=RUN)[:, blocks],
+                out=held[key][:].rearrange("p (t B i s) -> p B t i s", t=4, i=RUN, s=4)[:, :, first:],
+                in0=raw[:].rearrange("p s (B t i) -> p B t i s", t=4, i=RUN)[:, :, first:],
                 scalar1=1.0,
                 scalar2=0.0,
                 op0=MULT,
@@ -220,7 +211,7 @@ def tile_maxout_generated_head_f5_kernel(tc, x_bytes, x_scale, w, b, e, g, a, r,
             nc.vector.tensor_tensor(out=merged[:], in0=give(planes, ("aside", c, h))[:], in1=give(planes, ("plane", c - 1, h))[:], op=MAX)
 
         def plane_interleave(key, source, first, count, on_vector):
-            if first == 0:
+            if key not in held:
                 take(grouped, key)
             copy(
                 on_vector,
@@ -229,6 +220,16 @@ def tile_maxout_generated_head_f5_kernel(tc, x_bytes, x_scale, w, b, e, g, a, r,
             )
             if first + count == 4:
                 give(planes, source)
+
+        def plane_interleave_gpsimd(key, source, first):
+            nc.gpsimd.tensor_scalar(
+                out=held[key][:, 512 * first :].rearrange("p (c t) -> p c t", t=4),
+                in0=give(planes, source)[:, :, 128 * first :].rearrange("p t c -> p c t"),
+                scalar1=1.0,
+                scalar2=0.0,
+                op0=MULT,
+                op1=ADD,
+            )
 
         def h_quantize(group, h, part, last):
             quantize(h_mx[group][h], held["h", group, h], slice(256 * part, 256 * (part + 1)))
@@ -281,43 +282,37 @@ def tile_maxout_generated_head_f5_kernel(tc, x_bytes, x_scale, w, b, e, g, a, r,
         def y_scale(i):
             nc.vector.tensor_tensor(out=take(results, ("y", "out", i))[:], in0=give(banks, ("y", i))[:], in1=r_all[:], op=MULT)
 
-        def y_add(i, engine):
+        def y_add(i):
             t = held["y", "out", i]
-            engine.tensor_tensor(out=t[:], in0=t[:], in1=d_all[:], op=ADD)
+            nc.vector.tensor_tensor(out=t[:], in0=t[:], in1=d_all[:], op=ADD)
 
         def y_store(i):
             nc.sync.dma_start(out=out_rows[:, i, 512:1024], in_=give(results, ("y", "out", i))[:])
 
-        def yt_product(j, m):
-            bank = take(banks, ("yt", j, m))
-            samples = slice(256 * (j % 2), 256 * (j % 2 + 1))
+        def yt_product(h, n):
+            bank = take(banks, ("yt", h, n))
+            for q in range(2):
+                product(bank[:], v_mx[q][0], block(n), h_mx[q][h], whole, q == 0, q == 1)
+
+        def yt_scale(h, n):
+            nc.scalar.activation(
+                out=take(by_class, ("cls", h, n))[:], in_=give(banks, ("yt", h, n))[:], func=IDENTITY, scale=columns[:, 8, n : n + 1], bias=columns[:, 9, n : n + 1]
+            )
+
+        def yt_turn(h, m, j):
+            bank = take(banks, ("yr", h, m, j))
             for n in range(2):
-                for q in range(2):
-                    product(bank[:, 256 * n : 256 * (n + 1)], v_mx[q][0], block(2 * m + n), h_mx[q][j // 2], samples, q == 0, q == 1)
+                t = give(by_class, ("cls", h, 2 * m + n)) if j else held["cls", h, 2 * m + n]
+                for i in range(2):
+                    nc.tensor.transpose(bank[:, block(2 * i + n)], t[:, block(2 * j + i)], ident[:])
 
-        def yt_scale(j, m):
-            bank = give(banks, ("yt", j, m))
-            t = take(by_class, ("cls", j, m))
-            for n in range(2):
-                cols = slice(256 * n, 256 * (n + 1))
-                k = 2 * m + n
-                nc.scalar.activation(out=t[:, cols], in_=bank[:, cols], func=IDENTITY, scale=columns[:, 8, k : k + 1], bias=columns[:, 9, k : k + 1])
+        def yt_out(h, m, j):
+            nc.scalar.copy(out=take(results, ("yt", "out", h, m, j))[:], in_=give(banks, ("yr", h, m, j))[:])
 
-        def yt_turn(j, m):
-            bank = take(banks, ("yr", j, m))
-            t = give(by_class, ("cls", j, m))
-            for i in range(2):
-                for n in range(2):
-                    nc.tensor.transpose(bank[:, block(2 * i + n)], t[:, block(2 * n + i)], ident[:])
-
-        def yt_out(j, m):
-            nc.scalar.copy(out=take(results, ("yt", "out", j, m))[:], in_=give(banks, ("yr", j, m))[:])
-
-        def yt_store(j, m):
-            t = give(results, ("yt", "out", j, m))
+        def yt_store(h, m, j):
             nc.sync.dma_start(
-                out=out_rows[:, 2 * j : 2 * j + 2, 256 * m : 256 * (m + 1)],
-                in_=t[:].rearrange("p (i c) -> p i c", i=2),
+                out=out_rows[:, 4 * h + 2 * j : 4 * h + 2 * j + 2, 256 * m : 256 * (m + 1)],
+                in_=give(results, ("yt", "out", h, m, j))[:].rearrange("p (i c) -> p i c", i=2),
             )
 
         make_identity(nc, ident[:])
@@ -363,12 +358,12 @@ def tile_maxout_generated_head_f5_kernel(tc, x_bytes, x_scale, w, b, e, g, a, r,
         def z_merge_unit(c, h):
             return unit(z_merge, c, h, makes=[("z", c, h, t) for t in range(4)], needs=[("aside", c, h, t) for t in range(4)] + [("z", c - 1, h, t) for t in range(4)])
 
-        def parts(key, first, last, on_vector):
-            count = 2 if on_vector else 1
-            return [
-                unit(interleave, key, n, count, on_vector, makes=[key + (m,) for m in range(n, n + count)], needs=[("raw",) + key] + [key + (m,) for m in range(n) if m == 0 or n + count == 4])
-                for n in range(first, last, count)
-            ]
+        def lasting(first, turns):
+            return [first[:1] + ((),) + first[2:]] + [pause()] * (turns - 2) + [pause(first[1])] if turns > 1 else [first]
+
+        def part(key, first, last):
+            needs = [("raw",) + key] + [key + (m,) for m in range(first)]
+            return lasting(unit(interleave, key, first, last - first, False, makes=[key + (m,) for m in range(first, last)], needs=needs), last - first)
 
         def quant(mx, key, heir=None):
             return unit(finish, mx, key, heir, makes=[key, ("heir", heir)], needs=[key + (n,) for n in range(4)])
@@ -381,57 +376,45 @@ def tile_maxout_generated_head_f5_kernel(tc, x_bytes, x_scale, w, b, e, g, a, r,
             return quant(w_mx[c][q], ("w", c, q), heir)
 
         def x_outs(h, tiles):
-            return [
-                unit(x_out, h, i, q, makes=[("x", h, q, i)], feed=None if q else (x_turn, h, i), feed_needs=[] if q else [("wide", h, i)]) for i in tiles for q in range(2)
-            ]
+            return [u for i in tiles for u in lasting(unit(x_out, h, i, makes=[("x", h, "tile", i)], feed=(x_turn, h, i), feed_needs=[("wide", h, i)]), 2)]
 
-        def x_quant(h, q, heir=None):
-            return quant(x_mx[h][q], ("x", h, q), heir)
+        def x_quant(h, passes):
+            return unit(x_quantize, h, passes, makes=[("x", h, q) for q in passes], needs=[("x", h, "tile", i) for i in range(4)])
 
-        def widen(h, tiles):
-            return [unit(x_widen, h, i, q, makes=[("wide", h, i)] if q else [], needs=[("xraw", h, i // 2)]) for i in tiles for q in range(2)]
+        def widen(h, tiles, on_vector=False):
+            return [u for i in tiles for u in lasting(unit(x_widen, h, i, on_vector, makes=[("wide", h, i)], needs=[("xraw", h, i // 2)]), 1 if on_vector else 2)]
 
         def v_units(q, n):
             return [unit(v_out, q, n, j, makes=[("v", q, n, j)], feed=(v_tile, q, n, j), feed_needs=[("g", q), ("e", n)]) for j in range(4)]
 
         def v_scalar_units(q, n):
             reads = [unit(v_slot_out, q, n, t, feed=(v_slot, q, n, t), feed_needs=[("g", q), ("e", n)]) for t in range(4)]
-            return reads + [unit(plane_interleave, ("v", q, n), ("vplane", q, n), j, 1, False, makes=[("v", q, n, j)]) for j in range(4)]
+            return reads + lasting(unit(plane_interleave, ("v", q, n), ("vplane", q, n), 0, 4, False, makes=[("v", q, n, j) for j in range(4)]), 4)
 
         def v_quant(q, n, heir=None):
             return quant(v_mx[q][n], ("v", q, n), heir)
 
-        def h_parts(group, h, first, last, on_vector, split=False):
-            count = 2 if on_vector else 1
-            return [
-                unit(
-                    plane_interleave, ("h", group, h), ("plane", 3 * group + 2, h), n, count, on_vector, makes=[("h", group, h, m) for m in range(n, n + count)],
-                    needs=[("z", 3 * group + 2, h, s) for s in range(4) if not split or s // 2 == n // 2] + [("h", group, h, m) for m in range(n) if m == 0 or n + count == 4],
-                )
-                for n in range(first, last, count)
-            ]
+        def h_part(group, h, first, last, on_vector, slots=range(4), inherits=False):
+            key = ("h", group, h)
+            needs = [("z", 3 * group + 2, h, s) for s in slots] + [key + (m,) for m in range(first)] + ([("heir", key)] if inherits else [])
+            work = unit(plane_interleave, key, ("plane", 3 * group + 2, h), first, last - first, on_vector, makes=[key + (m,) for m in range(first, last)], needs=needs)
+            return lasting(work, (last - first) // 2 if on_vector else last - first)
 
-        def h_quants(group, h, order=(0, 1)):
-            return [unit(h_quantize, group, h, part, part == order[1], makes=[("hq", group, h, part)], needs=[("h", group, h, 2 * part + n) for n in range(2)]) for part in order]
+        def h_quants(group, h):
+            return [unit(h_quantize, group, h, part, part == 1, makes=[("h", group, h)] if part else [], needs=[("h", group, h, 2 * part + n) for n in range(2)]) for part in range(2)]
+
+        def h_quant(group, h, heir=None):
+            return quant(h_mx[group][h], ("h", group, h), heir)
 
         def w_s(c, q, first=0, last=4):
-            return parts(("w", c, q), first, last, False)
-
-        def w_v(c, q, first=0, last=4):
-            return parts(("w", c, q), first, last, True)
+            return part(("w", c, q), first, last)
 
         def mix(first, second):
             marked = [((n + 0.5) / len(first), 0, n) for n in range(len(first))] + [((n + 0.5) / len(second), 1, n) for n in range(len(second))]
             return [(first, second)[k][n] for at, k, n in sorted(marked)]
 
-        def y_needs(j, n):
-            return [("hq", q, j // 2, j % 2) for q in range(2)] + [("v", q, n) for q in range(2)]
-
-        def yt_scales(j):
-            return [unit(yt_scale, j, m, makes=[("yt", j, m)], feed=(yt_product, j, m), feed_needs=y_needs(j, 0)) for m in range(2)]
-
-        def yt_outs(j):
-            return [unit(yt_out, j, m, makes=[("yt", "out", j, m)], feed=(yt_turn, j, m), feed_needs=[("yt", j, m)]) for m in range(2)]
+        def y_needs(h, n):
+            return [("h", q, h) for q in range(2)] + [("v", q, n) for q in range(2)]
 
         def feeds(units):
             return [unit(*u[3], makes=[u[3]], needs=u[4]) for u in units if u[3]]
@@ -447,9 +430,15 @@ def tile_maxout_generated_head_f5_kernel(tc, x_bytes, x_scale, w, b, e, g, a, r,
         def g_quant(q, heir=None):
             return quant(g_mx[q], ("g", q), heir)
 
-        last = z_units(5, 1, True)
-        ys = [unit(y_scale, i, makes=[("y", i)], needs=["r"], feed=(y_product, i), feed_needs=y_needs(i // 2, 1)) for i in range(8)]
-        adds = [unit(y_add, i, nc.vector, makes=[("y", "out", i)]) for i in range(ADD_GP, 8)]
+        ys = [unit(y_scale, i, needs=["r"], feed=(y_product, i), feed_needs=y_needs(i // 4, 1)) for i in range(8)]
+        adds = [unit(y_add, i, makes=[("y", "out", i)]) for i in range(8)]
+        scales = [unit(yt_scale, h, n, makes=[("yt", h, n)], feed=(yt_product, h, n), feed_needs=y_needs(h, 0)) for h in range(2) for n in range(4)]
+        outs = [
+            unit(yt_out, h, m, j, makes=[("yt", "out", h, m, j)], feed=(yt_turn, h, m, j), feed_needs=[("yt", h, 2 * m), ("yt", h, 2 * m + 1)])
+            for h in range(2)
+            for m in range(2)
+            for j in range(2)
+        ]
 
         def w_loads(c):
             return [unit(load_w, c, q, makes=[("raw", "w", c, q)], needs=[("w", c - 3, q, 3)] if c > 2 else []) for q in range(2)]
@@ -458,52 +447,49 @@ def tile_maxout_generated_head_f5_kernel(tc, x_bytes, x_scale, w, b, e, g, a, r,
             return unit(load_x, h, j, makes=[("xraw", h, j)])
 
         sync_lane = (
-            [x_load(0, 0), unit(load, xs[:], x_scale.rearrange("o (q p t) -> p (o q) t", q=2, t=4)), x_load(0, 1)] + w_loads(0) + [x_load(1, 0)]
+            [x_load(0, 0), unit(load, xs[:], x_scale.rearrange("o (q p t) -> p (o q) t", q=2, t=4)), x_load(0, 1)] + w_loads(0)[:1] + [x_load(1, 0)] + w_loads(0)[1:] + w_loads(1) + [x_load(1, 1)]
             + [unit(load, rows_raw[0:6, :], b.rearrange("(c n) -> c n", n=512)), unit(load, rows_raw[6:8, :], a.rearrange("(c n) -> c n", n=512))]
-            + w_loads(1)
             + [unit(load, rows[8:9, :], r[0:512].rearrange("(o n) -> o n", o=1)), unit(load, rows[9:10, :], d[0:512].rearrange("(o n) -> o n", o=1))]
-            + [x_load(1, 1)] + w_loads(2)
+            + w_loads(2)
             + [unit(load_g, 0, makes=[("raw", "g", 0)]), unit(load_e, 0, makes=[("eraw", 0)]), unit(load_e, 1, makes=[("eraw", 1)]), unit(load_g, 1, makes=[("raw", "g", 1)])]
             + w_loads(3) + w_loads(4) + w_loads(5)
             + [unit(load, r_all[:], r[512:1024].partition_broadcast(P)), unit(load, d_all[:], d[512:1024].partition_broadcast(P), makes=["r"])]
         )
-        for j, direct in ((0, ()), (1, ()), (2, (0, 1)), (3, (2, 3)), (4, (4, 5, 6, 7))):
+        for pair, direct in enumerate(((), (0,), (1, 2, 3), (4, 5), (6, 7))):
             sync_lane += [unit(y_store, n, needs=[("y", "out", n)]) for n in direct]
-            sync_lane += [unit(yt_store, j, m, needs=[("yt", "out", j, m)]) for m in range(2) if j < 4]
-        gpsimd_lane = on_gpsimd(("w", 0, 0), False) + on_gpsimd(("w", 0, 1), False, 2) + on_gpsimd(("w", 1, 1)) + on_gpsimd(("g", 0)) + on_gpsimd(("g", 1)) + on_gpsimd(("w", 3, 0)) + on_gpsimd(("w", 3, 1), False, 2) + on_gpsimd(("w", 4, 0)) + on_gpsimd(("w", 4, 1), False, 2) + on_gpsimd(("w", 5, 0))
-        for i in range(ADD_GP):
-            gpsimd_lane += [unit(y_add, i, nc.gpsimd, needs=[("y", i)]), pause(), pause([("y", "out", i)])]
+            sync_lane += [unit(yt_store, pair // 2, pair % 2, j, needs=[("yt", "out", pair // 2, pair % 2, j)]) for j in range(2) if pair < 4]
+        gpsimd_lane = on_gpsimd(("w", 0, 0), False) + on_gpsimd(("w", 0, 1), False, 2) + on_gpsimd(("w", 1, 1)) + on_gpsimd(("g", 0)) + on_gpsimd(("g", 1))
+        for c in (3, 4):
+            gpsimd_lane += on_gpsimd(("w", c, 0)) + on_gpsimd(("w", c, 1), False, 2)
+        gpsimd_lane += on_gpsimd(("w", 5, 0))
+        gpsimd_lane += lasting(unit(plane_interleave_gpsimd, ("h", 0, 1), ("plane", 2, 1), 1, makes=[("h", 0, 1, n) for n in range(1, 4)], needs=[("h", 0, 1, 0)]), GP_TICKS - 1)
         closing = z_units(5, 0, True)
-        scales = [u for j in range(4) for u in yt_scales(j)]
-        outs = [u for j in range(4) for u in yt_outs(j)]
         column_unit = unit(columns_out, makes=["columns"], feed=(columns_product,), feed_needs=["rows"])
         z = {(c, h): z_units(c, h) for c in range(5) for h in range(2)}
         tensor_lane = feeds(
-            x_outs(0, range(4)) + x_outs(1, (0,)) + [column_unit] + z[0, 0][:1] + x_outs(1, (1,)) + z[0, 0][1:2] + x_outs(1, (2,)) + z[0, 0][2:] + x_outs(1, (3,))
-            + z[1, 0] + e_units + z[0, 1][:2] + mix(v_units(0, 0), z[0, 1][2:]) + z[1, 1]
+            x_outs(0, range(4)) + x_outs(1, (0, 1)) + z[0, 0][:1] + [column_unit] + z[0, 0][1:2] + x_outs(1, (2,)) + z[0, 0][2:3] + x_outs(1, (3,)) + z[0, 0][3:]
+            + z[1, 0] + e_units[:2] + z[0, 1][:2] + mix(v_units(0, 0), z[0, 1][2:]) + z[1, 1] + e_units[2:]
             + mix(z[2, 0], v_scalar_units(1, 0)[:4]) + z[2, 1] + mix(z[3, 0], v_units(0, 1)) + v_units(1, 1)[:2] + z[3, 1] + v_units(1, 1)[2:] + z[4, 0] + z_aside_units(4, 1)
-            + closing + last + scales[:3] + outs[:2] + scales[3:4] + ys[:2] + outs[2:4] + scales[4:6] + ys[2:3] + scales[6:7] + ys[3:4] + outs[4:6] + scales[7:] + ys[4:6] + outs[6:] + ys[6:]
+            + closing + z_aside_units(5, 1) + scales[:2] + ys[:1] + scales[2:3] + outs[:2] + scales[3:4] + ys[1:3] + outs[2:4] + ys[3:4] + scales[4:6] + ys[4:5] + scales[6:7] + outs[4:6] + ys[5:6] + scales[7:] + ys[6:] + outs[6:]
         )
         vector_lane = (
-            [unit(x_widen_vector, 0, i, makes=[("wide", 0, i)], needs=[("xraw", 0, 0)]) for i in range(2)]
-            + x_outs(0, range(4))
-            + [unit(permute_rows, makes=["rows"]), x_quant(0, 0), w_quant(0, 0), x_quant(0, 1), w_quant(0, 1)]
-            + [w_quant(1, 0, ("w", 1, 1))]
+            widen(0, (0, 1, 2), True) + x_outs(0, range(4))
+            + [x_quant(0, (0,)), w_quant(0, 0), x_quant(0, (1,)), w_quant(0, 1), unit(permute_rows, makes=["rows"]), w_quant(1, 0, ("w", 1, 1))]
             + x_outs(1, (0, 1, 2)) + [w_quant(1, 1, ("g", 0))]
-            + x_outs(1, (3,)) + z_units(1, 0) + [x_quant(1, 0), x_quant(1, 1), g_quant(0), e_quant(0), w_quant(2, 0, ("g", 1))]
-            + v_units(0, 0) + z_units(1, 1)[:2] + [w_quant(2, 1), g_quant(1), v_quant(0, 0, ("w", 3, 0))]
-            + z_units(1, 1)[2:] + z_units(2, 0) + z_units(2, 1)[:2] + [w_quant(3, 0), w_quant(3, 1), e_quant(1, ("w", 4, 0))]
-            + z_units(2, 1)[2:] + v_units(0, 1) + v_units(1, 1)[:2] + [w_quant(4, 0), w_quant(4, 1), v_quant(1, 0), v_quant(0, 1, ("w", 5, 0))]
-            + v_units(1, 1)[2:] + z_units(4, 0) + [w_quant(5, 0), w_quant(5, 1), v_quant(1, 1)] + h_quants(0, 0)
-            + closing + h_parts(1, 0, 2, 4, True, True) + h_quants(1, 0) + [z_merge_unit(4, 1)] + h_quants(0, 1)
-            + last[:3] + h_parts(1, 1, 0, 2, True, True) + last[3:] + h_quants(1, 1)[:1] + h_parts(1, 1, 2, 4, True, True) + ys[:1] + h_quants(1, 1)[1:] + mix(ys[1:], adds[:7]) + adds[7:]
+            + x_outs(1, (3,)) + z[1, 0] + [x_quant(1, (0,)), x_quant(1, (1,)), g_quant(0), e_quant(0, ("g", 1)), w_quant(2, 0)]
+            + v_units(0, 0) + z[1, 1][:2] + [w_quant(2, 1), g_quant(1, ("w", 3, 0)), v_quant(0, 0)]
+            + z[1, 1][2:] + z[2, 0] + z[2, 1][:2] + [w_quant(3, 0), w_quant(3, 1, ("w", 4, 0)), e_quant(1)]
+            + z[2, 1][2:] + v_units(0, 1) + v_units(1, 1)[:2] + [w_quant(4, 0), w_quant(4, 1), v_quant(1, 0, ("w", 5, 0)), v_quant(0, 1)]
+            + v_units(1, 1)[2:] + z[4, 0] + [w_quant(5, 1), w_quant(5, 0), v_quant(1, 1, ("h", 0, 1)), h_quant(0, 0)]
+            + closing + h_part(1, 0, 2, 4, True) + h_quants(1, 0) + [z_merge_unit(4, 1), h_quant(0, 1), z_merge_unit(5, 1)]
+            + ys[:1] + h_part(1, 1, 0, 4, True) + adds[:1] + [h_quant(1, 1)] + ys[1:2] + mix(ys[2:], adds[1:7]) + adds[7:]
         )
         scalar_lane = (
-            widen(0, (2, 3)) + w_s(0, 1, 0, 2) + widen(1, (0,)) + w_s(1, 0) + widen(1, (1, 2, 3))
-            + [column_unit] + z[0, 0] + w_s(2, 0) + e_units[:2] + w_s(2, 1, 0, 2) + z[0, 1] + w_s(2, 1, 2) + e_units[2:]
-            + w_s(3, 1, 0, 2) + v_scalar_units(1, 0)
-            + w_s(4, 1, 0, 2) + z[3, 0] + w_s(5, 1, 0, 2) + z[3, 1] + w_s(5, 1, 2) + h_parts(0, 0, 0, 4, False) + z_aside_units(4, 1)
-            + h_parts(0, 1, 0, 2, False) + h_parts(1, 0, 0, 2, False, True) + h_parts(0, 1, 2, 4, False)
+            widen(0, (3,)) + widen(1, (0, 1)) + w_s(0, 1, 0, 2) + w_s(1, 0) + widen(1, (2, 3))
+            + [column_unit] + z[0, 0] + w_s(2, 0) + e_units[:2] + w_s(2, 1, 0, 2) + z[0, 1] + w_s(2, 1, 2)
+            + w_s(3, 1, 0, 2) + e_units[2:] + v_scalar_units(1, 0)
+            + w_s(4, 1, 0, 2) + z[3, 0] + w_s(5, 1, 0, 2) + z[3, 1] + w_s(5, 1, 2) + h_part(0, 0, 0, 4, False) + z_aside_units(4, 1)
+            + h_part(0, 1, 0, 1, False, inherits=True) + h_part(1, 0, 0, 2, False, range(2)) + z_aside_units(5, 1)
             + scales[:3] + outs[:2] + scales[3:4] + outs[2:4] + scales[4:7] + outs[4:6] + scales[7:] + outs[6:]
         )
 

@@ -19,9 +19,11 @@ MAX = mybir.AluOpType.max
 IDENTITY = mybir.ActivationFunctionType.Identity
 
 RUN = 8
-GP_TICKS = 6
-WARM = 0
-MANUAL = True
+BANKS = 8
+WHOLE = slice(0, 512)
+ROW_A, ROW_R, ROW_D, ROWS = 6, 8, 9, 10
+SHARED_LONG, SHARED_SHORT, SHARED_H = 2, 3, 1
+STORED_BETWEEN = (1, 2)
 
 
 def tile_maxout_generated_head_f5_kernel(tc, x_bytes, x_scale, w, b, e, g, a, r, d, out):
@@ -29,20 +31,23 @@ def tile_maxout_generated_head_f5_kernel(tc, x_bytes, x_scale, w, b, e, g, a, r,
     with ExitStack() as ctx:
         keep = ctx.enter_context(tc.tile_pool(name="keep", bufs=1))
         psum = ctx.enter_context(tc.psum_pool(name="psum", bufs=1))
-        if MANUAL:
-            ctx.enter_context(tc.manual_schedule())
+        ctx.enter_context(tc.manual_schedule())
 
         def kept(name, shape, dtype):
             return keep.tile(shape, dtype, name=name, align_bytes=64)
 
-        banks = [psum.tile([P, 512], F32, name=f"bank{n}") for n in range(8)]
-        grouped = [kept(f"grouped{n}", [P, 2048], BF16) for n in range(6)]
+        def operand(name):
+            return kept(name + "_codes", [P, 512], U32), kept(name + "_scales", [P, 512], U8)
+
+        banks = [psum.tile([P, 512], F32, name=f"bank{n}") for n in range(BANKS)]
+        staged = [kept(f"staged{n}", [P, 2048], BF16) for n in range(6)]
         wide = [kept(f"x_wide{n}", [P, K], BF16) for n in range(4)]
         results = [kept(f"result{n}", [P, 512], F32) for n in range(10)]
         by_class = [kept(f"by_class{n}", [P, 512], F32) for n in range(4)]
         raws = [kept(f"raw{n}", [P, 4, 512], BF16) for n in range(8)]
         planes = [kept(f"plane{n}", [P, 4, 512], BF16) for n in range(7)]
         held = {}
+        fills = []
 
         def take(free, key):
             held[key] = free.pop(0)
@@ -52,458 +57,413 @@ def tile_maxout_generated_head_f5_kernel(tc, x_bytes, x_scale, w, b, e, g, a, r,
             free.append(held[key])
             return held.pop(key)
 
-        def operand(name):
-            return kept(name + "_codes", [P, 512], U32), kept(name + "_scales", [P, 512], U8)
+        def fill(key):
+            held[key] = banks[len(fills) % BANKS]
+            fills.append(key)
+            return held[key]
+
+        def next_bank_is_free():
+            return len(fills) < BANKS or fills[-BANKS] not in held
 
         x_raw = [[kept(f"x_raw{h}_{j}", [P, 2, K], U8) for j in range(2)] for h in range(2)]
         e_raw = [kept(f"e_raw{n}", [P, 4, D], BF16) for n in range(2)]
-        x_grouped = kept("x_grouped", [P, 2, 2048], BF16)
-        x_both = [(kept(f"x{h}_codes", [P, 1024], U32), kept(f"x{h}_scales", [P, 1024], U8)) for h in range(2)]
-        x_mx = [[(codes[:, 512 * q : 512 * (q + 1)], scales[:, 512 * q : 512 * (q + 1)]) for q in range(2)] for codes, scales in x_both]
-        w_mx = [[operand(f"w{c}_{q}") for q in range(2)] for c in range(6)]
-        e_mx = [operand(f"e{n}") for n in range(2)]
-        g_mx = [operand(f"g{q}") for q in range(2)]
-        v_mx = [[operand(f"v{q}_{n}") for n in range(2)] for q in range(2)]
-        h_mx = [[operand(f"h{q}_{h}") for h in range(2)] for q in range(2)]
+        x_staged = kept("x_staged", [P, 2, 2048], BF16)
+        mx = {}
+        for name, keys in (("x", (2, 2)), ("w", (6, 2)), ("e", (1, 2)), ("g", (1, 2)), ("v", (2, 2)), ("h", (2, 2))):
+            for first in range(keys[0]):
+                for second in range(keys[1]):
+                    mx[name, first, second] = operand(f"{name}{first}_{second}")
         xs = kept("xs", [P, 2, 4], F32)
         r_all = kept("r_all", [P, 512], BF16)
         d_all = kept("d_all", [P, 512], BF16)
-        rows_raw = kept("rows_raw", [8, 512], BF16)
+        rows_raw = kept("rows_raw", [ROW_R, 512], BF16)
         rows = kept("rows", [P, 512], BF16)
-        columns = kept("columns", [P, 10, 4], F32)
+        columns = kept("columns", [P, ROWS, 4], F32)
         ident = kept("ident", [P, P], F32)
         ident_bf = kept("ident_bf", [P, P], BF16)
 
         x_rows = x_bytes.rearrange("(p i) k -> p i k", i=8)
         out_rows = out.rearrange("(p i) c -> p i c", i=8)
 
-        def load_x(h, j):
-            nc.sync.dma_start(out=x_raw[h][j][:], in_=x_rows[:, 4 * h + 2 * j : 4 * h + 2 * j + 2, :])
-
-        def load_w(c, q):
-            col = (c % 3) * F + (c // 3) * 512
-            rows_q = w[q * 512 : (q + 1) * 512, col : col + 512]
-            nc.sync.dma_start(out=take(raws, ("raw", "w", c, q))[:], in_=rows_q.rearrange("(p s) n -> p s n", s=4))
-
-        def load_g(q):
-            nc.sync.dma_start(out=take(raws, ("raw", "g", q))[:], in_=g[:, 512 * q : 512 * (q + 1)].rearrange("(p s) f -> p s f", s=4))
-
-        def load_e(n):
-            nc.sync.dma_start(out=e_raw[n][:], in_=e[512 * n : 512 * (n + 1), :].rearrange("(i p) k -> p i k", p=P))
+        def block(n, width=P):
+            return slice(n * width, (n + 1) * width)
 
         def load(tile, source):
             nc.sync.dma_start(out=tile, in_=source)
 
-        def quantize(mx, grouped, cols=slice(0, 512)):
-            codes, scales = mx
-            nc.vector.quantize_mx(
-                out=codes[:, cols].bitcast(FP8X4), scales=scales[:, cols], in_=grouped[:, 4 * cols.start : 4 * cols.stop]
-            )
+        def load_raw(key, source):
+            load(take(raws, ("raw",) + key)[:], source.rearrange("(p s) n -> p s n", s=4))
+
+        def copy(engine, out, in_):
+            if engine is nc.vector:
+                nc.vector.tensor_copy(out=out, in_=in_)
+            elif engine is nc.scalar:
+                nc.scalar.copy(out=out, in_=in_)
+            else:
+                nc.gpsimd.tensor_scalar(out=out, in0=in_, scalar1=1.0, scalar2=0.0, op0=MULT, op1=ADD)
+
+        def quantize(key, source, cols=WHOLE):
+            codes, scales = mx[key]
+            nc.vector.quantize_mx(out=codes[:, cols].bitcast(FP8X4), scales=scales[:, cols], in_=source[:, 4 * cols.start : 4 * cols.stop])
 
         def product(bank, lhs, lhs_cols, rhs, rhs_cols, start, stop):
             nc.tensor.matmul_mx(
                 out=bank,
-                lhsT=lhs[0][:, lhs_cols].bitcast(FP8X4),
-                lhsT_scale=lhs[1][:, lhs_cols],
-                rhs=rhs[0][:, rhs_cols].bitcast(FP8X4),
-                rhs_scale=rhs[1][:, rhs_cols],
+                lhsT=mx[lhs][0][:, lhs_cols].bitcast(FP8X4),
+                lhsT_scale=mx[lhs][1][:, lhs_cols],
+                rhs=mx[rhs][0][:, rhs_cols].bitcast(FP8X4),
+                rhs_scale=mx[rhs][1][:, rhs_cols],
                 start=start,
                 stop=stop,
             )
 
-        def block(n):
-            return slice(n * P, (n + 1) * P)
-
-        def copy(on_vector, out, in_):
-            if on_vector:
-                nc.vector.tensor_copy(out=out, in_=in_)
+        def quantize_staged(key, heir):
+            if heir:
+                held[heir] = held.pop(key)
+                quantize(key, held[heir])
             else:
-                nc.scalar.copy(out=out, in_=in_)
+                quantize(key, give(staged, key))
 
-        whole = slice(0, 512)
+        def quantize_part(key, part):
+            quantize(key, give(staged, key) if part else held[key], block(part, 256))
 
-        def x_widen(h, i, on_vector):
-            copy(on_vector, take(wide, ("wide", h, i))[:], x_raw[h][i // 2][:, i % 2, :].bitcast(FP8))
+        def permute_rows():
+            nc.vector.tensor_copy(
+                out=rows[0:ROW_R, :].rearrange("p (t B i) -> p t B i", t=4, i=RUN),
+                in_=rows_raw[:].rearrange("p (B t i) -> p t B i", t=4, i=RUN),
+            )
+
+        def columns_product():
+            bank = fill("columns")
+            for t in range(4):
+                nc.tensor.matmul(bank[:, 16 * t : 16 * t + ROWS], lhsT=rows[:, block(t)], rhs=ident_bf[:, 0:ROWS], start=True, stop=True)
+
+        def columns_read():
+            nc.scalar.copy(out=columns[:], in_=held.pop("columns")[:, 0:64].rearrange("p (t j) -> p j t", t=4)[:, 0:ROWS, :])
+
+        def x_widen(h, i, engine):
+            copy(engine, wide[i][:], x_raw[h][i // 2][:, i % 2, :].bitcast(FP8))
 
         def x_turn(h, i):
-            bank = take(banks, ("xbank", h, i))
-            words = give(wide, ("wide", h, i))[:].bitcast(F32)
+            bank = fill(("x bank", h, i))
+            words = wide[i][:].bitcast(F32)
             for q in range(2):
                 for u in range(2):
                     nc.tensor.transpose(bank[:, block(2 * u + q)], words[:, 256 * q + u : 256 * (q + 1) : 2], ident[:])
 
-        def x_out(h, i):
+        def x_read(h, i):
             nc.vector.tensor_tensor(
-                out=x_grouped[:, :, 512 * i : 512 * (i + 1)].rearrange("p q (r u e) -> p q r u e", u=2, e=2),
-                in0=give(banks, ("xbank", h, i))[:].bitcast(BF16).rearrange("p (u q r e) -> p q r u e", u=2, q=2, e=2),
+                out=x_staged[:, :, block(i, 512)].rearrange("p q (r u e) -> p q r u e", u=2, e=2),
+                in0=held.pop(("x bank", h, i))[:].bitcast(BF16).rearrange("p (u q r e) -> p q r u e", u=2, q=2, e=2),
                 in1=xs[:].rearrange("p q (o u e) -> p q o u e", o=1, u=2).to_broadcast([P, 2, P, 2, 2]),
                 op=MULT,
             )
 
-        def x_quantize(h, passes):
-            quantize(x_both[h], x_grouped[:].rearrange("p q n -> p (q n)"), slice(512 * passes[0], 512 * (passes[-1] + 1)))
-
-        def finish(mx, key, heir):
-            if heir is None:
-                quantize(mx, give(grouped, key))
-            else:
-                held[heir] = held.pop(key)
-                quantize(mx, held[heir])
-
-        def interleave(key, first, count, on_vector):
-            if first == 0:
-                take(grouped, key)
-            raw = give(raws, ("raw",) + key) if first + count == 4 else held[("raw",) + key]
-            copy(
-                on_vector,
-                held[key][:].rearrange("p (t B i s) -> p t B s i", t=4, i=RUN, s=4)[:, first : first + count],
-                raw[:].rearrange("p s (B t i) -> p t B s i", t=4, i=RUN)[:, first : first + count],
-            )
-
-        def interleave_gpsimd(key, first):
-            if key not in held:
-                take(grouped, key)
-            raw = give(raws, ("raw",) + key)
-            nc.gpsimd.tensor_scalar(
-                out=held[key][:].rearrange("p (t B i s) -> p B t i s", t=4, i=RUN, s=4)[:, :, first:],
-                in0=raw[:].rearrange("p s (B t i) -> p B t i s", t=4, i=RUN)[:, :, first:],
-                scalar1=1.0,
-                scalar2=0.0,
-                op0=MULT,
-                op1=ADD,
-            )
-
-        def z_parts(s, split):
-            if split:
-                return [(2 * (s % 2) + n, slice(256 * (s // 2), 256 * (s // 2 + 1)), slice(256 * n, 256 * (n + 1))) for n in range(2)]
-            return [(s, whole, whole)]
-
-        def z_product(c, h, s, split):
-            bank = take(banks, ("z", c, h, s))
-            for t, samples, place in z_parts(s, split):
-                for q in range(2):
-                    product(bank[:, place], w_mx[c][q], block(t), x_mx[h][q], samples, q == 0, q == 1)
-
-        def z_out(c, h, s, split):
-            group, piece = divmod(c, 3)
-            bank = give(banks, ("z", c, h, s))
-            if s == 0:
-                take(planes, ("plane", c, h))
-            for t, samples, place in z_parts(s, split):
-                bias = columns[:, 2 * piece + group, t : t + 1]
-                now = held["plane", c, h][:, t, samples]
-                if piece == 0:
-                    nc.scalar.activation(out=now, in_=bank[:, place], func=IDENTITY, bias=bias)
-                else:
-                    nc.vector.scalar_tensor_tensor(out=now, in0=bank[:, place], scalar=bias, in1=held["plane", c - 1, h][:, t, samples], op0=ADD, op1=MAX)
-            if piece and s == 3:
-                give(planes, ("plane", c - 1, h))
-
-        def z_aside(c, h, t):
-            group, piece = divmod(c, 3)
-            if t == 0:
-                take(planes, ("aside", c, h))
-            bias = columns[:, 2 * piece + group, t : t + 1]
-            nc.scalar.activation(out=held["aside", c, h][:, t, :], in_=give(banks, ("z", c, h, t))[:], func=IDENTITY, bias=bias)
-
-        def z_merge(c, h):
-            merged = take(planes, ("plane", c, h))
-            nc.vector.tensor_tensor(out=merged[:], in0=give(planes, ("aside", c, h))[:], in1=give(planes, ("plane", c - 1, h))[:], op=MAX)
-
-        def plane_interleave(key, source, first, count, on_vector):
-            if key not in held:
-                take(grouped, key)
-            copy(
-                on_vector,
-                held[key][:, 512 * first : 512 * (first + count)].rearrange("p (c i t) -> p c t i", i=4, t=4),
-                held[source][:, :, 128 * first : 128 * (first + count)].rearrange("p t (c i) -> p c t i", i=4),
-            )
-            if first + count == 4:
-                give(planes, source)
-
-        def plane_interleave_gpsimd(key, source, first):
-            nc.gpsimd.tensor_scalar(
-                out=held[key][:, 512 * first :].rearrange("p (c t) -> p c t", t=4),
-                in0=give(planes, source)[:, :, 128 * first :].rearrange("p t c -> p c t"),
-                scalar1=1.0,
-                scalar2=0.0,
-                op0=MULT,
-                op1=ADD,
-            )
-
-        def h_quantize(group, h, part, last):
-            quantize(h_mx[group][h], held["h", group, h], slice(256 * part, 256 * (part + 1)))
-            if last:
-                give(grouped, ("h", group, h))
-
         def e_turn(n, j):
-            bank = take(banks, ("ebank", n, j))
+            bank = fill(("e bank", n, j))
             for i in range(2):
                 words = e_raw[n][:, 2 * j + i, :].bitcast(F32)
                 for u in range(2):
                     nc.tensor.transpose(bank[:, block(2 * i + u)], words[:, u:256:2], ident[:])
 
-        def e_out(n, j):
+        def e_read(n, j):
             if j == 0:
-                take(grouped, ("e", n))
+                take(staged, ("e", 0, n))
             nc.scalar.copy(
-                out=held["e", n][:].bitcast(F32)[:, 512 * j : 512 * (j + 1)].rearrange("p (i r u) -> p i r u", i=2, u=2),
-                in_=give(banks, ("ebank", n, j))[:].rearrange("p (i u r) -> p i r u", i=2, u=2),
+                out=held["e", 0, n][:].bitcast(F32)[:, block(j, 512)].rearrange("p (i r u) -> p i r u", i=2, u=2),
+                in_=held.pop(("e bank", n, j))[:].rearrange("p (i u r) -> p i r u", i=2, u=2),
             )
 
-        def v_tile(q, n, j):
-            bank = take(banks, ("vbank", q, n, j))
-            for t in range(4):
-                product(bank[:, block(t)], g_mx[q], block(t), e_mx[n], block(j), True, True)
+        def stage_raw(key, first, last, engine):
+            if key not in held:
+                take(staged, key)
+            raw = give(raws, ("raw",) + key) if last == 4 else held[("raw",) + key]
+            walk = "p t B s i" if engine is nc.scalar else "p t B i s"
+            source = raw[:].rearrange(f"p s (B t i) -> {walk}", t=4, i=RUN)[:, first:last]
+            target = held[key][:].rearrange(f"p (t B i s) -> {walk}", t=4, i=RUN, s=4)[:, first:last]
+            if engine is nc.gpsimd:
+                source, target = [side.rearrange("p t B i s -> p B t i s") for side in (source, target)]
+            copy(engine, target, source)
 
-        def v_out(q, n, j):
+        def stage_plane(key, source, first, last, engine):
+            if key not in held:
+                take(staged, key)
+            plane = give(planes, source) if last == 4 else held[source]
+            run = 1 if engine is nc.gpsimd else 4
+            copy(
+                engine,
+                held[key][:, 512 * first : 512 * last].rearrange("p (c i t) -> p c t i", i=run, t=4),
+                plane[:, :, P * first : P * last].rearrange("p t (c i) -> p c t i", i=run),
+            )
+
+        def z_parts(s, split):
+            if split:
+                return [(2 * (s % 2) + n, block(s // 2, 256), block(n, 256)) for n in range(2)]
+            return [(s, WHOLE, WHOLE)]
+
+        def z_product(c, h, s, split):
+            bank = fill(("z bank", c, h, s))
+            for t, samples, place in z_parts(s, split):
+                for q in range(2):
+                    product(bank[:, place], ("w", c, q), block(t), ("x", h, q), samples, q == 0, q == 1)
+
+        def z_bias(c, t):
+            return columns[:, 2 * (c % J) + c // J, t : t + 1]
+
+        def z_alone(c, h, t, name):
+            if t == 0:
+                take(planes, (name, c, h))
+            nc.scalar.activation(out=held[name, c, h][:, t, :], in_=held.pop(("z bank", c, h, t))[:], func=IDENTITY, bias=z_bias(c, t))
+
+        def z_max(c, h, s, split):
+            bank = held.pop(("z bank", c, h, s))
+            if s == 0:
+                take(planes, ("max", c, h))
+            for t, samples, place in z_parts(s, split):
+                nc.vector.scalar_tensor_tensor(
+                    out=held["max", c, h][:, t, samples], in0=bank[:, place], scalar=z_bias(c, t), in1=held["max", c - 1, h][:, t, samples], op0=ADD, op1=MAX
+                )
+            if s == 3:
+                give(planes, ("max", c - 1, h))
+
+        def z_merge(c, h):
+            merged = take(planes, ("max", c, h))
+            nc.vector.tensor_tensor(out=merged[:], in0=give(planes, ("aside", c, h))[:], in1=give(planes, ("max", c - 1, h))[:], op=MAX)
+
+        def v_four_slots(q, n, j):
+            bank = fill(("v bank", q, n, j))
+            for t in range(4):
+                product(bank[:, block(t)], ("g", 0, q), block(t), ("e", 0, n), block(j), True, True)
+
+        def v_read_staged(q, n, j):
             if j == 0:
-                take(grouped, ("v", q, n))
+                take(staged, ("v", q, n))
             nc.vector.tensor_tensor(
-                out=held["v", q, n][:, 512 * j : 512 * (j + 1)].rearrange("p (c t) -> p c t", t=4),
-                in0=give(banks, ("vbank", q, n, j))[:].rearrange("p (t c) -> p c t", t=4),
-                in1=columns[:, 6 + q : 7 + q, :].to_broadcast([P, P, 4]),
+                out=held["v", q, n][:, block(j, 512)].rearrange("p (c t) -> p c t", t=4),
+                in0=held.pop(("v bank", q, n, j))[:].rearrange("p (t c) -> p c t", t=4),
+                in1=columns[:, ROW_A + q : ROW_A + q + 1, :].to_broadcast([P, P, 4]),
                 op=ADD,
             )
 
-        def v_slot(q, n, t):
-            product(take(banks, ("vbank", q, n, t))[:], g_mx[q], block(t), e_mx[n], whole, True, True)
+        def v_parts(s, paired):
+            if paired:
+                return [(2 * s + k, block(1, 256), block(k, 256)) for k in range(2)]
+            return [(s, WHOLE, WHOLE)]
 
-        def v_slot_out(q, n, t):
-            if t == 0:
-                take(planes, ("vplane", q, n))
-            nc.scalar.activation(out=held["vplane", q, n][:, t, :], in_=give(banks, ("vbank", q, n, t))[:], func=IDENTITY, bias=columns[:, 6 + q, t : t + 1])
+        def v_by_slot(q, n, s, paired):
+            bank = fill(("v slot bank", q, n, s))
+            for t, classes, place in v_parts(s, paired):
+                product(bank[:, place], ("g", 0, q), block(t), ("e", 0, n), classes, True, True)
 
-        def y_product(i):
-            bank = take(banks, ("y", i))
+        def v_read_plane(q, n, s, paired):
+            if s == 0:
+                take(planes, ("v plane", q, n))
+            bank = held.pop(("v slot bank", q, n, s))
+            for t, classes, place in v_parts(s, paired):
+                nc.scalar.activation(out=held["v plane", q, n][:, t, classes], in_=bank[:, place], func=IDENTITY, bias=columns[:, ROW_A + q, t : t + 1])
+
+        def direct_product(i):
+            bank = fill(("direct bank", i))
             for q in range(2):
-                product(bank[:], h_mx[q][i // 4], block(i % 4), v_mx[q][1], whole, q == 0, q == 1)
+                product(bank[:], ("h", q, i // 4), block(i % 4), ("v", q, 1), WHOLE, q == 0, q == 1)
 
-        def y_scale(i):
-            nc.vector.tensor_tensor(out=take(results, ("y", "out", i))[:], in0=give(banks, ("y", i))[:], in1=r_all[:], op=MULT)
+        def direct_scale(i):
+            nc.vector.tensor_tensor(out=take(results, ("direct", i))[:], in0=held.pop(("direct bank", i))[:], in1=r_all[:], op=MULT)
 
-        def y_add(i):
-            t = held["y", "out", i]
-            nc.vector.tensor_tensor(out=t[:], in0=t[:], in1=d_all[:], op=ADD)
+        def direct_shift(i):
+            nc.vector.tensor_tensor(out=held["direct", i][:], in0=held["direct", i][:], in1=d_all[:], op=ADD)
 
-        def y_store(i):
-            nc.sync.dma_start(out=out_rows[:, i, 512:1024], in_=give(results, ("y", "out", i))[:])
+        def direct_store(i):
+            nc.sync.dma_start(out=out_rows[:, i, 512:C], in_=give(results, ("direct", i))[:])
 
-        def yt_product(h, n):
-            bank = take(banks, ("yt", h, n))
+        def class_product(h, n):
+            bank = fill(("class bank", h, n))
             for q in range(2):
-                product(bank[:], v_mx[q][0], block(n), h_mx[q][h], whole, q == 0, q == 1)
+                product(bank[:], ("v", q, 0), block(n), ("h", q, h), WHOLE, q == 0, q == 1)
 
-        def yt_scale(h, n):
+        def class_read(h, n):
             nc.scalar.activation(
-                out=take(by_class, ("cls", h, n))[:], in_=give(banks, ("yt", h, n))[:], func=IDENTITY, scale=columns[:, 8, n : n + 1], bias=columns[:, 9, n : n + 1]
+                out=take(by_class, ("by class", h, n))[:],
+                in_=held.pop(("class bank", h, n))[:],
+                func=IDENTITY,
+                scale=columns[:, ROW_R, n : n + 1],
+                bias=columns[:, ROW_D, n : n + 1],
             )
 
-        def yt_turn(h, m, j):
-            bank = take(banks, ("yr", h, m, j))
+        def turn_back(h, m, j):
+            bank = fill(("turned bank", h, m, j))
             for n in range(2):
-                t = give(by_class, ("cls", h, 2 * m + n)) if j else held["cls", h, 2 * m + n]
+                source = give(by_class, ("by class", h, 2 * m + n)) if j else held["by class", h, 2 * m + n]
                 for i in range(2):
-                    nc.tensor.transpose(bank[:, block(2 * i + n)], t[:, block(2 * j + i)], ident[:])
+                    nc.tensor.transpose(bank[:, block(2 * i + n)], source[:, block(2 * j + i)], ident[:])
 
-        def yt_out(h, m, j):
-            nc.scalar.copy(out=take(results, ("yt", "out", h, m, j))[:], in_=give(banks, ("yr", h, m, j))[:])
+        def turned_read(h, m, j):
+            nc.scalar.copy(out=take(results, ("turned", h, m, j))[:], in_=held.pop(("turned bank", h, m, j))[:])
 
-        def yt_store(h, m, j):
+        def turned_store(h, m, j):
             nc.sync.dma_start(
-                out=out_rows[:, 4 * h + 2 * j : 4 * h + 2 * j + 2, 256 * m : 256 * (m + 1)],
-                in_=give(results, ("yt", "out", h, m, j))[:].rearrange("p (i c) -> p i c", i=2),
+                out=out_rows[:, 4 * h + 2 * j : 4 * h + 2 * j + 2, block(m, 256)],
+                in_=give(results, ("turned", h, m, j))[:].rearrange("p (i c) -> p i c", i=2),
             )
+
+        def step(*call, makes=(), needs=(), feed=None, feed_needs=()):
+            return call, list(makes), list(needs) + ([feed] if feed else []), feed, list(feed_needs)
+
+        def feeds(steps):
+            return [step(*feed, makes=[feed], needs=feed_needs) for call, makes, needs, feed, feed_needs in steps]
+
+        def quarters(key, first=0, last=4):
+            return [key + (n,) for n in range(first, last)]
+
+        def both(name, n):
+            return [(name, q, n) for q in range(2)]
+
+        def alternate(first, second):
+            places = [((n + 0.5) / len(steps), k, n) for k, steps in enumerate((first, second)) for n in range(len(steps))]
+            return [(first, second)[k][n] for place, k, n in sorted(places)]
+
+        def widen(h, tiles, engine):
+            return [step(x_widen, h, i, engine, makes=[("wide", h, i)], needs=[("x raw", h, i // 2)] + [(x_turn, 0, i)] * h) for i in tiles]
+
+        def quant(*key, heir=None):
+            return step(quantize_staged, key, heir, makes=[key, ("inherited", heir)], needs=quarters(key))
+
+        def quant_x(h, q):
+            return step(quantize, ("x", h, q), x_staged[:, q, :], makes=[("x", h, q)], needs=quarters(("x read", h)))
+
+        def stage(engine, *key, first=0, last=4, inherited=False):
+            needs = [("raw",) + key] + quarters(key, 0, first) + [("inherited", key)] * inherited
+            return step(stage_raw, key, first, last, engine, makes=quarters(key, first, last), needs=needs)
+
+        def stage_h(engine, q, h, first=0, last=4, banks_read=4, inherited=False):
+            key, c = ("h", q, h), J * q + J - 1
+            needs = quarters(("max", c, h), 0, banks_read) + quarters(key, 0, first) + [("inherited", key)] * inherited
+            return step(stage_plane, key, ("max", c, h), first, last, engine, makes=quarters(key, first, last), needs=needs)
+
+        def z_steps(call, c, h, last_arg, makes, needs, split=False):
+            operands = [("w", c, q) for q in range(2)] + [("x", h, q) for q in range(2)]
+            return [
+                step(call, c, h, s, last_arg, makes=[(makes, c, h, s)], needs=needs + ["columns"], feed=(z_product, c, h, s, split), feed_needs=operands)
+                for s in range(4)
+            ]
+
+        def merge(c, h):
+            return step(z_merge, c, h, makes=quarters(("max", c, h)), needs=quarters(("aside", c, h)) + quarters(("max", c - 1, h)))
+
+        def loads_w(c):
+            col = (c % J) * F + (c // J) * 512
+            return [
+                step(load_raw, ("w", c, q), w[block(q, 512), col : col + 512], makes=[("raw", "w", c, q)], needs=[("w", c - J, q, 3)] * (c >= J))
+                for q in range(2)
+            ]
+
+        def load_x(h, j):
+            return step(load, x_raw[h][j][:], x_rows[:, 4 * h + 2 * j : 4 * h + 2 * j + 2, :], makes=[("x raw", h, j)])
+
+        def load_g(q):
+            return step(load_raw, ("g", 0, q), g[:, block(q, 512)], makes=[("raw", "g", 0, q)])
+
+        def load_e(n):
+            return step(load, e_raw[n][:], e[block(n, 512), :].rearrange("(i p) k -> p i k", p=P), makes=[("e raw", n)])
+
+        x_reads = [[step(x_read, h, i, makes=[("x read", h, i)], feed=(x_turn, h, i), feed_needs=[("wide", h, i)]) for i in range(4)] for h in range(2)]
+        e_reads = [[step(e_read, n, j, makes=quarters(("e", 0, n), 2 * j, 2 * j + 2), feed=(e_turn, n, j), feed_needs=[("e raw", n)]) for j in range(2)] for n in range(2)]
+        column_read = [step(columns_read, makes=["columns"], feed=(columns_product,), feed_needs=["rows"])]
+        z = {}
+        for c in range(2 * J):
+            for h in range(2):
+                if c % J == 0:
+                    z[c, h] = z_steps(z_alone, c, h, "max", "max", [])
+                elif c > J and h == 1:
+                    z[c, h] = z_steps(z_alone, c, h, "aside", "aside", [])
+                else:
+                    split = c == 2 * J - 1
+                    z[c, h] = z_steps(z_max, c, h, split, "max", quarters(("max", c - 1, h)), split)
+        v_vector = {
+            (q, n): [step(v_read_staged, q, n, j, makes=[("v", q, n, j)], feed=(v_four_slots, q, n, j), feed_needs=[("g", 0, q), ("e", 0, n)]) for j in range(blocks)]
+            for q, n, blocks in ((0, 0, 2), (0, 1, 4), (1, 1, 4))
+        }
+        v_scalar = [[step(v_read_plane, q, 0, s, q == 0, feed=(v_by_slot, q, 0, s, q == 0), feed_needs=[("g", 0, q), ("e", 0, 0)]) for s in range(2 + 2 * q)] for q in range(2)]
+        stage_v = [
+            step(stage_plane, ("v", q, 0), ("v plane", q, 0), first, 4, nc.scalar, makes=quarters(("v", q, 0), first), needs=quarters(("v", q, 0), 0, first)[:1])
+            for q, first in ((0, 2), (1, 0))
+        ]
+        h_halves = [step(quantize_part, ("h", 1, 0), part, makes=[("h", 1, 0)] * part, needs=quarters(("h", 1, 0), 2 * part, 2 * part + 2)) for part in range(2)]
+        scaled = [step(direct_scale, i, needs=["r and d"], feed=(direct_product, i), feed_needs=both("h", i // 4) + both("v", 1)) for i in range(8)]
+        shifted = [step(direct_shift, i, makes=[("direct", i)]) for i in range(8)]
+        classes = [[step(class_read, h, n, makes=[("by class", h, n)], feed=(class_product, h, n), feed_needs=both("h", h) + both("v", 0)) for n in range(4)] for h in range(2)]
+        turned = {
+            (h, m): [
+                step(turned_read, h, m, j, makes=[("turned", h, m, j)], feed=(turn_back, h, m, j), feed_needs=quarters(("by class", h), 2 * m, 2 * m + 2))
+                for j in range(2)
+            ]
+            for h in range(2)
+            for m in range(2)
+        }
+
+        sync_lane = (
+            [load_x(0, 0), step(load, xs[:], x_scale.rearrange("o (q p t) -> p (o q) t", q=2, t=4)), load_x(0, 1)]
+            + loads_w(0)[:1] + [load_x(1, 0)] + loads_w(0)[1:] + loads_w(1) + [load_x(1, 1)]
+            + [step(load, rows_raw[0:ROW_A, :], b.rearrange("(c n) -> c n", n=512)), step(load, rows_raw[ROW_A:ROW_R, :], a.rearrange("(c n) -> c n", n=512))]
+            + [step(load, rows[row : row + 1, :], vector[0:512].rearrange("(o n) -> o n", o=1)) for row, vector in ((ROW_R, r), (ROW_D, d))]
+            + loads_w(2) + [load_g(0), load_e(0), load_e(1), load_g(1)] + loads_w(3) + loads_w(4) + loads_w(5)
+            + [step(load, r_all[:], r[512:C].partition_broadcast(P)), step(load, d_all[:], d[512:C].partition_broadcast(P), makes=["r and d"])]
+        )
+        for h in range(2):
+            direct_stores = [step(direct_store, i, needs=[("direct", i)]) for i in range(4 * h, 4 * h + 4)]
+            pairs = [[step(turned_store, h, m, j, needs=[("turned", h, m, j)]) for j in range(2)] for m in range(2)]
+            sync_lane += pairs[0] + direct_stores[: STORED_BETWEEN[h]] + pairs[1] + direct_stores[STORED_BETWEEN[h] :]
+
+        vector_lane = (
+            widen(0, (0, 1, 2), nc.vector) + x_reads[0]
+            + [quant_x(0, 0), quant("w", 0, 0), quant_x(0, 1), quant("w", 0, 1), step(permute_rows, makes=["rows"]), quant("w", 1, 0, heir=("w", 1, 1))]
+            + x_reads[1][:3] + [quant("w", 1, 1, heir=("g", 0, 0))]
+            + x_reads[1][3:] + z[1, 0] + [quant_x(1, 0), quant_x(1, 1), quant("g", 0, 0), quant("e", 0, 0, heir=("g", 0, 1)), quant("w", 2, 0)]
+            + v_vector[0, 0] + z[1, 1][:3] + [quant("w", 2, 1), quant("g", 0, 1, heir=("w", 3, 0)), quant("e", 0, 1)]
+            + z[1, 1][3:] + z[2, 0] + z[2, 1][:2] + [quant("w", 3, 0), quant("w", 3, 1, heir=("w", 4, 0)), quant("v", 0, 0)]
+            + z[2, 1][2:] + v_vector[0, 1] + v_vector[1, 1][:2] + [quant("w", 4, 0), quant("w", 4, 1), quant("v", 1, 0, heir=("w", 5, 0)), quant("v", 0, 1)]
+            + v_vector[1, 1][2:] + z[4, 0] + [quant("w", 5, 1), quant("w", 5, 0), quant("v", 1, 1), quant("h", 0, 0, heir=("h", 0, 1))]
+            + z[5, 0] + [stage_h(nc.vector, 1, 0, first=2)] + h_halves + [merge(4, 1), quant("h", 0, 1), merge(5, 1)]
+            + [scaled[0], stage_h(nc.vector, 1, 1), shifted[0], quant("h", 1, 1), scaled[1]] + alternate(scaled[2:], shifted[1:7]) + shifted[7:]
+        )
+        gpsimd_lane = [stage(nc.gpsimd, "w", 0, 0), stage(nc.gpsimd, "w", 0, 1, first=SHARED_LONG)]
+        gpsimd_lane += [stage(nc.gpsimd, *key, inherited=True) for key in (("w", 1, 1), ("g", 0, 0), ("g", 0, 1))]
+        for c, shared in ((3, SHARED_SHORT), (4, SHARED_LONG)):
+            gpsimd_lane += [stage(nc.gpsimd, "w", c, 0, inherited=True), stage(nc.gpsimd, "w", c, 1, first=shared)]
+        gpsimd_lane += [stage(nc.gpsimd, "w", 5, 0, inherited=True), stage_h(nc.gpsimd, 0, 1, first=SHARED_H)]
+        scalar_lane = (
+            widen(0, (3,), nc.scalar) + widen(1, (0, 1), nc.scalar) + [stage(nc.scalar, "w", 0, 1, last=SHARED_LONG), stage(nc.scalar, "w", 1, 0)] + widen(1, (2, 3), nc.scalar)
+            + column_read + z[0, 0][:2] + [stage(nc.scalar, "w", 2, 0, last=2)] + z[0, 0][2:] + [stage(nc.scalar, "w", 2, 0, first=2), stage(nc.scalar, "w", 2, 1, last=2)]
+            + e_reads[0] + e_reads[1] + z[0, 1] + [stage(nc.scalar, "w", 2, 1, first=2)] + v_scalar[0] + [stage(nc.scalar, "w", 3, 1, last=SHARED_SHORT), stage_v[0]]
+            + v_scalar[1] + [stage_v[1], stage(nc.scalar, "w", 4, 1, last=SHARED_LONG)]
+            + z[3, 0] + [stage(nc.scalar, "w", 5, 1, last=2)] + z[3, 1] + [stage(nc.scalar, "w", 5, 1, first=2), stage_h(nc.scalar, 0, 0)]
+            + z[4, 1] + [stage_h(nc.scalar, 0, 1, last=SHARED_H, inherited=True), stage_h(nc.scalar, 1, 0, last=2, banks_read=2)] + z[5, 1]
+        )
+        for h in range(2):
+            scalar_lane += classes[h][:3] + turned[h, 0] + classes[h][3:] + turned[h, 1]
+        tensor_lane = feeds(
+            x_reads[0] + x_reads[1][:2] + z[0, 0][:1] + column_read + z[0, 0][1:2] + x_reads[1][2:3] + z[0, 0][2:3] + x_reads[1][3:] + z[0, 0][3:]
+            + z[1, 0] + e_reads[0] + e_reads[1] + z[0, 1][:2] + v_vector[0, 0] + z[0, 1][2:] + z[1, 1][:3] + v_scalar[0] + z[1, 1][3:]
+            + alternate(z[2, 0], v_scalar[1]) + z[2, 1] + alternate(z[3, 0], v_vector[0, 1]) + v_vector[1, 1][:2] + z[3, 1] + v_vector[1, 1][2:] + z[4, 0] + z[4, 1]
+            + z[5, 0] + z[5, 1]
+            + classes[0][:2] + scaled[:1] + classes[0][2:3] + turned[0, 0] + classes[0][3:] + scaled[1:3] + turned[0, 1] + scaled[3:4]
+            + classes[1][:2] + scaled[4:5] + classes[1][2:3] + turned[1, 0] + scaled[5:6] + classes[1][3:] + scaled[6:] + turned[1, 1]
+        )
 
         make_identity(nc, ident[:])
         nc.vector.memset(rows[:], 0.0)
         nc.scalar.activation(out=ident_bf[:], in_=ident[:], func=IDENTITY)
 
-        def run(stage):
-            stage[0](*stage[1:])
-
-        def permute_rows():
-            nc.vector.tensor_copy(
-                out=rows[0:8, :].rearrange("p (t B i) -> p t B i", t=4, i=RUN),
-                in_=rows_raw[:].rearrange("p (B t i) -> p t B i", t=4, i=RUN),
-            )
-
-        def columns_product():
-            bank = take(banks, "columns")
-            for n in range(WARM):
-                nc.tensor.matmul(bank[:], lhsT=ident_bf[:], rhs=rows[:], start=True, stop=True)
-            for t in range(4):
-                nc.tensor.matmul(bank[:, 16 * t : 16 * t + 10], lhsT=rows[:, block(t)], rhs=ident_bf[:, 0:10], start=True, stop=True)
-
-        def columns_out():
-            nc.scalar.copy(out=columns[:], in_=give(banks, "columns")[:, 0:64].rearrange("p (t j) -> p j t", t=4)[:, 0:10, :])
-
-        def unit(*stage, makes=(), needs=(), feed=None, feed_needs=()):
-            return (stage, makes, list(needs) + ([feed] if feed else []), feed, feed_needs)
-
-        def z_units(c, h, split=False):
-            units = []
-            for s in range(4):
-                slots = [t for t, samples, place in z_parts(s, split)]
-                needs = [("z", c - 1, h, t) for t in slots] if c % 3 else []
-                makes = [("z", c, h, s)]
-                feed_needs = [("w", c, q) for q in range(2)] + [("x", h, q) for q in range(2)]
-                units.append(unit(z_out, c, h, s, split, makes=makes, needs=needs + ["columns"], feed=(z_product, c, h, s, split), feed_needs=feed_needs))
-            return units
-
-        def z_aside_units(c, h):
-            feed_needs = [("w", c, q) for q in range(2)] + [("x", h, q) for q in range(2)]
-            return [unit(z_aside, c, h, t, makes=[("aside", c, h, t)], feed=(z_product, c, h, t, False), feed_needs=feed_needs) for t in range(4)]
-
-        def z_merge_unit(c, h):
-            return unit(z_merge, c, h, makes=[("z", c, h, t) for t in range(4)], needs=[("aside", c, h, t) for t in range(4)] + [("z", c - 1, h, t) for t in range(4)])
-
-        def lasting(first, turns):
-            return [first[:1] + ((),) + first[2:]] + [pause()] * (turns - 2) + [pause(first[1])] if turns > 1 else [first]
-
-        def part(key, first, last):
-            needs = [("raw",) + key] + [key + (m,) for m in range(first)]
-            return lasting(unit(interleave, key, first, last - first, False, makes=[key + (m,) for m in range(first, last)], needs=needs), last - first)
-
-        def quant(mx, key, heir=None):
-            return unit(finish, mx, key, heir, makes=[key, ("heir", heir)], needs=[key + (n,) for n in range(4)])
-
-        def on_gpsimd(key, inherits=True, first=0):
-            needs = [("raw",) + key] + ([("heir", key)] if inherits else []) + [key + (n,) for n in range(first)]
-            return [unit(interleave_gpsimd, key, first, needs=needs)] + [pause()] * (GP_TICKS - 2 - first) + [pause([key + (n,) for n in range(first, 4)])]
-
-        def w_quant(c, q, heir=None):
-            return quant(w_mx[c][q], ("w", c, q), heir)
-
-        def x_outs(h, tiles):
-            return [u for i in tiles for u in lasting(unit(x_out, h, i, makes=[("x", h, "tile", i)], feed=(x_turn, h, i), feed_needs=[("wide", h, i)]), 2)]
-
-        def x_quant(h, passes):
-            return unit(x_quantize, h, passes, makes=[("x", h, q) for q in passes], needs=[("x", h, "tile", i) for i in range(4)])
-
-        def widen(h, tiles, on_vector=False):
-            return [u for i in tiles for u in lasting(unit(x_widen, h, i, on_vector, makes=[("wide", h, i)], needs=[("xraw", h, i // 2)]), 1 if on_vector else 2)]
-
-        def v_units(q, n):
-            return [unit(v_out, q, n, j, makes=[("v", q, n, j)], feed=(v_tile, q, n, j), feed_needs=[("g", q), ("e", n)]) for j in range(4)]
-
-        def v_scalar_units(q, n):
-            reads = [unit(v_slot_out, q, n, t, feed=(v_slot, q, n, t), feed_needs=[("g", q), ("e", n)]) for t in range(4)]
-            return reads + lasting(unit(plane_interleave, ("v", q, n), ("vplane", q, n), 0, 4, False, makes=[("v", q, n, j) for j in range(4)]), 4)
-
-        def v_quant(q, n, heir=None):
-            return quant(v_mx[q][n], ("v", q, n), heir)
-
-        def h_part(group, h, first, last, on_vector, slots=range(4), inherits=False):
-            key = ("h", group, h)
-            needs = [("z", 3 * group + 2, h, s) for s in slots] + [key + (m,) for m in range(first)] + ([("heir", key)] if inherits else [])
-            work = unit(plane_interleave, key, ("plane", 3 * group + 2, h), first, last - first, on_vector, makes=[key + (m,) for m in range(first, last)], needs=needs)
-            return lasting(work, (last - first) // 2 if on_vector else last - first)
-
-        def h_quants(group, h):
-            return [unit(h_quantize, group, h, part, part == 1, makes=[("h", group, h)] if part else [], needs=[("h", group, h, 2 * part + n) for n in range(2)]) for part in range(2)]
-
-        def h_quant(group, h, heir=None):
-            return quant(h_mx[group][h], ("h", group, h), heir)
-
-        def w_s(c, q, first=0, last=4):
-            return part(("w", c, q), first, last)
-
-        def mix(first, second):
-            marked = [((n + 0.5) / len(first), 0, n) for n in range(len(first))] + [((n + 0.5) / len(second), 1, n) for n in range(len(second))]
-            return [(first, second)[k][n] for at, k, n in sorted(marked)]
-
-        def y_needs(h, n):
-            return [("h", q, h) for q in range(2)] + [("v", q, n) for q in range(2)]
-
-        def feeds(units):
-            return [unit(*u[3], makes=[u[3]], needs=u[4]) for u in units if u[3]]
-
-        def pause(makes=()):
-            return unit(makes=makes)
-
-        e_units = [unit(e_out, n, j, makes=[("e", n, 2 * j), ("e", n, 2 * j + 1)], feed=(e_turn, n, j), feed_needs=[("eraw", n)]) for n in range(2) for j in range(2)]
-
-        def e_quant(n, heir=None):
-            return quant(e_mx[n], ("e", n), heir)
-
-        def g_quant(q, heir=None):
-            return quant(g_mx[q], ("g", q), heir)
-
-        ys = [unit(y_scale, i, needs=["r"], feed=(y_product, i), feed_needs=y_needs(i // 4, 1)) for i in range(8)]
-        adds = [unit(y_add, i, makes=[("y", "out", i)]) for i in range(8)]
-        scales = [unit(yt_scale, h, n, makes=[("yt", h, n)], feed=(yt_product, h, n), feed_needs=y_needs(h, 0)) for h in range(2) for n in range(4)]
-        outs = [
-            unit(yt_out, h, m, j, makes=[("yt", "out", h, m, j)], feed=(yt_turn, h, m, j), feed_needs=[("yt", h, 2 * m), ("yt", h, 2 * m + 1)])
-            for h in range(2)
-            for m in range(2)
-            for j in range(2)
-        ]
-
-        def w_loads(c):
-            return [unit(load_w, c, q, makes=[("raw", "w", c, q)], needs=[("w", c - 3, q, 3)] if c > 2 else []) for q in range(2)]
-
-        def x_load(h, j):
-            return unit(load_x, h, j, makes=[("xraw", h, j)])
-
-        sync_lane = (
-            [x_load(0, 0), unit(load, xs[:], x_scale.rearrange("o (q p t) -> p (o q) t", q=2, t=4)), x_load(0, 1)] + w_loads(0)[:1] + [x_load(1, 0)] + w_loads(0)[1:] + w_loads(1) + [x_load(1, 1)]
-            + [unit(load, rows_raw[0:6, :], b.rearrange("(c n) -> c n", n=512)), unit(load, rows_raw[6:8, :], a.rearrange("(c n) -> c n", n=512))]
-            + [unit(load, rows[8:9, :], r[0:512].rearrange("(o n) -> o n", o=1)), unit(load, rows[9:10, :], d[0:512].rearrange("(o n) -> o n", o=1))]
-            + w_loads(2)
-            + [unit(load_g, 0, makes=[("raw", "g", 0)]), unit(load_e, 0, makes=[("eraw", 0)]), unit(load_e, 1, makes=[("eraw", 1)]), unit(load_g, 1, makes=[("raw", "g", 1)])]
-            + w_loads(3) + w_loads(4) + w_loads(5)
-            + [unit(load, r_all[:], r[512:1024].partition_broadcast(P)), unit(load, d_all[:], d[512:1024].partition_broadcast(P), makes=["r"])]
-        )
-        for pair, direct in enumerate(((), (0,), (1, 2, 3), (4, 5), (6, 7))):
-            sync_lane += [unit(y_store, n, needs=[("y", "out", n)]) for n in direct]
-            sync_lane += [unit(yt_store, pair // 2, pair % 2, j, needs=[("yt", "out", pair // 2, pair % 2, j)]) for j in range(2) if pair < 4]
-        gpsimd_lane = on_gpsimd(("w", 0, 0), False) + on_gpsimd(("w", 0, 1), False, 2) + on_gpsimd(("w", 1, 1)) + on_gpsimd(("g", 0)) + on_gpsimd(("g", 1))
-        for c in (3, 4):
-            gpsimd_lane += on_gpsimd(("w", c, 0)) + on_gpsimd(("w", c, 1), False, 2)
-        gpsimd_lane += on_gpsimd(("w", 5, 0))
-        gpsimd_lane += lasting(unit(plane_interleave_gpsimd, ("h", 0, 1), ("plane", 2, 1), 1, makes=[("h", 0, 1, n) for n in range(1, 4)], needs=[("h", 0, 1, 0)]), GP_TICKS - 1)
-        closing = z_units(5, 0, True)
-        column_unit = unit(columns_out, makes=["columns"], feed=(columns_product,), feed_needs=["rows"])
-        z = {(c, h): z_units(c, h) for c in range(5) for h in range(2)}
-        tensor_lane = feeds(
-            x_outs(0, range(4)) + x_outs(1, (0, 1)) + z[0, 0][:1] + [column_unit] + z[0, 0][1:2] + x_outs(1, (2,)) + z[0, 0][2:3] + x_outs(1, (3,)) + z[0, 0][3:]
-            + z[1, 0] + e_units[:2] + z[0, 1][:2] + mix(v_units(0, 0), z[0, 1][2:]) + z[1, 1] + e_units[2:]
-            + mix(z[2, 0], v_scalar_units(1, 0)[:4]) + z[2, 1] + mix(z[3, 0], v_units(0, 1)) + v_units(1, 1)[:2] + z[3, 1] + v_units(1, 1)[2:] + z[4, 0] + z_aside_units(4, 1)
-            + closing + z_aside_units(5, 1) + scales[:2] + ys[:1] + scales[2:3] + outs[:2] + scales[3:4] + ys[1:3] + outs[2:4] + ys[3:4] + scales[4:6] + ys[4:5] + scales[6:7] + outs[4:6] + ys[5:6] + scales[7:] + ys[6:] + outs[6:]
-        )
-        vector_lane = (
-            widen(0, (0, 1, 2), True) + x_outs(0, range(4))
-            + [x_quant(0, (0,)), w_quant(0, 0), x_quant(0, (1,)), w_quant(0, 1), unit(permute_rows, makes=["rows"]), w_quant(1, 0, ("w", 1, 1))]
-            + x_outs(1, (0, 1, 2)) + [w_quant(1, 1, ("g", 0))]
-            + x_outs(1, (3,)) + z[1, 0] + [x_quant(1, (0,)), x_quant(1, (1,)), g_quant(0), e_quant(0, ("g", 1)), w_quant(2, 0)]
-            + v_units(0, 0) + z[1, 1][:2] + [w_quant(2, 1), g_quant(1, ("w", 3, 0)), v_quant(0, 0)]
-            + z[1, 1][2:] + z[2, 0] + z[2, 1][:2] + [w_quant(3, 0), w_quant(3, 1, ("w", 4, 0)), e_quant(1)]
-            + z[2, 1][2:] + v_units(0, 1) + v_units(1, 1)[:2] + [w_quant(4, 0), w_quant(4, 1), v_quant(1, 0, ("w", 5, 0)), v_quant(0, 1)]
-            + v_units(1, 1)[2:] + z[4, 0] + [w_quant(5, 1), w_quant(5, 0), v_quant(1, 1, ("h", 0, 1)), h_quant(0, 0)]
-            + closing + h_part(1, 0, 2, 4, True) + h_quants(1, 0) + [z_merge_unit(4, 1), h_quant(0, 1), z_merge_unit(5, 1)]
-            + ys[:1] + h_part(1, 1, 0, 4, True) + adds[:1] + [h_quant(1, 1)] + ys[1:2] + mix(ys[2:], adds[1:7]) + adds[7:]
-        )
-        scalar_lane = (
-            widen(0, (3,)) + widen(1, (0, 1)) + w_s(0, 1, 0, 2) + w_s(1, 0) + widen(1, (2, 3))
-            + [column_unit] + z[0, 0] + w_s(2, 0) + e_units[:2] + w_s(2, 1, 0, 2) + z[0, 1] + w_s(2, 1, 2)
-            + w_s(3, 1, 0, 2) + e_units[2:] + v_scalar_units(1, 0)
-            + w_s(4, 1, 0, 2) + z[3, 0] + w_s(5, 1, 0, 2) + z[3, 1] + w_s(5, 1, 2) + h_part(0, 0, 0, 4, False) + z_aside_units(4, 1)
-            + h_part(0, 1, 0, 1, False, inherits=True) + h_part(1, 0, 0, 2, False, range(2)) + z_aside_units(5, 1)
-            + scales[:3] + outs[:2] + scales[3:4] + outs[2:4] + scales[4:7] + outs[4:6] + scales[7:] + outs[6:]
-        )
-
         lanes = [sync_lane, tensor_lane, vector_lane, scalar_lane, gpsimd_lane]
         made = set()
-        done = [0] * len(lanes)
-        while done != [len(lane) for lane in lanes]:
+        while any(lanes):
             fresh = []
-            for k, lane in enumerate(lanes):
-                turn = len(lane) if k < 2 else done[k] + 1
-                while done[k] < min(turn, len(lane)) and all(n in made for n in lane[done[k]][2]) and (banks or lane is not tensor_lane):
-                    if lane[done[k]][0]:
-                        run(lane[done[k]][0])
-                    fresh.extend(lane[done[k]][1])
-                    done[k] = done[k] + 1
-            for n in fresh:
-                made.add(n)
+            for lane in lanes:
+                allowed = len(lane) if lane is sync_lane or lane is tensor_lane else 1
+                while allowed and lane and all(name in made for name in lane[0][2]) and (lane is not tensor_lane or next_bank_is_free()):
+                    call, makes = lane.pop(0)[:2]
+                    call[0](*call[1:])
+                    fresh.extend(makes)
+                    allowed = allowed - 1
+            for name in fresh:
+                made.add(name)

@@ -19,11 +19,19 @@ MAX = mybir.AluOpType.max
 IDENTITY = mybir.ActivationFunctionType.Identity
 
 RUN = 8
-BANKS = 8
+BANKS = {"vector": 4, "scalar": 4}
 WHOLE = slice(0, 512)
-ROW_A, ROW_R, ROW_D, ROWS = 6, 8, 9, 10
+ROW_A, ROW_R, ROW_D, ROWS = 6, 8, 10, 12
 SHARED_LONG, SHARED_SHORT, SHARED_H = 2, 3, 1
 STORED_BETWEEN = (1, 2)
+
+ASIDE = ((4, 1),)
+PASSED = (("w", 0, 1, 0, 2), ("w", 1, 0, 0, 4), ("w", 1, 1, 0, 4), ("g", 0, 1, 0, 4))
+V_BLOCKS = {(0, 0): 2, (1, 0): 4, (0, 1): 0, (1, 1): 0}
+TURNED = (6, 4)
+DIRECT = [(0, 0, True), (0, 1, True)] + [(1, j, False) for j in range(4)]
+ON_GPSIMD = ()
+EARLY = [(1, 0, False), (1, 1, False)]
 
 
 def tile_maxout_generated_head_f5_kernel(tc, x_bytes, x_scale, w, b, e, g, a, r, d, out):
@@ -39,15 +47,15 @@ def tile_maxout_generated_head_f5_kernel(tc, x_bytes, x_scale, w, b, e, g, a, r,
         def operand(name):
             return kept(name + "_codes", [P, 512], U32), kept(name + "_scales", [P, 512], U8)
 
-        banks = [psum.tile([P, 512], F32, name=f"bank{n}") for n in range(BANKS)]
-        staged = [kept(f"staged{n}", [P, 2048], BF16) for n in range(6)]
+        banks = {reader: [psum.tile([P, 512], F32, name=f"bank_{reader}{n}") for n in range(count)] for reader, count in BANKS.items()}
+        staged = [kept(f"staged{n}", [P, 2048], BF16) for n in range(9)]
         wide = [kept(f"x_wide{n}", [P, K], BF16) for n in range(4)]
         results = [kept(f"result{n}", [P, 512], F32) for n in range(10)]
-        by_class = [kept(f"by_class{n}", [P, 512], F32) for n in range(4)]
-        raws = [kept(f"raw{n}", [P, 4, 512], BF16) for n in range(8)]
-        planes = [kept(f"plane{n}", [P, 4, 512], BF16) for n in range(7)]
+        by_class = [tile[:].bitcast(F32) for tile in wide] + [kept(f"by_class{n}", [P, 512], F32) for n in range(2)]
+        raws = [kept(f"raw{n}", [P, 4, 512], BF16) for n in range(9)]
+        planes = [kept(f"plane{n}", [P, 4, 512], BF16) for n in range(8)]
         held = {}
-        fills = []
+        reader_of = {}
 
         def take(free, key):
             held[key] = free.pop(0)
@@ -58,12 +66,10 @@ def tile_maxout_generated_head_f5_kernel(tc, x_bytes, x_scale, w, b, e, g, a, r,
             return held.pop(key)
 
         def fill(key):
-            held[key] = banks[len(fills) % BANKS]
-            fills.append(key)
-            return held[key]
+            return take(banks[reader_of["now"]], key)
 
-        def next_bank_is_free():
-            return len(fills) < BANKS or fills[-BANKS] not in held
+        def drain(key, reader):
+            return give(banks[reader], key)
 
         x_raw = [[kept(f"x_raw{h}_{j}", [P, 2, K], U8) for j in range(2)] for h in range(2)]
         e_raw = [kept(f"e_raw{n}", [P, 4, D], BF16) for n in range(2)]
@@ -128,10 +134,7 @@ def tile_maxout_generated_head_f5_kernel(tc, x_bytes, x_scale, w, b, e, g, a, r,
             quantize(key, give(staged, key) if part else held[key], block(part, 256))
 
         def permute_rows():
-            nc.vector.tensor_copy(
-                out=rows[0:ROW_R, :].rearrange("p (t B i) -> p t B i", t=4, i=RUN),
-                in_=rows_raw[:].rearrange("p (B t i) -> p t B i", t=4, i=RUN),
-            )
+            copy(nc.scalar, rows[0:ROW_R, :].rearrange("p (t B i) -> p t B i", t=4, i=RUN), rows_raw[:].rearrange("p (B t i) -> p t B i", t=4, i=RUN))
 
         def columns_product():
             bank = fill("columns")
@@ -139,7 +142,7 @@ def tile_maxout_generated_head_f5_kernel(tc, x_bytes, x_scale, w, b, e, g, a, r,
                 nc.tensor.matmul(bank[:, 16 * t : 16 * t + ROWS], lhsT=rows[:, block(t)], rhs=ident_bf[:, 0:ROWS], start=True, stop=True)
 
         def columns_read():
-            nc.scalar.copy(out=columns[:], in_=held.pop("columns")[:, 0:64].rearrange("p (t j) -> p j t", t=4)[:, 0:ROWS, :])
+            nc.scalar.copy(out=columns[:], in_=drain("columns", "scalar")[:, 0:64].rearrange("p (t j) -> p j t", t=4)[:, 0:ROWS, :])
 
         def x_widen(h, i, engine):
             copy(engine, wide[i][:], x_raw[h][i // 2][:, i % 2, :].bitcast(FP8))
@@ -154,7 +157,7 @@ def tile_maxout_generated_head_f5_kernel(tc, x_bytes, x_scale, w, b, e, g, a, r,
         def x_read(h, i):
             nc.vector.tensor_tensor(
                 out=x_staged[:, :, block(i, 512)].rearrange("p q (r u e) -> p q r u e", u=2, e=2),
-                in0=held.pop(("x bank", h, i))[:].bitcast(BF16).rearrange("p (u q r e) -> p q r u e", u=2, q=2, e=2),
+                in0=drain(("x bank", h, i), "vector")[:].bitcast(BF16).rearrange("p (u q r e) -> p q r u e", u=2, q=2, e=2),
                 in1=xs[:].rearrange("p q (o u e) -> p q o u e", o=1, u=2).to_broadcast([P, 2, P, 2, 2]),
                 op=MULT,
             )
@@ -171,7 +174,7 @@ def tile_maxout_generated_head_f5_kernel(tc, x_bytes, x_scale, w, b, e, g, a, r,
                 take(staged, ("e", 0, n))
             nc.scalar.copy(
                 out=held["e", 0, n][:].bitcast(F32)[:, block(j, 512)].rearrange("p (i r u) -> p i r u", i=2, u=2),
-                in_=held.pop(("e bank", n, j))[:].rearrange("p (i u r) -> p i r u", i=2, u=2),
+                in_=drain(("e bank", n, j), "scalar")[:].rearrange("p (i u r) -> p i r u", i=2, u=2),
             )
 
         def stage_raw(key, first, last, engine):
@@ -196,6 +199,18 @@ def tile_maxout_generated_head_f5_kernel(tc, x_bytes, x_scale, w, b, e, g, a, r,
                 plane[:, :, P * first : P * last].rearrange("p t (c i) -> p c t i", i=run),
             )
 
+        def pass_raw(key, j):
+            bank = fill(("pass bank", key, j))[:].bitcast(BF16)
+            raw = give(raws, ("raw",) + key) if j else held[("raw",) + key]
+            for n in range(2):
+                source = raw[:].rearrange("p s (B t i) -> p t B i s", t=4, i=RUN)[:, 2 * j + n]
+                nc.tensor.matmul(bank[:, block(n, 512)], lhsT=ident_bf[:], rhs=source, start=True, stop=True)
+
+        def passed_read(key, j):
+            if key not in held:
+                take(staged, key)
+            nc.scalar.copy(out=held[key][:].bitcast(F32)[:, block(j, 512)], in_=drain(("pass bank", key, j), "scalar")[:])
+
         def z_parts(s, split):
             if split:
                 return [(2 * (s % 2) + n, block(s // 2, 256), block(n, 256)) for n in range(2)]
@@ -213,10 +228,10 @@ def tile_maxout_generated_head_f5_kernel(tc, x_bytes, x_scale, w, b, e, g, a, r,
         def z_alone(c, h, t, name):
             if t == 0:
                 take(planes, (name, c, h))
-            nc.scalar.activation(out=held[name, c, h][:, t, :], in_=held.pop(("z bank", c, h, t))[:], func=IDENTITY, bias=z_bias(c, t))
+            nc.scalar.activation(out=held[name, c, h][:, t, :], in_=drain(("z bank", c, h, t), "scalar")[:], func=IDENTITY, bias=z_bias(c, t))
 
         def z_max(c, h, s, split):
-            bank = held.pop(("z bank", c, h, s))
+            bank = drain(("z bank", c, h, s), "vector")
             if s == 0:
                 take(planes, ("max", c, h))
             for t, samples, place in z_parts(s, split):
@@ -226,9 +241,11 @@ def tile_maxout_generated_head_f5_kernel(tc, x_bytes, x_scale, w, b, e, g, a, r,
             if s == 3:
                 give(planes, ("max", c - 1, h))
 
-        def z_merge(c, h):
+        def z_merge(c, h, heir):
             merged = take(planes, ("max", c, h))
-            nc.vector.tensor_tensor(out=merged[:], in0=give(planes, ("aside", c, h))[:], in1=give(planes, ("max", c - 1, h))[:], op=MAX)
+            aside = held.pop(("aside", c, h))
+            nc.vector.tensor_tensor(out=merged[:], in0=aside[:], in1=give(planes, ("max", c - 1, h))[:], op=MAX)
+            held[heir] = aside[:].rearrange("p t c -> p (t c)")
 
         def v_four_slots(q, n, j):
             bank = fill(("v bank", q, n, j))
@@ -240,7 +257,7 @@ def tile_maxout_generated_head_f5_kernel(tc, x_bytes, x_scale, w, b, e, g, a, r,
                 take(staged, ("v", q, n))
             nc.vector.tensor_tensor(
                 out=held["v", q, n][:, block(j, 512)].rearrange("p (c t) -> p c t", t=4),
-                in0=held.pop(("v bank", q, n, j))[:].rearrange("p (t c) -> p c t", t=4),
+                in0=drain(("v bank", q, n, j), "vector")[:].rearrange("p (t c) -> p c t", t=4),
                 in1=columns[:, ROW_A + q : ROW_A + q + 1, :].to_broadcast([P, P, 4]),
                 op=ADD,
             )
@@ -258,59 +275,88 @@ def tile_maxout_generated_head_f5_kernel(tc, x_bytes, x_scale, w, b, e, g, a, r,
         def v_read_plane(q, n, s, paired):
             if s == 0:
                 take(planes, ("v plane", q, n))
-            bank = held.pop(("v slot bank", q, n, s))
+            bank = drain(("v slot bank", q, n, s), "scalar")
             for t, classes, place in v_parts(s, paired):
                 nc.scalar.activation(out=held["v plane", q, n][:, t, classes], in_=bank[:, place], func=IDENTITY, bias=columns[:, ROW_A + q, t : t + 1])
 
-        def direct_product(i):
-            bank = fill(("direct bank", i))
-            for q in range(2):
-                product(bank[:], ("h", q, i // 4), block(i % 4), ("v", q, 1), WHOLE, q == 0, q == 1)
+        def direct_parts(key):
+            h, j, narrow = key
+            if narrow:
+                return [(2 * j + n, block(1, 256), block(n, 256)) for n in range(2)]
+            return [(j, WHOLE, WHOLE)]
 
-        def direct_scale(i):
-            nc.vector.tensor_tensor(out=take(results, ("direct", i))[:], in0=held.pop(("direct bank", i))[:], in1=r_all[:], op=MULT)
+        def spread(vector, key):
+            if key[2]:
+                return vector[:, block(1, 256)].rearrange("p (o c) -> p o c", o=1).to_broadcast([P, 2, 256])
+            return vector[:].rearrange("p (o c) -> p o c", o=1)
 
-        def direct_shift(i):
-            nc.vector.tensor_tensor(out=held["direct", i][:], in0=held["direct", i][:], in1=d_all[:], op=ADD)
+        def by_tile(tile, key):
+            return tile[:].rearrange("p (i c) -> p i c", i=2 if key[2] else 1)
 
-        def direct_store(i):
-            nc.sync.dma_start(out=out_rows[:, i, 512:C], in_=give(results, ("direct", i))[:])
+        def direct_product(key, passes):
+            bank = fill(("direct bank", key)) if 0 in passes else held["direct bank", key]
+            for i, classes, place in direct_parts(key):
+                for q in passes:
+                    product(bank[:, place], ("h", q, key[0]), block(i), ("v", q, 1), classes, q == 0, q == 1)
 
-        def class_product(h, n):
-            bank = fill(("class bank", h, n))
-            for q in range(2):
-                product(bank[:], ("v", q, 0), block(n), ("h", q, h), WHOLE, q == 0, q == 1)
+        def direct_scale(key):
+            nc.vector.tensor_tensor(out=by_tile(take(results, ("direct", key)), key), in0=by_tile(drain(("direct bank", key), "vector"), key), in1=spread(r_all, key), op=MULT)
+
+        def direct_shift(key, engine):
+            tile = by_tile(held["direct", key], key)
+            engine.tensor_tensor(out=tile, in0=tile, in1=spread(d_all, key), op=ADD)
+
+        def direct_store(key):
+            h, j, narrow = key
+            rows_out = out_rows[:, 4 * h + 2 * j : 4 * h + 2 * j + 2, 768:C] if narrow else out_rows[:, 4 * h + j : 4 * h + j + 1, 512:C]
+            nc.sync.dma_start(out=rows_out, in_=by_tile(give(results, ("direct", key)), key))
+
+        def class_product(h, n, passes):
+            bank = fill(("class bank", h, n)) if 0 in passes else held["class bank", h, n]
+            for q in passes:
+                product(bank[:], ("v", q, n // 4), block(n % 4), ("h", q, h), WHOLE, q == 0, q == 1)
 
         def class_read(h, n):
             nc.scalar.activation(
                 out=take(by_class, ("by class", h, n))[:],
-                in_=held.pop(("class bank", h, n))[:],
+                in_=drain(("class bank", h, n), "scalar")[:],
                 func=IDENTITY,
-                scale=columns[:, ROW_R, n : n + 1],
-                bias=columns[:, ROW_D, n : n + 1],
+                scale=columns[:, ROW_R + n // 4, n % 4 : n % 4 + 1],
+                bias=columns[:, ROW_D + n // 4, n % 4 : n % 4 + 1],
             )
+
+        def turned_parts(m, j):
+            if m == 0:
+                return [(n, j, n) for n in range(4)]
+            return [(4 + n, 2 * j + i, 2 * i + n) for n in range(2) for i in range(2)]
 
         def turn_back(h, m, j):
             bank = fill(("turned bank", h, m, j))
-            for n in range(2):
-                source = give(by_class, ("by class", h, 2 * m + n)) if j else held["by class", h, 2 * m + n]
-                for i in range(2):
-                    nc.tensor.transpose(bank[:, block(2 * i + n)], source[:, block(2 * j + i)], ident[:])
+            for n, i, place in turned_parts(m, j):
+                nc.tensor.transpose(bank[:, block(place)], held["by class", h, n][:, block(i)], ident[:])
+            if j == (1 if m else 3):
+                for n in sorted(set(part[0] for part in turned_parts(m, j))):
+                    give(by_class, ("by class", h, n))
 
         def turned_read(h, m, j):
-            nc.scalar.copy(out=take(results, ("turned", h, m, j))[:], in_=held.pop(("turned bank", h, m, j))[:])
+            nc.scalar.copy(out=take(results, ("turned", h, m, j))[:], in_=drain(("turned bank", h, m, j), "scalar")[:])
 
         def turned_store(h, m, j):
-            nc.sync.dma_start(
-                out=out_rows[:, 4 * h + 2 * j : 4 * h + 2 * j + 2, block(m, 256)],
-                in_=give(results, ("turned", h, m, j))[:].rearrange("p (i c) -> p i c", i=2),
-            )
+            tile = give(results, ("turned", h, m, j))
+            if m == 0:
+                nc.sync.dma_start(out=out_rows[:, 4 * h + j, 0:512], in_=tile[:])
+            else:
+                nc.sync.dma_start(out=out_rows[:, 4 * h + 2 * j : 4 * h + 2 * j + 2, 512:768], in_=tile[:].rearrange("p (i c) -> p i c", i=2))
 
-        def step(*call, makes=(), needs=(), feed=None, feed_needs=()):
-            return call, list(makes), list(needs) + ([feed] if feed else []), feed, list(feed_needs)
+        def step(*call, makes=(), needs=(), feed=None, feed_needs=(), lender=None):
+            return call, list(makes), list(needs) + ([feed] if feed else []), feed, list(feed_needs), lender
 
         def feeds(steps):
-            return [step(*feed, makes=[feed], needs=feed_needs) for call, makes, needs, feed, feed_needs in steps]
+            by_vector = (x_read, z_max, v_read_staged, direct_scale)
+            return [
+                step(*feed, makes=[feed], needs=feed_needs, lender=lender or (None if feed[-1] == (1,) else "vector" if call[0] in by_vector else "scalar"))
+                for call, makes, needs, feed, feed_needs, lender in steps
+            ]
 
         def quarters(key, first=0, last=4):
             return [key + (n,) for n in range(first, last)]
@@ -335,6 +381,12 @@ def tile_maxout_generated_head_f5_kernel(tc, x_bytes, x_scale, w, b, e, g, a, r,
             needs = [("raw",) + key] + quarters(key, 0, first) + [("inherited", key)] * inherited
             return step(stage_raw, key, first, last, engine, makes=quarters(key, first, last), needs=needs)
 
+        def passed(*key, first=0, last=4):
+            return [
+                step(passed_read, key, j, makes=quarters(key, 2 * j, 2 * j + 2), feed=(pass_raw, key, j), feed_needs=[("raw",) + key] + quarters(key, 0, first))
+                for j in range(first // 2, last // 2)
+            ]
+
         def stage_h(engine, q, h, first=0, last=4, banks_read=4, inherited=False):
             key, c = ("h", q, h), J * q + J - 1
             needs = quarters(("max", c, h), 0, banks_read) + quarters(key, 0, first) + [("inherited", key)] * inherited
@@ -347,21 +399,18 @@ def tile_maxout_generated_head_f5_kernel(tc, x_bytes, x_scale, w, b, e, g, a, r,
                 for s in range(4)
             ]
 
-        def merge(c, h):
-            return step(z_merge, c, h, makes=quarters(("max", c, h)), needs=quarters(("aside", c, h)) + quarters(("max", c - 1, h)))
+        def merge(c, h, heir):
+            return step(z_merge, c, h, heir, makes=quarters(("max", c, h)) + [("inherited", heir)], needs=quarters(("aside", c, h)) + quarters(("max", c - 1, h)))
 
         def loads_w(c):
             col = (c % J) * F + (c // J) * 512
-            return [
-                step(load_raw, ("w", c, q), w[block(q, 512), col : col + 512], makes=[("raw", "w", c, q)], needs=[("w", c - J, q, 3)] * (c >= J))
-                for q in range(2)
-            ]
+            return [step(load_raw, ("w", c, q), w[block(q, 512), col : col + 512], makes=[("raw", "w", c, q)], lender="raw") for q in range(2)]
 
         def load_x(h, j):
             return step(load, x_raw[h][j][:], x_rows[:, 4 * h + 2 * j : 4 * h + 2 * j + 2, :], makes=[("x raw", h, j)])
 
         def load_g(q):
-            return step(load_raw, ("g", 0, q), g[:, block(q, 512)], makes=[("raw", "g", 0, q)])
+            return step(load_raw, ("g", 0, q), g[:, block(q, 512)], makes=[("raw", "g", 0, q)], lender="raw")
 
         def load_e(n):
             return step(load, e_raw[n][:], e[block(n, 512), :].rearrange("(i p) k -> p i k", p=P), makes=[("e raw", n)])
@@ -374,80 +423,82 @@ def tile_maxout_generated_head_f5_kernel(tc, x_bytes, x_scale, w, b, e, g, a, r,
             for h in range(2):
                 if c % J == 0:
                     z[c, h] = z_steps(z_alone, c, h, "max", "max", [])
-                elif c > J and h == 1:
+                elif (c, h) in ASIDE:
                     z[c, h] = z_steps(z_alone, c, h, "aside", "aside", [])
                 else:
                     split = c == 2 * J - 1
                     z[c, h] = z_steps(z_max, c, h, split, "max", quarters(("max", c - 1, h)), split)
         v_vector = {
             (q, n): [step(v_read_staged, q, n, j, makes=[("v", q, n, j)], feed=(v_four_slots, q, n, j), feed_needs=[("g", 0, q), ("e", 0, n)]) for j in range(blocks)]
-            for q, n, blocks in ((0, 0, 2), (0, 1, 4), (1, 1, 4))
+            for (q, n), blocks in V_BLOCKS.items()
         }
-        v_scalar = [[step(v_read_plane, q, 0, s, q == 0, feed=(v_by_slot, q, 0, s, q == 0), feed_needs=[("g", 0, q), ("e", 0, 0)]) for s in range(2 + 2 * q)] for q in range(2)]
-        stage_v = [
-            step(stage_plane, ("v", q, 0), ("v plane", q, 0), first, 4, nc.scalar, makes=quarters(("v", q, 0), first), needs=quarters(("v", q, 0), 0, first)[:1])
-            for q, first in ((0, 2), (1, 0))
-        ]
+        v_scalar = {
+            (q, n): [step(v_read_plane, q, n, s, blocks == 2, makes=[("v plane", q, n, s)], feed=(v_by_slot, q, n, s, blocks == 2), feed_needs=[("g", 0, q), ("e", 0, n)]) for s in range(4 - blocks)]
+            for (q, n), blocks in V_BLOCKS.items()
+        }
+
+        def stage_v(engine, q, n, first=None, last=4, inherited=False):
+            key = ("v", q, n)
+            first = V_BLOCKS[q, n] if first is None else first
+            needs = quarters(("v plane", q, n), 0, 4 - V_BLOCKS[q, n]) + quarters(key, 0, first)[:1 if first == V_BLOCKS[q, n] else 4] + [("inherited", key)] * inherited
+            return step(stage_plane, key, ("v plane", q, n), first, last, engine, makes=quarters(key, first, last), needs=needs)
+
         h_halves = [step(quantize_part, ("h", 1, 0), part, makes=[("h", 1, 0)] * part, needs=quarters(("h", 1, 0), 2 * part, 2 * part + 2)) for part in range(2)]
-        scaled = [step(direct_scale, i, needs=["r and d"], feed=(direct_product, i), feed_needs=both("h", i // 4) + both("v", 1)) for i in range(8)]
-        shifted = [step(direct_shift, i, makes=[("direct", i)]) for i in range(8)]
-        classes = [[step(class_read, h, n, makes=[("by class", h, n)], feed=(class_product, h, n), feed_needs=both("h", h) + both("v", 0)) for n in range(4)] for h in range(2)]
+        scaled = [step(direct_scale, key, makes=[("scaled", key)], needs=["r and d"], feed=(direct_product, key, (1,) if key in EARLY else (0, 1)), feed_needs=both("h", key[0]) + both("v", 1)) for key in DIRECT]
+        shifted = [step(direct_shift, key, nc.gpsimd if n in ON_GPSIMD else nc.vector, makes=[("direct", key)], needs=[("scaled", key)]) for n, key in enumerate(DIRECT)]
+        classes = [[step(class_read, h, n, makes=[("by class", h, n)], feed=(class_product, h, n, (1,) if (h, n) in EARLY else (0, 1)), feed_needs=both("h", h) + both("v", n // 4)) for n in range(TURNED[h])] for h in range(2)]
         turned = {
             (h, m): [
-                step(turned_read, h, m, j, makes=[("turned", h, m, j)], feed=(turn_back, h, m, j), feed_needs=quarters(("by class", h), 2 * m, 2 * m + 2))
-                for j in range(2)
+                step(turned_read, h, m, j, makes=[("turned", h, m, j)], feed=(turn_back, h, m, j), feed_needs=[("by class", h, part[0]) for part in turned_parts(m, j)])
+                for j in range(2 if m else 4)
             ]
             for h in range(2)
-            for m in range(2)
+            for m in range(TURNED[h] // 2 - 1)
         }
+        small_loads = [step(load, rows_raw[0:ROW_A, :], b.rearrange("(c n) -> c n", n=512)), step(load, rows_raw[ROW_A:ROW_R, :], a.rearrange("(c n) -> c n", n=512))]
+        small_loads += [step(load, rows[row : row + 2, :], vector.rearrange("(o n) -> o n", o=2), makes=[("row", row)]) for row, vector in ((ROW_R, r), (ROW_D, d))]
 
+        def early(steps):
+            return [step(None, feed=feed[:-1] + ((0,),), feed_needs=[name for name in feed_needs if name[1] == 0], lender="vector" if call[0] is direct_scale else "scalar") for call, makes, needs, feed, feed_needs, lender in steps]
+
+        V, S, G = nc.vector, nc.scalar, nc.gpsimd
+        pw = {key[:3]: passed(*key[:3], first=key[3], last=key[4]) for key in PASSED}
         sync_lane = (
             [load_x(0, 0), step(load, xs[:], x_scale.rearrange("o (q p t) -> p (o q) t", q=2, t=4)), load_x(0, 1)]
-            + loads_w(0)[:1] + [load_x(1, 0)] + loads_w(0)[1:] + loads_w(1) + [load_x(1, 1)]
-            + [step(load, rows_raw[0:ROW_A, :], b.rearrange("(c n) -> c n", n=512)), step(load, rows_raw[ROW_A:ROW_R, :], a.rearrange("(c n) -> c n", n=512))]
-            + [step(load, rows[row : row + 1, :], vector[0:512].rearrange("(o n) -> o n", o=1)) for row, vector in ((ROW_R, r), (ROW_D, d))]
-            + loads_w(2) + [load_g(0), load_e(0), load_e(1), load_g(1)] + loads_w(3) + loads_w(4) + loads_w(5)
+            + loads_w(0)[:1] + [load_x(1, 0)] + loads_w(0)[1:] + loads_w(1) + [load_x(1, 1)] + small_loads + loads_w(2) + [load_g(0)] + loads_w(3)[:1] + [load_e(0), load_g(1)] + loads_w(3)[1:] + loads_w(4) + [load_e(1)] + loads_w(5)
             + [step(load, r_all[:], r[512:C].partition_broadcast(P)), step(load, d_all[:], d[512:C].partition_broadcast(P), makes=["r and d"])]
         )
-        for h in range(2):
-            direct_stores = [step(direct_store, i, needs=[("direct", i)]) for i in range(4 * h, 4 * h + 4)]
-            pairs = [[step(turned_store, h, m, j, needs=[("turned", h, m, j)]) for j in range(2)] for m in range(2)]
-            sync_lane += pairs[0] + direct_stores[: STORED_BETWEEN[h]] + pairs[1] + direct_stores[STORED_BETWEEN[h] :]
+        direct_stores = [step(direct_store, key, needs=[("direct", key)]) for key in DIRECT]
+        pairs = {(h, m): [step(turned_store, h, m, j, needs=[("turned", h, m, j)]) for j in range(len(turned[h, m]))] for h, m in turned}
+        sync_lane += pairs[0, 0] + direct_stores[:1] + pairs[0, 1] + direct_stores[1:4] + pairs[1, 0][:2] + direct_stores[4:5] + pairs[1, 0][2:3] + direct_stores[5:] + pairs[1, 0][3:]
 
         vector_lane = (
-            widen(0, (0, 1, 2), nc.vector) + x_reads[0]
-            + [quant_x(0, 0), quant("w", 0, 0), quant_x(0, 1), quant("w", 0, 1), step(permute_rows, makes=["rows"]), quant("w", 1, 0, heir=("w", 1, 1))]
-            + x_reads[1][:3] + [quant("w", 1, 1, heir=("g", 0, 0))]
-            + x_reads[1][3:] + z[1, 0] + [quant_x(1, 0), quant_x(1, 1), quant("g", 0, 0), quant("e", 0, 0, heir=("g", 0, 1)), quant("w", 2, 0)]
-            + v_vector[0, 0] + z[1, 1][:3] + [quant("w", 2, 1), quant("g", 0, 1, heir=("w", 3, 0)), quant("e", 0, 1)]
-            + z[1, 1][3:] + z[2, 0] + z[2, 1][:2] + [quant("w", 3, 0), quant("w", 3, 1, heir=("w", 4, 0)), quant("v", 0, 0)]
-            + z[2, 1][2:] + v_vector[0, 1] + v_vector[1, 1][:2] + [quant("w", 4, 0), quant("w", 4, 1), quant("v", 1, 0, heir=("w", 5, 0)), quant("v", 0, 1)]
-            + v_vector[1, 1][2:] + z[4, 0] + [quant("w", 5, 1), quant("w", 5, 0), quant("v", 1, 1), quant("h", 0, 0, heir=("h", 0, 1))]
-            + z[5, 0] + [stage_h(nc.vector, 1, 0, first=2)] + h_halves + [merge(4, 1), quant("h", 0, 1), merge(5, 1)]
-            + [scaled[0], stage_h(nc.vector, 1, 1), shifted[0], quant("h", 1, 1), scaled[1]] + alternate(scaled[2:], shifted[1:7]) + shifted[7:]
+            widen(0, (0, 1, 2), V) + x_reads[0]
+            + [quant_x(0, 0), quant("w", 0, 0), quant_x(0, 1), quant("w", 0, 1), quant("w", 1, 0), quant("w", 1, 1, heir=("w", 2, 0))]
+            + x_reads[1] + z[1, 0] + [quant("w", 2, 0), quant("w", 2, 1), quant_x(1, 0), quant_x(1, 1), quant("g", 0, 0, heir=("w", 3, 1)), quant("e", 0, 0)]
+            + z[2, 0] + v_vector[0, 0] + z[1, 1] + [quant("w", 3, 0), quant("w", 3, 1), quant("g", 0, 1), quant("w", 4, 0), quant("e", 0, 1, heir=("w", 5, 0)), quant("w", 4, 1)]
+            + z[2, 1] + v_vector[1, 0] + [quant("w", 5, 0), quant("w", 5, 1), quant("v", 0, 0), quant("h", 0, 0, heir=("v", 0, 1)), quant("v", 1, 0)]
+            + z[4, 0] + z[5, 0] + [stage_h(V, 1, 0, first=2), quant("v", 0, 1), quant("h", 1, 0), merge(4, 1, ("h", 0, 1)), quant("v", 1, 1)] + z[5, 1]
+            + [stage_h(V, 1, 1, first=2), quant("h", 0, 1), quant("h", 1, 1)]
+            + scaled[:1] + alternate(scaled[1:], shifted[:-1]) + shifted[-1:]
         )
-        gpsimd_lane = [stage(nc.gpsimd, "w", 0, 0), stage(nc.gpsimd, "w", 0, 1, first=SHARED_LONG)]
-        gpsimd_lane += [stage(nc.gpsimd, *key, inherited=True) for key in (("w", 1, 1), ("g", 0, 0), ("g", 0, 1))]
-        for c, shared in ((3, SHARED_SHORT), (4, SHARED_LONG)):
-            gpsimd_lane += [stage(nc.gpsimd, "w", c, 0, inherited=True), stage(nc.gpsimd, "w", c, 1, first=shared)]
-        gpsimd_lane += [stage(nc.gpsimd, "w", 5, 0, inherited=True), stage_h(nc.gpsimd, 0, 1, first=SHARED_H)]
+        gpsimd_lane = [stage(G, "w", 0, 0), stage(G, "w", 0, 1, first=2),
+            stage(G, "w", 2, 0, inherited=True), stage(G, "w", 2, 1), stage(G, "g", 0, 0, last=1),
+            stage(G, "w", 3, 1, inherited=True), stage(G, "w", 4, 1),
+            stage(G, "w", 5, 0, inherited=True), stage(G, "w", 5, 1, first=1),
+            stage_v(G, 0, 1, inherited=True), stage_v(G, 1, 1, last=3), stage_h(G, 0, 1, inherited=True)]
         scalar_lane = (
-            widen(0, (3,), nc.scalar) + widen(1, (0, 1), nc.scalar) + [stage(nc.scalar, "w", 0, 1, last=SHARED_LONG), stage(nc.scalar, "w", 1, 0)] + widen(1, (2, 3), nc.scalar)
-            + column_read + z[0, 0][:2] + [stage(nc.scalar, "w", 2, 0, last=2)] + z[0, 0][2:] + [stage(nc.scalar, "w", 2, 0, first=2), stage(nc.scalar, "w", 2, 1, last=2)]
-            + e_reads[0] + e_reads[1] + z[0, 1] + [stage(nc.scalar, "w", 2, 1, first=2)] + v_scalar[0] + [stage(nc.scalar, "w", 3, 1, last=SHARED_SHORT), stage_v[0]]
-            + v_scalar[1] + [stage_v[1], stage(nc.scalar, "w", 4, 1, last=SHARED_LONG)]
-            + z[3, 0] + [stage(nc.scalar, "w", 5, 1, last=2)] + z[3, 1] + [stage(nc.scalar, "w", 5, 1, first=2), stage_h(nc.scalar, 0, 0)]
-            + z[4, 1] + [stage_h(nc.scalar, 0, 1, last=SHARED_H, inherited=True), stage_h(nc.scalar, 1, 0, last=2, banks_read=2)] + z[5, 1]
+            widen(0, (3,), S) + widen(1, (0, 1), S) + pw["w", 0, 1] + pw["w", 1, 0] + pw["w", 1, 1] + [step(permute_rows, makes=["rows"], needs=[("row", ROW_D)])] + widen(1, (2,), S) + column_read + widen(1, (3,), S)
+            + z[0, 0] + [stage(S, "g", 0, 0, first=1), stage(S, "w", 3, 0)] + e_reads[0] + pw["g", 0, 1] + [stage(S, "w", 4, 0)] + z[0, 1] + [stage_h(S, 0, 0)] + e_reads[1] + v_scalar[0, 0]
+            + z[3, 0] + [stage(S, "w", 5, 1, last=1), stage_v(S, 0, 0)] + v_scalar[0, 1] + v_scalar[1, 1] + z[3, 1][:3] + [stage_v(S, 1, 1, first=3)] + z[3, 1][3:] + [stage_h(S, 1, 0, last=2, banks_read=2)] + z[4, 1]
         )
-        for h in range(2):
-            scalar_lane += classes[h][:3] + turned[h, 0] + classes[h][3:] + turned[h, 1]
+        scalar_lane += classes[0][:5] + [stage_h(S, 1, 1, last=2, banks_read=2)] + turned[0, 0][:3] + classes[0][5:] + turned[0, 0][3:] + turned[0, 1] + classes[1] + turned[1, 0]
         tensor_lane = feeds(
-            x_reads[0] + x_reads[1][:2] + z[0, 0][:1] + column_read + z[0, 0][1:2] + x_reads[1][2:3] + z[0, 0][2:3] + x_reads[1][3:] + z[0, 0][3:]
-            + z[1, 0] + e_reads[0] + e_reads[1] + z[0, 1][:2] + v_vector[0, 0] + z[0, 1][2:] + z[1, 1][:3] + v_scalar[0] + z[1, 1][3:]
-            + alternate(z[2, 0], v_scalar[1]) + z[2, 1] + alternate(z[3, 0], v_vector[0, 1]) + v_vector[1, 1][:2] + z[3, 1] + v_vector[1, 1][2:] + z[4, 0] + z[4, 1]
-            + z[5, 0] + z[5, 1]
-            + classes[0][:2] + scaled[:1] + classes[0][2:3] + turned[0, 0] + classes[0][3:] + scaled[1:3] + turned[0, 1] + scaled[3:4]
-            + classes[1][:2] + scaled[4:5] + classes[1][2:3] + turned[1, 0] + scaled[5:6] + classes[1][3:] + scaled[6:] + turned[1, 1]
+            x_reads[0] + x_reads[1][:1] + pw["w", 0, 1] + pw["w", 1, 0] + pw["w", 1, 1] + x_reads[1][1:2] + z[0, 0][:1] + column_read + z[0, 0][1:3] + x_reads[1][2:3] + z[0, 0][3:] + x_reads[1][3:]
+            + z[1, 0] + e_reads[0] + pw["g", 0, 1] + z[2, 0] + z[0, 1][:2] + v_vector[0, 0] + z[0, 1][2:] + z[1, 1] + e_reads[1] + v_scalar[0, 0] + z[2, 1]
+            + z[3, 0] + alternate(v_vector[1, 0], v_scalar[0, 1]) + z[4, 0] + v_scalar[1, 1] + z[3, 1][:3] + z[5, 0][:2] + z[3, 1][3:] + z[5, 0][2:] + z[4, 1]
+            + z[5, 1][:3] + classes[0][:2] + z[5, 1][3:] + classes[0][2:5] + turned[0, 0][:3] + classes[0][5:] + scaled[:2] + turned[0, 0][3:] + early(scaled[2:4]) + turned[0, 1]
+            + scaled[2:3] + classes[1][:2] + scaled[3:4] + classes[1][2:] + scaled[4:6] + turned[1, 0]
         )
 
         make_identity(nc, ident[:])
@@ -455,15 +506,20 @@ def tile_maxout_generated_head_f5_kernel(tc, x_bytes, x_scale, w, b, e, g, a, r,
         nc.scalar.activation(out=ident_bf[:], in_=ident[:], func=IDENTITY)
 
         lanes = [sync_lane, tensor_lane, vector_lane, scalar_lane, gpsimd_lane]
+        lenders = {"raw": raws, "vector": banks["vector"], "scalar": banks["scalar"], None: [None]}
         made = set()
         while any(lanes):
             fresh = []
+            moved = False
             for lane in lanes:
                 allowed = len(lane) if lane is sync_lane or lane is tensor_lane else 1
-                while allowed and lane and all(name in made for name in lane[0][2]) and (lane is not tensor_lane or next_bank_is_free()):
-                    call, makes = lane.pop(0)[:2]
+                while allowed and lane and all(name in made for name in lane[0][2]) and lenders[lane[0][5]]:
+                    call, makes, needs, feed, feed_needs, lender = lane.pop(0)
+                    reader_of["now"] = lender
                     call[0](*call[1:])
                     fresh.extend(makes)
                     allowed = allowed - 1
+                    moved = True
+            assert moved, [lane[0][0][1:] for lane in lanes if lane]
             for name in fresh:
                 made.add(name)

@@ -26,12 +26,12 @@ SHARED_LONG, SHARED_SHORT, SHARED_H = 2, 3, 1
 STORED_BETWEEN = (1, 2)
 
 ASIDE = ((4, 1),)
-PASSED = (("w", 0, 1, 0, 2), ("w", 1, 0, 0, 4), ("w", 1, 1, 0, 4), ("g", 0, 1, 0, 4))
-V_BLOCKS = {(0, 0): 2, (1, 0): 4, (0, 1): 0, (1, 1): 0}
+PASSED = (("w", 1, 0, 0, 4), ("w", 1, 1, 2, 4), ("g", 0, 1, 0, 4))
+V_BLOCKS = {(0, 0): 4, (1, 0): 4, (0, 1): 0, (1, 1): 0}
 TURNED = (6, 4)
 DIRECT = [(0, 0, True), (0, 1, True)] + [(1, j, False) for j in range(4)]
 ON_GPSIMD = ()
-EARLY = [(1, 0, False), (1, 1, False)]
+EARLY = [(0, 0), (0, 1), (0, 2), (0, 3), (1, 0), (1, 1), (1, 0, False), (1, 1, False)]
 
 
 def tile_maxout_generated_head_f5_kernel(tc, x_bytes, x_scale, w, b, e, g, a, r, d, out):
@@ -203,8 +203,9 @@ def tile_maxout_generated_head_f5_kernel(tc, x_bytes, x_scale, w, b, e, g, a, r,
             bank = fill(("pass bank", key, j))[:].bitcast(BF16)
             raw = give(raws, ("raw",) + key) if j else held[("raw",) + key]
             for n in range(2):
-                source = raw[:].rearrange("p s (B t i) -> p t B i s", t=4, i=RUN)[:, 2 * j + n]
-                nc.tensor.matmul(bank[:, block(n, 512)], lhsT=ident_bf[:], rhs=source, start=True, stop=True)
+                source = raw[:].rearrange("p s (B t i) -> p t B s i", t=4, i=RUN)[:, 2 * j + n]
+                target = bank[:, block(n, 512)].rearrange("p (B i s) -> p B s i", i=RUN, s=4)
+                nc.tensor.matmul(target, lhsT=ident_bf[:], rhs=source, start=True, stop=True)
 
         def passed_read(key, j):
             if key not in held:
@@ -245,7 +246,7 @@ def tile_maxout_generated_head_f5_kernel(tc, x_bytes, x_scale, w, b, e, g, a, r,
             merged = take(planes, ("max", c, h))
             aside = held.pop(("aside", c, h))
             nc.vector.tensor_tensor(out=merged[:], in0=aside[:], in1=give(planes, ("max", c - 1, h))[:], op=MAX)
-            held[heir] = aside[:].rearrange("p t c -> p (t c)")
+            planes.append(aside)
 
         def v_four_slots(q, n, j):
             bank = fill(("v bank", q, n, j))
@@ -465,40 +466,40 @@ def tile_maxout_generated_head_f5_kernel(tc, x_bytes, x_scale, w, b, e, g, a, r,
         pw = {key[:3]: passed(*key[:3], first=key[3], last=key[4]) for key in PASSED}
         sync_lane = (
             [load_x(0, 0), step(load, xs[:], x_scale.rearrange("o (q p t) -> p (o q) t", q=2, t=4)), load_x(0, 1)]
-            + loads_w(0)[:1] + [load_x(1, 0)] + loads_w(0)[1:] + loads_w(1) + [load_x(1, 1)] + small_loads + loads_w(2) + [load_g(0)] + loads_w(3)[:1] + [load_e(0), load_g(1)] + loads_w(3)[1:] + loads_w(4) + [load_e(1)] + loads_w(5)
+            + loads_w(0)[:1] + [load_x(1, 0)] + loads_w(0)[1:] + loads_w(1)[:1] + [load_x(1, 1)] + loads_w(1)[1:] + small_loads + loads_w(2) + [load_g(0)] + loads_w(3)[:1] + [load_e(0), load_g(1)] + loads_w(3)[1:] + loads_w(4) + [load_e(1)] + loads_w(5)
             + [step(load, r_all[:], r[512:C].partition_broadcast(P)), step(load, d_all[:], d[512:C].partition_broadcast(P), makes=["r and d"])]
         )
         direct_stores = [step(direct_store, key, needs=[("direct", key)]) for key in DIRECT]
         pairs = {(h, m): [step(turned_store, h, m, j, needs=[("turned", h, m, j)]) for j in range(len(turned[h, m]))] for h, m in turned}
-        sync_lane += pairs[0, 0] + direct_stores[:1] + pairs[0, 1] + direct_stores[1:4] + pairs[1, 0][:2] + direct_stores[4:5] + pairs[1, 0][2:3] + direct_stores[5:] + pairs[1, 0][3:]
+        sync_lane += pairs[0, 0] + pairs[0, 1][:1] + direct_stores[:1] + pairs[0, 1][1:] + direct_stores[1:4] + pairs[1, 0][:2] + direct_stores[4:5] + pairs[1, 0][2:3] + direct_stores[5:] + pairs[1, 0][3:]
 
         vector_lane = (
             widen(0, (0, 1, 2), V) + x_reads[0]
-            + [quant_x(0, 0), quant("w", 0, 0), quant_x(0, 1), quant("w", 0, 1), quant("w", 1, 0), quant("w", 1, 1, heir=("w", 2, 0))]
-            + x_reads[1] + z[1, 0] + [quant("w", 2, 0), quant("w", 2, 1), quant_x(1, 0), quant_x(1, 1), quant("g", 0, 0, heir=("w", 3, 1)), quant("e", 0, 0)]
+            + [quant_x(0, 0), quant("w", 0, 0), quant_x(0, 1), quant("w", 0, 1), quant("w", 1, 0, heir=("w", 1, 1))]
+            + x_reads[1][:2] + [quant("w", 1, 1, heir=("w", 2, 1))] + x_reads[1][2:] + z[1, 0] + [quant("w", 2, 0), quant("w", 2, 1), quant_x(1, 0), quant("g", 0, 0), quant("e", 0, 0, heir=("w", 3, 1)), quant_x(1, 1)]
             + z[2, 0] + v_vector[0, 0] + z[1, 1] + [quant("w", 3, 0), quant("w", 3, 1), quant("g", 0, 1), quant("w", 4, 0), quant("e", 0, 1, heir=("w", 5, 0)), quant("w", 4, 1)]
             + z[2, 1] + v_vector[1, 0] + [quant("w", 5, 0), quant("w", 5, 1), quant("v", 0, 0), quant("h", 0, 0, heir=("v", 0, 1)), quant("v", 1, 0)]
-            + z[4, 0] + z[5, 0] + [stage_h(V, 1, 0, first=2), quant("v", 0, 1), quant("h", 1, 0), merge(4, 1, ("h", 0, 1)), quant("v", 1, 1)] + z[5, 1]
-            + [stage_h(V, 1, 1, first=2), quant("h", 0, 1), quant("h", 1, 1)]
-            + scaled[:1] + alternate(scaled[1:], shifted[:-1]) + shifted[-1:]
+            + z[4, 0] + z[5, 0] + [h_halves[0], stage_h(V, 1, 0, first=2), quant("v", 0, 1), h_halves[1], merge(4, 1, None), quant("v", 1, 1), quant("h", 0, 1)] + z[5, 1]
+            + [scaled[0], stage_h(V, 1, 1, first=2), scaled[1], quant("h", 1, 1)]
+            + shifted[:2] + scaled[2:4] + shifted[2:4] + scaled[4:] + shifted[4:]
         )
         gpsimd_lane = [stage(G, "w", 0, 0), stage(G, "w", 0, 1, first=2),
-            stage(G, "w", 2, 0, inherited=True), stage(G, "w", 2, 1), stage(G, "g", 0, 0, last=1),
-            stage(G, "w", 3, 1, inherited=True), stage(G, "w", 4, 1),
+            stage(G, "w", 1, 1, last=2, inherited=True), stage(G, "w", 2, 1, inherited=True), stage(G, "w", 2, 0, last=2),
+            stage(G, "w", 3, 1, inherited=True), stage(G, "w", 4, 1), stage(G, "w", 4, 0, last=2),
             stage(G, "w", 5, 0, inherited=True), stage(G, "w", 5, 1, first=1),
-            stage_v(G, 0, 1, inherited=True), stage_v(G, 1, 1, last=3), stage_h(G, 0, 1, inherited=True)]
+            stage_v(G, 0, 1, inherited=True), stage_v(G, 1, 1, last=3), stage_h(G, 1, 1, last=2, banks_read=2)]
         scalar_lane = (
-            widen(0, (3,), S) + widen(1, (0, 1), S) + pw["w", 0, 1] + pw["w", 1, 0] + pw["w", 1, 1] + [step(permute_rows, makes=["rows"], needs=[("row", ROW_D)])] + widen(1, (2,), S) + column_read + widen(1, (3,), S)
-            + z[0, 0] + [stage(S, "g", 0, 0, first=1), stage(S, "w", 3, 0)] + e_reads[0] + pw["g", 0, 1] + [stage(S, "w", 4, 0)] + z[0, 1] + [stage_h(S, 0, 0)] + e_reads[1] + v_scalar[0, 0]
-            + z[3, 0] + [stage(S, "w", 5, 1, last=1), stage_v(S, 0, 0)] + v_scalar[0, 1] + v_scalar[1, 1] + z[3, 1][:3] + [stage_v(S, 1, 1, first=3)] + z[3, 1][3:] + [stage_h(S, 1, 0, last=2, banks_read=2)] + z[4, 1]
+            widen(0, (3,), S) + widen(1, (0, 1), S) + [stage(S, "w", 0, 1, last=2)] + widen(1, (2,), S) + pw["w", 1, 0] + [step(permute_rows, makes=["rows"], needs=[("row", ROW_D)])] + widen(1, (3,), S) + pw["w", 1, 1] + column_read
+            + z[0, 0] + [stage(S, "w", 2, 0, first=2), stage(S, "g", 0, 0)] + e_reads[0] + [stage(S, "w", 3, 0)] + pw["g", 0, 1] + z[0, 1] + [stage(S, "w", 4, 0, first=2), stage_h(S, 0, 0)] + e_reads[1] + [stage(S, "w", 5, 1, last=1)]
+            + z[3, 0] + z[3, 1] + v_scalar[0, 1] + [stage_h(S, 0, 1, last=2)] + v_scalar[1, 1] + z[4, 1][:1] + [stage_v(S, 1, 1, first=3)] + z[4, 1][1:2] + [stage_h(S, 1, 0, last=2, banks_read=2)] + z[4, 1][2:] + [stage_h(S, 0, 1, first=2)]
         )
-        scalar_lane += classes[0][:5] + [stage_h(S, 1, 1, last=2, banks_read=2)] + turned[0, 0][:3] + classes[0][5:] + turned[0, 0][3:] + turned[0, 1] + classes[1] + turned[1, 0]
+        scalar_lane += classes[0] + turned[0, 0] + turned[0, 1] + classes[1] + turned[1, 0]
         tensor_lane = feeds(
-            x_reads[0] + x_reads[1][:1] + pw["w", 0, 1] + pw["w", 1, 0] + pw["w", 1, 1] + x_reads[1][1:2] + z[0, 0][:1] + column_read + z[0, 0][1:3] + x_reads[1][2:3] + z[0, 0][3:] + x_reads[1][3:]
-            + z[1, 0] + e_reads[0] + pw["g", 0, 1] + z[2, 0] + z[0, 1][:2] + v_vector[0, 0] + z[0, 1][2:] + z[1, 1] + e_reads[1] + v_scalar[0, 0] + z[2, 1]
-            + z[3, 0] + alternate(v_vector[1, 0], v_scalar[0, 1]) + z[4, 0] + v_scalar[1, 1] + z[3, 1][:3] + z[5, 0][:2] + z[3, 1][3:] + z[5, 0][2:] + z[4, 1]
-            + z[5, 1][:3] + classes[0][:2] + z[5, 1][3:] + classes[0][2:5] + turned[0, 0][:3] + classes[0][5:] + scaled[:2] + turned[0, 0][3:] + early(scaled[2:4]) + turned[0, 1]
-            + scaled[2:3] + classes[1][:2] + scaled[3:4] + classes[1][2:] + scaled[4:6] + turned[1, 0]
+            x_reads[0] + x_reads[1][:2] + pw["w", 1, 0] + pw["w", 1, 1] + column_read + z[0, 0][:1] + x_reads[1][2:] + z[0, 0][1:]
+            + z[1, 0] + e_reads[0] + pw["g", 0, 1] + z[2, 0] + z[0, 1][:2] + v_vector[0, 0][:2] + z[0, 1][2:] + v_vector[0, 0][2:] + z[1, 1] + e_reads[1] + z[2, 1]
+            + z[3, 0] + z[3, 1][:2] + v_vector[1, 0][:2] + z[3, 1][2:] + v_vector[1, 0][2:] + v_scalar[0, 1] + z[4, 0] + v_scalar[1, 1] + z[4, 1][:1] + z[5, 0][:2] + z[4, 1][1:2] + z[5, 0][2:] + z[4, 1][2:]
+            + z[5, 1][:2] + early(classes[0][:4]) + z[5, 1][2:3] + classes[0][:4] + z[5, 1][3:] + classes[0][4:] + scaled[:1] + turned[0, 0] + scaled[1:2] + early(scaled[2:4]) + turned[0, 1]
+            + early(classes[1][:2]) + classes[1][:2] + scaled[2:4] + classes[1][2:] + scaled[4:] + turned[1, 0]
         )
 
         make_identity(nc, ident[:])

@@ -26,12 +26,12 @@ SHARED_LONG, SHARED_SHORT, SHARED_H = 2, 3, 1
 STORED_BETWEEN = (1, 2)
 
 ASIDE = ((4, 1),)
-PASSED = (("w", 1, 0, 0, 4), ("w", 1, 1, 2, 4), ("g", 0, 1, 0, 4))
+PASSED = (("w", 1, 0, 2, 4), ("w", 1, 1, 2, 4), ("g", 0, 1, 0, 2))
 V_BLOCKS = {(0, 0): 4, (1, 0): 4, (0, 1): 0, (1, 1): 0}
 TURNED = (6, 4)
 DIRECT = [(0, 0, True), (0, 1, True)] + [(1, j, False) for j in range(4)]
 ON_GPSIMD = ()
-EARLY = [(0, 0), (0, 1), (0, 2), (0, 3), (1, 0), (1, 1), (1, 0, False), (1, 1, False)]
+EARLY = [(0, 0), (0, 1), (0, 2), (0, 3), (1, 0), (1, 1), (1, 0, False), (1, 1, False), (1, 2, False), (1, 3, False)]
 
 
 def tile_maxout_generated_head_f5_kernel(tc, x_bytes, x_scale, w, b, e, g, a, r, d, out):
@@ -466,7 +466,7 @@ def tile_maxout_generated_head_f5_kernel(tc, x_bytes, x_scale, w, b, e, g, a, r,
         pw = {key[:3]: passed(*key[:3], first=key[3], last=key[4]) for key in PASSED}
         sync_lane = (
             [load_x(0, 0), step(load, xs[:], x_scale.rearrange("o (q p t) -> p (o q) t", q=2, t=4)), load_x(0, 1)]
-            + loads_w(0)[:1] + [load_x(1, 0)] + loads_w(0)[1:] + loads_w(1)[:1] + [load_x(1, 1)] + loads_w(1)[1:] + small_loads + loads_w(2) + [load_g(0)] + loads_w(3)[:1] + [load_e(0), load_g(1)] + loads_w(3)[1:] + loads_w(4) + [load_e(1)] + loads_w(5)
+            + loads_w(0)[:1] + [load_x(1, 0)] + loads_w(0)[1:] + loads_w(1)[:1] + [load_x(1, 1)] + loads_w(1)[1:] + small_loads + loads_w(2) + [load_g(0), load_e(0), load_g(1)] + loads_w(3) + loads_w(4) + [load_e(1)] + loads_w(5)
             + [step(load, r_all[:], r[512:C].partition_broadcast(P)), step(load, d_all[:], d[512:C].partition_broadcast(P), makes=["r and d"])]
         )
         direct_stores = [step(direct_store, key, needs=[("direct", key)]) for key in DIRECT]
@@ -479,27 +479,27 @@ def tile_maxout_generated_head_f5_kernel(tc, x_bytes, x_scale, w, b, e, g, a, r,
             + x_reads[1][:2] + [quant("w", 1, 1, heir=("w", 2, 1))] + x_reads[1][2:] + z[1, 0] + [quant("w", 2, 0), quant("w", 2, 1), quant_x(1, 0), quant("g", 0, 0), quant("e", 0, 0, heir=("w", 3, 1)), quant_x(1, 1)]
             + z[2, 0] + v_vector[0, 0] + z[1, 1] + [quant("w", 3, 0), quant("w", 3, 1), quant("g", 0, 1), quant("w", 4, 0), quant("e", 0, 1, heir=("w", 5, 0)), quant("w", 4, 1)]
             + z[2, 1] + v_vector[1, 0] + [quant("w", 5, 0), quant("w", 5, 1), quant("v", 0, 0), quant("h", 0, 0, heir=("v", 0, 1)), quant("v", 1, 0)]
-            + z[4, 0] + z[5, 0] + [h_halves[0], stage_h(V, 1, 0, first=2), quant("v", 0, 1), h_halves[1], merge(4, 1, None), quant("v", 1, 1), quant("h", 0, 1)] + z[5, 1]
+            + z[4, 0] + z[5, 0] + [h_halves[0], stage_h(V, 1, 0, first=2), quant("v", 0, 1), h_halves[1], merge(4, 1, None), quant("v", 1, 1)] + z[5, 1][:2] + [quant("h", 0, 1, heir=("h", 1, 1))] + z[5, 1][2:]
             + [scaled[0], stage_h(V, 1, 1, first=2), scaled[1], quant("h", 1, 1)]
             + shifted[:2] + scaled[2:4] + shifted[2:4] + scaled[4:] + shifted[4:]
         )
         gpsimd_lane = [stage(G, "w", 0, 0), stage(G, "w", 0, 1, first=2),
-            stage(G, "w", 1, 1, last=2, inherited=True), stage(G, "w", 2, 1, inherited=True), stage(G, "w", 2, 0, last=2),
+            stage(G, "w", 1, 1, last=2, inherited=True), stage(G, "w", 2, 1, inherited=True), stage(G, "w", 2, 0, last=1),
             stage(G, "w", 3, 1, inherited=True), stage(G, "w", 4, 1), stage(G, "w", 4, 0, last=2),
-            stage(G, "w", 5, 0, inherited=True), stage(G, "w", 5, 1, first=1),
-            stage_v(G, 0, 1, inherited=True), stage_v(G, 1, 1, last=3), stage_h(G, 1, 1, last=2, banks_read=2)]
+            stage(G, "w", 5, 0, inherited=True), stage(G, "w", 5, 1, first=2),
+            stage_v(G, 0, 1, inherited=True), stage_v(G, 1, 1, last=3), stage_h(G, 1, 1, last=2, banks_read=2, inherited=True)]
         scalar_lane = (
-            widen(0, (3,), S) + widen(1, (0, 1), S) + [stage(S, "w", 0, 1, last=2)] + widen(1, (2,), S) + pw["w", 1, 0] + [step(permute_rows, makes=["rows"], needs=[("row", ROW_D)])] + widen(1, (3,), S) + pw["w", 1, 1] + column_read
-            + z[0, 0] + [stage(S, "w", 2, 0, first=2), stage(S, "g", 0, 0)] + e_reads[0] + [stage(S, "w", 3, 0)] + pw["g", 0, 1] + z[0, 1] + [stage(S, "w", 4, 0, first=2), stage_h(S, 0, 0)] + e_reads[1] + [stage(S, "w", 5, 1, last=1)]
-            + z[3, 0] + z[3, 1] + v_scalar[0, 1] + [stage_h(S, 0, 1, last=2)] + v_scalar[1, 1] + z[4, 1][:1] + [stage_v(S, 1, 1, first=3)] + z[4, 1][1:2] + [stage_h(S, 1, 0, last=2, banks_read=2)] + z[4, 1][2:] + [stage_h(S, 0, 1, first=2)]
+            widen(0, (3,), S) + widen(1, (0, 1), S) + [stage(S, "w", 0, 1, last=2), stage(S, "w", 1, 0, last=2)] + pw["w", 1, 0] + widen(1, (2,), S) + [step(permute_rows, makes=["rows"], needs=[("row", ROW_D)])] + widen(1, (3,), S) + pw["w", 1, 1] + column_read
+            + z[0, 0] + [stage(S, "w", 2, 0, first=1), stage(S, "g", 0, 0)] + e_reads[0] + [stage(S, "w", 3, 0)] + pw["g", 0, 1] + z[0, 1][:2] + [stage(S, "g", 0, 1, first=2)] + z[0, 1][2:] + [stage(S, "w", 4, 0, first=2)] + e_reads[1] + [stage_h(S, 0, 0)]
+            + z[3, 0] + [stage(S, "w", 5, 1, last=2)] + z[3, 1] + v_scalar[0, 1] + v_scalar[1, 1] + z[4, 1][:2] + [stage_v(S, 1, 1, first=3)] + [stage_h(S, 1, 0, last=2, banks_read=2)] + z[4, 1][2:] + [stage_h(S, 0, 1)]
         )
         scalar_lane += classes[0] + turned[0, 0] + turned[0, 1] + classes[1] + turned[1, 0]
         tensor_lane = feeds(
-            x_reads[0] + x_reads[1][:2] + pw["w", 1, 0] + pw["w", 1, 1] + column_read + z[0, 0][:1] + x_reads[1][2:] + z[0, 0][1:]
+            x_reads[0] + x_reads[1][:2] + pw["w", 1, 0] + pw["w", 1, 1] + z[0, 0][:1] + column_read + z[0, 0][1:2] + x_reads[1][2:] + z[0, 0][2:]
             + z[1, 0] + e_reads[0] + pw["g", 0, 1] + z[2, 0] + z[0, 1][:2] + v_vector[0, 0][:2] + z[0, 1][2:] + v_vector[0, 0][2:] + z[1, 1] + e_reads[1] + z[2, 1]
-            + z[3, 0] + z[3, 1][:2] + v_vector[1, 0][:2] + z[3, 1][2:] + v_vector[1, 0][2:] + v_scalar[0, 1] + z[4, 0] + v_scalar[1, 1] + z[4, 1][:1] + z[5, 0][:2] + z[4, 1][1:2] + z[5, 0][2:] + z[4, 1][2:]
-            + z[5, 1][:2] + early(classes[0][:4]) + z[5, 1][2:3] + classes[0][:4] + z[5, 1][3:] + classes[0][4:] + scaled[:1] + turned[0, 0] + scaled[1:2] + early(scaled[2:4]) + turned[0, 1]
-            + early(classes[1][:2]) + classes[1][:2] + scaled[2:4] + classes[1][2:] + scaled[4:] + turned[1, 0]
+            + z[3, 0] + z[3, 1][:2] + v_vector[1, 0][:2] + z[3, 1][2:] + v_vector[1, 0][2:] + v_scalar[0, 1][:2] + z[4, 0][:2] + v_scalar[0, 1][2:] + z[4, 0][2:] + v_scalar[1, 1] + z[4, 1][:2] + z[5, 0] + z[4, 1][2:]
+            + z[5, 1][:2] + early(classes[0][:4]) + z[5, 1][2:] + classes[0] + scaled[:1] + turned[0, 0][:2] + scaled[1:2] + turned[0, 0][2:]
+            + early(scaled[2:4]) + turned[0, 1] + early(classes[1][:2]) + early(scaled[4:]) + alternate(classes[1][:2], scaled[2:4]) + classes[1][2:] + scaled[4:] + turned[1, 0]
         )
 
         make_identity(nc, ident[:])

@@ -19,19 +19,9 @@ MAX = mybir.AluOpType.max
 IDENTITY = mybir.ActivationFunctionType.Identity
 
 RUN = 8
-BANKS = {"vector": 4, "scalar": 4}
 WHOLE = slice(0, 512)
 ROW_A, ROW_R, ROW_D, ROWS = 6, 8, 10, 12
-SHARED_LONG, SHARED_SHORT, SHARED_H = 2, 3, 1
-STORED_BETWEEN = (1, 2)
-
-ASIDE = ((4, 1),)
-PASSED = (("w", 1, 0, 2, 4), ("w", 1, 1, 2, 4), ("g", 0, 1, 0, 2))
-V_BLOCKS = {(0, 0): 4, (1, 0): 4, (0, 1): 0, (1, 1): 0}
-TURNED = (6, 4)
-DIRECT = [(0, 0, True), (0, 1, True)] + [(1, j, False) for j in range(4)]
-ON_GPSIMD = ()
-EARLY = [(0, 0), (0, 1), (0, 2), (0, 3), (1, 0), (1, 1), (1, 0, False), (1, 1, False), (1, 2, False), (1, 3, False)]
+TURNED = ((0, 0), (1, 0), (0, 1), (2, 0), (3, 0))
 
 
 def tile_maxout_generated_head_f5_kernel(tc, x_bytes, x_scale, w, b, e, g, a, r, d, out):
@@ -47,7 +37,7 @@ def tile_maxout_generated_head_f5_kernel(tc, x_bytes, x_scale, w, b, e, g, a, r,
         def operand(name):
             return kept(name + "_codes", [P, 512], U32), kept(name + "_scales", [P, 512], U8)
 
-        banks = {reader: [psum.tile([P, 512], F32, name=f"bank_{reader}{n}") for n in range(count)] for reader, count in BANKS.items()}
+        banks = [[psum.tile([P, 512], F32, name=f"bank_{reader}{n}") for n in range(4)] for reader in ("vector", "scalar")]
         staged = [kept(f"staged{n}", [P, 2048], BF16) for n in range(9)]
         wide = [kept(f"x_wide{n}", [P, K], BF16) for n in range(4)]
         results = [kept(f"result{n}", [P, 512], F32) for n in range(10)]
@@ -55,7 +45,7 @@ def tile_maxout_generated_head_f5_kernel(tc, x_bytes, x_scale, w, b, e, g, a, r,
         raws = [kept(f"raw{n}", [P, 4, 512], BF16) for n in range(9)]
         planes = [kept(f"plane{n}", [P, 4, 512], BF16) for n in range(8)]
         held = {}
-        reader_of = {}
+        owner = {}
 
         def take(free, key):
             held[key] = free.pop(0)
@@ -65,11 +55,12 @@ def tile_maxout_generated_head_f5_kernel(tc, x_bytes, x_scale, w, b, e, g, a, r,
             free.append(held[key])
             return held.pop(key)
 
-        def fill(key):
-            return take(banks[reader_of["now"]], key)
+        def fill(free, key):
+            owner[key] = free
+            return take(free, key)
 
-        def drain(key, reader):
-            return give(banks[reader], key)
+        def drain(key):
+            return give(owner.pop(key), key)
 
         x_raw = [[kept(f"x_raw{h}_{j}", [P, 2, K], U8) for j in range(2)] for h in range(2)]
         e_raw = [kept(f"e_raw{n}", [P, 4, D], BF16) for n in range(2)]
@@ -93,6 +84,8 @@ def tile_maxout_generated_head_f5_kernel(tc, x_bytes, x_scale, w, b, e, g, a, r,
 
         def block(n, width=P):
             return slice(n * width, (n + 1) * width)
+
+        V, S, G = nc.vector, nc.scalar, nc.gpsimd
 
         def load(tile, source):
             nc.sync.dma_start(out=tile, in_=source)
@@ -134,21 +127,24 @@ def tile_maxout_generated_head_f5_kernel(tc, x_bytes, x_scale, w, b, e, g, a, r,
             quantize(key, give(staged, key) if part else held[key], block(part, 256))
 
         def permute_rows():
-            copy(nc.scalar, rows[0:ROW_R, :].rearrange("p (t B i) -> p t B i", t=4, i=RUN), rows_raw[:].rearrange("p (B t i) -> p t B i", t=4, i=RUN))
+            nc.scalar.copy(
+                out=rows[0:ROW_R, :].rearrange("p (t B i) -> p t B i", t=4, i=RUN),
+                in_=rows_raw[:].rearrange("p (B t i) -> p t B i", t=4, i=RUN),
+            )
 
-        def columns_product():
-            bank = fill("columns")
+        def columns_product(free):
+            bank = fill(free, "columns")
             for t in range(4):
                 nc.tensor.matmul(bank[:, 16 * t : 16 * t + ROWS], lhsT=rows[:, block(t)], rhs=ident_bf[:, 0:ROWS], start=True, stop=True)
 
         def columns_read():
-            nc.scalar.copy(out=columns[:], in_=drain("columns", "scalar")[:, 0:64].rearrange("p (t j) -> p j t", t=4)[:, 0:ROWS, :])
+            nc.scalar.copy(out=columns[:], in_=drain("columns")[:, 0:64].rearrange("p (t j) -> p j t", t=4)[:, 0:ROWS, :])
 
         def x_widen(h, i, engine):
             copy(engine, wide[i][:], x_raw[h][i // 2][:, i % 2, :].bitcast(FP8))
 
-        def x_turn(h, i):
-            bank = fill(("x bank", h, i))
+        def x_turn(free, h, i):
+            bank = fill(free, ("x bank", h, i))
             words = wide[i][:].bitcast(F32)
             for q in range(2):
                 for u in range(2):
@@ -157,36 +153,35 @@ def tile_maxout_generated_head_f5_kernel(tc, x_bytes, x_scale, w, b, e, g, a, r,
         def x_read(h, i):
             nc.vector.tensor_tensor(
                 out=x_staged[:, :, block(i, 512)].rearrange("p q (r u e) -> p q r u e", u=2, e=2),
-                in0=drain(("x bank", h, i), "vector")[:].bitcast(BF16).rearrange("p (u q r e) -> p q r u e", u=2, q=2, e=2),
+                in0=drain(("x bank", h, i))[:].bitcast(BF16).rearrange("p (u q r e) -> p q r u e", u=2, q=2, e=2),
                 in1=xs[:].rearrange("p q (o u e) -> p q o u e", o=1, u=2).to_broadcast([P, 2, P, 2, 2]),
                 op=MULT,
             )
 
-        def e_turn(n, j):
-            bank = fill(("e bank", n, j))
+        def e_turn(free, n, j):
+            bank = fill(free, ("e bank", n, j))
             for i in range(2):
                 words = e_raw[n][:, 2 * j + i, :].bitcast(F32)
                 for u in range(2):
                     nc.tensor.transpose(bank[:, block(2 * i + u)], words[:, u:256:2], ident[:])
 
-        def e_read(n, j):
+        def e_read(n, j, engine):
             if j == 0:
                 take(staged, ("e", 0, n))
-            nc.scalar.copy(
-                out=held["e", 0, n][:].bitcast(F32)[:, block(j, 512)].rearrange("p (i r u) -> p i r u", i=2, u=2),
-                in_=drain(("e bank", n, j), "scalar")[:].rearrange("p (i u r) -> p i r u", i=2, u=2),
+            copy(
+                engine,
+                held["e", 0, n][:].bitcast(F32)[:, block(j, 512)].rearrange("p (i r u) -> p i r u", i=2, u=2),
+                drain(("e bank", n, j))[:].rearrange("p (i u r) -> p i r u", i=2, u=2),
             )
 
         def stage_raw(key, first, last, engine):
             if key not in held:
                 take(staged, key)
             raw = give(raws, ("raw",) + key) if last == 4 else held[("raw",) + key]
-            walk = "p t B s i" if engine is nc.scalar else "p t B i s"
-            source = raw[:].rearrange(f"p s (B t i) -> {walk}", t=4, i=RUN)[:, first:last]
-            target = held[key][:].rearrange(f"p (t B i s) -> {walk}", t=4, i=RUN, s=4)[:, first:last]
-            if engine is nc.gpsimd:
-                source, target = [side.rearrange("p t B i s -> p B t i s") for side in (source, target)]
-            copy(engine, target, source)
+            walk = "p t B s i" if engine is nc.scalar else "p B t i s"
+            share = (slice(0, P), slice(first, last)) if engine is nc.scalar else (slice(0, P), slice(0, 16), slice(first, last))
+            source = raw[:].rearrange(f"p s (B t i) -> {walk}", t=4, i=RUN)[share]
+            copy(engine, held[key][:].rearrange(f"p (t B i s) -> {walk}", t=4, i=RUN, s=4)[share], source)
 
         def stage_plane(key, source, first, last, engine):
             if key not in held:
@@ -199,8 +194,8 @@ def tile_maxout_generated_head_f5_kernel(tc, x_bytes, x_scale, w, b, e, g, a, r,
                 plane[:, :, P * first : P * last].rearrange("p t (c i) -> p c t i", i=run),
             )
 
-        def pass_raw(key, j):
-            bank = fill(("pass bank", key, j))[:].bitcast(BF16)
+        def pass_raw(free, key, j):
+            bank = fill(free, ("pass bank", key))[:].bitcast(BF16)
             raw = give(raws, ("raw",) + key) if j else held[("raw",) + key]
             for n in range(2):
                 source = raw[:].rearrange("p s (B t i) -> p t B s i", t=4, i=RUN)[:, 2 * j + n]
@@ -210,15 +205,15 @@ def tile_maxout_generated_head_f5_kernel(tc, x_bytes, x_scale, w, b, e, g, a, r,
         def passed_read(key, j):
             if key not in held:
                 take(staged, key)
-            nc.scalar.copy(out=held[key][:].bitcast(F32)[:, block(j, 512)], in_=drain(("pass bank", key, j), "scalar")[:])
+            nc.scalar.copy(out=held[key][:].bitcast(F32)[:, block(j, 512)], in_=drain(("pass bank", key))[:])
 
         def z_parts(s, split):
             if split:
                 return [(2 * (s % 2) + n, block(s // 2, 256), block(n, 256)) for n in range(2)]
             return [(s, WHOLE, WHOLE)]
 
-        def z_product(c, h, s, split):
-            bank = fill(("z bank", c, h, s))
+        def z_product(free, c, h, s, split):
+            bank = fill(free, ("z bank", c, h, s))
             for t, samples, place in z_parts(s, split):
                 for q in range(2):
                     product(bank[:, place], ("w", c, q), block(t), ("x", h, q), samples, q == 0, q == 1)
@@ -229,10 +224,10 @@ def tile_maxout_generated_head_f5_kernel(tc, x_bytes, x_scale, w, b, e, g, a, r,
         def z_alone(c, h, t, name):
             if t == 0:
                 take(planes, (name, c, h))
-            nc.scalar.activation(out=held[name, c, h][:, t, :], in_=drain(("z bank", c, h, t), "scalar")[:], func=IDENTITY, bias=z_bias(c, t))
+            nc.scalar.activation(out=held[name, c, h][:, t, :], in_=drain(("z bank", c, h, t))[:], func=IDENTITY, bias=z_bias(c, t))
 
         def z_max(c, h, s, split):
-            bank = drain(("z bank", c, h, s), "vector")
+            bank = drain(("z bank", c, h, s))
             if s == 0:
                 take(planes, ("max", c, h))
             for t, samples, place in z_parts(s, split):
@@ -242,132 +237,90 @@ def tile_maxout_generated_head_f5_kernel(tc, x_bytes, x_scale, w, b, e, g, a, r,
             if s == 3:
                 give(planes, ("max", c - 1, h))
 
-        def z_merge(c, h, heir):
+        def z_merge(c, h):
             merged = take(planes, ("max", c, h))
-            aside = held.pop(("aside", c, h))
-            nc.vector.tensor_tensor(out=merged[:], in0=aside[:], in1=give(planes, ("max", c - 1, h))[:], op=MAX)
-            planes.append(aside)
+            before = give(planes, ("max", c - 1, h))
+            nc.vector.tensor_tensor(out=merged[:], in0=give(planes, ("aside", c, h))[:], in1=before[:], op=MAX)
 
-        def v_four_slots(q, n, j):
-            bank = fill(("v bank", q, n, j))
+        def v_four_slots(free, q, j):
+            bank = fill(free, ("v bank", q, j))
             for t in range(4):
-                product(bank[:, block(t)], ("g", 0, q), block(t), ("e", 0, n), block(j), True, True)
+                product(bank[:, block(t)], ("g", 0, q), block(t), ("e", 0, 0), block(j), True, True)
 
-        def v_read_staged(q, n, j):
+        def v_read_staged(q, j):
             if j == 0:
-                take(staged, ("v", q, n))
+                take(staged, ("v", q, 0))
             nc.vector.tensor_tensor(
-                out=held["v", q, n][:, block(j, 512)].rearrange("p (c t) -> p c t", t=4),
-                in0=drain(("v bank", q, n, j), "vector")[:].rearrange("p (t c) -> p c t", t=4),
+                out=held["v", q, 0][:, block(j, 512)].rearrange("p (c t) -> p c t", t=4),
+                in0=drain(("v bank", q, j))[:].rearrange("p (t c) -> p c t", t=4),
                 in1=columns[:, ROW_A + q : ROW_A + q + 1, :].to_broadcast([P, P, 4]),
                 op=ADD,
             )
 
-        def v_parts(s, paired):
-            if paired:
-                return [(2 * s + k, block(1, 256), block(k, 256)) for k in range(2)]
-            return [(s, WHOLE, WHOLE)]
+        def v_by_slot(free, q, t):
+            product(fill(free, ("v slot bank", q, t))[:], ("g", 0, q), block(t), ("e", 0, 1), WHOLE, True, True)
 
-        def v_by_slot(q, n, s, paired):
-            bank = fill(("v slot bank", q, n, s))
-            for t, classes, place in v_parts(s, paired):
-                product(bank[:, place], ("g", 0, q), block(t), ("e", 0, n), classes, True, True)
+        def v_read_plane(q, t):
+            if t == 0:
+                take(planes, ("v plane", q))
+            nc.scalar.activation(out=held["v plane", q][:, t, :], in_=drain(("v slot bank", q, t))[:], func=IDENTITY, bias=columns[:, ROW_A + q, t : t + 1])
 
-        def v_read_plane(q, n, s, paired):
-            if s == 0:
-                take(planes, ("v plane", q, n))
-            bank = drain(("v slot bank", q, n, s), "scalar")
-            for t, classes, place in v_parts(s, paired):
-                nc.scalar.activation(out=held["v plane", q, n][:, t, classes], in_=bank[:, place], func=IDENTITY, bias=columns[:, ROW_A + q, t : t + 1])
+        def direct_product(free, i):
+            bank = fill(free, ("direct bank", i))
+            for q in range(2):
+                product(bank[:], ("h", q, i // 4), block(i % 4), ("v", q, 1), WHOLE, q == 0, q == 1)
 
-        def direct_parts(key):
-            h, j, narrow = key
-            if narrow:
-                return [(2 * j + n, block(1, 256), block(n, 256)) for n in range(2)]
-            return [(j, WHOLE, WHOLE)]
+        def direct_scale(i):
+            nc.vector.tensor_tensor(out=take(results, ("direct", i))[:], in0=drain(("direct bank", i))[:], in1=r_all[:], op=MULT)
 
-        def spread(vector, key):
-            if key[2]:
-                return vector[:, block(1, 256)].rearrange("p (o c) -> p o c", o=1).to_broadcast([P, 2, 256])
-            return vector[:].rearrange("p (o c) -> p o c", o=1)
+        def direct_shift(i):
+            nc.vector.tensor_tensor(out=held["direct", i][:], in0=held["direct", i][:], in1=d_all[:], op=ADD)
 
-        def by_tile(tile, key):
-            return tile[:].rearrange("p (i c) -> p i c", i=2 if key[2] else 1)
+        def direct_store(i):
+            nc.sync.dma_start(out=out_rows[:, i, 512:C], in_=give(results, ("direct", i))[:])
 
-        def direct_product(key, passes):
-            bank = fill(("direct bank", key)) if 0 in passes else held["direct bank", key]
-            for i, classes, place in direct_parts(key):
-                for q in passes:
-                    product(bank[:, place], ("h", q, key[0]), block(i), ("v", q, 1), classes, q == 0, q == 1)
+        def class_product(free, group, n, m):
+            bank = fill(free, ("class bank", group, n, m))
+            for k in range(2):
+                for q in range(2):
+                    product(bank[:, block(k, 256)], ("v", q, n), block(2 * m + k), ("h", q, group // 2), block(group % 2, 256), q == 0, q == 1)
 
-        def direct_scale(key):
-            nc.vector.tensor_tensor(out=by_tile(take(results, ("direct", key)), key), in0=by_tile(drain(("direct bank", key), "vector"), key), in1=spread(r_all, key), op=MULT)
+        def class_read(group, n, m):
+            bank = drain(("class bank", group, n, m))
+            tile = take(by_class, ("by class", group, n, m))
+            for k in range(2):
+                column = slice(2 * m + k, 2 * m + k + 1)
+                nc.scalar.activation(out=tile[:, block(k, 256)], in_=bank[:, block(k, 256)], func=IDENTITY, scale=columns[:, ROW_R + n, column], bias=columns[:, ROW_D + n, column])
 
-        def direct_shift(key, engine):
-            tile = by_tile(held["direct", key], key)
-            engine.tensor_tensor(out=tile, in0=tile, in1=spread(d_all, key), op=ADD)
+        def turn_back(free, i, n):
+            bank = fill(free, ("turned bank", i, n))
+            for k in range(4):
+                nc.tensor.transpose(bank[:, block(k)], held["by class", i // 2, n, k // 2][:, block(2 * (k % 2) + i % 2)], ident[:])
+            if i % 2:
+                for m in range(2):
+                    give(by_class, ("by class", i // 2, n, m))
 
-        def direct_store(key):
-            h, j, narrow = key
-            rows_out = out_rows[:, 4 * h + 2 * j : 4 * h + 2 * j + 2, 768:C] if narrow else out_rows[:, 4 * h + j : 4 * h + j + 1, 512:C]
-            nc.sync.dma_start(out=rows_out, in_=by_tile(give(results, ("direct", key)), key))
+        def turned_read(i, n):
+            nc.scalar.copy(out=take(results, ("turned", i, n))[:], in_=drain(("turned bank", i, n))[:])
 
-        def class_product(h, n, passes):
-            bank = fill(("class bank", h, n)) if 0 in passes else held["class bank", h, n]
-            for q in passes:
-                product(bank[:], ("v", q, n // 4), block(n % 4), ("h", q, h), WHOLE, q == 0, q == 1)
+        def turned_store(i, n):
+            nc.sync.dma_start(out=out_rows[:, i, block(n, 512)], in_=give(results, ("turned", i, n))[:])
 
-        def class_read(h, n):
-            nc.scalar.activation(
-                out=take(by_class, ("by class", h, n))[:],
-                in_=drain(("class bank", h, n), "scalar")[:],
-                func=IDENTITY,
-                scale=columns[:, ROW_R + n // 4, n % 4 : n % 4 + 1],
-                bias=columns[:, ROW_D + n // 4, n % 4 : n % 4 + 1],
-            )
+        def step(*call, makes=(), needs=(), lender=None, feed=None):
+            return call, list(makes), list(needs), lender, feed
 
-        def turned_parts(m, j):
-            if m == 0:
-                return [(n, j, n) for n in range(4)]
-            return [(4 + n, 2 * j + i, 2 * i + n) for n in range(2) for i in range(2)]
-
-        def turn_back(h, m, j):
-            bank = fill(("turned bank", h, m, j))
-            for n, i, place in turned_parts(m, j):
-                nc.tensor.transpose(bank[:, block(place)], held["by class", h, n][:, block(i)], ident[:])
-            if j == (1 if m else 3):
-                for n in sorted(set(part[0] for part in turned_parts(m, j))):
-                    give(by_class, ("by class", h, n))
-
-        def turned_read(h, m, j):
-            nc.scalar.copy(out=take(results, ("turned", h, m, j))[:], in_=drain(("turned bank", h, m, j), "scalar")[:])
-
-        def turned_store(h, m, j):
-            tile = give(results, ("turned", h, m, j))
-            if m == 0:
-                nc.sync.dma_start(out=out_rows[:, 4 * h + j, 0:512], in_=tile[:])
-            else:
-                nc.sync.dma_start(out=out_rows[:, 4 * h + 2 * j : 4 * h + 2 * j + 2, 512:768], in_=tile[:].rearrange("p (i c) -> p i c", i=2))
-
-        def step(*call, makes=(), needs=(), feed=None, feed_needs=(), lender=None):
-            return call, list(makes), list(needs) + ([feed] if feed else []), feed, list(feed_needs), lender
+        def read(engine, *call, makes=(), needs=(), feed, feed_needs):
+            free = banks[0 if engine is nc.vector else 1]
+            return step(*call, makes=makes, needs=list(needs) + [feed], feed=step(feed[0], free, *feed[1:], makes=[feed], needs=feed_needs, lender=free))
 
         def feeds(steps):
-            by_vector = (x_read, z_max, v_read_staged, direct_scale)
-            return [
-                step(*feed, makes=[feed], needs=feed_needs, lender=lender or (None if feed[-1] == (1,) else "vector" if call[0] in by_vector else "scalar"))
-                for call, makes, needs, feed, feed_needs, lender in steps
-            ]
+            return [feed for call, makes, needs, lender, feed in steps]
 
         def quarters(key, first=0, last=4):
             return [key + (n,) for n in range(first, last)]
 
         def both(name, n):
             return [(name, q, n) for q in range(2)]
-
-        def alternate(first, second):
-            places = [((n + 0.5) / len(steps), k, n) for k, steps in enumerate((first, second)) for n in range(len(steps))]
-            return [(first, second)[k][n] for place, k, n in sorted(places)]
 
         def widen(h, tiles, engine):
             return [step(x_widen, h, i, engine, makes=[("wide", h, i)], needs=[("x raw", h, i // 2)] + [(x_turn, 0, i)] * h) for i in tiles]
@@ -382,124 +335,125 @@ def tile_maxout_generated_head_f5_kernel(tc, x_bytes, x_scale, w, b, e, g, a, r,
             needs = [("raw",) + key] + quarters(key, 0, first) + [("inherited", key)] * inherited
             return step(stage_raw, key, first, last, engine, makes=quarters(key, first, last), needs=needs)
 
-        def passed(*key, first=0, last=4):
-            return [
-                step(passed_read, key, j, makes=quarters(key, 2 * j, 2 * j + 2), feed=(pass_raw, key, j), feed_needs=[("raw",) + key] + quarters(key, 0, first))
-                for j in range(first // 2, last // 2)
-            ]
+        def passed(j, *key):
+            return [read(S, passed_read, key, j, makes=quarters(key, 2 * j, 2 * j + 2), feed=(pass_raw, key, j), feed_needs=[("raw",) + key] + quarters(key, 0, 2 * j))]
 
-        def stage_h(engine, q, h, first=0, last=4, banks_read=4, inherited=False):
+        def stage_h(engine, q, h, first=0, last=4):
             key, c = ("h", q, h), J * q + J - 1
-            needs = quarters(("max", c, h), 0, banks_read) + quarters(key, 0, first) + [("inherited", key)] * inherited
+            needs = quarters(("max", c, h), 0, last if q else 4) + quarters(key, 0, first)
             return step(stage_plane, key, ("max", c, h), first, last, engine, makes=quarters(key, first, last), needs=needs)
 
-        def z_steps(call, c, h, last_arg, makes, needs, split=False):
+        def stage_v(engine, q, first=0, last=4, inherited=False):
+            key = ("v", q, 1)
+            needs = quarters(("v plane", q)) + quarters(key, 0, first) + [("inherited", key)] * inherited
+            return step(stage_plane, key, ("v plane", q), first, last, engine, makes=quarters(key, first, last), needs=needs)
+
+        def quant_part(group):
+            key = ("h", 1, group // 2)
+            return step(quantize_part, key, group % 2, makes=[("h group", group)], needs=quarters(key, 2 * (group % 2), 2 * (group % 2) + 2))
+
+        def z_steps(engine, call, c, h, last_arg, makes, needs, split=False):
             operands = [("w", c, q) for q in range(2)] + [("x", h, q) for q in range(2)]
             return [
-                step(call, c, h, s, last_arg, makes=[(makes, c, h, s)], needs=needs + ["columns"], feed=(z_product, c, h, s, split), feed_needs=operands)
+                read(engine, call, c, h, s, last_arg, makes=[(makes, c, h, s)], needs=needs + ["columns"], feed=(z_product, c, h, s, split), feed_needs=operands)
                 for s in range(4)
             ]
 
-        def merge(c, h, heir):
-            return step(z_merge, c, h, heir, makes=quarters(("max", c, h)) + [("inherited", heir)], needs=quarters(("aside", c, h)) + quarters(("max", c - 1, h)))
-
         def loads_w(c):
             col = (c % J) * F + (c // J) * 512
-            return [step(load_raw, ("w", c, q), w[block(q, 512), col : col + 512], makes=[("raw", "w", c, q)], lender="raw") for q in range(2)]
+            return [step(load_raw, ("w", c, q), w[block(q, 512), col : col + 512], makes=[("raw", "w", c, q)], lender=raws) for q in range(2)]
 
         def load_x(h, j):
             return step(load, x_raw[h][j][:], x_rows[:, 4 * h + 2 * j : 4 * h + 2 * j + 2, :], makes=[("x raw", h, j)])
 
         def load_g(q):
-            return step(load_raw, ("g", 0, q), g[:, block(q, 512)], makes=[("raw", "g", 0, q)], lender="raw")
+            return step(load_raw, ("g", 0, q), g[:, block(q, 512)], makes=[("raw", "g", 0, q)], lender=raws)
 
         def load_e(n):
             return step(load, e_raw[n][:], e[block(n, 512), :].rearrange("(i p) k -> p i k", p=P), makes=[("e raw", n)])
 
-        x_reads = [[step(x_read, h, i, makes=[("x read", h, i)], feed=(x_turn, h, i), feed_needs=[("wide", h, i)]) for i in range(4)] for h in range(2)]
-        e_reads = [[step(e_read, n, j, makes=quarters(("e", 0, n), 2 * j, 2 * j + 2), feed=(e_turn, n, j), feed_needs=[("e raw", n)]) for j in range(2)] for n in range(2)]
-        column_read = [step(columns_read, makes=["columns"], feed=(columns_product,), feed_needs=["rows"])]
+        x_reads = [[read(V, x_read, h, i, makes=[("x read", h, i)], feed=(x_turn, h, i), feed_needs=[("wide", h, i)]) for i in range(4)] for h in range(2)]
+        e_reads = [
+            [read(engine, e_read, n, j, engine, makes=quarters(("e", 0, n), 2 * j, 2 * j + 2), feed=(e_turn, n, j), feed_needs=[("e raw", n)]) for j in range(2)]
+            for n, engine in enumerate((S, V))
+        ]
+        column_read = [read(S, columns_read, makes=["columns"], feed=(columns_product,), feed_needs=["rows"])]
+        passed_w10, passed_w11, passed_g1 = passed(1, "w", 1, 0), passed(1, "w", 1, 1), passed(0, "g", 0, 1)
         z = {}
         for c in range(2 * J):
             for h in range(2):
                 if c % J == 0:
-                    z[c, h] = z_steps(z_alone, c, h, "max", "max", [])
-                elif (c, h) in ASIDE:
-                    z[c, h] = z_steps(z_alone, c, h, "aside", "aside", [])
+                    z[c, h] = z_steps(S, z_alone, c, h, "max", "max", [])
+                elif (c, h) == (4, 1):
+                    z[c, h] = z_steps(S, z_alone, c, h, "aside", "aside", [])
                 else:
                     split = c == 2 * J - 1
-                    z[c, h] = z_steps(z_max, c, h, split, "max", quarters(("max", c - 1, h)), split)
-        v_vector = {
-            (q, n): [step(v_read_staged, q, n, j, makes=[("v", q, n, j)], feed=(v_four_slots, q, n, j), feed_needs=[("g", 0, q), ("e", 0, n)]) for j in range(blocks)]
-            for (q, n), blocks in V_BLOCKS.items()
-        }
-        v_scalar = {
-            (q, n): [step(v_read_plane, q, n, s, blocks == 2, makes=[("v plane", q, n, s)], feed=(v_by_slot, q, n, s, blocks == 2), feed_needs=[("g", 0, q), ("e", 0, n)]) for s in range(4 - blocks)]
-            for (q, n), blocks in V_BLOCKS.items()
-        }
-
-        def stage_v(engine, q, n, first=None, last=4, inherited=False):
-            key = ("v", q, n)
-            first = V_BLOCKS[q, n] if first is None else first
-            needs = quarters(("v plane", q, n), 0, 4 - V_BLOCKS[q, n]) + quarters(key, 0, first)[:1 if first == V_BLOCKS[q, n] else 4] + [("inherited", key)] * inherited
-            return step(stage_plane, key, ("v plane", q, n), first, last, engine, makes=quarters(key, first, last), needs=needs)
-
-        h_halves = [step(quantize_part, ("h", 1, 0), part, makes=[("h", 1, 0)] * part, needs=quarters(("h", 1, 0), 2 * part, 2 * part + 2)) for part in range(2)]
-        scaled = [step(direct_scale, key, makes=[("scaled", key)], needs=["r and d"], feed=(direct_product, key, (1,) if key in EARLY else (0, 1)), feed_needs=both("h", key[0]) + both("v", 1)) for key in DIRECT]
-        shifted = [step(direct_shift, key, nc.gpsimd if n in ON_GPSIMD else nc.vector, makes=[("direct", key)], needs=[("scaled", key)]) for n, key in enumerate(DIRECT)]
-        classes = [[step(class_read, h, n, makes=[("by class", h, n)], feed=(class_product, h, n, (1,) if (h, n) in EARLY else (0, 1)), feed_needs=both("h", h) + both("v", n // 4)) for n in range(TURNED[h])] for h in range(2)]
-        turned = {
-            (h, m): [
-                step(turned_read, h, m, j, makes=[("turned", h, m, j)], feed=(turn_back, h, m, j), feed_needs=[("by class", h, part[0]) for part in turned_parts(m, j)])
-                for j in range(2 if m else 4)
-            ]
-            for h in range(2)
-            for m in range(TURNED[h] // 2 - 1)
-        }
+                    z[c, h] = z_steps(V, z_max, c, h, split, "max", quarters(("max", c - 1, h)), split)
+        merge = step(z_merge, 4, 1, makes=quarters(("max", 4, 1)), needs=quarters(("aside", 4, 1)) + quarters(("max", 3, 1)))
+        v_low = [[read(V, v_read_staged, q, j, makes=[("v", q, 0, j)], feed=(v_four_slots, q, j), feed_needs=[("g", 0, q), ("e", 0, 0)]) for j in range(4)] for q in range(2)]
+        v_high = [[read(S, v_read_plane, q, t, makes=[("v plane", q, t)], feed=(v_by_slot, q, t), feed_needs=[("g", 0, q), ("e", 0, 1)]) for t in range(4)] for q in range(2)]
+        scaled, shifted, direct_stores, classes, turned, turned_stores = {}, {}, {}, {}, {}, {}
+        for i in range(2, 8):
+            scaled[i] = read(V, direct_scale, i, makes=[("scaled", i)], needs=["r and d"], feed=(direct_product, i), feed_needs=[("h", 0, i // 4), ("h group", i // 2)] + both("v", 1))
+            shifted[i] = step(direct_shift, i, makes=[("direct", i)], needs=[("scaled", i)])
+            direct_stores[i] = step(direct_store, i, needs=[("direct", i)])
+        for group, n in TURNED:
+            operands = [("h", 0, group // 2), ("h group", group)] + both("v", n)
+            classes[group, n] = [read(S, class_read, group, n, m, makes=[("by class", group, n, m)], feed=(class_product, group, n, m), feed_needs=operands) for m in range(2)]
+            tiles = (2 * group, 2 * group + 1)
+            turned[group, n] = [read(S, turned_read, i, n, makes=[("turned", i, n)], feed=(turn_back, i, n), feed_needs=quarters(("by class", group, n), 0, 2)) for i in tiles]
+            turned_stores[group, n] = [step(turned_store, i, n, needs=[("turned", i, n)]) for i in tiles]
         small_loads = [step(load, rows_raw[0:ROW_A, :], b.rearrange("(c n) -> c n", n=512)), step(load, rows_raw[ROW_A:ROW_R, :], a.rearrange("(c n) -> c n", n=512))]
         small_loads += [step(load, rows[row : row + 2, :], vector.rearrange("(o n) -> o n", o=2), makes=[("row", row)]) for row, vector in ((ROW_R, r), (ROW_D, d))]
 
-        def early(steps):
-            return [step(None, feed=feed[:-1] + ((0,),), feed_needs=[name for name in feed_needs if name[1] == 0], lender="vector" if call[0] is direct_scale else "scalar") for call, makes, needs, feed, feed_needs, lender in steps]
-
-        V, S, G = nc.vector, nc.scalar, nc.gpsimd
-        pw = {key[:3]: passed(*key[:3], first=key[3], last=key[4]) for key in PASSED}
         sync_lane = (
             [load_x(0, 0), step(load, xs[:], x_scale.rearrange("o (q p t) -> p (o q) t", q=2, t=4)), load_x(0, 1)]
-            + loads_w(0)[:1] + [load_x(1, 0)] + loads_w(0)[1:] + loads_w(1)[:1] + [load_x(1, 1)] + loads_w(1)[1:] + small_loads + loads_w(2) + [load_g(0), load_e(0), load_g(1)] + loads_w(3) + loads_w(4) + [load_e(1)] + loads_w(5)
+            + loads_w(0)[:1] + [load_x(1, 0)] + loads_w(0)[1:] + loads_w(1)[:1] + [load_x(1, 1)] + loads_w(1)[1:] + small_loads
+            + loads_w(2) + [load_g(0), load_e(0), load_g(1)] + loads_w(3) + loads_w(4) + [load_e(1)] + loads_w(5)
             + [step(load, r_all[:], r[512:C].partition_broadcast(P)), step(load, d_all[:], d[512:C].partition_broadcast(P), makes=["r and d"])]
+            + turned_stores[0, 0] + turned_stores[1, 0] + turned_stores[0, 1] + [direct_stores[i] for i in range(2, 6)]
+            + turned_stores[2, 0] + [direct_stores[6]] + turned_stores[3, 0] + [direct_stores[7]]
         )
-        direct_stores = [step(direct_store, key, needs=[("direct", key)]) for key in DIRECT]
-        pairs = {(h, m): [step(turned_store, h, m, j, needs=[("turned", h, m, j)]) for j in range(len(turned[h, m]))] for h, m in turned}
-        sync_lane += pairs[0, 0] + pairs[0, 1][:1] + direct_stores[:1] + pairs[0, 1][1:] + direct_stores[1:4] + pairs[1, 0][:2] + direct_stores[4:5] + pairs[1, 0][2:3] + direct_stores[5:] + pairs[1, 0][3:]
-
         vector_lane = (
             widen(0, (0, 1, 2), V) + x_reads[0]
             + [quant_x(0, 0), quant("w", 0, 0), quant_x(0, 1), quant("w", 0, 1), quant("w", 1, 0, heir=("w", 1, 1))]
-            + x_reads[1][:2] + [quant("w", 1, 1, heir=("w", 2, 1))] + x_reads[1][2:] + z[1, 0] + [quant("w", 2, 0), quant("w", 2, 1), quant_x(1, 0), quant("g", 0, 0), quant("e", 0, 0, heir=("w", 3, 1)), quant_x(1, 1)]
-            + z[2, 0] + v_vector[0, 0] + z[1, 1] + [quant("w", 3, 0), quant("w", 3, 1), quant("g", 0, 1), quant("w", 4, 0), quant("e", 0, 1, heir=("w", 5, 0)), quant("w", 4, 1)]
-            + z[2, 1] + v_vector[1, 0] + [quant("w", 5, 0), quant("w", 5, 1), quant("v", 0, 0), quant("h", 0, 0, heir=("v", 0, 1)), quant("v", 1, 0)]
-            + z[4, 0] + z[5, 0] + [h_halves[0], stage_h(V, 1, 0, first=2), quant("v", 0, 1), h_halves[1], merge(4, 1, None), quant("v", 1, 1)] + z[5, 1][:2] + [quant("h", 0, 1, heir=("h", 1, 1))] + z[5, 1][2:]
-            + [scaled[0], stage_h(V, 1, 1, first=2), scaled[1], quant("h", 1, 1)]
-            + shifted[:2] + scaled[2:4] + shifted[2:4] + scaled[4:] + shifted[4:]
+            + x_reads[1][:2] + [quant("w", 1, 1, heir=("w", 2, 1))] + x_reads[1][2:] + z[1, 0]
+            + [quant("w", 2, 0), quant("w", 2, 1), quant_x(1, 0), quant("g", 0, 0), quant("e", 0, 0, heir=("w", 3, 1)), quant_x(1, 1)]
+            + z[2, 0] + v_low[0] + z[1, 1] + e_reads[1]
+            + [quant("w", 3, 0), quant("w", 3, 1), quant("g", 0, 1), quant("w", 4, 0), quant("e", 0, 1, heir=("w", 5, 0)), quant("w", 4, 1)]
+            + z[2, 1] + v_low[1]
+            + [quant("w", 5, 0), quant("w", 5, 1), quant("v", 0, 0), quant("h", 0, 0, heir=("v", 0, 1)), quant("v", 1, 0)]
+            + z[4, 0] + z[5, 0]
+            + [stage_h(V, 1, 0, first=2), quant_part(0), quant("v", 0, 1), quant_part(1), merge, quant("v", 1, 1), quant("h", 0, 1)]
+            + z[5, 1] + [scaled[2], scaled[3], quant_part(2), stage_h(V, 1, 1, first=2), shifted[2], quant_part(3)]
+            + [scaled[4], shifted[3], scaled[5], shifted[4], shifted[5], scaled[6], shifted[6], scaled[7], shifted[7]]
         )
-        gpsimd_lane = [stage(G, "w", 0, 0), stage(G, "w", 0, 1, first=2),
-            stage(G, "w", 1, 1, last=2, inherited=True), stage(G, "w", 2, 1, inherited=True), stage(G, "w", 2, 0, last=1),
-            stage(G, "w", 3, 1, inherited=True), stage(G, "w", 4, 1), stage(G, "w", 4, 0, last=2),
+        gpsimd_lane = [
+            stage(G, "w", 0, 0, last=3), stage(G, "w", 0, 1, first=2),
+            stage(G, "w", 1, 1, last=2, inherited=True),
+            stage(G, "w", 2, 1, inherited=True), stage(G, "w", 2, 0, last=2),
+            stage(G, "w", 3, 1, inherited=True), stage(G, "w", 4, 1), stage(G, "w", 4, 0, last=3),
             stage(G, "w", 5, 0, inherited=True), stage(G, "w", 5, 1, first=2),
-            stage_v(G, 0, 1, inherited=True), stage_v(G, 1, 1, last=3), stage_h(G, 1, 1, last=2, banks_read=2, inherited=True)]
+            stage_v(G, 0, inherited=True), stage_v(G, 1, last=3),
+            stage_h(G, 1, 1, last=2),
+        ]
         scalar_lane = (
-            widen(0, (3,), S) + widen(1, (0, 1), S) + [stage(S, "w", 0, 1, last=2), stage(S, "w", 1, 0, last=2)] + pw["w", 1, 0] + widen(1, (2,), S) + [step(permute_rows, makes=["rows"], needs=[("row", ROW_D)])] + widen(1, (3,), S) + pw["w", 1, 1] + column_read
-            + z[0, 0] + [stage(S, "w", 2, 0, first=1), stage(S, "g", 0, 0)] + e_reads[0] + [stage(S, "w", 3, 0)] + pw["g", 0, 1] + z[0, 1][:2] + [stage(S, "g", 0, 1, first=2)] + z[0, 1][2:] + [stage(S, "w", 4, 0, first=2)] + e_reads[1] + [stage_h(S, 0, 0)]
-            + z[3, 0] + [stage(S, "w", 5, 1, last=2)] + z[3, 1] + v_scalar[0, 1] + v_scalar[1, 1] + z[4, 1][:2] + [stage_v(S, 1, 1, first=3)] + [stage_h(S, 1, 0, last=2, banks_read=2)] + z[4, 1][2:] + [stage_h(S, 0, 1)]
+            widen(0, (3,), S) + [stage(S, "w", 0, 0, first=3)] + widen(1, (0, 1), S) + [stage(S, "w", 0, 1, last=2), stage(S, "w", 1, 0, last=2)] + passed_w10
+            + widen(1, (2,), S) + [step(permute_rows, makes=["rows"], needs=[("row", ROW_D)])] + widen(1, (3,), S) + passed_w11 + column_read
+            + z[0, 0] + [stage(S, "w", 2, 0, first=2), stage(S, "g", 0, 0)] + e_reads[0] + [stage(S, "w", 3, 0)] + passed_g1
+            + z[0, 1][:2] + [stage(S, "g", 0, 1, first=2)] + z[0, 1][2:] + [stage(S, "w", 4, 0, first=3), stage_h(S, 0, 0), stage(S, "w", 5, 1, last=2)]
+            + z[3, 0] + z[3, 1] + v_high[0] + [stage_h(S, 0, 1, last=2)] + v_high[1]
+            + z[4, 1][:2] + [stage_v(S, 1, first=3), stage_h(S, 1, 0, last=2)] + z[4, 1][2:] + [stage_h(S, 0, 1, first=2)]
+            + classes[0, 0] + classes[1, 0] + turned[0, 0] + classes[0, 1] + turned[1, 0] + turned[0, 1]
+            + classes[2, 0] + classes[3, 0] + turned[2, 0] + turned[3, 0]
         )
-        scalar_lane += classes[0] + turned[0, 0] + turned[0, 1] + classes[1] + turned[1, 0]
         tensor_lane = feeds(
-            x_reads[0] + x_reads[1][:2] + pw["w", 1, 0] + pw["w", 1, 1] + z[0, 0][:1] + column_read + z[0, 0][1:2] + x_reads[1][2:] + z[0, 0][2:]
-            + z[1, 0] + e_reads[0] + pw["g", 0, 1] + z[2, 0] + z[0, 1][:2] + v_vector[0, 0][:2] + z[0, 1][2:] + v_vector[0, 0][2:] + z[1, 1] + e_reads[1] + z[2, 1]
-            + z[3, 0] + z[3, 1][:2] + v_vector[1, 0][:2] + z[3, 1][2:] + v_vector[1, 0][2:] + v_scalar[0, 1][:2] + z[4, 0][:2] + v_scalar[0, 1][2:] + z[4, 0][2:] + v_scalar[1, 1] + z[4, 1][:2] + z[5, 0] + z[4, 1][2:]
-            + z[5, 1][:2] + early(classes[0][:4]) + z[5, 1][2:] + classes[0] + scaled[:1] + turned[0, 0][:2] + scaled[1:2] + turned[0, 0][2:]
-            + early(scaled[2:4]) + turned[0, 1] + early(classes[1][:2]) + early(scaled[4:]) + alternate(classes[1][:2], scaled[2:4]) + classes[1][2:] + scaled[4:] + turned[1, 0]
+            x_reads[0] + x_reads[1][:2] + passed_w10 + passed_w11 + z[0, 0][:1] + column_read + z[0, 0][1:2] + x_reads[1][2:] + z[0, 0][2:]
+            + z[1, 0] + e_reads[0] + passed_g1 + z[2, 0] + z[0, 1][:2] + v_low[0][:2] + z[0, 1][2:] + v_low[0][2:] + z[1, 1] + e_reads[1] + z[2, 1]
+            + z[3, 0] + z[3, 1][:3] + v_low[1][:2] + z[3, 1][3:] + v_low[1][2:] + v_high[0] + z[4, 0][:3] + v_high[1][:2] + z[4, 0][3:] + v_high[1][2:]
+            + z[4, 1][:2] + z[5, 0] + z[4, 1][2:] + z[5, 1][:3] + classes[0, 0] + classes[1, 0] + z[5, 1][3:]
+            + turned[0, 0] + classes[0, 1] + [scaled[2], scaled[3]] + turned[1, 0] + turned[0, 1]
+            + [scaled[4]] + classes[2, 0] + [scaled[5]] + classes[3, 0] + [scaled[6]] + turned[2, 0] + [scaled[7]] + turned[3, 0]
         )
 
         make_identity(nc, ident[:])
@@ -507,20 +461,18 @@ def tile_maxout_generated_head_f5_kernel(tc, x_bytes, x_scale, w, b, e, g, a, r,
         nc.scalar.activation(out=ident_bf[:], in_=ident[:], func=IDENTITY)
 
         lanes = [sync_lane, tensor_lane, vector_lane, scalar_lane, gpsimd_lane]
-        lenders = {"raw": raws, "vector": banks["vector"], "scalar": banks["scalar"], None: [None]}
         made = set()
         while any(lanes):
             fresh = []
             moved = False
             for lane in lanes:
                 allowed = len(lane) if lane is sync_lane or lane is tensor_lane else 1
-                while allowed and lane and all(name in made for name in lane[0][2]) and lenders[lane[0][5]]:
-                    call, makes, needs, feed, feed_needs, lender = lane.pop(0)
-                    reader_of["now"] = lender
+                while allowed and lane and all(name in made for name in lane[0][2]) and lane[0][3] != []:
+                    call, makes, needs, lender, feed = lane.pop(0)
                     call[0](*call[1:])
                     fresh.extend(makes)
                     allowed = allowed - 1
                     moved = True
-            assert moved, [lane[0][0][1:] for lane in lanes if lane]
+            assert moved
             for name in fresh:
                 made.add(name)

@@ -431,8 +431,8 @@ def tile_maxout_generated_head_f5_kernel(tc, x_bytes, x_scale, w, b, e, g, a, r,
         gpsimd_lane = [
             stage(G, "w", 0, 0, last=3), stage(G, "w", 0, 1, first=2),
             stage(G, "w", 1, 1, last=2, inherited=True),
-            stage(G, "w", 2, 1, inherited=True), stage(G, "w", 2, 0, last=2),
-            stage(G, "w", 3, 1, inherited=True), stage(G, "w", 4, 1), stage(G, "w", 4, 0, last=3),
+            stage(G, "w", 2, 1, inherited=True), stage(G, "w", 2, 0, last=1),
+            stage(G, "w", 3, 1, inherited=True), stage(G, "w", 4, 1), stage(G, "w", 4, 0, last=2),
             stage(G, "w", 5, 0, inherited=True), stage(G, "w", 5, 1, first=2),
             stage_v(G, 0, inherited=True), stage_v(G, 1, last=3),
             stage_h(G, 1, 1, last=2),
@@ -440,9 +440,9 @@ def tile_maxout_generated_head_f5_kernel(tc, x_bytes, x_scale, w, b, e, g, a, r,
         scalar_lane = (
             widen(0, (3,), S) + [stage(S, "w", 0, 0, first=3)] + widen(1, (0, 1), S) + [stage(S, "w", 0, 1, last=2), stage(S, "w", 1, 0, last=2)] + passed_w10
             + widen(1, (2,), S) + [step(permute_rows, makes=["rows"], needs=[("row", ROW_D)])] + widen(1, (3,), S) + passed_w11 + column_read
-            + z[0, 0] + [stage(S, "w", 2, 0, first=2), stage(S, "g", 0, 0)] + e_reads[0] + [stage(S, "w", 3, 0)] + passed_g1
-            + z[0, 1][:2] + [stage(S, "g", 0, 1, first=2)] + z[0, 1][2:] + [stage(S, "w", 4, 0, first=3), stage_h(S, 0, 0), stage(S, "w", 5, 1, last=2)]
-            + z[3, 0] + z[3, 1] + v_high[0] + [stage_h(S, 0, 1, last=2)] + v_high[1]
+            + z[0, 0] + [stage(S, "w", 2, 0, first=1), stage(S, "g", 0, 0)] + e_reads[0] + [stage(S, "w", 3, 0)] + passed_g1
+            + z[0, 1][:2] + [stage(S, "g", 0, 1, first=2)] + z[0, 1][2:] + [stage(S, "w", 4, 0, first=2), stage_h(S, 0, 0), stage(S, "w", 5, 1, last=2)]
+            + z[3, 0] + z[3, 1] + v_high[0] + v_high[1][:2] + [stage_h(S, 0, 1, last=2)] + v_high[1][2:]
             + z[4, 1][:2] + [stage_v(S, 1, first=3), stage_h(S, 1, 0, last=2)] + z[4, 1][2:] + [stage_h(S, 0, 1, first=2)]
             + classes[0, 0] + classes[1, 0] + turned[0, 0] + classes[0, 1] + turned[1, 0] + turned[0, 1]
             + classes[2, 0] + classes[3, 0] + turned[2, 0] + turned[3, 0]

@@ -18,7 +18,7 @@ MULT = mybir.AluOpType.mult
 MAX = mybir.AluOpType.max
 IDENTITY = mybir.ActivationFunctionType.Identity
 
-RUN = 8
+RUN = 4
 WHOLE = slice(0, 512)
 ROW_A, ROW_R, ROW_D, ROWS = 6, 8, 10, 12
 TURNED = ((0, 0), (1, 0), (0, 1), (2, 0), (3, 0))
@@ -179,7 +179,7 @@ def tile_maxout_generated_head_f5_kernel(tc, x_bytes, x_scale, w, b, e, g, a, r,
                 take(staged, key)
             raw = give(raws, ("raw",) + key) if last == 4 else held[("raw",) + key]
             walk = "p t B s i" if engine is nc.scalar else "p B t i s"
-            share = (slice(0, P), slice(first, last)) if engine is nc.scalar else (slice(0, P), slice(0, 16), slice(first, last))
+            share = (slice(0, P), slice(first, last)) if engine is nc.scalar else (slice(0, P), slice(0, P // RUN), slice(first, last))
             source = raw[:].rearrange(f"p s (B t i) -> {walk}", t=4, i=RUN)[share]
             copy(engine, held[key][:].rearrange(f"p (t B i s) -> {walk}", t=4, i=RUN, s=4)[share], source)
 
@@ -416,7 +416,7 @@ def tile_maxout_generated_head_f5_kernel(tc, x_bytes, x_scale, w, b, e, g, a, r,
         )
         vector_lane = (
             widen(0, (0, 1, 2), V) + x_reads[0]
-            + [quant_x(0, 0), quant("w", 0, 0), quant_x(0, 1), quant("w", 0, 1), quant("w", 1, 0, heir=("w", 1, 1))]
+            + [quant("w", 0, 0), quant_x(0, 0), quant_x(0, 1), quant("w", 0, 1), quant("w", 1, 0, heir=("w", 1, 1))]
             + x_reads[1][:2] + [quant("w", 1, 1, heir=("w", 2, 1))] + x_reads[1][2:] + z[1, 0]
             + [quant("w", 2, 0), quant("w", 2, 1), quant_x(1, 0), quant("g", 0, 0), quant("e", 0, 0, heir=("w", 3, 1)), quant_x(1, 1)]
             + z[2, 0] + v_low[0] + z[1, 1] + e_reads[1]

@@ -19,13 +19,15 @@ MAX = mybir.AluOpType.max
 IDENTITY = mybir.ActivationFunctionType.Identity
 
 RUN = 4
-WHOLE = slice(0, 512)
+N_SINGLES, N_RAWS, N_PLANES, N_RESULTS, N_BY_CLASS = 9, 4, 6, 10, 4
+SPREAD = 512
+BY_HALVES = (("w", 0), ("w", 1), "g")
 ROW_A, ROW_R, ROW_D, ROWS = 6, 8, 10, 12
-TURNED = ((0, 0), (1, 0), (0, 1), (2, 0), (3, 0))
 
 
 def tile_maxout_generated_head_f5_kernel(tc, x_bytes, x_scale, w, b, e, g, a, r, d, out):
     nc = tc.nc
+    V, S, G = nc.vector, nc.scalar, nc.gpsimd
     with ExitStack() as ctx:
         keep = ctx.enter_context(tc.tile_pool(name="keep", bufs=1))
         psum = ctx.enter_context(tc.psum_pool(name="psum", bufs=1))
@@ -34,45 +36,41 @@ def tile_maxout_generated_head_f5_kernel(tc, x_bytes, x_scale, w, b, e, g, a, r,
         def kept(name, shape, dtype):
             return keep.tile(shape, dtype, name=name, align_bytes=64)
 
-        def operand(name):
-            return kept(name + "_codes", [P, 512], U32), kept(name + "_scales", [P, 512], U8)
+        def block(n, width=P):
+            return slice(n * width, (n + 1) * width)
 
-        banks = [[psum.tile([P, 512], F32, name=f"bank_{reader}{n}") for n in range(4)] for reader in ("vector", "scalar")]
-        staged = [kept(f"staged{n}", [P, 2048], BF16) for n in range(9)]
-        wide = [kept(f"x_wide{n}", [P, K], BF16) for n in range(4)]
-        results = [kept(f"result{n}", [P, 512], F32) for n in range(10)]
-        by_class = [tile[:].bitcast(F32) for tile in wide] + [kept(f"by_class{n}", [P, 512], F32) for n in range(2)]
-        raws = [kept(f"raw{n}", [P, 4, 512], BF16) for n in range(9)]
-        planes = [kept(f"plane{n}", [P, 4, 512], BF16) for n in range(8)]
+        banks = {engine: [psum.tile([P, 512], F32, name=f"bank_{name}{n}") for n in range(4)] for engine, name in (("V", "vector"), ("S", "scalar"))}
+        x_staged = kept("x_staged", [P, 4096], BF16)
+        singles = [kept(f"single{n}", [P, 2048], BF16) for n in range(N_SINGLES)]
+        raws = [kept(f"raw{n}", [P, 4096], BF16) for n in range(N_RAWS)]
+        planes = [kept(f"plane{n}", [P, 4, 512], BF16) for n in range(N_PLANES)]
+        wide = [kept(f"wide{n}", [P, K], BF16) for n in range(4)]
+        results = [kept(f"result{n}", [P, 512], F32) for n in range(N_RESULTS)]
+        by_class = [tile[:].bitcast(F32) for tile in wide] + [kept(f"by_class{n}", [P, 512], F32) for n in range(N_BY_CLASS)]
         held = {}
         owner = {}
 
         def take(free, key):
             held[key] = free.pop(0)
+            owner[key] = free
             return held[key]
 
-        def give(free, key):
-            free.append(held[key])
+        def give(key):
+            owner.pop(key).append(held[key])
             return held.pop(key)
 
-        def fill(free, key):
-            owner[key] = free
-            return take(free, key)
+        def hold(free, key):
+            return held[key] if key in held else take(free, key)
 
-        def drain(key):
-            return give(owner.pop(key), key)
-
-        x_raw = [[kept(f"x_raw{h}_{j}", [P, 2, K], U8) for j in range(2)] for h in range(2)]
+        x_raw = [kept(f"x_raw{j}", [P, 2, K], U8) for j in range(4)]
         e_raw = [kept(f"e_raw{n}", [P, 4, D], BF16) for n in range(2)]
-        x_staged = kept("x_staged", [P, 2, 2048], BF16)
         mx = {}
-        for name, keys in (("x", (2, 2)), ("w", (6, 2)), ("e", (1, 2)), ("g", (1, 2)), ("v", (2, 2)), ("h", (2, 2))):
-            for first in range(keys[0]):
-                for second in range(keys[1]):
-                    mx[name, first, second] = operand(f"{name}{first}_{second}")
+        for key in [("w", c) for c in range(6)] + ["g"] + [(name, n) for name in ("x", "h", "v") for n in range(2)] + ["e"]:
+            name = key if key in ("g", "e") else f"{key[0]}{key[1]}"
+            mx[key] = kept(name + "_codes", [P, 1024], U32), kept(name + "_scales", [P, 1024], U8)
         xs = kept("xs", [P, 2, 4], F32)
-        r_all = kept("r_all", [P, 512], BF16)
-        d_all = kept("d_all", [P, 512], BF16)
+        r_all = kept("r_all", [P, SPREAD], BF16)
+        d_all = kept("d_all", [P, SPREAD], BF16)
         rows_raw = kept("rows_raw", [ROW_R, 512], BF16)
         rows = kept("rows", [P, 512], BF16)
         columns = kept("columns", [P, ROWS, 4], F32)
@@ -82,49 +80,34 @@ def tile_maxout_generated_head_f5_kernel(tc, x_bytes, x_scale, w, b, e, g, a, r,
         x_rows = x_bytes.rearrange("(p i) k -> p i k", i=8)
         out_rows = out.rearrange("(p i) c -> p i c", i=8)
 
-        def block(n, width=P):
-            return slice(n * width, (n + 1) * width)
-
-        V, S, G = nc.vector, nc.scalar, nc.gpsimd
-
         def load(tile, source):
             nc.sync.dma_start(out=tile, in_=source)
 
-        def load_raw(key, source):
-            load(take(raws, ("raw",) + key)[:], source.rearrange("(p s) n -> p s n", s=4))
-
         def copy(engine, out, in_):
-            if engine is nc.vector:
+            if engine is V:
                 nc.vector.tensor_copy(out=out, in_=in_)
-            elif engine is nc.scalar:
+            elif engine is S:
                 nc.scalar.copy(out=out, in_=in_)
             else:
                 nc.gpsimd.tensor_scalar(out=out, in0=in_, scalar1=1.0, scalar2=0.0, op0=MULT, op1=ADD)
 
-        def quantize(key, source, cols=WHOLE):
+        def quantize(key, words, source):
             codes, scales = mx[key]
-            nc.vector.quantize_mx(out=codes[:, cols].bitcast(FP8X4), scales=scales[:, cols], in_=source[:, 4 * cols.start : 4 * cols.stop])
+            nc.vector.quantize_mx(out=codes[:, words].bitcast(FP8X4), scales=scales[:, words], in_=source)
 
-        def product(bank, lhs, lhs_cols, rhs, rhs_cols, start, stop):
+        def product(bank, lhs, lhs_words, rhs, rhs_words, start, stop):
             nc.tensor.matmul_mx(
                 out=bank,
-                lhsT=mx[lhs][0][:, lhs_cols].bitcast(FP8X4),
-                lhsT_scale=mx[lhs][1][:, lhs_cols],
-                rhs=mx[rhs][0][:, rhs_cols].bitcast(FP8X4),
-                rhs_scale=mx[rhs][1][:, rhs_cols],
+                lhsT=mx[lhs][0][:, lhs_words].bitcast(FP8X4),
+                lhsT_scale=mx[lhs][1][:, lhs_words],
+                rhs=mx[rhs][0][:, rhs_words].bitcast(FP8X4),
+                rhs_scale=mx[rhs][1][:, rhs_words],
                 start=start,
                 stop=stop,
             )
 
-        def quantize_staged(key, heir):
-            if heir:
-                held[heir] = held.pop(key)
-                quantize(key, held[heir])
-            else:
-                quantize(key, give(staged, key))
-
-        def quantize_part(key, part):
-            quantize(key, give(staged, key) if part else held[key], block(part, 256))
+        def span(first, count):
+            return slice(first, first + count)
 
         def permute_rows():
             nc.scalar.copy(
@@ -133,327 +116,425 @@ def tile_maxout_generated_head_f5_kernel(tc, x_bytes, x_scale, w, b, e, g, a, r,
             )
 
         def columns_product(free):
-            bank = fill(free, "columns")
+            bank = take(free, "columns")
             for t in range(4):
                 nc.tensor.matmul(bank[:, 16 * t : 16 * t + ROWS], lhsT=rows[:, block(t)], rhs=ident_bf[:, 0:ROWS], start=True, stop=True)
 
         def columns_read():
-            nc.scalar.copy(out=columns[:], in_=drain("columns")[:, 0:64].rearrange("p (t j) -> p j t", t=4)[:, 0:ROWS, :])
+            nc.scalar.copy(out=columns[:], in_=give("columns")[:, 0:64].rearrange("p (t j) -> p j t", t=4)[:, 0:ROWS, :])
 
-        def x_widen(h, i, engine):
-            copy(engine, wide[i][:], x_raw[h][i // 2][:, i % 2, :].bitcast(FP8))
+        def x_widen(i, engine):
+            copy(engine, wide[i % 4][:], x_raw[i // 2][:, i % 2, :].bitcast(FP8))
 
-        def x_turn(free, h, i):
-            bank = fill(free, ("x bank", h, i))
-            words = wide[i][:].bitcast(F32)
+        def x_turn(free, i):
+            bank = take(free, ("x bank", i))
+            words = wide[i % 4][:].bitcast(F32)
             for q in range(2):
                 for u in range(2):
                     nc.tensor.transpose(bank[:, block(2 * u + q)], words[:, 256 * q + u : 256 * (q + 1) : 2], ident[:])
 
-        def x_read(h, i):
+        def x_read(i):
             nc.vector.tensor_tensor(
-                out=x_staged[:, :, block(i, 512)].rearrange("p q (r u e) -> p q r u e", u=2, e=2),
-                in0=drain(("x bank", h, i))[:].bitcast(BF16).rearrange("p (u q r e) -> p q r u e", u=2, q=2, e=2),
+                out=x_staged[:].rearrange("p (q i r u e) -> p i q r u e", q=2, i=4, u=2, e=2)[:, i % 4],
+                in0=give(("x bank", i))[:].bitcast(BF16).rearrange("p (u q r e) -> p q r u e", u=2, q=2, e=2),
                 in1=xs[:].rearrange("p q (o u e) -> p q o u e", o=1, u=2).to_broadcast([P, 2, P, 2, 2]),
                 op=MULT,
             )
 
         def e_turn(free, n, j):
-            bank = fill(free, ("e bank", n, j))
+            bank = take(free, ("e bank", n, j))
             for i in range(2):
                 words = e_raw[n][:, 2 * j + i, :].bitcast(F32)
                 for u in range(2):
                     nc.tensor.transpose(bank[:, block(2 * i + u)], words[:, u:256:2], ident[:])
 
         def e_read(n, j, engine):
-            if j == 0:
-                take(staged, ("e", 0, n))
             copy(
                 engine,
-                held["e", 0, n][:].bitcast(F32)[:, block(j, 512)].rearrange("p (i r u) -> p i r u", i=2, u=2),
-                drain(("e bank", n, j))[:].rearrange("p (i u r) -> p i r u", i=2, u=2),
+                hold(singles, ("e", n))[:].bitcast(F32)[:, block(j, 512)].rearrange("p (i r u) -> p i r u", i=2, u=2),
+                give(("e bank", n, j))[:].rearrange("p (i u r) -> p i r u", i=2, u=2),
             )
 
-        def stage_raw(key, first, last, engine):
-            if key not in held:
-                take(staged, key)
-            raw = give(raws, ("raw",) + key) if last == 4 else held[("raw",) + key]
-            walk = "p t B s i" if engine is nc.scalar else "p B t i s"
-            share = (slice(0, P), slice(first, last)) if engine is nc.scalar else (slice(0, P), slice(0, P // RUN), slice(first, last))
-            source = raw[:].rearrange(f"p s (B t i) -> {walk}", t=4, i=RUN)[share]
-            copy(engine, held[key][:].rearrange(f"p (t B i s) -> {walk}", t=4, i=RUN, s=4)[share], source)
+        def raw_rows(tile, key, q):
+            if key in BY_HALVES:
+                return tile[:, block(q, 2048)].rearrange("p (s n) -> p s n", s=4)
+            return tile[:].rearrange("p (s n) -> p s n", s=4)[:, :, block(q, 512)]
 
-        def stage_plane(key, source, first, last, engine):
-            if key not in held:
-                take(staged, key)
-            plane = give(planes, source) if last == 4 else held[source]
-            run = 1 if engine is nc.gpsimd else 4
-            copy(
-                engine,
-                held[key][:, 512 * first : 512 * last].rearrange("p (c i t) -> p c t i", i=run, t=4),
-                plane[:, :, P * first : P * last].rearrange("p t (c i) -> p c t i", i=run),
-            )
+        def load_w(c, q):
+            col = (c % J) * F + (c // J) * 512
+            load(raw_rows(hold(raws, ("raw", ("w", c))), ("w", c), q), w[block(q, 512), col : col + 512].rearrange("(p s) n -> p s n", s=4))
 
-        def pass_raw(free, key, j):
-            bank = fill(free, ("pass bank", key))[:].bitcast(BF16)
-            raw = give(raws, ("raw",) + key) if j else held[("raw",) + key]
+        def load_g(f):
+            load(raw_rows(hold(raws, ("raw", "g")), "g", f), g[:, block(f, 512)].rearrange("(p s) n -> p s n", s=4))
+
+        def half_of(key, q, t):
+            return q if key == "g" else t // 2
+
+        def stage_raw(key, qs, ts, engine, last):
+            half = half_of(key, qs.start // 2, ts.start)
+            tile = hold(singles, (key, half))
+            raw = give(("raw", key)) if last else held["raw", key]
+            blocks = slice(16 * qs.start, 16 * qs.stop)
+            walk = "p B t i s" if engine is G else "p t B s i"
+            if key in BY_HALVES:
+                source = raw_rows(raw, key, qs.start // 2).rearrange(f"p s (B t i) -> {walk}", t=4, i=RUN)
+                columns_of = slice(blocks.start % 32, (blocks.stop - 1) % 32 + 1)
+            else:
+                source = raw[:].rearrange(f"p (s B t i) -> {walk}", s=4, t=4, i=RUN)
+                columns_of = blocks
+            target = tile[:].rearrange(f"p (t B i s) -> {walk}", t=4 if key == "g" else 2, i=RUN, s=4)
+            places, within = (slice(blocks.start - 32 * half, blocks.stop - 32 * half), ts) if key == "g" else (blocks, slice(ts.start - 2 * half, ts.stop - 2 * half))
+            if engine is G:
+                copy(engine, target[:, places, within], source[:, columns_of, ts])
+            else:
+                copy(engine, target[:, within, places], source[:, ts, columns_of])
+
+        def pass_raw(free, key, q, j, last):
+            bank = take(free, ("pass bank", key, q, j))[:].bitcast(BF16)
+            raw = give(("raw", key)) if last else held["raw", key]
             for n in range(2):
-                source = raw[:].rearrange("p s (B t i) -> p t B s i", t=4, i=RUN)[:, 2 * j + n]
+                source = raw_rows(raw, key, q).rearrange("p s (B t i) -> p t B s i", t=4, i=RUN)[:, 2 * j + n]
                 target = bank[:, block(n, 512)].rearrange("p (B i s) -> p B s i", i=RUN, s=4)
                 nc.tensor.matmul(target, lhsT=ident_bf[:], rhs=source, start=True, stop=True)
 
-        def passed_read(key, j):
-            if key not in held:
-                take(staged, key)
-            nc.scalar.copy(out=held[key][:].bitcast(F32)[:, block(j, 512)], in_=drain(("pass bank", key))[:])
+        def passed_read(key, q, j):
+            words = hold(singles, (key, half_of(key, q, 2 * j)))[:].bitcast(F32)
+            target = words.rearrange("p (j t n) -> p j t n", j=2, t=2)[:, j] if key == "g" else words.rearrange("p (t q n) -> p q t n", t=2, q=2)[:, q]
+            nc.scalar.copy(out=target, in_=give(("pass bank", key, q, j))[:].rearrange("p (t n) -> p t n", t=2))
+
+        def quantize_part(key, operand, first, last, heir, release=True):
+            tile = held[key]
+            if release:
+                if heir:
+                    held[heir] = held.pop(key)
+                    owner[heir] = owner.pop(key)
+                else:
+                    give(key)
+            base = 512 * key[-1]
+            quantize(operand, slice(base + 256 * first, base + 256 * last), tile[:, 1024 * first : 1024 * last])
+
+        def quantize_x(h, first, last, heir):
+            quantize(("x", h), slice(512 * first, 512 * last), x_staged[:, 2048 * first : 2048 * last])
+            if h:
+                for q in range(first, last):
+                    if heir and q == last - 1:
+                        held[heir], owner[heir] = x_staged[:, block(q, 2048)], singles
+                    else:
+                        singles.append(x_staged[:, block(q, 2048)])
+
+        def stage_plane(key, source, first, last, engine):
+            tile = hold(singles, key)
+            plane = give(source) if last == 4 else held[source]
+            run = 1 if engine is G else 4
+            copy(
+                engine,
+                tile[:, 512 * first : 512 * last].rearrange("p (c i t) -> p c t i", i=run, t=4),
+                plane[:, :, P * first : P * last].rearrange("p t (c i) -> p c t i", i=run),
+            )
 
         def z_parts(s, split):
             if split:
-                return [(2 * (s % 2) + n, block(s // 2, 256), block(n, 256)) for n in range(2)]
-            return [(s, WHOLE, WHOLE)]
+                return [(2 * (s % 2) + n, 256 * (s // 2), 256, block(n, 256)) for n in range(2)]
+            return [(s, 0, 512, slice(0, 512))]
 
         def z_product(free, c, h, s, split):
-            bank = fill(free, ("z bank", c, h, s))
-            for t, samples, place in z_parts(s, split):
+            bank = take(free, ("z bank", c, h, s))
+            for t, first, count, place in z_parts(s, split):
                 for q in range(2):
-                    product(bank[:, place], ("w", c, q), block(t), ("x", h, q), samples, q == 0, q == 1)
+                    product(bank[:, place], ("w", c), block(2 * t + q), ("x", h), span(512 * q + first, count), q == 0, q == 1)
 
         def z_bias(c, t):
             return columns[:, 2 * (c % J) + c // J, t : t + 1]
 
         def z_alone(c, h, t, name):
-            if t == 0:
-                take(planes, (name, c, h))
-            nc.scalar.activation(out=held[name, c, h][:, t, :], in_=drain(("z bank", c, h, t))[:], func=IDENTITY, bias=z_bias(c, t))
+            nc.scalar.activation(out=hold(planes, (name, c // J, h))[:, t, :], in_=give(("z bank", c, h, t))[:], func=IDENTITY, bias=z_bias(c, t))
 
         def z_max(c, h, s, split):
-            bank = drain(("z bank", c, h, s))
-            if s == 0:
-                take(planes, ("max", c, h))
-            for t, samples, place in z_parts(s, split):
-                nc.vector.scalar_tensor_tensor(
-                    out=held["max", c, h][:, t, samples], in0=bank[:, place], scalar=z_bias(c, t), in1=held["max", c - 1, h][:, t, samples], op0=ADD, op1=MAX
-                )
-            if s == 3:
-                give(planes, ("max", c - 1, h))
+            bank = give(("z bank", c, h, s))
+            for t, first, count, place in z_parts(s, split):
+                part = held["max", c // J, h][:, t, span(first, count)]
+                nc.vector.scalar_tensor_tensor(out=part, in0=bank[:, place], scalar=z_bias(c, t), in1=part, op0=ADD, op1=MAX)
 
-        def z_merge(c, h):
-            merged = take(planes, ("max", c, h))
-            before = give(planes, ("max", c - 1, h))
-            nc.vector.tensor_tensor(out=merged[:], in0=give(planes, ("aside", c, h))[:], in1=before[:], op=MAX)
+        def z_merge(f, h, slots):
+            part = held["max", f, h][:, 0:slots, :]
+            nc.vector.tensor_tensor(out=part, in0=give(("aside", f, h))[:, 0:slots, :], in1=part, op=MAX)
 
-        def v_four_slots(free, q, j):
-            bank = fill(free, ("v bank", q, j))
+        def v_four_slots(free, f, n, j):
+            bank = take(free, ("v bank", f, n, j))
             for t in range(4):
-                product(bank[:, block(t)], ("g", 0, q), block(t), ("e", 0, 0), block(j), True, True)
+                product(bank[:, block(t)], "g", block(4 * f + t), "e", span(512 * n + P * j, P), True, True)
 
-        def v_read_staged(q, j):
-            if j == 0:
-                take(staged, ("v", q, 0))
+        def v_read_staged(f, n, j):
             nc.vector.tensor_tensor(
-                out=held["v", q, 0][:, block(j, 512)].rearrange("p (c t) -> p c t", t=4),
-                in0=drain(("v bank", q, j))[:].rearrange("p (t c) -> p c t", t=4),
-                in1=columns[:, ROW_A + q : ROW_A + q + 1, :].to_broadcast([P, P, 4]),
+                out=hold(singles, ("v", n, f))[:, block(j, 512)].rearrange("p (c t) -> p c t", t=4),
+                in0=give(("v bank", f, n, j))[:].rearrange("p (t c) -> p c t", t=4),
+                in1=columns[:, ROW_A + f : ROW_A + f + 1, :].to_broadcast([P, P, 4]),
                 op=ADD,
             )
 
-        def v_by_slot(free, q, t):
-            product(fill(free, ("v slot bank", q, t))[:], ("g", 0, q), block(t), ("e", 0, 1), WHOLE, True, True)
+        def v_by_slot(free, f, n, t):
+            product(take(free, ("v slot bank", f, n, t))[:], "g", block(4 * f + t), "e", block(n, 512), True, True)
 
-        def v_read_plane(q, t):
-            if t == 0:
-                take(planes, ("v plane", q))
-            nc.scalar.activation(out=held["v plane", q][:, t, :], in_=drain(("v slot bank", q, t))[:], func=IDENTITY, bias=columns[:, ROW_A + q, t : t + 1])
+        def v_read_plane(f, n, t):
+            nc.scalar.activation(out=hold(planes, ("v plane", f, n))[:, t, :], in_=give(("v slot bank", f, n, t))[:], func=IDENTITY, bias=columns[:, ROW_A + f, t : t + 1])
 
-        def direct_product(free, i):
-            bank = fill(free, ("direct bank", i))
-            for q in range(2):
-                product(bank[:], ("h", q, i // 4), block(i % 4), ("v", q, 1), WHOLE, q == 0, q == 1)
+        def direct_product(free, i, n):
+            bank = take(free, ("direct bank", i, n))
+            for f in range(2):
+                product(bank[:], ("h", i // 4), span(512 * f + P * (i % 4), P), ("v", n), block(f, 512), f == 0, f == 1)
 
-        def direct_scale(i):
-            nc.vector.tensor_tensor(out=take(results, ("direct", i))[:], in0=drain(("direct bank", i))[:], in1=r_all[:], op=MULT)
+        def spread_cols(n, cols):
+            return slice(cols.start + 512 * n - (C - SPREAD), cols.stop + 512 * n - (C - SPREAD))
 
-        def direct_shift(i):
-            nc.vector.tensor_tensor(out=held["direct", i][:], in0=held["direct", i][:], in1=d_all[:], op=ADD)
+        def direct_scale(i, n, cols):
+            bank = give(("direct bank", i, n)) if cols.stop == 512 else held["direct bank", i, n]
+            nc.vector.tensor_tensor(out=hold(results, ("result", i, n))[:, cols], in0=bank[:, cols], in1=r_all[:, spread_cols(n, cols)], op=MULT)
 
-        def direct_store(i):
-            nc.sync.dma_start(out=out_rows[:, i, 512:C], in_=give(results, ("direct", i))[:])
+        def direct_shift(i, n, cols, engine):
+            part = held["result", i, n][:, cols]
+            engine.tensor_tensor(out=part, in0=part, in1=d_all[:, spread_cols(n, cols)], op=ADD)
 
-        def class_product(free, group, n, m):
-            bank = fill(free, ("class bank", group, n, m))
-            for k in range(2):
-                for q in range(2):
-                    product(bank[:, block(k, 256)], ("v", q, n), block(2 * m + k), ("h", q, group // 2), block(group % 2, 256), q == 0, q == 1)
+        def shift_into_heir(i, n):
+            target = held.pop(("sum", i, n))[:].bitcast(F32)[:, 512:1024]
+            nc.gpsimd.tensor_tensor(out=target, in0=give(("result", i, n))[:], in1=d_all[:, spread_cols(n, slice(0, 512))], op=ADD)
+            held["result", i, n], owner["result", i, n] = target, []
 
-        def class_read(group, n, m):
-            bank = drain(("class bank", group, n, m))
-            tile = take(by_class, ("by class", group, n, m))
-            for k in range(2):
-                column = slice(2 * m + k, 2 * m + k + 1)
-                nc.scalar.activation(out=tile[:, block(k, 256)], in_=bank[:, block(k, 256)], func=IDENTITY, scale=columns[:, ROW_R + n, column], bias=columns[:, ROW_D + n, column])
+        def store(i, n, cols):
+            tile = give(("result", i, n)) if cols.stop == 512 else held["result", i, n]
+            nc.sync.dma_start(out=out_rows[:, i, 512 * n + cols.start : 512 * n + cols.stop], in_=tile[:, cols])
 
-        def turn_back(free, i, n):
-            bank = fill(free, ("turned bank", i, n))
-            for k in range(4):
-                nc.tensor.transpose(bank[:, block(k)], held["by class", i // 2, n, k // 2][:, block(2 * (k % 2) + i % 2)], ident[:])
-            if i % 2:
-                for m in range(2):
-                    give(by_class, ("by class", i // 2, n, m))
+        def class_parts(tiles, m):
+            if len(tiles) == 2:
+                return [(2 * m + k, block(k, 256)) for k in range(2)]
+            return [(m, slice(0, 512))]
 
-        def turned_read(i, n):
-            nc.scalar.copy(out=take(results, ("turned", i, n))[:], in_=drain(("turned bank", i, n))[:])
+        def class_product(free, tiles, n, m):
+            bank = take(free, ("class bank", tiles, n, m))
+            for k, place in class_parts(tiles, m):
+                for f in range(2):
+                    product(bank[:, place], ("v", n), span(512 * f + P * k, P), ("h", tiles[0] // 4), span(512 * f + P * (tiles[0] % 4), P * len(tiles)), f == 0, f == 1)
 
-        def turned_store(i, n):
-            nc.sync.dma_start(out=out_rows[:, i, block(n, 512)], in_=give(results, ("turned", i, n))[:])
+        def class_read(tiles, n, m):
+            bank = give(("class bank", tiles, n, m))
+            tile = take(by_class, ("by class", tiles, n, m))
+            for k, place in class_parts(tiles, m):
+                nc.scalar.activation(out=tile[:, place], in_=bank[:, place], func=IDENTITY, scale=columns[:, ROW_R + n, k : k + 1], bias=columns[:, ROW_D + n, k : k + 1])
+
+        def turn_back(free, tiles, i, n):
+            bank = take(free, ("turned bank", i, n))
+            for m in range(len(tiles)):
+                for k, place in class_parts(tiles, m):
+                    nc.tensor.transpose(bank[:, block(k)], held["by class", tiles, n, m][:, span(place.start + P * (i - tiles[0]), P)], ident[:])
+            if i == tiles[-1]:
+                for m in range(len(tiles)):
+                    give(("by class", tiles, n, m))
+
+        def turned_read(i, n, engine):
+            copy(engine, take(results, ("result", i, n))[:], give(("turned bank", i, n))[:])
 
         def step(*call, makes=(), needs=(), lender=None, feed=None):
             return call, list(makes), list(needs), lender, feed
 
-        def read(engine, *call, makes=(), needs=(), feed, feed_needs):
-            free = banks[0 if engine is nc.vector else 1]
-            return step(*call, makes=makes, needs=list(needs) + [feed], feed=step(feed[0], free, *feed[1:], makes=[feed], needs=feed_needs, lender=free))
+        def read(engine, *call, makes=(), needs=(), feed, feed_needs, lender=None):
+            free = banks["V" if engine is V else "S"]
+            return step(*call, makes=makes, needs=list(needs) + [feed], lender=lender, feed=step(feed[0], free, *feed[1:], makes=[feed], needs=feed_needs, lender=free))
 
         def feeds(steps):
             return [feed for call, makes, needs, lender, feed in steps]
 
-        def quarters(key, first=0, last=4):
-            return [key + (n,) for n in range(first, last)]
+        def parts(key, first=0, last=4):
+            return [(key, n) for n in range(first, last)]
 
-        def both(name, n):
-            return [(name, q, n) for q in range(2)]
+        def cells(key, qs, ts):
+            return [(key, q, t) for q in range(qs.start, qs.stop) for t in range(ts.start, ts.stop)]
 
-        def widen(h, tiles, engine):
-            return [step(x_widen, h, i, engine, makes=[("wide", h, i)], needs=[("x raw", h, i // 2)] + [(x_turn, 0, i)] * h) for i in tiles]
+        staged_cells = {}
 
-        def quant(*key, heir=None):
-            return step(quantize_staged, key, heir, makes=[key, ("inherited", heir)], needs=quarters(key))
+        def stage(engine, key, first, last, q=None, inherited=False, quarters=(0, 4)):
+            qs, ts = slice(*quarters) if q is None else slice(2 * q, 2 * q + 2), slice(first, last)
+            before = list(staged_cells.setdefault(key, []))
+            staged_cells[key].extend(cells(key, qs, ts))
+            final = len(staged_cells[key]) == 16
+            needs = [("raw", key, n // 2) for n in range(qs.start, qs.stop)] + [("inherited", (key, half_of(key, qs.start // 2, first)))] * inherited + before * final
+            return step(stage_raw, key, qs, ts, engine, final, makes=cells(key, qs, ts), needs=needs, lender=None if inherited else singles)
 
-        def quant_x(h, q):
-            return step(quantize, ("x", h, q), x_staged[:, q, :], makes=[("x", h, q)], needs=quarters(("x read", h)))
+        def passed(key, q, j, inherited=False):
+            qs, ts = slice(2 * q, 2 * q + 2), slice(2 * j, 2 * j + 2)
+            before = list(staged_cells.setdefault(key, []))
+            staged_cells[key].extend(cells(key, qs, ts))
+            final = len(staged_cells[key]) == 16
+            return read(S, passed_read, key, q, j, makes=cells(key, qs, ts), needs=[("inherited", (key, half_of(key, q, 2 * j)))] * inherited, lender=None if inherited else singles, feed=(pass_raw, key, q, j, final), feed_needs=[("raw", key, q)] + before * final)
 
-        def stage(engine, *key, first=0, last=4, inherited=False):
-            needs = [("raw",) + key] + quarters(key, 0, first) + [("inherited", key)] * inherited
-            return step(stage_raw, key, first, last, engine, makes=quarters(key, first, last), needs=needs)
+        def quant_w(key, half, heir=None):
+            return step(quantize_part, (key, half), key, 0, 2, heir, makes=parts(("codes", key), 2 * half, 2 * half + 2) + [("inherited", heir)], needs=cells(key, slice(0, 4), slice(2 * half, 2 * half + 2)))
 
-        def passed(j, *key):
-            return [read(S, passed_read, key, j, makes=quarters(key, 2 * j, 2 * j + 2), feed=(pass_raw, key, j), feed_needs=[("raw",) + key] + quarters(key, 0, 2 * j))]
+        def quant_g(f, heir=None):
+            return step(quantize_part, ("g", f), "g", 0, 2, heir, makes=[("g codes", f), ("inherited", heir)], needs=cells("g", slice(2 * f, 2 * f + 2), slice(0, 4)))
 
-        def stage_h(engine, q, h, first=0, last=4):
-            key, c = ("h", q, h), J * q + J - 1
-            needs = quarters(("max", c, h), 0, last if q else 4) + quarters(key, 0, first)
-            return step(stage_plane, key, ("max", c, h), first, last, engine, makes=quarters(key, first, last), needs=needs)
+        def quant_x(h, first=0, last=2, heir=None):
+            return step(quantize_x, h, first, last, heir, makes=parts(("codes", ("x", h)), first, last) + [("inherited", heir)], needs=parts(("x read", h)))
 
-        def stage_v(engine, q, first=0, last=4, inherited=False):
-            key = ("v", q, 1)
-            needs = quarters(("v plane", q)) + quarters(key, 0, first) + [("inherited", key)] * inherited
-            return step(stage_plane, key, ("v plane", q), first, last, engine, makes=quarters(key, first, last), needs=needs)
+        def quant(key, first=0, last=2, heir=None, home=None, release=None):
+            operand = "e" if key[0] == "e" else key[0:2]
+            return step(quantize_part, (home,) + key[1:] if home else key, operand, first, last, heir, last == 2 if release is None else release, makes=parts(("codes", key), first, last) + [("inherited", heir)], needs=parts(key, 2 * first, 2 * last))
 
-        def quant_part(group):
-            key = ("h", 1, group // 2)
-            return step(quantize_part, key, group % 2, makes=[("h group", group)], needs=quarters(key, 2 * (group % 2), 2 * (group % 2) + 2))
+        def codes(key, first=0, last=2):
+            return parts(("codes", key), first, last)
 
-        def z_steps(engine, call, c, h, last_arg, makes, needs, split=False):
-            operands = [("w", c, q) for q in range(2)] + [("x", h, q) for q in range(2)]
-            return [
-                read(engine, call, c, h, s, last_arg, makes=[(makes, c, h, s)], needs=needs + ["columns"], feed=(z_product, c, h, s, split), feed_needs=operands)
-                for s in range(4)
-            ]
+        def stage_h(engine, h, f, first=0, last=4, split=False, inherited=False, home="h"):
+            key = ("h", h, f)
+            needs = parts(("max", J * f + J - 1, h), 0, last if split else 4) + parts(key, 0, first) + [("inherited", (home, h, f))] * inherited
+            return step(stage_plane, (home, h, f), ("max", f, h), first, last, engine, makes=parts(key, first, last), needs=needs)
+
+        def stage_v(engine, n, f, first=0, last=4, inherited=False):
+            key = ("v", n, f)
+            needs = parts(("v plane", f, n)) + parts(key, 0, first) + [("inherited", key)] * inherited
+            return step(stage_plane, key, ("v plane", f, n), first, last, engine, makes=parts(key, first, last), needs=needs)
+
+        def z_steps(c, h, aside=0, split=False):
+            steps = []
+            for s in range(4):
+                slots = (2 * (s % 2), 2 * (s % 2) + 2) if split else (s, s + 1)
+                operands = codes(("w", c), *slots) + codes(("x", h))
+                if c % J == 0 or s < aside:
+                    how = "aside" if c % J else "max"
+                    steps.append(read(S, z_alone, c, h, s, how, makes=[((how, c, h), s)], needs=["columns"], feed=(z_product, c, h, s, False), feed_needs=operands))
+                else:
+                    needs = parts(("max", c - 1, h)) if split else [(("max", c - 1, h), s)]
+                    steps.append(read(V, z_max, c, h, s, split, makes=[(("max", c, h), s)], needs=needs, feed=(z_product, c, h, s, split), feed_needs=operands))
+            return steps
+
+        def merge(c, h, slots):
+            return step(z_merge, c // J, h, slots, makes=parts(("max", c, h), 0, slots), needs=parts(("aside", c, h), 0, slots) + parts(("max", c - 1, h), 0, slots))
+
+        def v_low(f, n):
+            return [read(V, v_read_staged, f, n, j, makes=[(("v", n, f), j)], needs=["columns"], feed=(v_four_slots, f, n, j), feed_needs=[("g codes", f)] + codes(("e", n))) for j in range(4)]
+
+        def v_high(f, n):
+            return [read(S, v_read_plane, f, n, t, makes=[(("v plane", f, n), t)], needs=["columns"], feed=(v_by_slot, f, n, t), feed_needs=[("g codes", f)] + codes(("e", n))) for t in range(4)]
+
+        def h_codes(tiles):
+            h = tiles[0] // 4
+            return [(("codes", ("h", h, f)), part) for f in range(2) for part in sorted(set(i % 4 // 2 for i in tiles))]
+
+        def v_codes(n):
+            return codes(("v", n, 0)) + codes(("v", n, 1))
+
+        WHOLE = slice(0, 512)
+
+        def scaled(i, n, cols=WHOLE):
+            if cols.start:
+                return step(direct_scale, i, n, cols, makes=[("scaled", i, n, cols.start)], needs=[("scaled", i, n, 0)])
+            return read(V, direct_scale, i, n, cols, makes=[("scaled", i, n, 0)], needs=["r and d"], lender=results, feed=(direct_product, i, n), feed_needs=h_codes((i,)) + v_codes(n))
+
+        def shifted(engine, i, n, cols=WHOLE):
+            return step(direct_shift, i, n, cols, engine, makes=[("done", i, n, cols.start)], needs=[("scaled", i, n, cols.start)])
+
+        def shifted_heir(i, n):
+            return step(shift_into_heir, i, n, makes=[("done", i, n, 0)], needs=[("scaled", i, n, 0), ("inherited", ("sum", i, n))])
+
+        def stored(i, n, cols=WHOLE):
+            return step(store, i, n, cols, needs=[("done", i, n, cols.start)])
+
+        def classes(tiles, n):
+            return [read(S, class_read, tiles, n, m, makes=[(("by class", tiles, n), m)], lender=by_class, feed=(class_product, tiles, n, m), feed_needs=h_codes(tiles) + v_codes(n)) for m in range(len(tiles))]
+
+        def turned(tiles, n, engine=S):
+            return [read(engine, turned_read, i, n, engine, makes=[("done", i, n, 0)], lender=results, feed=(turn_back, tiles, i, n), feed_needs=parts(("by class", tiles, n), 0, len(tiles))) for i in tiles]
 
         def loads_w(c):
-            col = (c % J) * F + (c // J) * 512
-            return [step(load_raw, ("w", c, q), w[block(q, 512), col : col + 512], makes=[("raw", "w", c, q)], lender=raws) for q in range(2)]
+            return [step(load_w, c, q, makes=[("raw", ("w", c), q)], lender=None if q else raws) for q in range(2)]
 
-        def load_x(h, j):
-            return step(load, x_raw[h][j][:], x_rows[:, 4 * h + 2 * j : 4 * h + 2 * j + 2, :], makes=[("x raw", h, j)])
-
-        def load_g(q):
-            return step(load_raw, ("g", 0, q), g[:, block(q, 512)], makes=[("raw", "g", 0, q)], lender=raws)
+        def load_x(first, last):
+            return step(load, x_raw[first // 2][:, first % 2 : first % 2 + last - first, :], x_rows[:, first:last, :], makes=[("x raw", i) for i in range(first, last)])
 
         def load_e(n):
             return step(load, e_raw[n][:], e[block(n, 512), :].rearrange("(i p) k -> p i k", p=P), makes=[("e raw", n)])
 
-        x_reads = [[read(V, x_read, h, i, makes=[("x read", h, i)], feed=(x_turn, h, i), feed_needs=[("wide", h, i)]) for i in range(4)] for h in range(2)]
-        e_reads = [
-            [read(engine, e_read, n, j, engine, makes=quarters(("e", 0, n), 2 * j, 2 * j + 2), feed=(e_turn, n, j), feed_needs=[("e raw", n)]) for j in range(2)]
-            for n, engine in enumerate((S, V))
-        ]
-        column_read = [read(S, columns_read, makes=["columns"], feed=(columns_product,), feed_needs=["rows"])]
-        passed_w10, passed_w11, passed_g1 = passed(1, "w", 1, 0), passed(1, "w", 1, 1), passed(0, "g", 0, 1)
-        z = {}
-        for c in range(2 * J):
-            for h in range(2):
-                if c % J == 0:
-                    z[c, h] = z_steps(S, z_alone, c, h, "max", "max", [])
-                elif (c, h) == (4, 1):
-                    z[c, h] = z_steps(S, z_alone, c, h, "aside", "aside", [])
-                else:
-                    split = c == 2 * J - 1
-                    z[c, h] = z_steps(V, z_max, c, h, split, "max", quarters(("max", c - 1, h)), split)
-        merge = step(z_merge, 4, 1, makes=quarters(("max", 4, 1)), needs=quarters(("aside", 4, 1)) + quarters(("max", 3, 1)))
-        v_low = [[read(V, v_read_staged, q, j, makes=[("v", q, 0, j)], feed=(v_four_slots, q, j), feed_needs=[("g", 0, q), ("e", 0, 0)]) for j in range(4)] for q in range(2)]
-        v_high = [[read(S, v_read_plane, q, t, makes=[("v plane", q, t)], feed=(v_by_slot, q, t), feed_needs=[("g", 0, q), ("e", 0, 1)]) for t in range(4)] for q in range(2)]
-        scaled, shifted, direct_stores, classes, turned, turned_stores = {}, {}, {}, {}, {}, {}
-        for i in range(2, 8):
-            scaled[i] = read(V, direct_scale, i, makes=[("scaled", i)], needs=["r and d"], feed=(direct_product, i), feed_needs=[("h", 0, i // 4), ("h group", i // 2)] + both("v", 1))
-            shifted[i] = step(direct_shift, i, makes=[("direct", i)], needs=[("scaled", i)])
-            direct_stores[i] = step(direct_store, i, needs=[("direct", i)])
-        for group, n in TURNED:
-            operands = [("h", 0, group // 2), ("h group", group)] + both("v", n)
-            classes[group, n] = [read(S, class_read, group, n, m, makes=[("by class", group, n, m)], feed=(class_product, group, n, m), feed_needs=operands) for m in range(2)]
-            tiles = (2 * group, 2 * group + 1)
-            turned[group, n] = [read(S, turned_read, i, n, makes=[("turned", i, n)], feed=(turn_back, i, n), feed_needs=quarters(("by class", group, n), 0, 2)) for i in tiles]
-            turned_stores[group, n] = [step(turned_store, i, n, needs=[("turned", i, n)]) for i in tiles]
-        small_loads = [step(load, rows_raw[0:ROW_A, :], b.rearrange("(c n) -> c n", n=512)), step(load, rows_raw[ROW_A:ROW_R, :], a.rearrange("(c n) -> c n", n=512))]
-        small_loads += [step(load, rows[row : row + 2, :], vector.rearrange("(o n) -> o n", o=2), makes=[("row", row)]) for row, vector in ((ROW_R, r), (ROW_D, d))]
+        def widen(engine, *tiles):
+            return [step(x_widen, i, engine, makes=[("wide", i)], needs=[("x raw", i)] + [(x_turn, i - 4)] * (i >= 4)) for i in tiles]
 
-        sync_lane = (
-            [load_x(0, 0), step(load, xs[:], x_scale.rearrange("o (q p t) -> p (o q) t", q=2, t=4)), load_x(0, 1)]
-            + loads_w(0)[:1] + [load_x(1, 0)] + loads_w(0)[1:] + loads_w(1)[:1] + [load_x(1, 1)] + loads_w(1)[1:] + small_loads
-            + loads_w(2) + [load_g(0), load_e(0), load_g(1)] + loads_w(3) + loads_w(4) + [load_e(1)] + loads_w(5)
-            + [step(load, r_all[:], r[512:C].partition_broadcast(P)), step(load, d_all[:], d[512:C].partition_broadcast(P), makes=["r and d"])]
-            + turned_stores[0, 0] + turned_stores[1, 0] + turned_stores[0, 1] + [direct_stores[i] for i in range(2, 6)]
-            + turned_stores[2, 0] + [direct_stores[6]] + turned_stores[3, 0] + [direct_stores[7]]
-        )
-        vector_lane = (
-            widen(0, (0, 1, 2), V) + x_reads[0]
-            + [quant("w", 0, 0), quant_x(0, 0), quant_x(0, 1), quant("w", 0, 1), quant("w", 1, 0, heir=("w", 1, 1))]
-            + x_reads[1][:2] + [quant("w", 1, 1, heir=("w", 2, 1))] + x_reads[1][2:] + z[1, 0]
-            + [quant("w", 2, 0), quant("w", 2, 1), quant_x(1, 0), quant("g", 0, 0), quant("e", 0, 0, heir=("w", 3, 1)), quant_x(1, 1)]
-            + z[2, 0] + v_low[0] + z[1, 1] + e_reads[1]
-            + [quant("w", 3, 0), quant("w", 3, 1), quant("g", 0, 1), quant("w", 4, 0), quant("e", 0, 1, heir=("w", 5, 0)), quant("w", 4, 1)]
-            + z[2, 1] + v_low[1]
-            + [quant("w", 5, 0), quant("w", 5, 1), quant("v", 0, 0), quant("h", 0, 0, heir=("v", 0, 1)), quant("v", 1, 0)]
-            + z[4, 0] + z[5, 0]
-            + [stage_h(V, 1, 0, first=2), quant_part(0), quant("v", 0, 1), quant_part(1), merge, quant("v", 1, 1), quant("h", 0, 1)]
-            + z[5, 1] + [scaled[2], scaled[3], quant_part(2), stage_h(V, 1, 1, first=2), shifted[2], quant_part(3)]
-            + [scaled[4], shifted[3], scaled[5], shifted[4], shifted[5], scaled[6], shifted[6], scaled[7], shifted[7]]
-        )
-        gpsimd_lane = [
-            stage(G, "w", 0, 0, last=3), stage(G, "w", 0, 1, first=2),
-            stage(G, "w", 1, 1, last=2, inherited=True),
-            stage(G, "w", 2, 1, inherited=True), stage(G, "w", 2, 0, last=1),
-            stage(G, "w", 3, 1, inherited=True), stage(G, "w", 4, 1), stage(G, "w", 4, 0, last=2),
-            stage(G, "w", 5, 0, inherited=True), stage(G, "w", 5, 1, first=2),
-            stage_v(G, 0, inherited=True), stage_v(G, 1, last=3),
-            stage_h(G, 1, 1, last=2),
+        def last_first(steps):
+            return steps[-1:] + steps[:-1]
+
+        def pairs(steps):
+            return [steps[n ^ 1] for n in range(len(steps))]
+
+        x_reads = [read(V, x_read, i, makes=[(("x read", i // 4), i % 4)], needs=parts(("codes", ("x", 0)), 0, 2 * (i // 4)), feed=(x_turn, i), feed_needs=[("wide", i)]) for i in range(8)]
+        column_read = [read(S, columns_read, makes=["columns"], feed=(columns_product,), feed_needs=["rows"])]
+        small_loads = [step(load, rows_raw[0:4, :], b[0:2048].rearrange("(c n) -> c n", n=512)), step(load, rows_raw[4:ROW_A, :], b[2048:3072].rearrange("(c n) -> c n", n=512))]
+        small_loads += [step(load, rows_raw[ROW_A:ROW_R, :], a.rearrange("(c n) -> c n", n=512))]
+        small_loads += [step(load, rows[row : row + 2, :], vector.rearrange("(o n) -> o n", o=2), makes=[("row", row)]) for row, vector in ((ROW_R, r), (ROW_D, d))]
+        load_xs = step(load, xs[:], x_scale.rearrange("o (q p t) -> p (o q) t", q=2, t=4), makes=["xs"])
+        load_rd = [step(load, r_all[:], r[C - SPREAD : C].partition_broadcast(P)), step(load, d_all[:], d[C - SPREAD : C].partition_broadcast(P), makes=["r and d"])]
+        g_loads = [step(load_g, f, makes=[("raw", "g", f)], lender=None if f else raws) for f in range(2)]
+
+        def e_reads(n, engine):
+            return [read(engine, e_read, n, j, engine, makes=parts(("e", n), 2 * j, 2 * j + 2), feed=(e_turn, n, j), feed_needs=[("e raw", n)]) for j in range(2)]
+
+        def W(c):
+            return ("w", c)
+
+        z = {(c, h): z_steps(c, h, split=c == 5) for c in range(6) for h in range(2)}
+        z[4, 1] = z_steps(4, 1, aside=4)
+        e0, e1 = e_reads(0, S), e_reads(1, V)
+        vl = [v_low(f, 0) for f in range(2)]
+        vh = [v_high(f, 1) for f in range(2)]
+        TURNED = [((0, 1), 0), ((2, 3), 0), ((0, 1), 1), ((4, 5), 0), ((6, 7), 0)]
+        cl = [classes(*unit) for unit in TURNED]
+        tu = [turned(*unit) for unit in TURNED]
+        sc = {i: scaled(i, 1) for i in range(8)}
+        HALF = (slice(0, 256), slice(256, 512))
+        sc[7] = scaled(7, 1, HALF[0])
+
+        def late_first(steps):
+            return steps[2:] + steps[:2]
+
+        head_g = [stage(G, W(0), 2, 4, q=0), stage(G, W(0), 2, 4, q=1)]
+        head_s = [stage(S, W(0), 0, 2, q=0), stage(S, W(0), 0, 2, q=1), stage(S, W(1), 0, 2, q=0), stage(S, W(1), 0, 2, q=1)]
+        p1, pg = passed(W(1), 0, 1, inherited=True), passed("g", 1, 0)
+        gpsimd_lane = head_g + [
+            stage(G, W(1), 2, 4, q=1, inherited=True),
+            stage(G, W(2), 2, 4, inherited=True), stage(G, W(2), 1, 2),
+            stage(G, W(3), 2, 4, inherited=True), stage(G, W(4), 2, 4), stage(G, W(4), 0, 2, quarters=(0, 3)),
+            stage(G, W(5), 2, 4, inherited=True), stage(G, W(5), 1, 2),
+            stage_v(G, 1, 0, inherited=True), stage_v(G, 1, 1, last=2),
+            stage_h(G, 1, 0, first=2, inherited=True, home="late h"), stage_h(G, 1, 1, last=2, split=True),
         ]
         scalar_lane = (
-            widen(0, (3,), S) + [stage(S, "w", 0, 0, first=3)] + widen(1, (0, 1), S) + [stage(S, "w", 0, 1, last=2), stage(S, "w", 1, 0, last=2)] + passed_w10
-            + widen(1, (2,), S) + [step(permute_rows, makes=["rows"], needs=[("row", ROW_D)])] + widen(1, (3,), S) + passed_w11 + column_read
-            + z[0, 0] + [stage(S, "w", 2, 0, first=1), stage(S, "g", 0, 0)] + e_reads[0] + [stage(S, "w", 3, 0)] + passed_g1
-            + z[0, 1][:2] + [stage(S, "g", 0, 1, first=2)] + z[0, 1][2:] + [stage(S, "w", 4, 0, first=2), stage_h(S, 0, 0), stage(S, "w", 5, 1, last=2)]
-            + z[3, 0] + z[3, 1] + v_high[0] + v_high[1][:2] + [stage_h(S, 0, 1, last=2)] + v_high[1][2:]
-            + z[4, 1][:2] + [stage_v(S, 1, first=3), stage_h(S, 1, 0, last=2)] + z[4, 1][2:] + [stage_h(S, 0, 1, first=2)]
-            + classes[0, 0] + classes[1, 0] + turned[0, 0] + classes[0, 1] + turned[1, 0] + turned[0, 1]
-            + classes[2, 0] + classes[3, 0] + turned[2, 0] + turned[3, 0]
+            widen(S, 3) + head_s[:2] + widen(S, 4) + head_s[2:] + widen(S, 5) + [step(permute_rows, makes=["rows"], needs=[("row", ROW_D)]), p1] + widen(S, 6) + column_read + widen(S, 7)
+            + late_first(z[0, 0]) + [stage(S, W(2), 0, 1), stage(S, "g", 0, 4, q=0)] + e0 + [stage(S, W(3), 0, 2), pg]
+            + z[0, 1][:2] + [stage(S, "g", 2, 4, q=1)] + z[0, 1][2:] + [stage(S, W(4), 0, 2, quarters=(3, 4)), stage_h(S, 0, 0), stage(S, W(5), 0, 1)]
+            + late_first(z[3, 0]) + z[3, 1] + vh[0] + vh[1][:2] + [stage_h(S, 1, 0, last=2)] + vh[1][2:]
+            + [stage_v(S, 1, 1, first=2)] + z[4, 1][:1] + [stage_h(S, 0, 1, last=2, split=True)] + z[4, 1][1:]
+            + cl[0] + cl[1] + tu[0] + cl[2][:1] + tu[1] + cl[2][1:] + cl[3][:1] + tu[2] + cl[3][1:] + cl[4][:1] + tu[3] + cl[4][1:] + tu[4]
+        )
+        vector_lane = (
+            widen(V, 0, 1, 2) + x_reads[0:4]
+            + [quant_w(W(0), 1), quant_x(0), quant_w(W(0), 0), quant_w(W(1), 0, heir=(W(1), 1))]
+            + x_reads[4:6] + [quant_w(W(1), 1, heir=(W(2), 1))] + x_reads[6:8] + z[1, 0]
+            + [quant_w(W(2), 0), quant_x(1), quant_g(0), quant_w(W(2), 1), quant(("e", 0), heir=(W(3), 1))]
+            + z[2, 0] + vl[0] + z[1, 1] + e1
+            + [quant_w(W(3), 1), quant_w(W(3), 0), quant_g(1), quant_w(W(4), 0), quant(("e", 1), heir=(W(5), 1)), quant_w(W(4), 1)]
+            + z[2, 1] + vl[1]
+            + [quant_w(W(5), 1), quant_w(W(5), 0), quant(("v", 0, 0)), quant(("h", 0, 0), heir=("v", 1, 0)), quant(("v", 0, 1))]
+            + z[4, 0] + z[5, 0]
+            + [stage_h(V, 0, 1, first=2), quant(("h", 0, 1), last=1), quant(("v", 1, 0)), quant(("h", 0, 1), first=1), quant(("h", 1, 0), last=1, release=True), merge(4, 1, 4), quant(("v", 1, 1), heir=("late h", 1, 0))]
+            + z[5, 1] + [sc[2], quant(("h", 1, 1), last=1), stage_h(V, 1, 1, first=2), quant(("h", 1, 0), first=1, home="late h"), shifted(V, 2, 1), quant(("h", 1, 1), first=1)]
+            + [sc[3], sc[4], shifted(V, 3, 1), shifted(V, 4, 1), sc[5], sc[6], shifted(V, 5, 1), shifted(V, 6, 1), sc[7], scaled(7, 1, HALF[1]), shifted(V, 7, 1, HALF[0]), shifted(V, 7, 1, HALF[1])]
         )
         tensor_lane = feeds(
-            x_reads[0] + x_reads[1][:2] + passed_w10 + passed_w11 + z[0, 0][:1] + column_read + z[0, 0][1:2] + x_reads[1][2:] + z[0, 0][2:]
-            + z[1, 0] + e_reads[0] + passed_g1 + z[2, 0] + z[0, 1][:2] + v_low[0][:2] + z[0, 1][2:] + v_low[0][2:] + z[1, 1] + e_reads[1] + z[2, 1]
-            + z[3, 0] + z[3, 1][:3] + v_low[1][:2] + z[3, 1][3:] + v_low[1][2:] + v_high[0] + z[4, 0][:3] + v_high[1][:2] + z[4, 0][3:] + v_high[1][2:]
-            + z[4, 1][:2] + z[5, 0] + z[4, 1][2:] + z[5, 1][:3] + classes[0, 0] + classes[1, 0] + z[5, 1][3:]
-            + turned[0, 0] + classes[0, 1] + [scaled[2], scaled[3]] + turned[1, 0] + turned[0, 1]
-            + [scaled[4]] + classes[2, 0] + [scaled[5]] + classes[3, 0] + [scaled[6]] + turned[2, 0] + [scaled[7]] + turned[3, 0]
+            x_reads[0:4] + [p1] + x_reads[4:5] + late_first(z[0, 0])[:1] + x_reads[5:6] + column_read + late_first(z[0, 0])[1:2] + x_reads[6:7] + late_first(z[0, 0])[2:3] + x_reads[7:8] + late_first(z[0, 0])[3:]
+            + z[1, 0] + e0 + [pg] + z[2, 0][:2] + z[0, 1][:2] + z[2, 0][2:] + z[0, 1][2:3] + vl[0][:2] + z[0, 1][3:] + vl[0][2:] + z[1, 1] + e1 + z[2, 1]
+            + late_first(z[3, 0]) + z[3, 1][:3] + vl[1][:2] + z[3, 1][3:] + vl[1][2:] + vh[0] + z[4, 0][:3] + vh[1][:2] + z[4, 0][3:] + vh[1][2:]
+            + z[4, 1][:2] + z[5, 0] + z[4, 1][2:] + z[5, 1][:3] + cl[0] + cl[1] + z[5, 1][3:] + tu[0] + cl[2][:1] + tu[1] + [sc[2]] + cl[2][1:] + [sc[3], sc[4]] + cl[3][:1] + tu[2] + cl[3][1:]
+            + [sc[5]] + cl[4][:1] + [sc[6]] + tu[3] + cl[4][1:] + [sc[7]] + tu[4]
+        )
+        sync_lane = (
+            [load_x(0, 2), load_xs, load_x(2, 4)] + loads_w(0) + [load_x(4, 6)] + loads_w(1) + [load_x(6, 8)] + small_loads + loads_w(2) + [g_loads[0], load_e(0), g_loads[1]]
+            + loads_w(3) + loads_w(4) + [load_e(1)] + loads_w(5) + load_rd
+            + [stored(0, 0), stored(1, 0), stored(2, 0), stored(3, 0), stored(2, 1), stored(0, 1), stored(1, 1), stored(3, 1), stored(4, 1)]
+            + [stored(4, 0), stored(5, 0), stored(5, 1), stored(6, 1), stored(6, 0), stored(7, 1, HALF[0]), stored(7, 1, HALF[1]), stored(7, 0)]
         )
 
         make_identity(nc, ident[:])
@@ -473,6 +554,6 @@ def tile_maxout_generated_head_f5_kernel(tc, x_bytes, x_scale, w, b, e, g, a, r,
                     fresh.extend(makes)
                     allowed = allowed - 1
                     moved = True
-            assert moved
+            assert moved, [(lane[0][0][0], lane[0][0][1:], [name for name in lane[0][2] if name not in made]) for lane in lanes if lane]
             for name in fresh:
                 made.add(name)

@@ -476,11 +476,11 @@ def tile_maxout_generated_head_f5_kernel(tc, x_bytes, x_scale, w, b, e, g, a, r,
             return ("w", c)
 
         z = {(c, h): z_steps(c, h, split=c == 5) for c in range(6) for h in range(2)}
-        z[4, 1] = z_steps(4, 1, aside=4)
+        z[4, 1] = z_steps(4, 1, aside=2)
         e0, e1 = e_reads(0, S), e_reads(1, V)
         vl = [v_low(f, 0) for f in range(2)]
         vh = [v_high(f, 1) for f in range(2)]
-        TURNED = [((0, 1), 0), ((2, 3), 0), ((0, 1), 1), ((4, 5), 0), ((6, 7), 0)]
+        TURNED = [((0, 1), 0), ((2, 3), 0), ((4, 5), 0), ((6, 7), 0)]
         cl = [classes(*unit) for unit in TURNED]
         tu = [turned(*unit) for unit in TURNED]
         sc = {i: scaled(i, 1) for i in range(8)}
@@ -495,19 +495,19 @@ def tile_maxout_generated_head_f5_kernel(tc, x_bytes, x_scale, w, b, e, g, a, r,
         p1, pg = passed(W(1), 0, 1, inherited=True), passed("g", 1, 0)
         gpsimd_lane = head_g + [
             stage(G, W(1), 2, 4, q=1, inherited=True),
-            stage(G, W(2), 2, 4, inherited=True), stage(G, W(2), 1, 2),
-            stage(G, W(3), 2, 4, inherited=True), stage(G, W(4), 2, 4), stage(G, W(4), 0, 2, quarters=(0, 3)),
-            stage(G, W(5), 2, 4, inherited=True), stage(G, W(5), 1, 2),
+            stage(G, W(2), 2, 4, inherited=True), stage(G, W(2), 0, 2, quarters=(3, 4)),
+            stage(G, W(3), 2, 4, inherited=True), stage(G, W(4), 2, 4), stage(G, W(4), 1, 2),
+            stage(G, W(5), 2, 4, inherited=True), stage(G, W(5), 0, 2, quarters=(3, 4)),
             stage_v(G, 1, 0, inherited=True), stage_v(G, 1, 1, last=2),
             stage_h(G, 1, 0, first=2, inherited=True, home="late h"), stage_h(G, 1, 1, last=2, split=True),
         ]
         scalar_lane = (
-            widen(S, 3) + head_s[:2] + widen(S, 4) + head_s[2:] + widen(S, 5) + [step(permute_rows, makes=["rows"], needs=[("row", ROW_D)]), p1] + widen(S, 6) + column_read + widen(S, 7)
-            + late_first(z[0, 0]) + [stage(S, W(2), 0, 1), stage(S, "g", 0, 4, q=0)] + e0 + [stage(S, W(3), 0, 2), pg]
-            + z[0, 1][:2] + [stage(S, "g", 2, 4, q=1)] + z[0, 1][2:] + [stage(S, W(4), 0, 2, quarters=(3, 4)), stage_h(S, 0, 0), stage(S, W(5), 0, 1)]
-            + late_first(z[3, 0]) + z[3, 1] + vh[0] + vh[1][:2] + [stage_h(S, 1, 0, last=2)] + vh[1][2:]
-            + [stage_v(S, 1, 1, first=2)] + z[4, 1][:1] + [stage_h(S, 0, 1, last=2, split=True)] + z[4, 1][1:]
-            + cl[0] + cl[1] + tu[0] + cl[2][:1] + tu[1] + cl[2][1:] + cl[3][:1] + tu[2] + cl[3][1:] + cl[4][:1] + tu[3] + cl[4][1:] + tu[4]
+            widen(S, 3) + head_s[:1] + widen(S, 4, 5) + head_s[1:3] + widen(S, 6) + head_s[3:] + [step(permute_rows, makes=["rows"], needs=[("row", ROW_D)])] + widen(S, 7) + [p1] + column_read
+            + late_first(z[0, 0]) + [stage(S, W(2), 0, 2, quarters=(0, 3)), stage(S, "g", 0, 4, q=0)] + e0 + [stage(S, W(3), 0, 2), pg]
+            + z[0, 1][:2] + [stage(S, "g", 2, 4, q=1)] + z[0, 1][2:] + [stage(S, W(4), 0, 1), stage_h(S, 0, 0), stage(S, W(5), 0, 2, quarters=(0, 3))]
+            + late_first(z[3, 0]) + z[3, 1] + vh[0] + vh[1]
+            + [stage_v(S, 1, 1, first=2)] + z[4, 1][:1] + [stage_h(S, 0, 1, last=2, split=True), stage_h(S, 0, 1, first=2)] + z[4, 1][1:2] + [stage_h(S, 1, 0, last=2)]
+            + cl[0] + cl[1] + tu[0] + [stage_h(S, 1, 1, first=2)] + tu[1] + cl[2] + tu[2] + cl[3] + tu[3]
         )
         vector_lane = (
             widen(V, 0, 1, 2) + x_reads[0:4]
@@ -519,22 +519,21 @@ def tile_maxout_generated_head_f5_kernel(tc, x_bytes, x_scale, w, b, e, g, a, r,
             + z[2, 1] + vl[1]
             + [quant_w(W(5), 1), quant_w(W(5), 0), quant(("v", 0, 0)), quant(("h", 0, 0), heir=("v", 1, 0)), quant(("v", 0, 1))]
             + z[4, 0] + z[5, 0]
-            + [stage_h(V, 0, 1, first=2), quant(("h", 0, 1), last=1), quant(("v", 1, 0)), quant(("h", 0, 1), first=1), quant(("h", 1, 0), last=1, release=True), merge(4, 1, 4), quant(("v", 1, 1), heir=("late h", 1, 0))]
-            + z[5, 1] + [sc[2], quant(("h", 1, 1), last=1), stage_h(V, 1, 1, first=2), quant(("h", 1, 0), first=1, home="late h"), shifted(V, 2, 1), quant(("h", 1, 1), first=1)]
-            + [sc[3], sc[4], shifted(V, 3, 1), shifted(V, 4, 1), sc[5], sc[6], shifted(V, 5, 1), shifted(V, 6, 1), sc[7], scaled(7, 1, HALF[1]), shifted(V, 7, 1, HALF[0]), shifted(V, 7, 1, HALF[1])]
+            + z[4, 1][2:] + [quant(("h", 0, 1), last=1), quant(("v", 1, 0)), quant(("h", 0, 1), first=1), merge(4, 1, 2), quant(("v", 1, 1), heir=("late h", 1, 0))]
+            + z[5, 1] + [sc[0], sc[1], shifted(V, 0, 1), quant(("h", 1, 0), last=1, release=True), quant(("h", 1, 1), last=1), quant(("h", 1, 0), first=1, home="late h"), shifted(V, 1, 1), sc[2], sc[3], quant(("h", 1, 1), first=1), shifted(V, 2, 1), shifted(V, 3, 1)]
+            + [sc[4], sc[5], shifted(V, 4, 1), shifted(V, 5, 1), sc[6], sc[7], shifted(V, 6, 1), scaled(7, 1, HALF[1]), shifted(V, 7, 1, HALF[0]), shifted(V, 7, 1, HALF[1])]
         )
         tensor_lane = feeds(
-            x_reads[0:4] + [p1] + x_reads[4:5] + late_first(z[0, 0])[:1] + x_reads[5:6] + column_read + late_first(z[0, 0])[1:2] + x_reads[6:7] + late_first(z[0, 0])[2:3] + x_reads[7:8] + late_first(z[0, 0])[3:]
+            x_reads[0:6] + [p1] + late_first(z[0, 0])[:2] + column_read + x_reads[6:8] + late_first(z[0, 0])[2:]
             + z[1, 0] + e0 + [pg] + z[2, 0][:2] + z[0, 1][:2] + z[2, 0][2:] + z[0, 1][2:3] + vl[0][:2] + z[0, 1][3:] + vl[0][2:] + z[1, 1] + e1 + z[2, 1]
-            + late_first(z[3, 0]) + z[3, 1][:3] + vl[1][:2] + z[3, 1][3:] + vl[1][2:] + vh[0] + z[4, 0][:3] + vh[1][:2] + z[4, 0][3:] + vh[1][2:]
-            + z[4, 1][:2] + z[5, 0] + z[4, 1][2:] + z[5, 1][:3] + cl[0] + cl[1] + z[5, 1][3:] + tu[0] + cl[2][:1] + tu[1] + [sc[2]] + cl[2][1:] + [sc[3], sc[4]] + cl[3][:1] + tu[2] + cl[3][1:]
-            + [sc[5]] + cl[4][:1] + [sc[6]] + tu[3] + cl[4][1:] + [sc[7]] + tu[4]
+            + late_first(z[3, 0]) + z[3, 1][:3] + vl[1][:2] + z[3, 1][3:] + vl[1][2:] + vh[0] + z[4, 0][:2] + vh[1][:2] + z[4, 0][2:3] + vh[1][2:] + z[4, 0][3:]
+            + z[4, 1][:2] + z[5, 0] + z[4, 1][2:] + z[5, 1] + cl[0] + cl[1] + tu[0] + [sc[0], sc[1]] + tu[1] + [sc[2], sc[3]] + cl[2] + [sc[4], sc[5]] + tu[2] + cl[3] + [sc[6], sc[7]] + tu[3]
         )
         sync_lane = (
-            [load_x(0, 2), load_xs, load_x(2, 4)] + loads_w(0) + [load_x(4, 6)] + loads_w(1) + [load_x(6, 8)] + small_loads + loads_w(2) + [g_loads[0], load_e(0), g_loads[1]]
+            [load_x(0, 2), load_xs, load_x(2, 4)] + loads_w(0)[:1] + [load_x(4, 6)] + loads_w(0)[1:] + loads_w(1)[:1] + [load_x(6, 8)] + loads_w(1)[1:] + small_loads + loads_w(2) + [g_loads[0], load_e(0), g_loads[1]]
             + loads_w(3) + loads_w(4) + [load_e(1)] + loads_w(5) + load_rd
-            + [stored(0, 0), stored(1, 0), stored(2, 0), stored(3, 0), stored(2, 1), stored(0, 1), stored(1, 1), stored(3, 1), stored(4, 1)]
-            + [stored(4, 0), stored(5, 0), stored(5, 1), stored(6, 1), stored(6, 0), stored(7, 1, HALF[0]), stored(7, 1, HALF[1]), stored(7, 0)]
+            + [stored(0, 0), stored(1, 0), stored(0, 1), stored(2, 0), stored(1, 1), stored(3, 0), stored(2, 1), stored(4, 0), stored(3, 1), stored(5, 0), stored(4, 1), stored(5, 1)]
+            + [stored(6, 0), stored(6, 1), stored(7, 0), stored(7, 1, HALF[0]), stored(7, 1, HALF[1])]
         )
 
         make_identity(nc, ident[:])

@@ -170,10 +170,16 @@ def tile_maxout_generated_head_f5_kernel(tc, x_bytes, x_scale, w, b, e, g, a, r,
         def half_of(key, q, t):
             return q if key == "g" else t // 2
 
-        def stage_raw(key, qs, ts, engine, last):
+        unstaged = {}
+
+        def raw_of(key, count):
+            unstaged[key] = unstaged.get(key, 16) - count
+            return held["raw", key] if unstaged[key] else give(("raw", key))
+
+        def stage_raw(key, qs, ts, engine):
             half = half_of(key, qs.start // 2, ts.start)
             tile = hold(singles, (key, half))
-            raw = give(("raw", key)) if last else held["raw", key]
+            raw = raw_of(key, (qs.stop - qs.start) * (ts.stop - ts.start))
             blocks = slice(16 * qs.start, 16 * qs.stop)
             walk = "p B t i s" if engine is G else "p t B s i"
             if key in BY_HALVES:
@@ -189,9 +195,9 @@ def tile_maxout_generated_head_f5_kernel(tc, x_bytes, x_scale, w, b, e, g, a, r,
             else:
                 copy(engine, target[:, within, places], source[:, ts, columns_of])
 
-        def pass_raw(free, key, q, j, last):
+        def pass_raw(free, key, q, j):
             bank = take(free, ("pass bank", key, q, j))[:].bitcast(BF16)
-            raw = give(("raw", key)) if last else held["raw", key]
+            raw = raw_of(key, 4)
             for n in range(2):
                 source = raw_rows(raw, key, q).rearrange("p s (B t i) -> p t B s i", t=4, i=RUN)[:, 2 * j + n]
                 target = bank[:, block(n, 512)].rearrange("p (B i s) -> p B s i", i=RUN, s=4)
@@ -290,9 +296,15 @@ def tile_maxout_generated_head_f5_kernel(tc, x_bytes, x_scale, w, b, e, g, a, r,
             bank = give(("direct bank", i, n)) if cols.stop == 512 else held["direct bank", i, n]
             nc.vector.tensor_tensor(out=hold(results, ("result", i, n))[:, cols], in0=bank[:, cols], in1=r_all[:, spread_cols(n, cols)], op=MULT)
 
+        def spread_d(free):
+            nc.tensor.matmul(take(free, "d bank")[:], lhsT=ident_bf[:, ROW_D + 1 : ROW_D + 2].to_broadcast([P, P]), rhs=rows[:], start=True, stop=True)
+
         def direct_shift(i, n, cols, engine):
             part = held["result", i, n][:, cols]
-            engine.tensor_tensor(out=part, in0=part, in1=d_all[:, spread_cols(n, cols)], op=ADD)
+            if engine is V and "d bank" in held:
+                nc.vector.tensor_tensor(out=part, in0=held["d bank"][:, cols], in1=part, op=ADD)
+            else:
+                engine.tensor_tensor(out=part, in0=part, in1=d_all[:, spread_cols(n, cols)], op=ADD)
 
         def shift_into_heir(i, n):
             target = held.pop(("sum", i, n))[:].bitcast(F32)[:, 512:1024]
@@ -332,6 +344,10 @@ def tile_maxout_generated_head_f5_kernel(tc, x_bytes, x_scale, w, b, e, g, a, r,
         def turned_read(i, n, engine):
             copy(engine, take(results, ("result", i, n))[:], give(("turned bank", i, n))[:])
 
+        def warm_up(count):
+            for n in range(count):
+                nc.tensor.matmul(banks["S"][-1][:, 0:256], lhsT=ident[:].bitcast(BF16)[:, 0:P], rhs=ident[:].bitcast(BF16), start=True, stop=True)
+
         def step(*call, makes=(), needs=(), lender=None, feed=None):
             return call, list(makes), list(needs), lender, feed
 
@@ -348,22 +364,14 @@ def tile_maxout_generated_head_f5_kernel(tc, x_bytes, x_scale, w, b, e, g, a, r,
         def cells(key, qs, ts):
             return [(key, q, t) for q in range(qs.start, qs.stop) for t in range(ts.start, ts.stop)]
 
-        staged_cells = {}
-
         def stage(engine, key, first, last, q=None, inherited=False, quarters=(0, 4)):
             qs, ts = slice(*quarters) if q is None else slice(2 * q, 2 * q + 2), slice(first, last)
-            before = list(staged_cells.setdefault(key, []))
-            staged_cells[key].extend(cells(key, qs, ts))
-            final = len(staged_cells[key]) == 16
-            needs = [("raw", key, n // 2) for n in range(qs.start, qs.stop)] + [("inherited", (key, half_of(key, qs.start // 2, first)))] * inherited + before * final
-            return step(stage_raw, key, qs, ts, engine, final, makes=cells(key, qs, ts), needs=needs, lender=None if inherited else singles)
+            needs = [("raw", key, n // 2) for n in range(qs.start, qs.stop)] + [("inherited", (key, half_of(key, qs.start // 2, first)))] * inherited
+            return step(stage_raw, key, qs, ts, engine, makes=cells(key, qs, ts), needs=needs, lender=None if inherited else singles)
 
         def passed(key, q, j, inherited=False):
             qs, ts = slice(2 * q, 2 * q + 2), slice(2 * j, 2 * j + 2)
-            before = list(staged_cells.setdefault(key, []))
-            staged_cells[key].extend(cells(key, qs, ts))
-            final = len(staged_cells[key]) == 16
-            return read(S, passed_read, key, q, j, makes=cells(key, qs, ts), needs=[("inherited", (key, half_of(key, q, 2 * j)))] * inherited, lender=None if inherited else singles, feed=(pass_raw, key, q, j, final), feed_needs=[("raw", key, q)] + before * final)
+            return read(S, passed_read, key, q, j, makes=cells(key, qs, ts), needs=[("inherited", (key, half_of(key, q, 2 * j)))] * inherited, lender=None if inherited else singles, feed=(pass_raw, key, q, j), feed_needs=[("raw", key, q)])
 
         def quant_w(key, half, heir=None):
             return step(quantize_part, (key, half), key, 0, 2, heir, makes=parts(("codes", key), 2 * half, 2 * half + 2) + [("inherited", heir)], needs=cells(key, slice(0, 4), slice(2 * half, 2 * half + 2)))
@@ -427,8 +435,8 @@ def tile_maxout_generated_head_f5_kernel(tc, x_bytes, x_scale, w, b, e, g, a, r,
                 return step(direct_scale, i, n, cols, makes=[("scaled", i, n, cols.start)], needs=[("scaled", i, n, 0)])
             return read(V, direct_scale, i, n, cols, makes=[("scaled", i, n, 0)], needs=["r and d"], lender=results, feed=(direct_product, i, n), feed_needs=h_codes((i,)) + v_codes(n))
 
-        def shifted(engine, i, n, cols=WHOLE):
-            return step(direct_shift, i, n, cols, engine, makes=[("done", i, n, cols.start)], needs=[("scaled", i, n, cols.start)])
+        def shifted(engine, i, n, cols=WHOLE, after_d=False):
+            return step(direct_shift, i, n, cols, engine, makes=[("done", i, n, cols.start)], needs=[("scaled", i, n, cols.start)] + ["d bank"] * after_d)
 
         def shifted_heir(i, n):
             return step(shift_into_heir, i, n, makes=[("done", i, n, 0)], needs=[("scaled", i, n, 0), ("inherited", ("sum", i, n))])
@@ -485,28 +493,28 @@ def tile_maxout_generated_head_f5_kernel(tc, x_bytes, x_scale, w, b, e, g, a, r,
         tu = [turned(*unit) for unit in TURNED]
         sc = {i: scaled(i, 1) for i in range(8)}
         HALF = (slice(0, 256), slice(256, 512))
-        sc[7] = scaled(7, 1, HALF[0])
 
         def late_first(steps):
             return steps[2:] + steps[:2]
 
         head_g = [stage(G, W(0), 2, 4, q=0), stage(G, W(0), 2, 4, q=1)]
-        head_s = [stage(S, W(0), 0, 2, q=0), stage(S, W(0), 0, 2, q=1), stage(S, W(1), 0, 2, q=0), stage(S, W(1), 0, 2, q=1)]
+        p0 = passed(W(0), 1, 0)
+        head_s = [stage(S, W(0), 0, 2, q=0), p0, stage(S, W(1), 0, 2, q=0), stage(S, W(1), 0, 2, q=1)]
         p1, pg = passed(W(1), 0, 1, inherited=True), passed("g", 1, 0)
         gpsimd_lane = head_g + [
             stage(G, W(1), 2, 4, q=1, inherited=True),
             stage(G, W(2), 2, 4, inherited=True), stage(G, W(2), 0, 2, quarters=(3, 4)),
             stage(G, W(3), 2, 4, inherited=True), stage(G, W(4), 2, 4), stage(G, W(4), 1, 2),
-            stage(G, W(5), 2, 4, inherited=True), stage(G, W(5), 0, 2, quarters=(3, 4)),
+            stage(G, W(5), 2, 4, inherited=True), stage(G, W(5), 1, 2),
             stage_v(G, 1, 0, inherited=True), stage_v(G, 1, 1, last=2),
-            stage_h(G, 1, 0, first=2, inherited=True, home="late h"), stage_h(G, 1, 1, last=2, split=True),
+            stage_h(G, 1, 0, first=2, inherited=True, home="late h"), stage_h(G, 1, 1, last=2, split=True), shifted_heir(1, 1), shifted(G, 3, 1), shifted(G, 5, 1),
         ]
         scalar_lane = (
-            widen(S, 3) + head_s[:1] + widen(S, 4, 5) + head_s[1:3] + widen(S, 6) + head_s[3:] + [step(permute_rows, makes=["rows"], needs=[("row", ROW_D)])] + widen(S, 7) + [p1] + column_read
+            widen(S, 3) + head_s[:1] + widen(S, 4, 5) + head_s[2:3] + head_s[1:2] + head_s[3:] + widen(S, 6) + [step(permute_rows, makes=["rows"], needs=[("row", ROW_D)])] + widen(S, 7) + [p1] + column_read
             + late_first(z[0, 0]) + [stage(S, W(2), 0, 2, quarters=(0, 3)), stage(S, "g", 0, 4, q=0)] + e0 + [stage(S, W(3), 0, 2), pg]
-            + z[0, 1][:2] + [stage(S, "g", 2, 4, q=1)] + z[0, 1][2:] + [stage(S, W(4), 0, 1), stage_h(S, 0, 0), stage(S, W(5), 0, 2, quarters=(0, 3))]
+            + z[0, 1][:2] + [stage(S, "g", 2, 4, q=1)] + z[0, 1][2:] + [stage(S, W(4), 0, 1), stage_h(S, 0, 0), stage(S, W(5), 0, 1)]
             + late_first(z[3, 0]) + z[3, 1] + vh[0] + vh[1]
-            + [stage_v(S, 1, 1, first=2)] + z[4, 1][:1] + [stage_h(S, 0, 1, last=2, split=True), stage_h(S, 0, 1, first=2)] + z[4, 1][1:2] + [stage_h(S, 1, 0, last=2)]
+            + [stage_v(S, 1, 1, first=2)] + z[4, 1][:2] + [stage_h(S, 0, 1, last=2, split=True), stage_h(S, 0, 1, first=2), stage_h(S, 1, 0, last=2)]
             + cl[0] + cl[1] + tu[0] + [stage_h(S, 1, 1, first=2)] + tu[1] + cl[2] + tu[2] + cl[3] + tu[3]
         )
         vector_lane = (
@@ -520,20 +528,22 @@ def tile_maxout_generated_head_f5_kernel(tc, x_bytes, x_scale, w, b, e, g, a, r,
             + [quant_w(W(5), 1), quant_w(W(5), 0), quant(("v", 0, 0)), quant(("h", 0, 0), heir=("v", 1, 0)), quant(("v", 0, 1))]
             + z[4, 0] + z[5, 0]
             + z[4, 1][2:] + [quant(("h", 0, 1), last=1), quant(("v", 1, 0)), quant(("h", 0, 1), first=1), merge(4, 1, 2), quant(("v", 1, 1), heir=("late h", 1, 0))]
-            + z[5, 1] + [sc[0], sc[1], shifted(V, 0, 1), quant(("h", 1, 0), last=1, release=True), quant(("h", 1, 1), last=1), quant(("h", 1, 0), first=1, home="late h"), shifted(V, 1, 1), sc[2], sc[3], quant(("h", 1, 1), first=1), shifted(V, 2, 1), shifted(V, 3, 1)]
-            + [sc[4], sc[5], shifted(V, 4, 1), shifted(V, 5, 1), sc[6], sc[7], shifted(V, 6, 1), scaled(7, 1, HALF[1]), shifted(V, 7, 1, HALF[0]), shifted(V, 7, 1, HALF[1])]
+            + z[5, 1] + [sc[0], sc[1], shifted(V, 0, 1), quant(("h", 1, 0), last=1, release=True), quant(("h", 1, 1), last=1), quant(("h", 1, 0), first=1, home="late h"), quant(("h", 1, 1), first=1, heir=("sum", 1, 1)), sc[2], sc[3], shifted(V, 2, 1, after_d=True)]
+            + [sc[4], sc[5], shifted(V, 4, 1, after_d=True), sc[6], shifted(V, 6, 1, after_d=True), sc[7], shifted(V, 7, 1, after_d=True)]
         )
         tensor_lane = feeds(
-            x_reads[0:6] + [p1] + late_first(z[0, 0])[:2] + column_read + x_reads[6:8] + late_first(z[0, 0])[2:]
+            x_reads[0:4] + [p0] + x_reads[4:6] + [p1] + late_first(z[0, 0])[:2] + column_read + x_reads[6:8] + late_first(z[0, 0])[2:]
             + z[1, 0] + e0 + [pg] + z[2, 0][:2] + z[0, 1][:2] + z[2, 0][2:] + z[0, 1][2:3] + vl[0][:2] + z[0, 1][3:] + vl[0][2:] + z[1, 1] + e1 + z[2, 1]
             + late_first(z[3, 0]) + z[3, 1][:3] + vl[1][:2] + z[3, 1][3:] + vl[1][2:] + vh[0] + z[4, 0][:2] + vh[1][:2] + z[4, 0][2:3] + vh[1][2:] + z[4, 0][3:]
-            + z[4, 1][:2] + z[5, 0] + z[4, 1][2:] + z[5, 1] + cl[0] + cl[1] + tu[0] + [sc[0], sc[1]] + tu[1] + [sc[2], sc[3]] + cl[2] + [sc[4], sc[5]] + tu[2] + cl[3] + [sc[6], sc[7]] + tu[3]
+            + z[4, 1][:2] + z[5, 0] + z[4, 1][2:] + z[5, 1] + cl[0] + cl[1] + tu[0] + [sc[0], sc[1]] + tu[1] + [sc[2], sc[3]] + cl[2] + [sc[4], sc[5]] + tu[2] + [sc[6]] + cl[3] + [sc[7]] + tu[3]
         )
+        place = tensor_lane.index(feeds(tu[1])[0])
+        tensor_lane = tensor_lane[:place] + [step(spread_d, banks["S"], makes=["d bank"], lender=banks["S"])] + tensor_lane[place:]
         sync_lane = (
-            [load_x(0, 2), load_xs, load_x(2, 4)] + loads_w(0)[:1] + [load_x(4, 6)] + loads_w(0)[1:] + loads_w(1)[:1] + [load_x(6, 8)] + loads_w(1)[1:] + small_loads + loads_w(2) + [g_loads[0], load_e(0), g_loads[1]]
+            [load_x(0, 2), load_xs, load_x(2, 4)] + loads_w(0)[:1] + [load_x(4, 6)] + loads_w(0)[1:] + loads_w(1) + [load_x(6, 8)] + small_loads + loads_w(2) + [g_loads[0], load_e(0), g_loads[1]]
             + loads_w(3) + loads_w(4) + [load_e(1)] + loads_w(5) + load_rd
-            + [stored(0, 0), stored(1, 0), stored(0, 1), stored(2, 0), stored(1, 1), stored(3, 0), stored(2, 1), stored(4, 0), stored(3, 1), stored(5, 0), stored(4, 1), stored(5, 1)]
-            + [stored(6, 0), stored(6, 1), stored(7, 0), stored(7, 1, HALF[0]), stored(7, 1, HALF[1])]
+            + [stored(0, 0), stored(1, 0), stored(0, 1), stored(2, 0), stored(3, 0), stored(2, 1), stored(1, 1), stored(4, 0), stored(3, 1), stored(5, 0), stored(4, 1), stored(5, 1)]
+            + [stored(6, 1), stored(7, 1), stored(6, 0), stored(7, 0)]
         )
 
         make_identity(nc, ident[:])

@@ -507,7 +507,7 @@ def tile_maxout_generated_head_f5_kernel(tc, x_bytes, x_scale, w, b, e, g, a, r,
             stage(G, W(3), 2, 4, inherited=True), stage(G, W(4), 2, 4), stage(G, W(4), 1, 2),
             stage(G, W(5), 2, 4, inherited=True), stage(G, W(5), 1, 2),
             stage_v(G, 1, 0, inherited=True), stage_v(G, 1, 1, last=2),
-            stage_h(G, 1, 0, first=2, inherited=True, home="late h"), stage_h(G, 1, 1, last=2, split=True), shifted_heir(1, 1), shifted(G, 3, 1), shifted(G, 5, 1),
+            stage_h(G, 1, 0, first=2, inherited=True, home="late h"), stage_h(G, 1, 1, last=2, split=True), shifted_heir(1, 1), shifted(G, 4, 1),
         ]
         scalar_lane = (
             widen(S, 3) + head_s[:1] + widen(S, 4, 5) + head_s[2:3] + head_s[1:2] + head_s[3:] + widen(S, 6) + [step(permute_rows, makes=["rows"], needs=[("row", ROW_D)])] + widen(S, 7) + [p1] + column_read
@@ -528,8 +528,8 @@ def tile_maxout_generated_head_f5_kernel(tc, x_bytes, x_scale, w, b, e, g, a, r,
             + [quant_w(W(5), 1), quant_w(W(5), 0), quant(("v", 0, 0)), quant(("h", 0, 0), heir=("v", 1, 0)), quant(("v", 0, 1))]
             + z[4, 0] + z[5, 0]
             + z[4, 1][2:] + [quant(("h", 0, 1), last=1), quant(("v", 1, 0)), quant(("h", 0, 1), first=1), merge(4, 1, 2), quant(("v", 1, 1), heir=("late h", 1, 0))]
-            + z[5, 1] + [sc[0], sc[1], shifted(V, 0, 1), quant(("h", 1, 0), last=1, release=True), quant(("h", 1, 1), last=1), quant(("h", 1, 0), first=1, home="late h"), quant(("h", 1, 1), first=1, heir=("sum", 1, 1)), sc[2], sc[3], shifted(V, 2, 1, after_d=True)]
-            + [sc[4], sc[5], shifted(V, 4, 1, after_d=True), sc[6], shifted(V, 6, 1, after_d=True), sc[7], shifted(V, 7, 1, after_d=True)]
+            + z[5, 1] + [sc[0], sc[1], shifted(V, 0, 1), quant(("h", 1, 0), last=1, release=True), quant(("h", 1, 1), last=1), quant(("h", 1, 0), first=1, home="late h"), quant(("h", 1, 1), first=1, heir=("sum", 1, 1)), sc[2], sc[3], shifted(V, 2, 1, after_d=True), shifted(V, 3, 1, after_d=True)]
+            + [sc[4], sc[5], sc[6], shifted(V, 5, 1, after_d=True), shifted(V, 6, 1, after_d=True), sc[7], shifted(V, 7, 1, after_d=True)]
         )
         tensor_lane = feeds(
             x_reads[0:4] + [p0] + x_reads[4:6] + [p1] + late_first(z[0, 0])[:2] + column_read + x_reads[6:8] + late_first(z[0, 0])[2:]
@@ -542,8 +542,8 @@ def tile_maxout_generated_head_f5_kernel(tc, x_bytes, x_scale, w, b, e, g, a, r,
         sync_lane = (
             [load_x(0, 2), load_xs, load_x(2, 4)] + loads_w(0)[:1] + [load_x(4, 6)] + loads_w(0)[1:] + loads_w(1) + [load_x(6, 8)] + small_loads + loads_w(2) + [g_loads[0], load_e(0), g_loads[1]]
             + loads_w(3) + loads_w(4) + [load_e(1)] + loads_w(5) + load_rd
-            + [stored(0, 0), stored(1, 0), stored(0, 1), stored(2, 0), stored(3, 0), stored(2, 1), stored(1, 1), stored(4, 0), stored(3, 1), stored(5, 0), stored(4, 1), stored(5, 1)]
-            + [stored(6, 1), stored(7, 1), stored(6, 0), stored(7, 0)]
+            + [stored(0, 0), stored(1, 0), stored(0, 1), stored(2, 0), stored(3, 0), stored(2, 1), stored(3, 1), stored(1, 1), stored(4, 0), stored(5, 0), stored(5, 1), stored(4, 1)]
+            + [stored(6, 1), stored(6, 0), stored(7, 1), stored(7, 0)]
         )
 
         make_identity(nc, ident[:])

@@ -168,7 +168,7 @@ def tile_maxout_generated_head_f5_kernel(tc, x_bytes, x_scale, w, b, e, g, a, r,
             load(raw_rows(hold(raws, ("raw", "g")), "g", f), g[:, block(f, 512)].rearrange("(p s) n -> p s n", s=4))
 
         def half_of(key, q, t):
-            return q if key == "g" else t // 2
+            return q if key in BY_HALVES else t // 2
 
         unstaged = {}
 
@@ -188,8 +188,8 @@ def tile_maxout_generated_head_f5_kernel(tc, x_bytes, x_scale, w, b, e, g, a, r,
             else:
                 source = raw[:].rearrange(f"p (s B t i) -> {walk}", s=4, t=4, i=RUN)
                 columns_of = blocks
-            target = tile[:].rearrange(f"p (t B i s) -> {walk}", t=4 if key == "g" else 2, i=RUN, s=4)
-            places, within = (slice(blocks.start - 32 * half, blocks.stop - 32 * half), ts) if key == "g" else (blocks, slice(ts.start - 2 * half, ts.stop - 2 * half))
+            target = tile[:].rearrange(f"p (t B i s) -> {walk}", t=4 if key in BY_HALVES else 2, i=RUN, s=4)
+            places, within = (slice(blocks.start - 32 * half, blocks.stop - 32 * half), ts) if key in BY_HALVES else (blocks, slice(ts.start - 2 * half, ts.stop - 2 * half))
             if engine is G:
                 copy(engine, target[:, places, within], source[:, columns_of, ts])
             else:
@@ -205,7 +205,7 @@ def tile_maxout_generated_head_f5_kernel(tc, x_bytes, x_scale, w, b, e, g, a, r,
 
         def passed_read(key, q, j):
             words = hold(singles, (key, half_of(key, q, 2 * j)))[:].bitcast(F32)
-            target = words.rearrange("p (j t n) -> p j t n", j=2, t=2)[:, j] if key == "g" else words.rearrange("p (t q n) -> p q t n", t=2, q=2)[:, q]
+            target = words.rearrange("p (j t n) -> p j t n", j=2, t=2)[:, j] if key in BY_HALVES else words.rearrange("p (t q n) -> p q t n", t=2, q=2)[:, q]
             nc.scalar.copy(out=target, in_=give(("pass bank", key, q, j))[:].rearrange("p (t n) -> p t n", t=2))
 
         def quantize_part(key, operand, first, last, heir, release=True):
@@ -247,7 +247,7 @@ def tile_maxout_generated_head_f5_kernel(tc, x_bytes, x_scale, w, b, e, g, a, r,
             bank = take(free, ("z bank", c, h, s))
             for t, first, count, place in z_parts(s, split):
                 for q in range(2):
-                    product(bank[:, place], ("w", c), block(2 * t + q), ("x", h), span(512 * q + first, count), q == 0, q == 1)
+                    product(bank[:, place], ("w", c), block(4 * q + t if ("w", c) in BY_HALVES else 2 * t + q), ("x", h), span(512 * q + first, count), q == 0, q == 1)
 
         def z_bias(c, t):
             return columns[:, 2 * (c % J) + c // J, t : t + 1]
@@ -376,6 +376,9 @@ def tile_maxout_generated_head_f5_kernel(tc, x_bytes, x_scale, w, b, e, g, a, r,
         def quant_w(key, half, heir=None):
             return step(quantize_part, (key, half), key, 0, 2, heir, makes=parts(("codes", key), 2 * half, 2 * half + 2) + [("inherited", heir)], needs=cells(key, slice(0, 4), slice(2 * half, 2 * half + 2)))
 
+        def quant_pass(key, q, heir=None):
+            return step(quantize_part, (key, q), key, 0, 2, heir, makes=[("pass codes", key, q), ("inherited", heir)], needs=cells(key, slice(2 * q, 2 * q + 2), slice(0, 4)))
+
         def quant_g(f, heir=None):
             return step(quantize_part, ("g", f), "g", 0, 2, heir, makes=[("g codes", f), ("inherited", heir)], needs=cells("g", slice(2 * f, 2 * f + 2), slice(0, 4)))
 
@@ -403,7 +406,8 @@ def tile_maxout_generated_head_f5_kernel(tc, x_bytes, x_scale, w, b, e, g, a, r,
             steps = []
             for s in range(4):
                 slots = (2 * (s % 2), 2 * (s % 2) + 2) if split else (s, s + 1)
-                operands = codes(("w", c), *slots) + codes(("x", h))
+                weights = [("pass codes", ("w", c), q) for q in range(2)] if ("w", c) in BY_HALVES else codes(("w", c), *slots)
+                operands = weights + codes(("x", h))
                 if c % J == 0 or s < aside:
                     how = "aside" if c % J else "max"
                     steps.append(read(S, z_alone, c, h, s, how, makes=[((how, c, h), s)], needs=["columns"], feed=(z_product, c, h, s, False), feed_needs=operands))
@@ -497,12 +501,10 @@ def tile_maxout_generated_head_f5_kernel(tc, x_bytes, x_scale, w, b, e, g, a, r,
         def late_first(steps):
             return steps[2:] + steps[:2]
 
-        head_g = [stage(G, W(0), 2, 4, q=0), stage(G, W(0), 2, 4, q=1)]
-        p0 = passed(W(0), 1, 0)
-        head_s = [stage(S, W(0), 0, 2, q=0), p0, stage(S, W(1), 0, 2, q=0), stage(S, W(1), 0, 2, q=1)]
-        p1, pg = passed(W(1), 0, 1, inherited=True), passed("g", 1, 0)
-        gpsimd_lane = head_g + [
-            stage(G, W(1), 2, 4, q=1, inherited=True),
+        p0, p1, pg = passed(W(1), 0, 1), passed(W(1), 1, 1), passed("g", 1, 0)
+        gpsimd_lane = [
+            stage(G, W(0), 0, 3, q=0), stage(G, W(0), 2, 4, q=1),
+            stage(G, W(1), 0, 2, q=1, inherited=True),
             stage(G, W(2), 2, 4, inherited=True), stage(G, W(2), 0, 2, quarters=(3, 4)),
             stage(G, W(3), 2, 4, inherited=True), stage(G, W(4), 2, 4), stage(G, W(4), 1, 2),
             stage(G, W(5), 2, 4, inherited=True), stage(G, W(5), 1, 2),
@@ -510,8 +512,8 @@ def tile_maxout_generated_head_f5_kernel(tc, x_bytes, x_scale, w, b, e, g, a, r,
             stage_h(G, 1, 0, first=2, inherited=True, home="late h"), stage_h(G, 1, 1, last=2, split=True), shifted_heir(1, 1), shifted(G, 4, 1),
         ]
         scalar_lane = (
-            widen(S, 3) + head_s[:1] + widen(S, 4, 5) + head_s[2:3] + head_s[1:2] + head_s[3:] + widen(S, 6) + [step(permute_rows, makes=["rows"], needs=[("row", ROW_D)])] + widen(S, 7) + [p1] + column_read
-            + late_first(z[0, 0]) + [stage(S, W(2), 0, 2, quarters=(0, 3)), stage(S, "g", 0, 4, q=0)] + e0 + [stage(S, W(3), 0, 2), pg]
+            widen(S, 3) + [stage(S, W(0), 3, 4, q=0)] + widen(S, 4, 5) + [stage(S, W(0), 0, 2, q=1), stage(S, W(1), 0, 2, q=0), p0]
+            + widen(S, 6) + [step(permute_rows, makes=["rows"], needs=[("row", ROW_D)])] + widen(S, 7) + [p1] + column_read + z[0, 0] + [stage(S, W(2), 0, 2, quarters=(0, 3)), stage(S, "g", 0, 4, q=0)] + e0 + [stage(S, W(3), 0, 2), pg]
             + z[0, 1][:2] + [stage(S, "g", 2, 4, q=1)] + z[0, 1][2:] + [stage(S, W(4), 0, 1), stage_h(S, 0, 0), stage(S, W(5), 0, 1)]
             + late_first(z[3, 0]) + z[3, 1] + vh[0] + vh[1]
             + [stage_v(S, 1, 1, first=2)] + z[4, 1][:2] + [stage_h(S, 0, 1, last=2, split=True), stage_h(S, 0, 1, first=2), stage_h(S, 1, 0, last=2)]
@@ -519,9 +521,9 @@ def tile_maxout_generated_head_f5_kernel(tc, x_bytes, x_scale, w, b, e, g, a, r,
         )
         vector_lane = (
             widen(V, 0, 1, 2) + x_reads[0:4]
-            + [quant_w(W(0), 1), quant_x(0), quant_w(W(0), 0), quant_w(W(1), 0, heir=(W(1), 1))]
-            + x_reads[4:6] + [quant_w(W(1), 1, heir=(W(2), 1))] + x_reads[6:8] + z[1, 0]
-            + [quant_w(W(2), 0), quant_x(1), quant_g(0), quant_w(W(2), 1), quant(("e", 0), heir=(W(3), 1))]
+            + [quant_pass(W(0), 0), quant_x(0), quant_pass(W(0), 1), quant_pass(W(1), 0, heir=(W(1), 1))]
+            + x_reads[4:6] + [quant_pass(W(1), 1, heir=(W(2), 1))] + x_reads[6:8] + z[1, 0]
+            + [quant_w(W(2), 0), quant_w(W(2), 1), quant_x(1, last=1), quant_g(0), quant(("e", 0), heir=(W(3), 1)), quant_x(1, first=1)]
             + z[2, 0] + vl[0] + z[1, 1] + e1
             + [quant_w(W(3), 1), quant_w(W(3), 0), quant_g(1), quant_w(W(4), 0), quant(("e", 1), heir=(W(5), 1)), quant_w(W(4), 1)]
             + z[2, 1] + vl[1]
@@ -532,15 +534,15 @@ def tile_maxout_generated_head_f5_kernel(tc, x_bytes, x_scale, w, b, e, g, a, r,
             + [sc[4], sc[5], sc[6], shifted(V, 5, 1, after_d=True), shifted(V, 6, 1, after_d=True), sc[7], shifted(V, 7, 1, after_d=True)]
         )
         tensor_lane = feeds(
-            x_reads[0:4] + [p0] + x_reads[4:6] + [p1] + late_first(z[0, 0])[:2] + column_read + x_reads[6:8] + late_first(z[0, 0])[2:]
-            + z[1, 0] + e0 + [pg] + z[2, 0][:2] + z[0, 1][:2] + z[2, 0][2:] + z[0, 1][2:3] + vl[0][:2] + z[0, 1][3:] + vl[0][2:] + z[1, 1] + e1 + z[2, 1]
+            x_reads[0:6] + [p0, p1] + z[0, 0][:1] + column_read + z[0, 0][1:2] + x_reads[6:8] + z[0, 0][2:]
+            + z[1, 0] + e0 + [pg] + z[2, 0] + z[0, 1][:2] + vl[0][:2] + z[0, 1][2:] + vl[0][2:] + z[1, 1] + e1 + z[2, 1]
             + late_first(z[3, 0]) + z[3, 1][:3] + vl[1][:2] + z[3, 1][3:] + vl[1][2:] + vh[0] + z[4, 0][:2] + vh[1][:2] + z[4, 0][2:3] + vh[1][2:] + z[4, 0][3:]
             + z[4, 1][:2] + z[5, 0] + z[4, 1][2:] + z[5, 1] + cl[0] + cl[1] + tu[0] + [sc[0], sc[1]] + tu[1] + [sc[2], sc[3]] + cl[2] + [sc[4], sc[5]] + tu[2] + [sc[6]] + cl[3] + [sc[7]] + tu[3]
         )
         place = tensor_lane.index(feeds(tu[1])[0])
         tensor_lane = tensor_lane[:place] + [step(spread_d, banks["S"], makes=["d bank"], lender=banks["S"])] + tensor_lane[place:]
         sync_lane = (
-            [load_x(0, 2), load_xs, load_x(2, 4)] + loads_w(0)[:1] + [load_x(4, 6)] + loads_w(0)[1:] + loads_w(1) + [load_x(6, 8)] + small_loads + loads_w(2) + [g_loads[0], load_e(0), g_loads[1]]
+            [load_x(0, 2), load_xs, load_x(2, 4)] + loads_w(0)[:1] + [load_x(4, 6)] + loads_w(0)[1:] + loads_w(1)[:1] + [load_x(6, 8)] + loads_w(1)[1:] + small_loads + loads_w(2) + [g_loads[0], load_e(0), g_loads[1]]
             + loads_w(3) + loads_w(4) + [load_e(1)] + loads_w(5) + load_rd
             + [stored(0, 0), stored(1, 0), stored(0, 1), stored(2, 0), stored(3, 0), stored(2, 1), stored(3, 1), stored(1, 1), stored(4, 0), stored(5, 0), stored(5, 1), stored(4, 1)]
             + [stored(6, 1), stored(6, 0), stored(7, 1), stored(7, 0)]

@@ -173,17 +173,17 @@ def tile_maxout_generated_head_f5_kernel(tc, x_bytes, x_scale, w, b, e, g, a, r,
         unstaged = {}
 
         def raw_of(key, count):
-            unstaged[key] = unstaged.get(key, 16) - count
+            unstaged[key] = unstaged.get(key, 32) - count
             return held["raw", key] if unstaged[key] else give(("raw", key))
 
         def stage_raw(key, qs, ts, engine):
-            half = half_of(key, qs.start // 2, ts.start)
+            half = half_of(key, qs.start // 4, ts.start)
             tile = hold(singles, (key, half))
             raw = raw_of(key, (qs.stop - qs.start) * (ts.stop - ts.start))
-            blocks = slice(16 * qs.start, 16 * qs.stop)
+            blocks = slice(8 * qs.start, 8 * qs.stop)
             walk = "p B t i s" if engine is G else "p t B s i"
             if key in BY_HALVES:
-                source = raw_rows(raw, key, qs.start // 2).rearrange(f"p s (B t i) -> {walk}", t=4, i=RUN)
+                source = raw_rows(raw, key, qs.start // 4).rearrange(f"p s (B t i) -> {walk}", t=4, i=RUN)
                 columns_of = slice(blocks.start % 32, (blocks.stop - 1) % 32 + 1)
             else:
                 source = raw[:].rearrange(f"p (s B t i) -> {walk}", s=4, t=4, i=RUN)
@@ -197,7 +197,7 @@ def tile_maxout_generated_head_f5_kernel(tc, x_bytes, x_scale, w, b, e, g, a, r,
 
         def pass_raw(free, key, q, j):
             bank = take(free, ("pass bank", key, q, j))[:].bitcast(BF16)
-            raw = raw_of(key, 4)
+            raw = raw_of(key, 8)
             for n in range(2):
                 source = raw_rows(raw, key, q).rearrange("p s (B t i) -> p t B s i", t=4, i=RUN)[:, 2 * j + n]
                 target = bank[:, block(n, 512)].rearrange("p (B i s) -> p B s i", i=RUN, s=4)
@@ -364,23 +364,23 @@ def tile_maxout_generated_head_f5_kernel(tc, x_bytes, x_scale, w, b, e, g, a, r,
         def cells(key, qs, ts):
             return [(key, q, t) for q in range(qs.start, qs.stop) for t in range(ts.start, ts.stop)]
 
-        def stage(engine, key, first, last, q=None, inherited=False, quarters=(0, 4)):
-            qs, ts = slice(*quarters) if q is None else slice(2 * q, 2 * q + 2), slice(first, last)
-            needs = [("raw", key, n // 2) for n in range(qs.start, qs.stop)] + [("inherited", (key, half_of(key, qs.start // 2, first)))] * inherited
+        def stage(engine, key, first, last, q=None, inherited=False, eighths=(0, 8)):
+            qs, ts = slice(*eighths) if q is None else slice(4 * q, 4 * q + 4), slice(first, last)
+            needs = [("raw", key, n // 4) for n in range(qs.start, qs.stop)] + [("inherited", (key, half_of(key, qs.start // 4, first)))] * inherited
             return step(stage_raw, key, qs, ts, engine, makes=cells(key, qs, ts), needs=needs, lender=None if inherited else singles)
 
         def passed(key, q, j, inherited=False):
-            qs, ts = slice(2 * q, 2 * q + 2), slice(2 * j, 2 * j + 2)
+            qs, ts = slice(4 * q, 4 * q + 4), slice(2 * j, 2 * j + 2)
             return read(S, passed_read, key, q, j, makes=cells(key, qs, ts), needs=[("inherited", (key, half_of(key, q, 2 * j)))] * inherited, lender=None if inherited else singles, feed=(pass_raw, key, q, j), feed_needs=[("raw", key, q)])
 
         def quant_w(key, half, heir=None):
-            return step(quantize_part, (key, half), key, 0, 2, heir, makes=parts(("codes", key), 2 * half, 2 * half + 2) + [("inherited", heir)], needs=cells(key, slice(0, 4), slice(2 * half, 2 * half + 2)))
+            return step(quantize_part, (key, half), key, 0, 2, heir, makes=parts(("codes", key), 2 * half, 2 * half + 2) + [("inherited", heir)], needs=cells(key, slice(0, 8), slice(2 * half, 2 * half + 2)))
 
         def quant_pass(key, q, heir=None):
-            return step(quantize_part, (key, q), key, 0, 2, heir, makes=[("pass codes", key, q), ("inherited", heir)], needs=cells(key, slice(2 * q, 2 * q + 2), slice(0, 4)))
+            return step(quantize_part, (key, q), key, 0, 2, heir, makes=[("pass codes", key, q), ("inherited", heir)], needs=cells(key, slice(4 * q, 4 * q + 4), slice(0, 4)))
 
         def quant_g(f, heir=None):
-            return step(quantize_part, ("g", f), "g", 0, 2, heir, makes=[("g codes", f), ("inherited", heir)], needs=cells("g", slice(2 * f, 2 * f + 2), slice(0, 4)))
+            return step(quantize_part, ("g", f), "g", 0, 2, heir, makes=[("g codes", f), ("inherited", heir)], needs=cells("g", slice(4 * f, 4 * f + 4), slice(0, 4)))
 
         def quant_x(h, first=0, last=2, heir=None):
             return step(quantize_x, h, first, last, heir, makes=parts(("codes", ("x", h)), first, last) + [("inherited", heir)], needs=parts(("x read", h)))
@@ -505,7 +505,7 @@ def tile_maxout_generated_head_f5_kernel(tc, x_bytes, x_scale, w, b, e, g, a, r,
         gpsimd_lane = [
             stage(G, W(0), 0, 3, q=0), stage(G, W(0), 2, 4, q=1),
             stage(G, W(1), 0, 2, q=1, inherited=True),
-            stage(G, W(2), 2, 4, inherited=True), stage(G, W(2), 0, 2, quarters=(3, 4)),
+            stage(G, W(2), 2, 4, inherited=True), stage(G, W(2), 0, 2, eighths=(5, 8)),
             stage(G, W(3), 2, 4, inherited=True), stage(G, W(4), 2, 4), stage(G, W(4), 1, 2),
             stage(G, W(5), 2, 4, inherited=True), stage(G, W(5), 1, 2),
             stage_v(G, 1, 0, inherited=True), stage_v(G, 1, 1, last=2),
@@ -513,7 +513,7 @@ def tile_maxout_generated_head_f5_kernel(tc, x_bytes, x_scale, w, b, e, g, a, r,
         ]
         scalar_lane = (
             widen(S, 3) + [stage(S, W(0), 3, 4, q=0)] + widen(S, 4, 5) + [stage(S, W(0), 0, 2, q=1), stage(S, W(1), 0, 2, q=0), p0]
-            + widen(S, 6) + [step(permute_rows, makes=["rows"], needs=[("row", ROW_D)])] + widen(S, 7) + [p1] + column_read + z[0, 0] + [stage(S, W(2), 0, 2, quarters=(0, 3)), stage(S, "g", 0, 4, q=0)] + e0 + [stage(S, W(3), 0, 2), pg]
+            + widen(S, 6) + [step(permute_rows, makes=["rows"], needs=[("row", ROW_D)])] + widen(S, 7) + [p1] + column_read + z[0, 0] + [stage(S, W(2), 0, 2, eighths=(0, 5)), stage(S, "g", 0, 4, q=0)] + e0 + [stage(S, W(3), 0, 2), pg]
             + z[0, 1][:2] + [stage(S, "g", 2, 4, q=1)] + z[0, 1][2:] + [stage(S, W(4), 0, 1), stage_h(S, 0, 0), stage(S, W(5), 0, 1)]
             + late_first(z[3, 0]) + z[3, 1] + vh[0] + vh[1]
             + [stage_v(S, 1, 1, first=2)] + z[4, 1][:2] + [stage_h(S, 0, 1, last=2, split=True), stage_h(S, 0, 1, first=2), stage_h(S, 1, 0, last=2)]
@@ -523,7 +523,7 @@ def tile_maxout_generated_head_f5_kernel(tc, x_bytes, x_scale, w, b, e, g, a, r,
             widen(V, 0, 1, 2) + x_reads[0:4]
             + [quant_pass(W(0), 0), quant_x(0), quant_pass(W(0), 1), quant_pass(W(1), 0, heir=(W(1), 1))]
             + x_reads[4:6] + [quant_pass(W(1), 1, heir=(W(2), 1))] + x_reads[6:8] + z[1, 0]
-            + [quant_w(W(2), 0), quant_w(W(2), 1), quant_x(1, last=1), quant_g(0), quant(("e", 0), heir=(W(3), 1)), quant_x(1, first=1)]
+            + [quant_w(W(2), 0), quant_w(W(2), 1), quant_x(1), quant(("e", 0), heir=(W(3), 1)), quant_g(0)]
             + z[2, 0] + vl[0] + z[1, 1] + e1
             + [quant_w(W(3), 1), quant_w(W(3), 0), quant_g(1), quant_w(W(4), 0), quant(("e", 1), heir=(W(5), 1)), quant_w(W(4), 1)]
             + z[2, 1] + vl[1]
@@ -542,7 +542,7 @@ def tile_maxout_generated_head_f5_kernel(tc, x_bytes, x_scale, w, b, e, g, a, r,
         place = tensor_lane.index(feeds(tu[1])[0])
         tensor_lane = tensor_lane[:place] + [step(spread_d, banks["S"], makes=["d bank"], lender=banks["S"])] + tensor_lane[place:]
         sync_lane = (
-            [load_x(0, 2), load_xs, load_x(2, 4)] + loads_w(0)[:1] + [load_x(4, 6)] + loads_w(0)[1:] + loads_w(1)[:1] + [load_x(6, 8)] + loads_w(1)[1:] + small_loads + loads_w(2) + [g_loads[0], load_e(0), g_loads[1]]
+            [load_x(0, 2), load_xs, load_x(2, 4)] + loads_w(0)[:1] + [load_x(4, 6)] + loads_w(0)[1:] + loads_w(1) + [load_x(6, 8)] + small_loads + loads_w(2) + [g_loads[0], load_e(0), g_loads[1]]
             + loads_w(3) + loads_w(4) + [load_e(1)] + loads_w(5) + load_rd
             + [stored(0, 0), stored(1, 0), stored(0, 1), stored(2, 0), stored(3, 0), stored(2, 1), stored(3, 1), stored(1, 1), stored(4, 0), stored(5, 0), stored(5, 1), stored(4, 1)]
             + [stored(6, 1), stored(6, 0), stored(7, 1), stored(7, 0)]

from contextlib import ExitStack

import concourse.mybir as mybir
from concourse.masks import make_identity

M, K, J, F, D, C = 1024, 1024, 3, 1024, 512, 1024
FLOPS = 2 * M * K * J * F + 2 * C * D * F + 2 * M * F * C

P = 128
F32 = mybir.dt.float32
BF16 = mybir.dt.bfloat16
U8 = mybir.dt.uint8
U32 = mybir.dt.uint32
FP8 = mybir.dt.float8_e4m3fn
FP8X4 = mybir.dt.float8_e4m3fn_x4
ADD = mybir.AluOpType.add
MULT = mybir.AluOpType.mult
MAX = mybir.AluOpType.max
IDENTITY = mybir.ActivationFunctionType.Identity

RUN = 4
N_SINGLES, N_RAWS, N_PLANES, N_RESULTS, N_BY_CLASS = 9, 4, 6, 10, 4
SPREAD = 512
BY_HALVES = (("w", 0), ("w", 1), "g")
ROW_A, ROW_R, ROW_D, ROWS = 6, 8, 10, 12


def tile_maxout_generated_head_f5_kernel(tc, x_bytes, x_scale, w, b, e, g, a, r, d, out):
    nc = tc.nc
    V, S, G = nc.vector, nc.scalar, nc.gpsimd
    with ExitStack() as ctx:
        keep = ctx.enter_context(tc.tile_pool(name="keep", bufs=1))
        psum = ctx.enter_context(tc.psum_pool(name="psum", bufs=1))
        ctx.enter_context(tc.manual_schedule())

        def kept(name, shape, dtype):
            return keep.tile(shape, dtype, name=name, align_bytes=64)

        def block(n, width=P):
            return slice(n * width, (n + 1) * width)

        banks = {engine: [psum.tile([P, 512], F32, name=f"bank_{name}{n}") for n in range(4)] for engine, name in (("V", "vector"), ("S", "scalar"))}
        x_staged = kept("x_staged", [P, 4096], BF16)
        singles = [kept(f"single{n}", [P, 2048], BF16) for n in range(N_SINGLES)]
        raws = [kept(f"raw{n}", [P, 4096], BF16) for n in range(N_RAWS)]
        planes = [kept(f"plane{n}", [P, 4, 512], BF16) for n in range(N_PLANES)]
        wide = [kept(f"wide{n}", [P, K], BF16) for n in range(4)]
        results = [kept(f"result{n}", [P, 512], F32) for n in range(N_RESULTS)]
        by_class = [tile[:].bitcast(F32) for tile in wide] + [kept(f"by_class{n}", [P, 512], F32) for n in range(N_BY_CLASS)]
        held = {}
        owner = {}

        def take(free, key):
            held[key] = free.pop(0)
            owner[key] = free
            return held[key]

        def give(key):
            owner.pop(key).append(held[key])
            return held.pop(key)

        def hold(free, key):
            return held[key] if key in held else take(free, key)

        x_raw = [kept(f"x_raw{j}", [P, 2, K], U8) for j in range(4)]
        e_raw = [kept(f"e_raw{n}", [P, 4, D], BF16) for n in range(2)]
        mx = {}
        for key in [("w", c) for c in range(6)] + ["g"] + [(name, n) for name in ("x", "h", "v") for n in range(2)] + ["e"]:
            name = key if key in ("g", "e") else f"{key[0]}{key[1]}"
            mx[key] = kept(name + "_codes", [P, 1024], U32), kept(name + "_scales", [P, 1024], U8)
        xs = kept("xs", [P, 2, 4], F32)
        r_all = kept("r_all", [P, SPREAD], BF16)
        d_all = kept("d_all", [P, SPREAD], BF16)
        rows_raw = kept("rows_raw", [ROW_R, 512], BF16)
        rows = kept("rows", [P, 512], BF16)
        columns = kept("columns", [P, ROWS, 4], F32)
        ident = kept("ident", [P, P], F32)
        ident_bf = kept("ident_bf", [P, P], BF16)

        x_rows = x_bytes.rearrange("(p i) k -> p i k", i=8)
        out_rows = out.rearrange("(p i) c -> p i c", i=8)

        def load(tile, source):
            nc.sync.dma_start(out=tile, in_=source)

        def copy(engine, out, in_):
            if engine is V:
                nc.vector.tensor_copy(out=out, in_=in_)
            elif engine is S:
                nc.scalar.copy(out=out, in_=in_)
            else:
                nc.gpsimd.tensor_scalar(out=out, in0=in_, scalar1=1.0, scalar2=0.0, op0=MULT, op1=ADD)

        def quantize(key, words, source):
            codes, scales = mx[key]
            nc.vector.quantize_mx(out=codes[:, words].bitcast(FP8X4), scales=scales[:, words], in_=source)

        def product(bank, lhs, lhs_words, rhs, rhs_words, start, stop):
            nc.tensor.matmul_mx(
                out=bank,
                lhsT=mx[lhs][0][:, lhs_words].bitcast(FP8X4),
                lhsT_scale=mx[lhs][1][:, lhs_words],
                rhs=mx[rhs][0][:, rhs_words].bitcast(FP8X4),
                rhs_scale=mx[rhs][1][:, rhs_words],
                start=start,
                stop=stop,
            )

        def span(first, count):
            return slice(first, first + count)

        def permute_rows():
            nc.scalar.copy(
                out=rows[0:ROW_R, :].rearrange("p (t B i) -> p t B i", t=4, i=RUN),
                in_=rows_raw[:].rearrange("p (B t i) -> p t B i", t=4, i=RUN),
            )

        def columns_product(free):
            bank = take(free, "columns")
            for t in range(4):
                nc.tensor.matmul(bank[:, 16 * t : 16 * t + ROWS], lhsT=rows[:, block(t)], rhs=ident_bf[:, 0:ROWS], start=True, stop=True)

        def columns_read():
            nc.scalar.copy(out=columns[:], in_=give("columns")[:, 0:64].rearrange("p (t j) -> p j t", t=4)[:, 0:ROWS, :])

        def x_widen(i, engine):
            copy(engine, wide[i % 4][:], x_raw[i // 2][:, i % 2, :].bitcast(FP8))

        def x_turn(free, i):
            bank = take(free, ("x bank", i))
            words = wide[i % 4][:].bitcast(F32)
            for q in range(2):
                for u in range(2):
                    nc.tensor.transpose(bank[:, block(2 * u + q)], words[:, 256 * q + u : 256 * (q + 1) : 2], ident[:])

        def x_read(i):
            nc.vector.tensor_tensor(
                out=x_staged[:].rearrange("p (q i r u e) -> p i q r u e", q=2, i=4, u=2, e=2)[:, i % 4],
                in0=give(("x bank", i))[:].bitcast(BF16).rearrange("p (u q r e) -> p q r u e", u=2, q=2, e=2),
                in1=xs[:].rearrange("p q (o u e) -> p q o u e", o=1, u=2).to_broadcast([P, 2, P, 2, 2]),
                op=MULT,
            )

        def e_turn(free, n, j):
            bank = take(free, ("e bank", n, j))
            for i in range(2):
                words = e_raw[n][:, 2 * j + i, :].bitcast(F32)
                for u in range(2):
                    nc.tensor.transpose(bank[:, block(2 * i + u)], words[:, u:256:2], ident[:])

        def e_read(n, j, engine):
            copy(
                engine,
                hold(singles, ("e", n))[:].bitcast(F32)[:, block(j, 512)].rearrange("p (i r u) -> p i r u", i=2, u=2),
                give(("e bank", n, j))[:].rearrange("p (i u r) -> p i r u", i=2, u=2),
            )

        def raw_rows(tile, key, q):
            if key in BY_HALVES:
                return tile[:, block(q, 2048)].rearrange("p (s n) -> p s n", s=4)
            return tile[:].rearrange("p (s n) -> p s n", s=4)[:, :, block(q, 512)]

        def load_w(c, q):
            col = (c % J) * F + (c // J) * 512
            load(raw_rows(hold(raws, ("raw", ("w", c))), ("w", c), q), w[block(q, 512), col : col + 512].rearrange("(p s) n -> p s n", s=4))

        def load_g(f):
            load(raw_rows(hold(raws, ("raw", "g")), "g", f), g[:, block(f, 512)].rearrange("(p s) n -> p s n", s=4))

        def half_of(key, q, t):
            return q if key in BY_HALVES else t // 2

        unstaged = {}

        def raw_of(key, count):
            unstaged[key] = unstaged.get(key, 32) - count
            return held["raw", key] if unstaged[key] else give(("raw", key))

        def stage_raw(key, qs, ts, engine):
            half = half_of(key, qs.start // 4, ts.start)
            tile = hold(singles, (key, half))
            raw = raw_of(key, (qs.stop - qs.start) * (ts.stop - ts.start))
            blocks = slice(8 * qs.start, 8 * qs.stop)
            walk = "p B t i s" if engine is G else "p t B s i"
            if key in BY_HALVES:
                source = raw_rows(raw, key, qs.start // 4).rearrange(f"p s (B t i) -> {walk}", t=4, i=RUN)
                columns_of = slice(blocks.start % 32, (blocks.stop - 1) % 32 + 1)
            else:
                source = raw[:].rearrange(f"p (s B t i) -> {walk}", s=4, t=4, i=RUN)
                columns_of = blocks
            target = tile[:].rearrange(f"p (t B i s) -> {walk}", t=4 if key in BY_HALVES else 2, i=RUN, s=4)
            places, within = (slice(blocks.start - 32 * half, blocks.stop - 32 * half), ts) if key in BY_HALVES else (blocks, slice(ts.start - 2 * half, ts.stop - 2 * half))
            if engine is G:
                copy(engine, target[:, places, within], source[:, columns_of, ts])
            else:
                copy(engine, target[:, within, places], source[:, ts, columns_of])

        def pass_raw(free, key, q, j):
            bank = take(free, ("pass bank", key, q, j))[:].bitcast(BF16)
            raw = raw_of(key, 8)
            for n in range(2):
                source = raw_rows(raw, key, q).rearrange("p s (B t i) -> p t B s i", t=4, i=RUN)[:, 2 * j + n]
                target = bank[:, block(n, 512)].rearrange("p (B i s) -> p B s i", i=RUN, s=4)
                nc.tensor.matmul(target, lhsT=ident_bf[:], rhs=source, start=True, stop=True)

        def passed_read(key, q, j):
            words = hold(singles, (key, half_of(key, q, 2 * j)))[:].bitcast(F32)
            target = words.rearrange("p (j t n) -> p j t n", j=2, t=2)[:, j] if key in BY_HALVES else words.rearrange("p (t q n) -> p q t n", t=2, q=2)[:, q]
            nc.scalar.copy(out=target, in_=give(("pass bank", key, q, j))[:].rearrange("p (t n) -> p t n", t=2))

        def quantize_part(key, operand, first, last, heir, release=True):
            tile = held[key]
            if release:
                if heir:
                    held[heir] = held.pop(key)
                    owner[heir] = owner.pop(key)
                else:
                    give(key)
            base = 512 * key[-1]
            quantize(operand, slice(base + 256 * first, base + 256 * last), tile[:, 1024 * first : 1024 * last])

        def quantize_x(h, first, last, heir):
            quantize(("x", h), slice(512 * first, 512 * last), x_staged[:, 2048 * first : 2048 * last])
            if h:
                for q in range(first, last):
                    if heir and q == last - 1:
                        held[heir], owner[heir] = x_staged[:, block(q, 2048)], singles
                    else:
                        singles.append(x_staged[:, block(q, 2048)])

        def stage_plane(key, source, first, last, engine):
            tile = hold(singles, key)
            plane = give(source) if last == 4 else held[source]
            run = 1 if engine is G else 4
            copy(
                engine,
                tile[:, 512 * first : 512 * last].rearrange("p (c i t) -> p c t i", i=run, t=4),
                plane[:, :, P * first : P * last].rearrange("p t (c i) -> p c t i", i=run),
            )

        def z_parts(s, split):
            if split:
                return [(2 * (s % 2) + n, 256 * (s // 2), 256, block(n, 256)) for n in range(2)]
            return [(s, 0, 512, slice(0, 512))]

        def z_product(free, c, h, s, split):
            bank = take(free, ("z bank", c, h, s))
            for t, first, count, place in z_parts(s, split):
                for q in range(2):
                    product(bank[:, place], ("w", c), block(4 * q + t if ("w", c) in BY_HALVES else 2 * t + q), ("x", h), span(512 * q + first, count), q == 0, q == 1)

        def z_bias(c, t):
            return columns[:, 2 * (c % J) + c // J, t : t + 1]

        def z_alone(c, h, t, name):
            nc.scalar.activation(out=hold(planes, (name, c // J, h))[:, t, :], in_=give(("z bank", c, h, t))[:], func=IDENTITY, bias=z_bias(c, t))

        def z_max(c, h, s, split):
            bank = give(("z bank", c, h, s))
            for t, first, count, place in z_parts(s, split):
                part = held["max", c // J, h][:, t, span(first, count)]
                nc.vector.scalar_tensor_tensor(out=part, in0=bank[:, place], scalar=z_bias(c, t), in1=part, op0=ADD, op1=MAX)

        def z_merge(f, h, slots):
            part = held["max", f, h][:, 0:slots, :]
            nc.vector.tensor_tensor(out=part, in0=give(("aside", f, h))[:, 0:slots, :], in1=part, op=MAX)

        def v_four_slots(free, f, n, j):
            bank = take(free, ("v bank", f, n, j))
            for t in range(4):
                product(bank[:, block(t)], "g", block(4 * f + t), "e", span(512 * n + P * j, P), True, True)

        def v_read_staged(f, n, j):
            nc.vector.tensor_tensor(
                out=hold(singles, ("v", n, f))[:, block(j, 512)].rearrange("p (c t) -> p c t", t=4),
                in0=give(("v bank", f, n, j))[:].rearrange("p (t c) -> p c t", t=4),
                in1=columns[:, ROW_A + f : ROW_A + f + 1, :].to_broadcast([P, P, 4]),
                op=ADD,
            )

        def v_by_slot(free, f, n, t):
            product(take(free, ("v slot bank", f, n, t))[:], "g", block(4 * f + t), "e", block(n, 512), True, True)

        def v_read_plane(f, n, t):
            nc.scalar.activation(out=hold(planes, ("v plane", f, n))[:, t, :], in_=give(("v slot bank", f, n, t))[:], func=IDENTITY, bias=columns[:, ROW_A + f, t : t + 1])

        def direct_product(free, i, n):
            bank = take(free, ("direct bank", i, n))
            for f in range(2):
                product(bank[:], ("h", i // 4), span(512 * f + P * (i % 4), P), ("v", n), block(f, 512), f == 0, f == 1)

        def spread_cols(n, cols):
            return slice(cols.start + 512 * n - (C - SPREAD), cols.stop + 512 * n - (C - SPREAD))

        def direct_scale(i, n, cols):
            bank = give(("direct bank", i, n)) if cols.stop == 512 else held["direct bank", i, n]
            nc.vector.tensor_tensor(out=hold(results, ("result", i, n))[:, cols], in0=bank[:, cols], in1=r_all[:, spread_cols(n, cols)], op=MULT)

        def spread_d(free):
            nc.tensor.matmul(take(free, "d bank")[:], lhsT=ident_bf[:, ROW_D + 1 : ROW_D + 2].to_broadcast([P, P]), rhs=rows[:], start=True, stop=True)

        def direct_shift(i, n, cols, engine):
            part = held["result", i, n][:, cols]
            if engine is V and "d bank" in held:
                nc.vector.tensor_tensor(out=part, in0=held["d bank"][:, cols], in1=part, op=ADD)
            else:
                engine.tensor_tensor(out=part, in0=part, in1=d_all[:, spread_cols(n, cols)], op=ADD)

        def shift_into_heir(i, n):
            target = held.pop(("sum", i, n))[:].bitcast(F32)[:, 512:1024]
            nc.gpsimd.tensor_tensor(out=target, in0=give(("result", i, n))[:], in1=d_all[:, spread_cols(n, slice(0, 512))], op=ADD)
            held["result", i, n], owner["result", i, n] = target, []

        def store(i, n, cols):
            tile = give(("result", i, n)) if cols.stop == 512 else held["result", i, n]
            nc.sync.dma_start(out=out_rows[:, i, 512 * n + cols.start : 512 * n + cols.stop], in_=tile[:, cols])

        def class_parts(tiles, m):
            if len(tiles) == 2:
                return [(2 * m + k, block(k, 256)) for k in range(2)]
            return [(m, slice(0, 512))]

        def class_product(free, tiles, n, m):
            bank = take(free, ("class bank", tiles, n, m))
            for k, place in class_parts(tiles, m):
                for f in range(2):
                    product(bank[:, place], ("v", n), span(512 * f + P * k, P), ("h", tiles[0] // 4), span(512 * f + P * (tiles[0] % 4), P * len(tiles)), f == 0, f == 1)

        def class_read(tiles, n, m):
            bank = give(("class bank", tiles, n, m))
            tile = take(by_class, ("by class", tiles, n, m))
            for k, place in class_parts(tiles, m):
                nc.scalar.activation(out=tile[:, place], in_=bank[:, place], func=IDENTITY, scale=columns[:, ROW_R + n, k : k + 1], bias=columns[:, ROW_D + n, k : k + 1])

        def turn_back(free, tiles, i, n):
            bank = take(free, ("turned bank", i, n))
            for m in range(len(tiles)):
                for k, place in class_parts(tiles, m):
                    nc.tensor.transpose(bank[:, block(k)], held["by class", tiles, n, m][:, span(place.start + P * (i - tiles[0]), P)], ident[:])
            if i == tiles[-1]:
                for m in range(len(tiles)):
                    give(("by class", tiles, n, m))

        def turned_read(i, n, engine):
            copy(engine, take(results, ("result", i, n))[:], give(("turned bank", i, n))[:])

        def warm_up(count):
            for n in range(count):
                nc.tensor.matmul(banks["S"][-1][:, 0:256], lhsT=ident[:].bitcast(BF16)[:, 0:P], rhs=ident[:].bitcast(BF16), start=True, stop=True)

        def step(*call, makes=(), needs=(), lender=None, feed=None):
            return call, list(makes), list(needs), lender, feed

        def read(engine, *call, makes=(), needs=(), feed, feed_needs, lender=None):
            free = banks["V" if engine is V else "S"]
            return step(*call, makes=makes, needs=list(needs) + [feed], lender=lender, feed=step(feed[0], free, *feed[1:], makes=[feed], needs=feed_needs, lender=free))

        def feeds(steps):
            return [feed for call, makes, needs, lender, feed in steps]

        def parts(key, first=0, last=4):
            return [(key, n) for n in range(first, last)]

        def cells(key, qs, ts):
            return [(key, q, t) for q in range(qs.start, qs.stop) for t in range(ts.start, ts.stop)]

        def stage(engine, key, first, last, q=None, inherited=False, eighths=(0, 8)):
            qs, ts = slice(*eighths) if q is None else slice(4 * q, 4 * q + 4), slice(first, last)
            needs = [("raw", key, n // 4) for n in range(qs.start, qs.stop)] + [("inherited", (key, half_of(key, qs.start // 4, first)))] * inherited
            return step(stage_raw, key, qs, ts, engine, makes=cells(key, qs, ts), needs=needs, lender=None if inherited else singles)

        def passed(key, q, j, inherited=False):
            qs, ts = slice(4 * q, 4 * q + 4), slice(2 * j, 2 * j + 2)
            return read(S, passed_read, key, q, j, makes=cells(key, qs, ts), needs=[("inherited", (key, half_of(key, q, 2 * j)))] * inherited, lender=None if inherited else singles, feed=(pass_raw, key, q, j), feed_needs=[("raw", key, q)])

        def quant_w(key, half, heir=None):
            return step(quantize_part, (key, half), key, 0, 2, heir, makes=parts(("codes", key), 2 * half, 2 * half + 2) + [("inherited", heir)], needs=cells(key, slice(0, 8), slice(2 * half, 2 * half + 2)))

        def quant_pass(key, q, heir=None):
            return step(quantize_part, (key, q), key, 0, 2, heir, makes=[("pass codes", key, q), ("inherited", heir)], needs=cells(key, slice(4 * q, 4 * q + 4), slice(0, 4)))

        def quant_g(f, heir=None):
            return step(quantize_part, ("g", f), "g", 0, 2, heir, makes=[("g codes", f), ("inherited", heir)], needs=cells("g", slice(4 * f, 4 * f + 4), slice(0, 4)))

        def quant_x(h, first=0, last=2, heir=None):
            return step(quantize_x, h, first, last, heir, makes=parts(("codes", ("x", h)), first, last) + [("inherited", heir)], needs=parts(("x read", h)))

        def quant(key, first=0, last=2, heir=None, home=None, release=None):
            operand = "e" if key[0] == "e" else key[0:2]
            return step(quantize_part, (home,) + key[1:] if home else key, operand, first, last, heir, last == 2 if release is None else release, makes=parts(("codes", key), first, last) + [("inherited", heir)], needs=parts(key, 2 * first, 2 * last))

        def codes(key, first=0, last=2):
            return parts(("codes", key), first, last)

        def stage_h(engine, h, f, first=0, last=4, split=False, inherited=False, home="h"):
            key = ("h", h, f)
            needs = parts(("max", J * f + J - 1, h), 0, last if split else 4) + parts(key, 0, first) + [("inherited", (home, h, f))] * inherited
            return step(stage_plane, (home, h, f), ("max", f, h), first, last, engine, makes=parts(key, first, last), needs=needs)

        def stage_v(engine, n, f, first=0, last=4, inherited=False):
            key = ("v", n, f)
            needs = parts(("v plane", f, n)) + parts(key, 0, first) + [("inherited", key)] * inherited
            return step(stage_plane, key, ("v plane", f, n), first, last, engine, makes=parts(key, first, last), needs=needs)

        def z_steps(c, h, aside=0, split=False):
            steps = []
            for s in range(4):
                slots = (2 * (s % 2), 2 * (s % 2) + 2) if split else (s, s + 1)
                weights = [("pass codes", ("w", c), q) for q in range(2)] if ("w", c) in BY_HALVES else codes(("w", c), *slots)
                operands = weights + codes(("x", h))
                if c % J == 0 or s < aside:
                    how = "aside" if c % J else "max"
                    steps.append(read(S, z_alone, c, h, s, how, makes=[((how, c, h), s)], needs=["columns"], feed=(z_product, c, h, s, False), feed_needs=operands))
                else:
                    needs = parts(("max", c - 1, h)) if split else [(("max", c - 1, h), s)]
                    steps.append(read(V, z_max, c, h, s, split, makes=[(("max", c, h), s)], needs=needs, feed=(z_product, c, h, s, split), feed_needs=operands))
            return steps

        def merge(c, h, slots):
            return step(z_merge, c // J, h, slots, makes=parts(("max", c, h), 0, slots), needs=parts(("aside", c, h), 0, slots) + parts(("max", c - 1, h), 0, slots))

        def v_low(f, n):
            return [read(V, v_read_staged, f, n, j, makes=[(("v", n, f), j)], needs=["columns"], feed=(v_four_slots, f, n, j), feed_needs=[("g codes", f)] + codes(("e", n))) for j in range(4)]

        def v_high(f, n):
            return [read(S, v_read_plane, f, n, t, makes=[(("v plane", f, n), t)], needs=["columns"], feed=(v_by_slot, f, n, t), feed_needs=[("g codes", f)] + codes(("e", n))) for t in range(4)]

        def h_codes(tiles):
            h = tiles[0] // 4
            return [(("codes", ("h", h, f)), part) for f in range(2) for part in sorted(set(i % 4 // 2 for i in tiles))]

        def v_codes(n):
            return codes(("v", n, 0)) + codes(("v", n, 1))

        WHOLE = slice(0, 512)

        def scaled(i, n, cols=WHOLE):
            if cols.start:
                return step(direct_scale, i, n, cols, makes=[("scaled", i, n, cols.start)], needs=[("scaled", i, n, 0)])
            return read(V, direct_scale, i, n, cols, makes=[("scaled", i, n, 0)], needs=["r and d"], lender=results, feed=(direct_product, i, n), feed_needs=h_codes((i,)) + v_codes(n))

        def shifted(engine, i, n, cols=WHOLE, after_d=False):
            return step(direct_shift, i, n, cols, engine, makes=[("done", i, n, cols.start)], needs=[("scaled", i, n, cols.start)] + ["d bank"] * after_d)

        def shifted_heir(i, n):
            return step(shift_into_heir, i, n, makes=[("done", i, n, 0)], needs=[("scaled", i, n, 0), ("inherited", ("sum", i, n))])

        def stored(i, n, cols=WHOLE):
            return step(store, i, n, cols, needs=[("done", i, n, cols.start)])

        def classes(tiles, n):
            return [read(S, class_read, tiles, n, m, makes=[(("by class", tiles, n), m)], lender=by_class, feed=(class_product, tiles, n, m), feed_needs=h_codes(tiles) + v_codes(n)) for m in range(len(tiles))]

        def turned(tiles, n, engine=S):
            return [read(engine, turned_read, i, n, engine, makes=[("done", i, n, 0)], lender=results, feed=(turn_back, tiles, i, n), feed_needs=parts(("by class", tiles, n), 0, len(tiles))) for i in tiles]

        def loads_w(c):
            return [step(load_w, c, q, makes=[("raw", ("w", c), q)], lender=None if q else raws) for q in range(2)]

        def load_x(first, last):
            return step(load, x_raw[first // 2][:, first % 2 : first % 2 + last - first, :], x_rows[:, first:last, :], makes=[("x raw", i) for i in range(first, last)])

        def load_e(n):
            return step(load, e_raw[n][:], e[block(n, 512), :].rearrange("(i p) k -> p i k", p=P), makes=[("e raw", n)])

        def widen(engine, *tiles):
            return [step(x_widen, i, engine, makes=[("wide", i)], needs=[("x raw", i)] + [(x_turn, i - 4)] * (i >= 4)) for i in tiles]

        def last_first(steps):
            return steps[-1:] + steps[:-1]

        def pairs(steps):
            return [steps[n ^ 1] for n in range(len(steps))]

        x_reads = [read(V, x_read, i, makes=[(("x read", i // 4), i % 4)], needs=parts(("codes", ("x", 0)), 0, 2 * (i // 4)), feed=(x_turn, i), feed_needs=[("wide", i)]) for i in range(8)]
        column_read = [read(S, columns_read, makes=["columns"], feed=(columns_product,), feed_needs=["rows"])]
        small_loads = [step(load, rows_raw[0:4, :], b[0:2048].rearrange("(c n) -> c n", n=512)), step(load, rows_raw[4:ROW_A, :], b[2048:3072].rearrange("(c n) -> c n", n=512))]
        small_loads += [step(load, rows_raw[ROW_A:ROW_R, :], a.rearrange("(c n) -> c n", n=512))]
        small_loads += [step(load, rows[row : row + 2, :], vector.rearrange("(o n) -> o n", o=2), makes=[("row", row)]) for row, vector in ((ROW_R, r), (ROW_D, d))]
        load_xs = step(load, xs[:], x_scale.rearrange("o (q p t) -> p (o q) t", q=2, t=4), makes=["xs"])
        load_rd = [step(load, r_all[:], r[C - SPREAD : C].partition_broadcast(P)), step(load, d_all[:], d[C - SPREAD : C].partition_broadcast(P), makes=["r and d"])]
        g_loads = [step(load_g, f, makes=[("raw", "g", f)], lender=None if f else raws) for f in range(2)]

        def e_reads(n, engine):
            return [read(engine, e_read, n, j, engine, makes=parts(("e", n), 2 * j, 2 * j + 2), feed=(e_turn, n, j), feed_needs=[("e raw", n)]) for j in range(2)]

        def W(c):
            return ("w", c)

        z = {(c, h): z_steps(c, h, split=c == 5) for c in range(6) for h in range(2)}
        z[4, 1] = z_steps(4, 1, aside=2)
        e0, e1 = e_reads(0, S), e_reads(1, V)
        vl = [v_low(f, 0) for f in range(2)]
        vh = [v_high(f, 1) for f in range(2)]
        TURNED = [((0, 1), 0), ((2, 3), 0), ((4, 5), 0), ((6, 7), 0)]
        cl = [classes(*unit) for unit in TURNED]
        tu = [turned(*unit) for unit in TURNED]
        sc = {i: scaled(i, 1) for i in range(8)}
        HALF = (slice(0, 256), slice(256, 512))

        def late_first(steps):
            return steps[2:] + steps[:2]

        p0, p1, pg = passed(W(1), 0, 1), passed(W(1), 1, 1), passed("g", 1, 0)
        gpsimd_lane = [
            stage(G, W(0), 0, 3, q=0), stage(G, W(0), 2, 4, q=1),
            stage(G, W(1), 0, 2, q=1, inherited=True),
            stage(G, W(2), 2, 4, inherited=True), stage(G, W(2), 0, 2, eighths=(5, 8)),
            stage(G, W(3), 2, 4, inherited=True), stage(G, W(4), 2, 4), stage(G, W(4), 1, 2),
            stage(G, W(5), 2, 4, inherited=True), stage(G, W(5), 1, 2),
            stage_v(G, 1, 0, inherited=True), stage_v(G, 1, 1, last=2),
            stage_h(G, 1, 0, first=2, inherited=True, home="late h"), stage_h(G, 1, 1, last=2, split=True), shifted_heir(1, 1), shifted(G, 4, 1),
        ]
        scalar_lane = (
            widen(S, 3) + [stage(S, W(0), 3, 4, q=0)] + widen(S, 4, 5) + [stage(S, W(0), 0, 2, q=1), stage(S, W(1), 0, 2, q=0), p0]
            + widen(S, 6) + [step(permute_rows, makes=["rows"], needs=[("row", ROW_D)])] + widen(S, 7) + [p1] + column_read + z[0, 0] + [stage(S, W(2), 0, 2, eighths=(0, 5)), stage(S, "g", 0, 4, q=0)] + e0 + [stage(S, W(3), 0, 2), pg]
            + z[0, 1][:2] + [stage(S, "g", 2, 4, q=1)] + z[0, 1][2:] + [stage(S, W(4), 0, 1), stage_h(S, 0, 0), stage(S, W(5), 0, 1)]
            + late_first(z[3, 0]) + z[3, 1] + vh[0] + vh[1]
            + [stage_v(S, 1, 1, first=2)] + z[4, 1][:2] + [stage_h(S, 0, 1, last=2, split=True), stage_h(S, 0, 1, first=2), stage_h(S, 1, 0, last=2)]
            + cl[0] + cl[1] + tu[0] + [stage_h(S, 1, 1, first=2)] + tu[1] + cl[2] + tu[2] + cl[3] + tu[3]
        )
        vector_lane = (
            widen(V, 0, 1, 2) + x_reads[0:4]
            + [quant_pass(W(0), 0), quant_x(0), quant_pass(W(0), 1), quant_pass(W(1), 0, heir=(W(1), 1))]
            + x_reads[4:6] + [quant_pass(W(1), 1, heir=(W(2), 1))] + x_reads[6:8] + z[1, 0]
            + [quant_w(W(2), 0), quant_w(W(2), 1), quant_x(1), quant(("e", 0), heir=(W(3), 1)), quant_g(0)]
            + z[2, 0] + vl[0] + z[1, 1] + e1
            + [quant_w(W(3), 1), quant_w(W(3), 0), quant_g(1), quant_w(W(4), 0), quant(("e", 1), heir=(W(5), 1)), quant_w(W(4), 1)]
            + z[2, 1] + vl[1]
            + [quant_w(W(5), 1), quant_w(W(5), 0), quant(("v", 0, 0)), quant(("h", 0, 0), heir=("v", 1, 0)), quant(("v", 0, 1))]
            + z[4, 0] + z[5, 0]
            + z[4, 1][2:] + [quant(("h", 0, 1), last=1), quant(("v", 1, 0)), quant(("h", 0, 1), first=1), merge(4, 1, 2), quant(("v", 1, 1), heir=("late h", 1, 0))]
            + z[5, 1] + [sc[0], sc[1], shifted(V, 0, 1), quant(("h", 1, 0), last=1, release=True), quant(("h", 1, 1), last=1), quant(("h", 1, 0), first=1, home="late h"), quant(("h", 1, 1), first=1, heir=("sum", 1, 1)), sc[2], sc[3], shifted(V, 2, 1, after_d=True), shifted(V, 3, 1, after_d=True)]
            + [sc[4], sc[5], sc[6], shifted(V, 5, 1, after_d=True), shifted(V, 6, 1, after_d=True), sc[7], shifted(V, 7, 1, after_d=True)]
        )
        tensor_lane = feeds(
            x_reads[0:6] + [p0, p1] + z[0, 0][:1] + column_read + z[0, 0][1:2] + x_reads[6:8] + z[0, 0][2:]
            + z[1, 0] + e0 + [pg] + z[2, 0] + z[0, 1][:2] + vl[0][:2] + z[0, 1][2:] + vl[0][2:] + z[1, 1] + e1 + z[2, 1]
            + late_first(z[3, 0]) + z[3, 1][:3] + vl[1][:2] + z[3, 1][3:] + vl[1][2:] + vh[0] + z[4, 0][:2] + vh[1][:2] + z[4, 0][2:3] + vh[1][2:] + z[4, 0][3:]
            + z[4, 1][:2] + z[5, 0] + z[4, 1][2:] + z[5, 1] + cl[0] + cl[1] + tu[0] + [sc[0], sc[1]] + tu[1] + [sc[2], sc[3]] + cl[2] + [sc[4], sc[5]] + tu[2] + [sc[6]] + cl[3] + [sc[7]] + tu[3]
        )
        place = tensor_lane.index(feeds(tu[1])[0])
        tensor_lane = tensor_lane[:place] + [step(spread_d, banks["S"], makes=["d bank"], lender=banks["S"])] + tensor_lane[place:]
        sync_lane = (
            [load_x(0, 2), load_xs, load_x(2, 4)] + loads_w(0)[:1] + [load_x(4, 6)] + loads_w(0)[1:] + loads_w(1) + [load_x(6, 8)] + small_loads + loads_w(2) + [g_loads[0], load_e(0), g_loads[1]]
            + loads_w(3) + loads_w(4) + [load_e(1)] + loads_w(5) + load_rd
            + [stored(0, 0), stored(1, 0), stored(0, 1), stored(2, 0), stored(3, 0), stored(2, 1), stored(3, 1), stored(1, 1), stored(4, 0), stored(5, 0), stored(5, 1), stored(4, 1)]
            + [stored(6, 1), stored(6, 0), stored(7, 1), stored(7, 0)]
        )

        make_identity(nc, ident[:])
        nc.vector.memset(rows[:], 0.0)
        nc.scalar.activation(out=ident_bf[:], in_=ident[:], func=IDENTITY)

        lanes = [sync_lane, tensor_lane, vector_lane, scalar_lane, gpsimd_lane]
        made = set()
        while any(lanes):
            fresh = []
            moved = False
            for lane in lanes:
                allowed = len(lane) if lane is sync_lane or lane is tensor_lane else 1
                while allowed and lane and all(name in made for name in lane[0][2]) and lane[0][3] != []:
                    call, makes, needs, lender, feed = lane.pop(0)
                    call[0](*call[1:])
                    fresh.extend(makes)
                    allowed = allowed - 1
                    moved = True
            assert moved, [(lane[0][0][0], lane[0][0][1:], [name for name in lane[0][2] if name not in made]) for lane in lanes if lane]
            for name in fresh:
                made.add(name)
